import numpy as np
import ml_dtypes


def mxq(x, axis, fmt="e4m3"):
    dtype, down = {"e4m3": (ml_dtypes.float8_e4m3fn, 7), "e5m2": (ml_dtypes.float8_e5m2, 14)}[fmt]
    v = np.moveaxis(np.asarray(x, np.float32).astype(ml_dtypes.bfloat16).astype(np.float64), axis, -1)
    blocks = v.reshape(v.shape[:-1] + (-1, 32))
    amax = np.abs(blocks).max(-1, keepdims=True)
    byte = np.maximum(np.where(amax > 0, np.frexp(amax)[1] - 1 + 127, 0) - down, 1)
    scale = np.exp2(byte - 127.0)
    codes = (blocks / scale).astype(np.float32).astype(dtype).astype(np.float64)
    return np.moveaxis((codes * scale).reshape(v.shape), -1, axis)


WIDE = False


def mx_kscale(k):
    if not WIDE:
        return np.ones(k)
    levels = np.array([24, -24, 12, -12, 0])
    if k % 512:
        return np.exp2(np.random.permutation(np.resize(levels, k // 32))).repeat(32)
    a = np.empty((k // 512, 16))
    for p in range(k // 512):
        a[p, :8] = np.random.permutation(np.resize(levels, 8))
        for g in range(8):
            far = levels[np.abs(levels - a[p, g]) >= 10]
            a[p, g + 8] = far[np.random.randint(len(far))]
    return np.exp2(a.ravel()).repeat(32)


def f64(x):
    return np.asarray(x).astype(np.float64)


def striped(idx):
    return np.tile(idx.reshape(-1, 16).T, (8, 1)).astype(np.uint16)


def unstriped(offs):
    return offs[:16].T.reshape(-1).astype(np.int64)


E2M1 = np.array([0.0, 0.5, 1.0, 1.5, 2.0, 3.0, 4.0, 6.0, -0.0, -0.5, -1.0, -1.5, -2.0, -3.0, -4.0, -6.0])


def pack_weight(w, fmt):
    k, n = w.shape
    w = f64(np.asarray(w, np.float32).astype(ml_dtypes.bfloat16)).reshape(k // 32, 32, n)
    amax = np.abs(w).max(1)
    if fmt == "e4m3":
        byte = np.frexp(amax)[1] - 1 + 127 - 7
    else:
        mant, ex = np.frexp(amax / 6.0)
        byte = np.where(mant > 0.5, ex, ex - 1) + 127
    byte = np.clip(np.where(amax > 0, byte, 1), 1, 254)
    scaled = (w * np.exp2(127.0 - byte)[:, None, :]).reshape(k, n).astype(np.float32)
    by_word = np.ascontiguousarray(scaled.reshape(k // 512, 128, 4, n).transpose(0, 1, 3, 2))
    if fmt == "e4m3":
        words = by_word.astype(ml_dtypes.float8_e4m3fn).view(np.uint8)
    else:
        c = by_word.astype(ml_dtypes.float4_e2m1fn).view(np.uint8) & 0xF
        words = (c[..., 0::2] | (c[..., 1::2] << 4)).reshape(k // 512, 128, 2 * n)
    return np.ascontiguousarray(words), np.ascontiguousarray(byte.astype(np.uint8).reshape(k // 512, 16, n))


def unpack_weight(words, scales, fmt):
    g, _, n = scales.shape
    words = np.ascontiguousarray(words).reshape(g, 128, n, -1)
    if fmt == "e4m3":
        vals = words.view(ml_dtypes.float8_e4m3fn).astype(np.float64)
    else:
        nib = np.empty((g, 128, n, 4), np.uint8)
        nib[..., 0::2] = words & 0xF
        nib[..., 1::2] = words >> 4
        vals = E2M1[nib]
    vals = vals * np.repeat(np.exp2(scales.astype(np.float64) - 127.0), 8, axis=1)[..., None]
    return vals.transpose(0, 1, 3, 2).reshape(g * 512, n)


def pack_table4(v):
    words, scales = pack_weight(v, "e2m1")
    g, t = words.shape[0] // 2, v.shape[1]
    return np.ascontiguousarray(words.reshape(g, 2, 128, t, 2).transpose(0, 2, 3, 1, 4).reshape(g, 128, t, 4)), scales


def unpack_table4(words, scales):
    g, _, t, _ = words.shape
    return unpack_weight(words.reshape(g, 128, t, 2, 2).transpose(0, 3, 1, 2, 4).reshape(2 * g, 128, 2 * t), scales, "e2m1")


def sigm(f):
    return 1.0 / (1.0 + np.exp(-np.maximum(f, -700.0)))


K, R, N, T, J = 1024, 1024, 512, 2048, 1024


def setup_inputs():
    n = np.random.standard_normal
    s = mx_kscale(K)[:, None]
    u = mx_kscale(R)[:, None]
    wd = n((R, N)) / np.sqrt(R) / u
    wd4 = pack_weight(wd, "e2m1")
    wdrest = wd - unpack_weight(*wd4, "e2m1")
    p_tab = pack_table4(n((K, T)) * s)
    p_wg = pack_weight(n((K, R)) / np.sqrt(K) / s, "e2m1")
    p_wd8 = pack_weight(wdrest, "e4m3")
    return {
        "tab_words": p_tab[0],
        "tab_scales": p_tab[1],
        "wg_words": p_wg[0],
        "wg_scales": p_wg[1],
        "wu": (n((K, R)) / np.sqrt(K) / s * u.T).astype(np.float32),
        "wd4_words": wd4[0],
        "wd4_scales": wd4[1],
        "wd8_words": p_wd8[0],
        "wd8_scales": p_wd8[1],
        "b": (0.3 * n(N)).astype(np.float32),
        "wgo": np.tile(np.random.uniform(0.5, 2.0, J), (128, 1)).astype(np.float32),
        "offs": striped(np.random.permutation(T)[:J]),
    }


def reference(tab_words, tab_scales, wg_words, wg_scales, wu, wd4_words, wd4_scales, wd8_words, wd8_scales, b, wgo, offs):
    idx = unstriped(offs)
    tab_ = unpack_table4(tab_words, tab_scales)[:, idx]
    wg_ = unpack_weight(wg_words, wg_scales, "e2m1")
    wu_ = mxq(f64(wu), 0, "e4m3")
    ga = wg_.T @ tab_
    ub = wu_.T @ tab_
    h = sigm(ga) * ub
    h_ = mxq(h, 0, "e4m3")
    wd4_ = unpack_weight(wd4_words, wd4_scales, "e2m1")
    wd8_ = unpack_weight(wd8_words, wd8_scales, "e4m3")
    y = wd4_.T @ h_ + wd8_.T @ h_
    out = np.zeros((N, T))
    out[:, idx] = f64(wgo)[0] * (y + f64(b)[:, None])
    return out

@@ -1,0 +1,222 @@
+from contextlib import ExitStack
+
+import concourse.mybir as mybir
+
+K, R, N, T, J = 1024, 1024, 512, 2048, 1024
+FLOPS = 2 * J * (2 * K * R + 2 * R * N)
+
+F32 = mybir.dt.float32
+BF16 = mybir.dt.bfloat16
+I32 = mybir.dt.int32
+U32 = mybir.dt.uint32
+U16 = mybir.dt.uint16
+U8 = mybir.dt.uint8
+FP8X4 = mybir.dt.float8_e4m3fn_x4
+FP4X4 = mybir.dt.float4_e2m1fn_x4
+ACT = mybir.ActivationFunctionType
+MULT = mybir.AluOpType.mult
+
+P = 128
+GATHER = 256
+HALF = 512
+
+
+def tile_list_modp_gsigm_res_noneb_kernel(
+    tc, tab_words, tab_scales, wg_words, wg_scales, wu, wd4_words, wd4_scales, wd8_words, wd8_scales, b, wgo, offs, out
+):
+    nc = tc.nc
+    with ExitStack() as ctx:
+        keep = ctx.enter_context(tc.tile_pool(name="keep", bufs=1))
+        ring = ctx.enter_context(tc.tile_pool(name="ring", bufs=3))
+        psum = ctx.enter_context(tc.psum_pool(name="psum", bufs=3))
+        psum_y = ctx.enter_context(tc.psum_pool(name="psum_y", bufs=2))
+
+        def held(name, shape, dtype):
+            return keep.tile(shape, dtype, name=name, align_bytes=64)
+
+        offsets = keep.tile([P, J // 16], U16, name="offsets")
+        nc.sync.dma_start(offsets[:], offs)
+
+        def load_scales(name, src):
+            width = src.shape[2]
+            plane = held(name, [P, 2, width // 4], I32)
+            nc.vector.memset(plane[:], 0)
+            for q in range(4):
+                nc.sync.dma_start(
+                    out=plane[32 * q : 32 * q + 4, :, :],
+                    in_=src[:, 4 * q : 4 * q + 4, :].rearrange("a r x -> r a x").bitcast(I32),
+                )
+            return plane[:].bitcast(U8)
+
+        warm_in = held("warm_in", [P, 8], F32)
+        warm_out = held("warm_out", [P, 8], F32)
+        nc.gpsimd.memset(warm_in[:], 0.0)
+        nc.scalar.activation(out=warm_out[:], in_=warm_in[:], func=ACT.Sigmoid)
+
+        wg_raw = held("wg_raw", [P, 2, R // 2], I32)
+        nc.sync.dma_start(out=wg_raw[:], in_=wg_words.rearrange("a p x -> p a x").bitcast(I32))
+        tab_w = held("tab_w", [P, T], I32)
+        nc.sync.dma_start(out=tab_w[:], in_=tab_words[0].rearrange("p t x -> p (t x)").bitcast(I32))
+        tab_s = load_scales("tab_s", tab_scales)
+        wg_s_raw = load_scales("wg_s_raw", wg_scales)
+
+        wu_raw = {}
+        for rb in range(2):
+            for a in range(2):
+                raw = held(f"wu_raw{rb}{a}", [P, 4, 512], F32)
+                nc.sync.dma_start(
+                    out=raw[:],
+                    in_=wu[512 * a : 512 * (a + 1), 512 * rb : 512 * (rb + 1)].rearrange("(p j) c -> p j c", j=4),
+                )
+                wu_raw[rb, a] = raw
+
+        wd4_s = load_scales("wd4_s", wd4_scales)
+        wd8_s = load_scales("wd8_s", wd8_scales)
+        wd4_w = held("wd4_w", [P, 2, N // 2], I32)
+        nc.sync.dma_start(out=wd4_w[:], in_=wd4_words.rearrange("a p x -> p a x").bitcast(I32))
+        wd8_w = held("wd8_w", [P, 2, N], I32)
+        nc.sync.dma_start(out=wd8_w[:], in_=wd8_words.rearrange("a p n x -> p a (n x)").bitcast(I32))
+        bias = held("bias", [P, N // P], F32)
+        with nc.allow_non_contiguous_dma(reason="one bias value a partition"):
+            nc.sync.dma_start(out=bias[:], in_=b.rearrange("(c p) -> p c", p=P))
+        weight = held("weight", [P, J], F32)
+        nc.sync.dma_start(out=weight[:], in_=wgo)
+
+        wg_w, wg_s, wu_w, wu_s, tok_w, tok_s = {}, {}, {}, {}, {}, {}
+        h_w = {(rb, c): held(f"h_w{rb}{c}", [P, HALF], U32) for rb in range(2) for c in range(2)}
+        h_s = {(rb, c): held(f"h_s{rb}{c}", [P, HALF], U8) for rb in range(2) for c in range(2)}
+
+        def permute_wg(rb):
+            cols = slice(512 * rb, 512 * (rb + 1))
+            words = held(f"wg_w{rb}", [P, 2, 4, 2 * P], U8)
+            nc.vector.tensor_copy(
+                out=words[:].bitcast(U16),
+                in_=wg_raw[:].bitcast(U16)[:, :, cols].rearrange("p a (m t) -> p a t m", t=4),
+            )
+            scales = held(f"wg_s{rb}", [P, 2, 4, P], U8)
+            nc.vector.tensor_copy(out=scales[:], in_=wg_s_raw[:, :, cols].rearrange("p a (m t) -> p a t m", t=4))
+            wg_w[rb], wg_s[rb] = words, scales
+
+        def quantize_wu(rb):
+            for a in range(2):
+                grouped = ring.tile([P, 4, P, 4], BF16, name="wu_grouped", align_bytes=64)
+                source = wu_raw[rb, a][:].rearrange("p j (m t) -> p m j t", t=4)
+                for t0 in (0, 2):
+                    nc.scalar.copy(
+                        out=grouped[:, t0 : t0 + 2, :, :].rearrange("p t m j -> p m j t"),
+                        in_=source[:, :, :, t0 : t0 + 2],
+                    )
+                words = held(f"wu_w{rb}{a}", [P, 512], U32)
+                scales = held(f"wu_s{rb}{a}", [P, 512], U8)
+                nc.vector.quantize_mx(
+                    out=words[:].bitcast(FP8X4), scales=scales[:], in_=grouped[:].rearrange("p t m j -> p (t m j)")
+                )
+                wu_w[rb, a], wu_s[rb, a] = words, scales
+
+        def gather_tokens(g):
+            listed = offsets[:, g * GATHER // 16 : (g + 1) * GATHER // 16]
+            both = held(f"tok_both{g}", [P, GATHER], U32)
+            nc.vector.tensor_copy(both[:], tab_w[:].bitcast(U32).indirect(listed))
+            scales = held(f"tok_s{g}", [P, 2, GATHER], U8)
+            for a in range(2):
+                nc.vector.tensor_copy(scales[:, a, :], tab_s[:, a, :].indirect(listed))
+            words = held(f"tok_w{g}", [P, 2, 2 * GATHER], U8)
+            nc.vector.tensor_copy(
+                out=words[:].bitcast(U16), in_=both[:].bitcast(U16).rearrange("p (j a) -> p a j", a=2)
+            )
+            tok_w[g], tok_s[g] = words, scales
+
+        def hidden(rb, g):
+            h = ring.tile([P, GATHER, 4], BF16, name="h", align_bytes=64)
+            for j0 in range(0, GATHER, P):
+                rhs = [tok_w[g][:, a, 2 * j0 : 2 * (j0 + P)].bitcast(FP4X4) for a in range(2)]
+                rhs_s = [tok_s[g][:, a, j0 : j0 + P] for a in range(2)]
+                ga = psum.tile([P, 4, P], F32, name="ga")
+                for t in range(4):
+                    for a in range(2):
+                        nc.tensor.matmul_mx(
+                            out=ga[:, t, :], lhsT=wg_w[rb][:, a, t, :].bitcast(FP4X4), lhsT_scale=wg_s[rb][:, a, t, :],
+                            rhs=rhs[a], rhs_scale=rhs_s[a], start=(a == 0), stop=(a == 1),
+                        )
+                gate = keep.tile([P, P, 4], F32, name=f"gate{rb}_{g}_{j0}")
+                nc.scalar.activation(out=gate[:], in_=ga[:].rearrange("p t j -> p j t"), func=ACT.Sigmoid)
+                ub = psum.tile([P, 4, P], F32, name="ub")
+                for t in range(4):
+                    cols = slice(P * t, P * (t + 1))
+                    for a in range(2):
+                        nc.tensor.matmul_mx(
+                            out=ub[:, t, :], lhsT=wu_w[rb, a][:, cols].bitcast(FP8X4), lhsT_scale=wu_s[rb, a][:, cols],
+                            rhs=rhs[a], rhs_scale=rhs_s[a], start=(a == 0), stop=(a == 1),
+                        )
+                nc.vector.tensor_tensor(h[:, j0 : j0 + P, :], ub[:].rearrange("p t j -> p j t"), gate[:], MULT)
+            c, j0 = divmod(g * GATHER, HALF)
+            nc.vector.quantize_mx(
+                out=h_w[rb, c][:, j0 : j0 + GATHER].bitcast(FP8X4),
+                scales=h_s[rb, c][:, j0 : j0 + GATHER],
+                in_=h[:].rearrange("p j t -> p (j t)"),
+            )
+
+        y_sb = {}
+
+        def down(c):
+            for n in range(N // P):
+                y = psum_y.tile([P, HALF], F32, name="y")
+                cols = slice(P * n, P * (n + 1))
+                for rb in range(2):
+                    nc.tensor.matmul_mx(
+                        out=y[:], lhsT=wd4_w[:].bitcast(U8)[:, rb, 2 * P * n : 2 * P * (n + 1)].bitcast(FP4X4),
+                        lhsT_scale=wd4_s[:, rb, cols], rhs=h_w[rb, c][:].bitcast(FP8X4), rhs_scale=h_s[rb, c][:],
+                        start=(rb == 0), stop=False,
+                    )
+                    nc.tensor.matmul_mx(
+                        out=y[:], lhsT=wd8_w[:, rb, cols].bitcast(FP8X4),
+                        lhsT_scale=wd8_s[:, rb, cols], rhs=h_w[rb, c][:].bitcast(FP8X4), rhs_scale=h_s[rb, c][:],
+                        start=False, stop=(rb == 1),
+                    )
+                biased = keep.tile([P, HALF], F32, name=f"y_sb{n}{c}")
+                nc.scalar.activation(out=biased[:], in_=y[:], func=ACT.Identity, bias=bias[:, n : n + 1])
+                y_sb[n, c] = biased
+
+        placed = {}
+
+        def zero_rows(n, engine):
+            rows = ring.tile([P, T], F32, name="placed")
+            engine.memset(rows[:], 0.0)
+            placed[n] = rows
+
+        def scatter(n, c):
+            listed = offsets[:, c * HALF // 16 : (c + 1) * HALF // 16]
+            nc.vector.tensor_tensor(
+                placed[n][:].indirect(listed), y_sb[n, c][:], weight[:, c * HALF : (c + 1) * HALF], MULT
+            )
+
+        def store(n):
+            nc.sync.dma_start(out=out[P * n : P * (n + 1), :], in_=placed[n][:])
+
+        permute_wg(0)
+        gather_tokens(0)
+        quantize_wu(0)
+        hidden(0, 0)
+        gather_tokens(1)
+        hidden(0, 1)
+        permute_wg(1)
+        quantize_wu(1)
+        hidden(1, 0)
+        hidden(1, 1)
+        down(0)
+        for g in (2, 3):
+            gather_tokens(g)
+            hidden(0, g)
+            hidden(1, g)
+        down(1)
+        for n in range(3):
+            zero_rows(n, nc.vector)
+        for n in range(3):
+            scatter(n, 0)
+        for n in range(3):
+            scatter(n, 1)
+            store(n)
+        zero_rows(3, nc.gpsimd)
+        scatter(3, 0)
+        scatter(3, 1)
+        store(3)

@@ -15,10 +15,12 @@ FP8X4 = mybir.dt.float8_e4m3fn_x4
 FP4X4 = mybir.dt.float4_e2m1fn_x4
 ACT = mybir.ActivationFunctionType
 MULT = mybir.AluOpType.mult
+ADD = mybir.AluOpType.add
 
 P = 128
 GATHER = 256
-HALF = 512
+CHUNKS = ((0, 256), (256, 256), (512, 512))
+ROW_BYTES = 8192
 
 
 def tile_list_modp_gsigm_res_noneb_kernel(
@@ -27,6 +29,7 @@ def tile_list_modp_gsigm_res_noneb_kernel(
     nc = tc.nc
     with ExitStack() as ctx:
         keep = ctx.enter_context(tc.tile_pool(name="keep", bufs=1))
+        reuse = ctx.enter_context(tc.tile_pool(name="reuse", bufs=1))
         ring = ctx.enter_context(tc.tile_pool(name="ring", bufs=3))
         psum = ctx.enter_context(tc.psum_pool(name="psum", bufs=3))
         psum_y = ctx.enter_context(tc.psum_pool(name="psum_y", bufs=2))
@@ -34,44 +37,169 @@ def tile_list_modp_gsigm_res_noneb_kernel(
         def held(name, shape, dtype):
             return keep.tile(shape, dtype, name=name, align_bytes=64)
 
-        offsets = keep.tile([P, J // 16], U16, name="offsets")
-        nc.sync.dma_start(offsets[:], offs)
+        def at(name, shape, dtype, offset):
+            return reuse.tile(shape, dtype, name=name, align_bytes=64, offset=offset)
 
-        def load_scales(name, src):
-            width = src.shape[2]
-            plane = held(name, [P, 2, width // 4], I32)
-            nc.vector.memset(plane[:], 0)
+        def load_scales(plane, src, queue, zeroing):
+            zeroing.memset(plane[:], 0)
             for q in range(4):
-                nc.sync.dma_start(
+                queue.dma_start(
                     out=plane[32 * q : 32 * q + 4, :, :],
                     in_=src[:, 4 * q : 4 * q + 4, :].rearrange("a r x -> r a x").bitcast(I32),
                 )
             return plane[:].bitcast(U8)
 
+        wu_raw, wg_w, wg_s, wu_w, wu_s, tok_w, y_sb, placed = {}, {}, {}, {}, {}, {}, {}, {}
+        h_w = [held(f"h_w{rb}", [P, J], U32) for rb in range(2)]
+        h_s = [held(f"h_s{rb}", [P, J], U8) for rb in range(2)]
+
+        def load_wu(rb, a, raw, queue):
+            queue.dma_start(
+                out=raw[:],
+                in_=wu[512 * a : 512 * (a + 1), 512 * rb : 512 * (rb + 1)].rearrange("(p j) c -> p j c", j=4),
+            )
+            wu_raw[rb, a] = raw
+
+        def permute_wg_words(rb, words):
+            cols = slice(512 * rb, 512 * (rb + 1))
+            nc.vector.tensor_copy(
+                out=words[:].bitcast(U16),
+                in_=wg_raw[:].bitcast(U16)[:, :, cols].rearrange("p a (m t) -> p a t m", t=4),
+            )
+            wg_w[rb] = words
+
+        def permute_wg_scales(rb, scales):
+            cols = slice(512 * rb, 512 * (rb + 1))
+            nc.vector.tensor_copy(out=scales[:], in_=wg_s_raw[:, :, cols].rearrange("p a (m t) -> p a t m", t=4))
+            wg_s[rb] = scales
+
+        def quantize_wu(rb, a, on_vector=()):
+            grouped = ring.tile([P, 4, P, 4], BF16, name="wu_grouped", align_bytes=64)
+            source = wu_raw[rb, a][:].rearrange("p j (m t) -> p m j t", t=4)
+            for t0 in (0, 2):
+                copy = nc.vector.tensor_copy if t0 in on_vector else nc.scalar.copy
+                copy(
+                    out=grouped[:, t0 : t0 + 2, :, :].rearrange("p t m j -> p m j t"),
+                    in_=source[:, :, :, t0 : t0 + 2],
+                )
+            words = held(f"wu_w{rb}{a}", [P, 512], U32)
+            scales = held(f"wu_s{rb}{a}", [P, 512], U8)
+            nc.vector.quantize_mx(
+                out=words[:].bitcast(FP8X4), scales=scales[:], in_=grouped[:].rearrange("p t m j -> p (t m j)")
+            )
+            wu_w[rb, a], wu_s[rb, a] = words, scales
+
+        def gather_tokens(g):
+            listed = offsets[:, g * GATHER // 16 : (g + 1) * GATHER // 16]
+            both = held(f"tok_both{g}", [P, GATHER], U32)
+            nc.vector.tensor_copy(both[:], tab_w[:].bitcast(U32).indirect(listed))
+            words = held(f"tok_w{g}", [P, 2, 2 * GATHER], U8)
+            nc.vector.tensor_copy(
+                out=words[:].bitcast(U16), in_=both[:].bitcast(U16).rearrange("p (j a) -> p a j", a=2)
+            )
+            tok_w[g] = words
+
+        def hidden(rb, g, on_gpsimd=False):
+            h = ring.tile([P, GATHER, 4], BF16, name="h", align_bytes=64)
+            for j0 in range(0, GATHER, P):
+                rhs = [tok_w[g][:, a, 2 * j0 : 2 * (j0 + P)].bitcast(FP4X4) for a in range(2)]
+                rhs_s = [tok_s[a][:, g * GATHER + j0 : g * GATHER + j0 + P] for a in range(2)]
+                ga = psum.tile([P, 4, P], F32, name="ga")
+                for t in range(4):
+                    for a in range(2):
+                        nc.tensor.matmul_mx(
+                            out=ga[:, t, :], lhsT=wg_w[rb][:, a, t, :].bitcast(FP4X4), lhsT_scale=wg_s[rb][:, a, t, :],
+                            rhs=rhs[a], rhs_scale=rhs_s[a], start=(a == 0), stop=(a == 1),
+                        )
+                if rb == 0:
+                    gate = at(f"gate{rb}_{g}_{j0}", [P, P, 4], F32, 16 * (g * GATHER + j0))
+                else:
+                    gate = held(f"gate{rb}_{g}_{j0}", [P, P, 4], F32)
+                nc.scalar.activation(out=gate[:], in_=ga[:].rearrange("p t j -> p j t"), func=ACT.Sigmoid)
+                ub = psum.tile([P, 4, P], F32, name="ub")
+                for t in range(4):
+                    cols = slice(P * t, P * (t + 1))
+                    for a in range(2):
+                        nc.tensor.matmul_mx(
+                            out=ub[:, t, :], lhsT=wu_w[rb, a][:, cols].bitcast(FP8X4), lhsT_scale=wu_s[rb, a][:, cols],
+                            rhs=rhs[a], rhs_scale=rhs_s[a], start=(a == 0), stop=(a == 1),
+                        )
+                if on_gpsimd:
+                    up = ring.tile([P, P, 4], F32, name="up", align_bytes=64)
+                    nc.scalar.copy(out=up[:], in_=ub[:].rearrange("p t j -> p j t"))
+                    nc.gpsimd.tensor_tensor(h[:, j0 : j0 + P, :], up[:], gate[:], MULT)
+                else:
+                    nc.vector.tensor_tensor(h[:, j0 : j0 + P, :], ub[:].rearrange("p t j -> p j t"), gate[:], MULT)
+            cols = slice(g * GATHER, (g + 1) * GATHER)
+            nc.vector.quantize_mx(
+                out=h_w[rb][:, cols].bitcast(FP8X4),
+                scales=h_s[rb][:, cols],
+                in_=h[:].rearrange("p j t -> p (j t)"),
+            )
+
+        def down(c):
+            first, width = CHUNKS[c]
+            step = width if width == 512 else P
+            for n in range(N // P):
+                y = psum_y.tile([P, width], F32, name="y")
+                cols = slice(P * n, P * (n + 1))
+                for j0 in range(0, width, step):
+                    tokens = slice(first + j0, first + j0 + step)
+                    for rb in range(2):
+                        rhs, rhs_s = h_w[rb][:, tokens].bitcast(FP8X4), h_s[rb][:, tokens]
+                        nc.tensor.matmul_mx(
+                            out=y[:, j0 : j0 + step],
+                            lhsT=wd4_w[:].bitcast(U8)[:, rb, 2 * P * n : 2 * P * (n + 1)].bitcast(FP4X4),
+                            lhsT_scale=wd4_s[:, rb, cols], rhs=rhs, rhs_scale=rhs_s, start=(rb == 0), stop=False,
+                        )
+                        nc.tensor.matmul_mx(
+                            out=y[:, j0 : j0 + step], lhsT=wd8_w[:, rb, cols].bitcast(FP8X4),
+                            lhsT_scale=wd8_s[:, rb, cols], rhs=rhs, rhs_scale=rhs_s, start=False, stop=(rb == 1),
+                        )
+                biased = held(f"y_sb{n}{c}", [P, width], F32)
+                nc.vector.scalar_tensor_tensor(
+                    biased[:], y[:], bias[:, n : n + 1], weight[:, first : first + width], ADD, MULT
+                )
+                y_sb[n, c] = biased
+
+        def scatter(n, c):
+            first, width = CHUNKS[c]
+            listed = offsets[:, first // 16 : (first + width) // 16]
+            nc.vector.tensor_copy(placed[n][:].indirect(listed), y_sb[n, c][:])
+
+        def load_tab_scales(tile, queue, zeroing):
+            zeroing.memset(tile[:], 0)
+            for q in range(4):
+                queue.dma_start(
+                    out=tile[32 * q : 32 * q + 8, :], in_=tab_scales[:, 4 * q : 4 * q + 4, :].bitcast(I32)
+                )
+
+        offsets = keep.tile([P, J // 16], U16, name="offsets")
+        nc.sync.dma_start(offsets[:], offs)
+        load_wu(0, 0, held("wu_raw00", [P, 4, 512], F32), nc.sync)
+        tab_s = at("tab_s", [P, T // 4], I32, 3 * ROW_BYTES + 1024)
+        load_tab_scales(tab_s, nc.scalar, nc.vector)
+        wg_s_raw = load_scales(held("wg_s_raw", [P, 2, R // 4], I32), wg_scales, nc.scalar, nc.vector)
         warm_in = held("warm_in", [P, 8], F32)
         warm_out = held("warm_out", [P, 8], F32)
-        nc.gpsimd.memset(warm_in[:], 0.0)
+        nc.vector.memset(warm_in[:], 0.0)
         nc.scalar.activation(out=warm_out[:], in_=warm_in[:], func=ACT.Sigmoid)
-
-        wg_raw = held("wg_raw", [P, 2, R // 2], I32)
-        nc.sync.dma_start(out=wg_raw[:], in_=wg_words.rearrange("a p x -> p a x").bitcast(I32))
+        tok_s = [held("tok_s0", [P, J], U8), held("tok_s1", [P, J], U8)]
+        nc.vector.memset(tok_s[1][:].bitcast(I32), 0)
+        nc.vector.tensor_copy(tok_s[0][:], tab_s[:].bitcast(U8).indirect(offsets[:]))
         tab_w = held("tab_w", [P, T], I32)
         nc.sync.dma_start(out=tab_w[:], in_=tab_words[0].rearrange("p t x -> p (t x)").bitcast(I32))
-        tab_s = load_scales("tab_s", tab_scales)
-        wg_s_raw = load_scales("wg_s_raw", wg_scales)
-
-        wu_raw = {}
-        for rb in range(2):
-            for a in range(2):
-                raw = held(f"wu_raw{rb}{a}", [P, 4, 512], F32)
-                nc.sync.dma_start(
-                    out=raw[:],
-                    in_=wu[512 * a : 512 * (a + 1), 512 * rb : 512 * (rb + 1)].rearrange("(p j) c -> p j c", j=4),
-                )
-                wu_raw[rb, a] = raw
-
-        wd4_s = load_scales("wd4_s", wd4_scales)
-        wd8_s = load_scales("wd8_s", wd8_scales)
+        wg_raw = held("wg_raw", [P, 2, R // 2], I32)
+        nc.sync.dma_start(out=wg_raw[:], in_=wg_words.rearrange("a p x -> p a x").bitcast(I32))
+        load_wu(0, 1, held("wu_raw01", [P, 4, 512], F32), nc.sync)
+        nc.sync.dma_start(out=tok_s[1][0:112, :].bitcast(I32), in_=tok_s[0][4:116, :].bitcast(I32))
+        load_wu(1, 0, held("wu_raw10", [P, 4, 512], F32), nc.sync)
+        load_wu(1, 1, held("wu_raw11", [P, 4, 512], F32), nc.sync)
+        gather_tokens(0)
+        permute_wg_words(0, held("wg_w0", [P, 2, 4, 2 * P], U8))
+        permute_wg_scales(0, held("wg_s0", [P, 2, 4, P], U8))
+        wd4_s = load_scales(held("wd4_s", [P, 2, N // 4], I32), wd4_scales, nc.gpsimd, nc.vector)
+        wd8_s = load_scales(held("wd8_s", [P, 2, N // 4], I32), wd8_scales, nc.gpsimd, nc.vector)
         wd4_w = held("wd4_w", [P, 2, N // 2], I32)
         nc.sync.dma_start(out=wd4_w[:], in_=wd4_words.rearrange("a p x -> p a x").bitcast(I32))
         wd8_w = held("wd8_w", [P, 2, N], I32)
@@ -82,141 +210,35 @@ def tile_list_modp_gsigm_res_noneb_kernel(
         weight = held("weight", [P, J], F32)
         nc.sync.dma_start(out=weight[:], in_=wgo)
 
-        wg_w, wg_s, wu_w, wu_s, tok_w, tok_s = {}, {}, {}, {}, {}, {}
-        h_w = {(rb, c): held(f"h_w{rb}{c}", [P, HALF], U32) for rb in range(2) for c in range(2)}
-        h_s = {(rb, c): held(f"h_s{rb}{c}", [P, HALF], U8) for rb in range(2) for c in range(2)}
-
-        def permute_wg(rb):
-            cols = slice(512 * rb, 512 * (rb + 1))
-            words = held(f"wg_w{rb}", [P, 2, 4, 2 * P], U8)
-            nc.vector.tensor_copy(
-                out=words[:].bitcast(U16),
-                in_=wg_raw[:].bitcast(U16)[:, :, cols].rearrange("p a (m t) -> p a t m", t=4),
-            )
-            scales = held(f"wg_s{rb}", [P, 2, 4, P], U8)
-            nc.vector.tensor_copy(out=scales[:], in_=wg_s_raw[:, :, cols].rearrange("p a (m t) -> p a t m", t=4))
-            wg_w[rb], wg_s[rb] = words, scales
-
-        def quantize_wu(rb):
-            for a in range(2):
-                grouped = ring.tile([P, 4, P, 4], BF16, name="wu_grouped", align_bytes=64)
-                source = wu_raw[rb, a][:].rearrange("p j (m t) -> p m j t", t=4)
-                for t0 in (0, 2):
-                    nc.scalar.copy(
-                        out=grouped[:, t0 : t0 + 2, :, :].rearrange("p t m j -> p m j t"),
-                        in_=source[:, :, :, t0 : t0 + 2],
-                    )
-                words = held(f"wu_w{rb}{a}", [P, 512], U32)
-                scales = held(f"wu_s{rb}{a}", [P, 512], U8)
-                nc.vector.quantize_mx(
-                    out=words[:].bitcast(FP8X4), scales=scales[:], in_=grouped[:].rearrange("p t m j -> p (t m j)")
-                )
-                wu_w[rb, a], wu_s[rb, a] = words, scales
-
-        def gather_tokens(g):
-            listed = offsets[:, g * GATHER // 16 : (g + 1) * GATHER // 16]
-            both = held(f"tok_both{g}", [P, GATHER], U32)
-            nc.vector.tensor_copy(both[:], tab_w[:].bitcast(U32).indirect(listed))
-            scales = held(f"tok_s{g}", [P, 2, GATHER], U8)
-            for a in range(2):
-                nc.vector.tensor_copy(scales[:, a, :], tab_s[:, a, :].indirect(listed))
-            words = held(f"tok_w{g}", [P, 2, 2 * GATHER], U8)
-            nc.vector.tensor_copy(
-                out=words[:].bitcast(U16), in_=both[:].bitcast(U16).rearrange("p (j a) -> p a j", a=2)
-            )
-            tok_w[g], tok_s[g] = words, scales
-
-        def hidden(rb, g):
-            h = ring.tile([P, GATHER, 4], BF16, name="h", align_bytes=64)
-            for j0 in range(0, GATHER, P):
-                rhs = [tok_w[g][:, a, 2 * j0 : 2 * (j0 + P)].bitcast(FP4X4) for a in range(2)]
-                rhs_s = [tok_s[g][:, a, j0 : j0 + P] for a in range(2)]
-                ga = psum.tile([P, 4, P], F32, name="ga")
-                for t in range(4):
-                    for a in range(2):
-                        nc.tensor.matmul_mx(
-                            out=ga[:, t, :], lhsT=wg_w[rb][:, a, t, :].bitcast(FP4X4), lhsT_scale=wg_s[rb][:, a, t, :],
-                            rhs=rhs[a], rhs_scale=rhs_s[a], start=(a == 0), stop=(a == 1),
-                        )
-                gate = keep.tile([P, P, 4], F32, name=f"gate{rb}_{g}_{j0}")
-                nc.scalar.activation(out=gate[:], in_=ga[:].rearrange("p t j -> p j t"), func=ACT.Sigmoid)
-                ub = psum.tile([P, 4, P], F32, name="ub")
-                for t in range(4):
-                    cols = slice(P * t, P * (t + 1))
-                    for a in range(2):
-                        nc.tensor.matmul_mx(
-                            out=ub[:, t, :], lhsT=wu_w[rb, a][:, cols].bitcast(FP8X4), lhsT_scale=wu_s[rb, a][:, cols],
-                            rhs=rhs[a], rhs_scale=rhs_s[a], start=(a == 0), stop=(a == 1),
-                        )
-                nc.vector.tensor_tensor(h[:, j0 : j0 + P, :], ub[:].rearrange("p t j -> p j t"), gate[:], MULT)
-            c, j0 = divmod(g * GATHER, HALF)
-            nc.vector.quantize_mx(
-                out=h_w[rb, c][:, j0 : j0 + GATHER].bitcast(FP8X4),
-                scales=h_s[rb, c][:, j0 : j0 + GATHER],
-                in_=h[:].rearrange("p j t -> p (j t)"),
-            )
-
-        y_sb = {}
-
-        def down(c):
-            for n in range(N // P):
-                y = psum_y.tile([P, HALF], F32, name="y")
-                cols = slice(P * n, P * (n + 1))
-                for rb in range(2):
-                    nc.tensor.matmul_mx(
-                        out=y[:], lhsT=wd4_w[:].bitcast(U8)[:, rb, 2 * P * n : 2 * P * (n + 1)].bitcast(FP4X4),
-                        lhsT_scale=wd4_s[:, rb, cols], rhs=h_w[rb, c][:].bitcast(FP8X4), rhs_scale=h_s[rb, c][:],
-                        start=(rb == 0), stop=False,
-                    )
-                    nc.tensor.matmul_mx(
-                        out=y[:], lhsT=wd8_w[:, rb, cols].bitcast(FP8X4),
-                        lhsT_scale=wd8_s[:, rb, cols], rhs=h_w[rb, c][:].bitcast(FP8X4), rhs_scale=h_s[rb, c][:],
-                        start=False, stop=(rb == 1),
-                    )
-                biased = keep.tile([P, HALF], F32, name=f"y_sb{n}{c}")
-                nc.scalar.activation(out=biased[:], in_=y[:], func=ACT.Identity, bias=bias[:, n : n + 1])
-                y_sb[n, c] = biased
-
-        placed = {}
-
-        def zero_rows(n, engine):
-            rows = ring.tile([P, T], F32, name="placed")
-            engine.memset(rows[:], 0.0)
-            placed[n] = rows
-
-        def scatter(n, c):
-            listed = offsets[:, c * HALF // 16 : (c + 1) * HALF // 16]
-            nc.vector.tensor_tensor(
-                placed[n][:].indirect(listed), y_sb[n, c][:], weight[:, c * HALF : (c + 1) * HALF], MULT
-            )
-
-        def store(n):
-            nc.sync.dma_start(out=out[P * n : P * (n + 1), :], in_=placed[n][:])
-
-        permute_wg(0)
-        gather_tokens(0)
-        quantize_wu(0)
+        quantize_wu(0, 0)
+        quantize_wu(0, 1)
         hidden(0, 0)
         gather_tokens(1)
+        permute_wg_words(1, at("wg_w1", [P, 2, 4, 2 * P], U8, 3 * ROW_BYTES + 2048))
+        permute_wg_scales(1, held("wg_s1", [P, 2, 4, P], U8))
+        quantize_wu(1, 0, (2,))
+        quantize_wu(1, 1, (2,))
         hidden(0, 1)
-        permute_wg(1)
-        quantize_wu(1)
         hidden(1, 0)
-        hidden(1, 1)
         down(0)
-        for g in (2, 3):
-            gather_tokens(g)
-            hidden(0, g)
-            hidden(1, g)
+        hidden(1, 1)
         down(1)
-        for n in range(3):
-            zero_rows(n, nc.vector)
-        for n in range(3):
-            scatter(n, 0)
-        for n in range(3):
-            scatter(n, 1)
-            store(n)
-        zero_rows(3, nc.gpsimd)
-        scatter(3, 0)
-        scatter(3, 1)
-        store(3)
+        gather_tokens(2)
+        hidden(0, 2)
+        hidden(1, 2)
+        gather_tokens(3)
+        hidden(0, 3)
+        hidden(1, 3)
+        down(2)
+        for n in range(2):
+            placed[n] = held(f"placed{n}", [P, T], F32)
+            nc.vector.memset(placed[n][:], 0.0)
+        for n in range(2, 4):
+            placed[n] = at(f"placed{n}", [P, T], F32, (n - 2) * ROW_BYTES)
+            for j0 in range(0, T, 512):
+                nc.gpsimd.memset(placed[n][:, j0 : j0 + 512], 0.0)
+        for c in range(len(CHUNKS)):
+            for n in range(N // P):
+                scatter(n, c)
+                if c == len(CHUNKS) - 1:
+                    nc.sync.dma_start(out=out[P * n : P * (n + 1), :], in_=placed[n][:])

@@ -77,11 +77,16 @@ def tile_list_modp_gsigm_res_noneb_kernel(
             grouped = ring.tile([P, 4, P, 4], BF16, name="wu_grouped", align_bytes=64)
             source = wu_raw[rb, a][:].rearrange("p j (m t) -> p m j t", t=4)
             for t0 in (0, 2):
-                copy = nc.vector.tensor_copy if t0 in on_vector else nc.scalar.copy
-                copy(
-                    out=grouped[:, t0 : t0 + 2, :, :].rearrange("p t m j -> p m j t"),
-                    in_=source[:, :, :, t0 : t0 + 2],
-                )
+                if t0 in on_vector:
+                    nc.vector.tensor_copy(
+                        out=grouped[:, t0 : t0 + 2, :, :],
+                        in_=source[:, :, :, t0 : t0 + 2].rearrange("p m j t -> p t m j"),
+                    )
+                else:
+                    nc.scalar.copy(
+                        out=grouped[:, t0 : t0 + 2, :, :].rearrange("p t m j -> p m j t"),
+                        in_=source[:, :, :, t0 : t0 + 2],
+                    )
             words = held(f"wu_w{rb}{a}", [P, 512], U32)
             scales = held(f"wu_s{rb}{a}", [P, 512], U8)
             nc.vector.quantize_mx(
@@ -114,7 +119,7 @@ def tile_list_modp_gsigm_res_noneb_kernel(
                 if rb == 0:
                     gate = at(f"gate{rb}_{g}_{j0}", [P, P, 4], F32, 16 * (g * GATHER + j0))
                 else:
-                    gate = held(f"gate{rb}_{g}_{j0}", [P, P, 4], F32)
+                    gate = at(f"gate{rb}_{g}_{j0}", [P, P, 4], F32, 4 * ROW_BYTES + 16 * (g * GATHER + j0))
                 nc.scalar.activation(out=gate[:], in_=ga[:].rearrange("p t j -> p j t"), func=ACT.Sigmoid)
                 ub = psum.tile([P, 4, P], F32, name="ub")
                 for t in range(4):
@@ -137,10 +142,10 @@ def tile_list_modp_gsigm_res_noneb_kernel(
                 in_=h[:].rearrange("p j t -> p (j t)"),
             )
 
-        def down(c):
+        def down(c, tiles=range(N // P)):
             first, width = CHUNKS[c]
             step = width if width == 512 else P
-            for n in range(N // P):
+            for n in tiles:
                 y = psum_y.tile([P, width], F32, name="y")
                 cols = slice(P * n, P * (n + 1))
                 for j0 in range(0, width, step):
@@ -156,16 +161,19 @@ def tile_list_modp_gsigm_res_noneb_kernel(
                             out=y[:, j0 : j0 + step], lhsT=wd8_w[:, rb, cols].bitcast(FP8X4),
                             lhsT_scale=wd8_s[:, rb, cols], rhs=rhs, rhs_scale=rhs_s, start=False, stop=(rb == 1),
                         )
-                biased = held(f"y_sb{n}{c}", [P, width], F32)
-                nc.vector.scalar_tensor_tensor(
-                    biased[:], y[:], bias[:, n : n + 1], weight[:, first : first + width], ADD, MULT
-                )
+                if c == len(CHUNKS) - 2 and n >= 2:
+                    biased = at(f"y_sb{n}{c}", [P, width], F32, 6 * ROW_BYTES - 1024 * (N // P - n))
+                else:
+                    biased = held(f"y_sb{n}{c}", [P, width], F32)
+                nc.scalar.activation(out=biased[:], in_=y[:], func=ACT.Identity, bias=bias[:, n : n + 1])
                 y_sb[n, c] = biased
 
         def scatter(n, c):
             first, width = CHUNKS[c]
             listed = offsets[:, first // 16 : (first + width) // 16]
-            nc.vector.tensor_copy(placed[n][:].indirect(listed), y_sb[n, c][:])
+            nc.vector.tensor_tensor(
+                placed[n][:].indirect(listed), y_sb[n, c][:], weight[:, first : first + width], MULT
+            )
 
         def load_tab_scales(tile, queue, zeroing):
             zeroing.memset(tile[:], 0)
@@ -178,7 +186,7 @@ def tile_list_modp_gsigm_res_noneb_kernel(
         nc.sync.dma_start(offsets[:], offs)
         load_wu(0, 0, held("wu_raw00", [P, 4, 512], F32), nc.sync)
         tab_s = at("tab_s", [P, T // 4], I32, 3 * ROW_BYTES + 1024)
-        load_tab_scales(tab_s, nc.scalar, nc.vector)
+        load_tab_scales(tab_s, nc.scalar, nc.gpsimd)
         wg_s_raw = load_scales(held("wg_s_raw", [P, 2, R // 4], I32), wg_scales, nc.scalar, nc.vector)
         warm_in = held("warm_in", [P, 8], F32)
         warm_out = held("warm_out", [P, 8], F32)
@@ -198,45 +206,41 @@ def tile_list_modp_gsigm_res_noneb_kernel(
         gather_tokens(0)
         permute_wg_words(0, held("wg_w0", [P, 2, 4, 2 * P], U8))
         permute_wg_scales(0, held("wg_s0", [P, 2, 4, P], U8))
-        wd4_s = load_scales(held("wd4_s", [P, 2, N // 4], I32), wd4_scales, nc.gpsimd, nc.vector)
-        wd8_s = load_scales(held("wd8_s", [P, 2, N // 4], I32), wd8_scales, nc.gpsimd, nc.vector)
         wd4_w = held("wd4_w", [P, 2, N // 2], I32)
         nc.sync.dma_start(out=wd4_w[:], in_=wd4_words.rearrange("a p x -> p a x").bitcast(I32))
         wd8_w = held("wd8_w", [P, 2, N], I32)
         nc.sync.dma_start(out=wd8_w[:], in_=wd8_words.rearrange("a p n x -> p a (n x)").bitcast(I32))
+        wd4_s = load_scales(held("wd4_s", [P, 2, N // 4], I32), wd4_scales, nc.sync, nc.vector)
+        wd8_s = load_scales(held("wd8_s", [P, 2, N // 4], I32), wd8_scales, nc.sync, nc.vector)
         bias = held("bias", [P, N // P], F32)
         with nc.allow_non_contiguous_dma(reason="one bias value a partition"):
             nc.sync.dma_start(out=bias[:], in_=b.rearrange("(c p) -> p c", p=P))
         weight = held("weight", [P, J], F32)
         nc.sync.dma_start(out=weight[:], in_=wgo)
-
         quantize_wu(0, 0)
         quantize_wu(0, 1)
         hidden(0, 0)
         gather_tokens(1)
-        permute_wg_words(1, at("wg_w1", [P, 2, 4, 2 * P], U8, 3 * ROW_BYTES + 2048))
+        permute_wg_words(1, held("wg_w1", [P, 2, 4, 2 * P], U8))
         permute_wg_scales(1, held("wg_s1", [P, 2, 4, P], U8))
-        quantize_wu(1, 0, (2,))
-        quantize_wu(1, 1, (2,))
+        quantize_wu(1, 0)
+        quantize_wu(1, 1)
         hidden(0, 1)
         hidden(1, 0)
         down(0)
         hidden(1, 1)
-        down(1)
+        down(1, (0, 1,))
         gather_tokens(2)
         hidden(0, 2)
         hidden(1, 2)
         gather_tokens(3)
         hidden(0, 3)
         hidden(1, 3)
+        down(1, (2, 3,))
         down(2)
-        for n in range(2):
+        for n in range(4):
             placed[n] = held(f"placed{n}", [P, T], F32)
             nc.vector.memset(placed[n][:], 0.0)
-        for n in range(2, 4):
-            placed[n] = at(f"placed{n}", [P, T], F32, (n - 2) * ROW_BYTES)
-            for j0 in range(0, T, 512):
-                nc.gpsimd.memset(placed[n][:, j0 : j0 + 512], 0.0)
         for c in range(len(CHUNKS)):
             for n in range(N // P):
                 scatter(n, c)

@@ -104,37 +104,38 @@ def tile_list_modp_gsigm_res_noneb_kernel(
             )
             tok_w[g] = words
 
-        def hidden(rb, g, on_gpsimd=False):
-            h = ring.tile([P, GATHER, 4], BF16, name="h", align_bytes=64)
-            for j0 in range(0, GATHER, P):
-                rhs = [tok_w[g][:, a, 2 * j0 : 2 * (j0 + P)].bitcast(FP4X4) for a in range(2)]
-                rhs_s = [tok_s[a][:, g * GATHER + j0 : g * GATHER + j0 + P] for a in range(2)]
-                ga = psum.tile([P, 4, P], F32, name="ga")
-                for t in range(4):
+        def hidden(rb, g):
+            tokens = slice(g * GATHER, (g + 1) * GATHER)
+            gate = at(f"gate{rb}_{g}", [P, 4, GATHER], F32, 4096 * g + 4 * ROW_BYTES * rb)
+            for t0 in (0, 2):
+                ga = psum.tile([P, 2, GATHER], F32, name="ga", bufs=3)
+                for t in range(2):
                     for a in range(2):
                         nc.tensor.matmul_mx(
-                            out=ga[:, t, :], lhsT=wg_w[rb][:, a, t, :].bitcast(FP4X4), lhsT_scale=wg_s[rb][:, a, t, :],
-                            rhs=rhs[a], rhs_scale=rhs_s[a], start=(a == 0), stop=(a == 1),
+                            out=ga[:, t, :], lhsT=wg_w[rb][:, a, t0 + t, :].bitcast(FP4X4),
+                            lhsT_scale=wg_s[rb][:, a, t0 + t, :],
+                            rhs=tok_w[g][:, a, :].bitcast(FP4X4), rhs_scale=tok_s[a][:, tokens],
+                            start=(a == 0), stop=(a == 1),
                         )
-                if rb == 0:
-                    gate = at(f"gate{rb}_{g}_{j0}", [P, P, 4], F32, 16 * (g * GATHER + j0))
-                else:
-                    gate = at(f"gate{rb}_{g}_{j0}", [P, P, 4], F32, 4 * ROW_BYTES + 16 * (g * GATHER + j0))
-                nc.scalar.activation(out=gate[:], in_=ga[:].rearrange("p t j -> p j t"), func=ACT.Sigmoid)
-                ub = psum.tile([P, 4, P], F32, name="ub")
+                nc.scalar.activation(out=gate[:, t0 : t0 + 2, :], in_=ga[:], func=ACT.Sigmoid)
+            h = ring.tile([P, GATHER, 4], BF16, name="h", align_bytes=64)
+            for j0 in range(0, GATHER, P):
+                ub = psum.tile([P, 4, P], F32, name="ub", bufs=3)
                 for t in range(4):
                     cols = slice(P * t, P * (t + 1))
                     for a in range(2):
                         nc.tensor.matmul_mx(
                             out=ub[:, t, :], lhsT=wu_w[rb, a][:, cols].bitcast(FP8X4), lhsT_scale=wu_s[rb, a][:, cols],
-                            rhs=rhs[a], rhs_scale=rhs_s[a], start=(a == 0), stop=(a == 1),
+                            rhs=tok_w[g][:, a, 2 * j0 : 2 * (j0 + P)].bitcast(FP4X4),
+                            rhs_scale=tok_s[a][:, g * GATHER + j0 : g * GATHER + j0 + P],
+                            start=(a == 0), stop=(a == 1),
                         )
-                if on_gpsimd:
-                    up = ring.tile([P, P, 4], F32, name="up", align_bytes=64)
-                    nc.scalar.copy(out=up[:], in_=ub[:].rearrange("p t j -> p j t"))
-                    nc.gpsimd.tensor_tensor(h[:, j0 : j0 + P, :], up[:], gate[:], MULT)
-                else:
-                    nc.vector.tensor_tensor(h[:, j0 : j0 + P, :], ub[:].rearrange("p t j -> p j t"), gate[:], MULT)
+                nc.vector.tensor_tensor(
+                    h[:, j0 : j0 + P, :].rearrange("p (c i) t -> p c t i", i=2),
+                    ub[:].rearrange("p t (c i) -> p c t i", i=2),
+                    gate[:, :, j0 : j0 + P].rearrange("p t (c i) -> p c t i", i=2),
+                    MULT,
+                )
             cols = slice(g * GATHER, (g + 1) * GATHER)
             nc.vector.quantize_mx(
                 out=h_w[rb][:, cols].bitcast(FP8X4),
@@ -227,12 +228,12 @@ def tile_list_modp_gsigm_res_noneb_kernel(
         quantize_wu(1, 1)
         hidden(0, 1)
         hidden(1, 0)
-        down(0)
         hidden(1, 1)
-        down(1, (0, 1,))
         gather_tokens(2)
         hidden(0, 2)
+        down(0)
         hidden(1, 2)
+        down(1, (0, 1,))
         gather_tokens(3)
         hidden(0, 3)
         hidden(1, 3)
@@ -240,7 +241,7 @@ def tile_list_modp_gsigm_res_noneb_kernel(
         down(2)
         for n in range(4):
             placed[n] = held(f"placed{n}", [P, T], F32)
-            nc.vector.memset(placed[n][:], 0.0)
+            nc.vector.memset(placed[n][:].bitcast(I32), 0)
         for c in range(len(CHUNKS)):
             for n in range(N // P):
                 scatter(n, c)

@@ -15,12 +15,21 @@ FP8X4 = mybir.dt.float8_e4m3fn_x4
 FP4X4 = mybir.dt.float4_e2m1fn_x4
 ACT = mybir.ActivationFunctionType
 MULT = mybir.AluOpType.mult
-ADD = mybir.AluOpType.add
 
 P = 128
-GATHER = 256
-CHUNKS = ((0, 256), (256, 256), (512, 512))
-ROW_BYTES = 8192
+PASS = 512
+QUADRANT = 32
+LIST_COLUMN = 16
+HALF = J // 2
+GROUP = 256
+PIECES = ((0, 256), (256, 256), (512, 512))
+SHIFT_ROWS = 112
+
+TAB_SCALES_THEN_WG_WORDS = 0
+WG_SCALES_THEN_TOKEN_WORDS = 4096
+LAST_GATE_THEN_Y = 6144
+WU_THEN_ROWS = 10240
+ROW_BYTES = 4 * T
 
 
 def tile_list_modp_gsigm_res_noneb_kernel(
@@ -29,221 +38,227 @@ def tile_list_modp_gsigm_res_noneb_kernel(
     nc = tc.nc
     with ExitStack() as ctx:
         keep = ctx.enter_context(tc.tile_pool(name="keep", bufs=1))
-        reuse = ctx.enter_context(tc.tile_pool(name="reuse", bufs=1))
+        shared = ctx.enter_context(tc.tile_pool(name="shared", bufs=1))
         ring = ctx.enter_context(tc.tile_pool(name="ring", bufs=3))
-        psum = ctx.enter_context(tc.psum_pool(name="psum", bufs=3))
+        psum_ga = ctx.enter_context(tc.psum_pool(name="psum_ga", bufs=3))
+        psum_ub = ctx.enter_context(tc.psum_pool(name="psum_ub", bufs=3))
         psum_y = ctx.enter_context(tc.psum_pool(name="psum_y", bufs=2))
 
         def held(name, shape, dtype):
             return keep.tile(shape, dtype, name=name, align_bytes=64)
 
-        def at(name, shape, dtype, offset):
-            return reuse.tile(shape, dtype, name=name, align_bytes=64, offset=offset)
+        def sharing(name, shape, dtype, offset):
+            return shared.tile(shape, dtype, name=name, align_bytes=64, offset=offset)
 
-        def load_scales(plane, src, queue, zeroing):
-            zeroing.memset(plane[:], 0)
-            for q in range(4):
-                queue.dma_start(
-                    out=plane[32 * q : 32 * q + 4, :, :],
+        def load_scales(tile, src):
+            for q in range(P // QUADRANT):
+                nc.sync.dma_start(
+                    out=tile[QUADRANT * q : QUADRANT * q + 4, :, :],
                     in_=src[:, 4 * q : 4 * q + 4, :].rearrange("a r x -> r a x").bitcast(I32),
                 )
-            return plane[:].bitcast(U8)
 
-        wu_raw, wg_w, wg_s, wu_w, wu_s, tok_w, y_sb, placed = {}, {}, {}, {}, {}, {}, {}, {}
-        h_w = [held(f"h_w{rb}", [P, J], U32) for rb in range(2)]
-        h_s = [held(f"h_s{rb}", [P, J], U8) for rb in range(2)]
+        def load_wu(raw, rb, a):
+            block = wu[PASS * a : PASS * (a + 1), PASS * rb : PASS * (rb + 1)]
+            nc.sync.dma_start(out=raw[:], in_=block.rearrange("(p i) c -> p i c", i=4))
+            return raw
 
-        def load_wu(rb, a, raw, queue):
-            queue.dma_start(
-                out=raw[:],
-                in_=wu[512 * a : 512 * (a + 1), 512 * rb : 512 * (rb + 1)].rearrange("(p j) c -> p j c", j=4),
-            )
-            wu_raw[rb, a] = raw
-
-        def permute_wg_words(rb, words):
-            cols = slice(512 * rb, 512 * (rb + 1))
-            nc.vector.tensor_copy(
-                out=words[:].bitcast(U16),
-                in_=wg_raw[:].bitcast(U16)[:, :, cols].rearrange("p a (m t) -> p a t m", t=4),
-            )
-            wg_w[rb] = words
-
-        def permute_wg_scales(rb, scales):
-            cols = slice(512 * rb, 512 * (rb + 1))
-            nc.vector.tensor_copy(out=scales[:], in_=wg_s_raw[:, :, cols].rearrange("p a (m t) -> p a t m", t=4))
-            wg_s[rb] = scales
-
-        def quantize_wu(rb, a, on_vector=()):
-            grouped = ring.tile([P, 4, P, 4], BF16, name="wu_grouped", align_bytes=64)
-            source = wu_raw[rb, a][:].rearrange("p j (m t) -> p m j t", t=4)
-            for t0 in (0, 2):
-                if t0 in on_vector:
-                    nc.vector.tensor_copy(
-                        out=grouped[:, t0 : t0 + 2, :, :],
-                        in_=source[:, :, :, t0 : t0 + 2].rearrange("p m j t -> p t m j"),
-                    )
-                else:
-                    nc.scalar.copy(
-                        out=grouped[:, t0 : t0 + 2, :, :].rearrange("p t m j -> p m j t"),
-                        in_=source[:, :, :, t0 : t0 + 2],
-                    )
-            words = held(f"wu_w{rb}{a}", [P, 512], U32)
-            scales = held(f"wu_s{rb}{a}", [P, 512], U8)
-            nc.vector.quantize_mx(
-                out=words[:].bitcast(FP8X4), scales=scales[:], in_=grouped[:].rearrange("p t m j -> p (t m j)")
-            )
-            wu_w[rb, a], wu_s[rb, a] = words, scales
-
-        def gather_tokens(g):
-            listed = offsets[:, g * GATHER // 16 : (g + 1) * GATHER // 16]
-            both = held(f"tok_both{g}", [P, GATHER], U32)
-            nc.vector.tensor_copy(both[:], tab_w[:].bitcast(U32).indirect(listed))
-            words = held(f"tok_w{g}", [P, 2, 2 * GATHER], U8)
-            nc.vector.tensor_copy(
-                out=words[:].bitcast(U16), in_=both[:].bitcast(U16).rearrange("p (j a) -> p a j", a=2)
-            )
-            tok_w[g] = words
-
-        def hidden(rb, g):
-            tokens = slice(g * GATHER, (g + 1) * GATHER)
-            gate = at(f"gate{rb}_{g}", [P, 4, GATHER], F32, 4096 * g + 4 * ROW_BYTES * rb)
-            for t0 in (0, 2):
-                ga = psum.tile([P, 2, GATHER], F32, name="ga", bufs=3)
-                for t in range(2):
-                    for a in range(2):
-                        nc.tensor.matmul_mx(
-                            out=ga[:, t, :], lhsT=wg_w[rb][:, a, t0 + t, :].bitcast(FP4X4),
-                            lhsT_scale=wg_s[rb][:, a, t0 + t, :],
-                            rhs=tok_w[g][:, a, :].bitcast(FP4X4), rhs_scale=tok_s[a][:, tokens],
-                            start=(a == 0), stop=(a == 1),
-                        )
-                nc.scalar.activation(out=gate[:, t0 : t0 + 2, :], in_=ga[:], func=ACT.Sigmoid)
-            h = ring.tile([P, GATHER, 4], BF16, name="h", align_bytes=64)
-            for j0 in range(0, GATHER, P):
-                ub = psum.tile([P, 4, P], F32, name="ub", bufs=3)
-                for t in range(4):
-                    cols = slice(P * t, P * (t + 1))
-                    for a in range(2):
-                        nc.tensor.matmul_mx(
-                            out=ub[:, t, :], lhsT=wu_w[rb, a][:, cols].bitcast(FP8X4), lhsT_scale=wu_s[rb, a][:, cols],
-                            rhs=tok_w[g][:, a, 2 * j0 : 2 * (j0 + P)].bitcast(FP4X4),
-                            rhs_scale=tok_s[a][:, g * GATHER + j0 : g * GATHER + j0 + P],
-                            start=(a == 0), stop=(a == 1),
-                        )
-                nc.vector.tensor_tensor(
-                    h[:, j0 : j0 + P, :].rearrange("p (c i) t -> p c t i", i=2),
-                    ub[:].rearrange("p t (c i) -> p c t i", i=2),
-                    gate[:, :, j0 : j0 + P].rearrange("p t (c i) -> p c t i", i=2),
-                    MULT,
-                )
-            cols = slice(g * GATHER, (g + 1) * GATHER)
-            nc.vector.quantize_mx(
-                out=h_w[rb][:, cols].bitcast(FP8X4),
-                scales=h_s[rb][:, cols],
-                in_=h[:].rearrange("p j t -> p (j t)"),
-            )
-
-        def down(c, tiles=range(N // P)):
-            first, width = CHUNKS[c]
-            step = width if width == 512 else P
-            for n in tiles:
-                y = psum_y.tile([P, width], F32, name="y")
-                cols = slice(P * n, P * (n + 1))
-                for j0 in range(0, width, step):
-                    tokens = slice(first + j0, first + j0 + step)
-                    for rb in range(2):
-                        rhs, rhs_s = h_w[rb][:, tokens].bitcast(FP8X4), h_s[rb][:, tokens]
-                        nc.tensor.matmul_mx(
-                            out=y[:, j0 : j0 + step],
-                            lhsT=wd4_w[:].bitcast(U8)[:, rb, 2 * P * n : 2 * P * (n + 1)].bitcast(FP4X4),
-                            lhsT_scale=wd4_s[:, rb, cols], rhs=rhs, rhs_scale=rhs_s, start=(rb == 0), stop=False,
-                        )
-                        nc.tensor.matmul_mx(
-                            out=y[:, j0 : j0 + step], lhsT=wd8_w[:, rb, cols].bitcast(FP8X4),
-                            lhsT_scale=wd8_s[:, rb, cols], rhs=rhs, rhs_scale=rhs_s, start=False, stop=(rb == 1),
-                        )
-                if c == len(CHUNKS) - 2 and n >= 2:
-                    biased = at(f"y_sb{n}{c}", [P, width], F32, 6 * ROW_BYTES - 1024 * (N // P - n))
-                else:
-                    biased = held(f"y_sb{n}{c}", [P, width], F32)
-                nc.scalar.activation(out=biased[:], in_=y[:], func=ACT.Identity, bias=bias[:, n : n + 1])
-                y_sb[n, c] = biased
-
-        def scatter(n, c):
-            first, width = CHUNKS[c]
-            listed = offsets[:, first // 16 : (first + width) // 16]
-            nc.vector.tensor_tensor(
-                placed[n][:].indirect(listed), y_sb[n, c][:], weight[:, first : first + width], MULT
-            )
-
-        def load_tab_scales(tile, queue, zeroing):
-            zeroing.memset(tile[:], 0)
-            for q in range(4):
-                queue.dma_start(
-                    out=tile[32 * q : 32 * q + 8, :], in_=tab_scales[:, 4 * q : 4 * q + 4, :].bitcast(I32)
-                )
-
-        offsets = keep.tile([P, J // 16], U16, name="offsets")
+        offsets = keep.tile([P, J // LIST_COLUMN], U16, name="offsets")
         nc.sync.dma_start(offsets[:], offs)
-        load_wu(0, 0, held("wu_raw00", [P, 4, 512], F32), nc.sync)
-        tab_s = at("tab_s", [P, T // 4], I32, 3 * ROW_BYTES + 1024)
-        load_tab_scales(tab_s, nc.scalar, nc.gpsimd)
-        wg_s_raw = load_scales(held("wg_s_raw", [P, 2, R // 4], I32), wg_scales, nc.scalar, nc.vector)
-        warm_in = held("warm_in", [P, 8], F32)
-        warm_out = held("warm_out", [P, 8], F32)
-        nc.vector.memset(warm_in[:], 0.0)
-        nc.scalar.activation(out=warm_out[:], in_=warm_in[:], func=ACT.Sigmoid)
-        tok_s = [held("tok_s0", [P, J], U8), held("tok_s1", [P, J], U8)]
-        nc.vector.memset(tok_s[1][:].bitcast(I32), 0)
-        nc.vector.tensor_copy(tok_s[0][:], tab_s[:].bitcast(U8).indirect(offsets[:]))
-        tab_w = held("tab_w", [P, T], I32)
-        nc.sync.dma_start(out=tab_w[:], in_=tab_words[0].rearrange("p t x -> p (t x)").bitcast(I32))
         wg_raw = held("wg_raw", [P, 2, R // 2], I32)
         nc.sync.dma_start(out=wg_raw[:], in_=wg_words.rearrange("a p x -> p a x").bitcast(I32))
-        load_wu(0, 1, held("wu_raw01", [P, 4, 512], F32), nc.sync)
-        nc.sync.dma_start(out=tok_s[1][0:112, :].bitcast(I32), in_=tok_s[0][4:116, :].bitcast(I32))
-        load_wu(1, 0, held("wu_raw10", [P, 4, 512], F32), nc.sync)
-        load_wu(1, 1, held("wu_raw11", [P, 4, 512], F32), nc.sync)
-        gather_tokens(0)
-        permute_wg_words(0, held("wg_w0", [P, 2, 4, 2 * P], U8))
-        permute_wg_scales(0, held("wg_s0", [P, 2, 4, P], U8))
+
+        tab_s = sharing("tab_s", [P, T // 4], I32, TAB_SCALES_THEN_WG_WORDS)
+        nc.gpsimd.memset(tab_s[:], 0)
+        for q in range(P // QUADRANT):
+            nc.sync.dma_start(
+                out=tab_s[QUADRANT * q : QUADRANT * q + 8, :], in_=tab_scales[:, 4 * q : 4 * q + 4, :].bitcast(I32)
+            )
+        tok_s = [held(f"tok_s{a}", [P, J], U8) for a in range(2)]
+        nc.vector.memset(tok_s[1][:].bitcast(I32), 0)
+        nc.vector.tensor_copy(tok_s[0][:], tab_s[:].bitcast(U8).indirect(offsets[:]))
+
+        tab_w = held("tab_w", [P, T], I32)
+        nc.sync.dma_start(out=tab_w[:], in_=tab_words[0].rearrange("p t x -> p (t x)").bitcast(I32))
+        wg_s_raw = sharing("wg_s_raw", [P, 2, R // 4], I32, WG_SCALES_THEN_TOKEN_WORDS)
+        nc.vector.memset(wg_s_raw[:], 0)
+        load_scales(wg_s_raw, wg_scales)
+
+        wu_raw = {}
+        for a in range(2):
+            wu_raw[0, a] = load_wu(sharing(f"wu_raw0{a}", [P, 4, PASS], F32, WU_THEN_ROWS + ROW_BYTES * a), 0, a)
+        nc.sync.dma_start(out=tok_s[1][0:SHIFT_ROWS, :].bitcast(I32), in_=tok_s[0][4 : 4 + SHIFT_ROWS, :].bitcast(I32))
+        for a in range(2):
+            wu_raw[1, a] = load_wu(held(f"wu_raw1{a}", [P, 4, PASS], F32), 1, a)
+
         wd4_w = held("wd4_w", [P, 2, N // 2], I32)
         nc.sync.dma_start(out=wd4_w[:], in_=wd4_words.rearrange("a p x -> p a x").bitcast(I32))
         wd8_w = held("wd8_w", [P, 2, N], I32)
         nc.sync.dma_start(out=wd8_w[:], in_=wd8_words.rearrange("a p n x -> p a (n x)").bitcast(I32))
-        wd4_s = load_scales(held("wd4_s", [P, 2, N // 4], I32), wd4_scales, nc.sync, nc.vector)
-        wd8_s = load_scales(held("wd8_s", [P, 2, N // 4], I32), wd8_scales, nc.sync, nc.vector)
+        wd_s = held("wd_s", [P, 2, 2, N // 4], I32)
+        nc.vector.memset(wd_s[:], 0)
+        load_scales(wd_s[:, 0], wd4_scales)
+        load_scales(wd_s[:, 1], wd8_scales)
+        wd4_s, wd8_s = wd_s[:, 0].bitcast(U8), wd_s[:, 1].bitcast(U8)
         bias = held("bias", [P, N // P], F32)
-        with nc.allow_non_contiguous_dma(reason="one bias value a partition"):
+        with nc.allow_non_contiguous_dma(reason="one bias value for each partition and output tile"):
             nc.sync.dma_start(out=bias[:], in_=b.rearrange("(c p) -> p c", p=P))
         weight = held("weight", [P, J], F32)
         nc.sync.dma_start(out=weight[:], in_=wgo)
+
+        wg_w = sharing("wg_w", [P, 2, 2, 4, 2 * P], U8, TAB_SCALES_THEN_WG_WORDS)
+        nc.vector.tensor_copy(
+            out=wg_w[:].bitcast(U16).rearrange("p a rb t m -> p (a rb) t m"),
+            in_=wg_raw[:].bitcast(U16).rearrange("p a (rb m t) -> p (a rb) t m", rb=2, t=4),
+        )
+        wg_s = held("wg_s", [P, 2, 2, 4, P], U8)
+
+        tok_w, wu_w, wu_s, y_sb, rows = {}, {}, {}, {}, {}
+        h_w = [held(f"h_w{rb}", [P, J], U32) for rb in range(2)]
+        h_s = [held(f"h_s{rb}", [P, J], U8) for rb in range(2)]
+
+        def gather_words(half, both):
+            listed = offsets[:, half * HALF // LIST_COLUMN : (half + 1) * HALF // LIST_COLUMN]
+            nc.vector.tensor_copy(both[:], tab_w[:].bitcast(U32).indirect(listed))
+            tok_w[half] = held(f"tok_w{half}", [P, 2, 2 * HALF], U8)
+            nc.vector.tensor_copy(
+                out=tok_w[half][:].bitcast(U16), in_=both[:].bitcast(U16).rearrange("p (j a) -> p a j", a=2)
+            )
+
+        def token_operand(a, first, count):
+            half, j0 = divmod(first, HALF)
+            return tok_w[half][:, a, 2 * j0 : 2 * (j0 + count)].bitcast(FP4X4), tok_s[a][:, first : first + count]
+
+        def quantize_wu(rb, a):
+            grouped = ring.tile([P, 4, P, 4], BF16, name="wu_grouped", align_bytes=64)
+            source = wu_raw[rb, a][:].rearrange("p i (m t) -> p m i t", t=4)
+            for t0 in (0, 2):
+                nc.scalar.copy(
+                    out=grouped[:, t0 : t0 + 2, :, :].rearrange("p t m i -> p m i t"), in_=source[:, :, :, t0 : t0 + 2]
+                )
+            wu_w[rb, a] = held(f"wu_w{rb}{a}", [P, PASS], U32)
+            wu_s[rb, a] = held(f"wu_s{rb}{a}", [P, PASS], U8)
+            nc.vector.quantize_mx(
+                out=wu_w[rb, a][:].bitcast(FP8X4),
+                scales=wu_s[rb, a][:],
+                in_=grouped[:].rearrange("p t m i -> p (t m i)"),
+            )
+
+        def hidden(rb, g):
+            first = g * GROUP
+            if (rb, g) == (1, J // GROUP - 1):
+                gate = sharing("last_gate", [P, 4, GROUP], F32, LAST_GATE_THEN_Y)
+            else:
+                gate = held(f"gate{rb}{g}", [P, 4, GROUP], F32)
+            for t0 in (0, 2):
+                ga = psum_ga.tile([P, 2, GROUP], F32, name="ga")
+                for t in range(2):
+                    for a in range(2):
+                        words, scales = token_operand(a, first, GROUP)
+                        nc.tensor.matmul_mx(
+                            out=ga[:, t, :],
+                            lhsT=wg_w[:, a, rb, t0 + t, :].bitcast(FP4X4),
+                            lhsT_scale=wg_s[:, a, rb, t0 + t, :],
+                            rhs=words,
+                            rhs_scale=scales,
+                            start=(a == 0),
+                            stop=(a == 1),
+                        )
+                nc.scalar.activation(out=gate[:, t0 : t0 + 2, :], in_=ga[:], func=ACT.Sigmoid)
+            h = ring.tile([P, GROUP, 4], BF16, name="h", align_bytes=64)
+            for j0 in range(0, GROUP, P):
+                ub = psum_ub.tile([P, 4, P], F32, name="ub")
+                for t in range(4):
+                    for a in range(2):
+                        words, scales = token_operand(a, first + j0, P)
+                        nc.tensor.matmul_mx(
+                            out=ub[:, t, :],
+                            lhsT=wu_w[rb, a][:, P * t : P * (t + 1)].bitcast(FP8X4),
+                            lhsT_scale=wu_s[rb, a][:, P * t : P * (t + 1)],
+                            rhs=words,
+                            rhs_scale=scales,
+                            start=(a == 0),
+                            stop=(a == 1),
+                        )
+                nc.vector.tensor_tensor(
+                    h[:, j0 : j0 + P, :].rearrange("p (c e) t -> p c t e", e=2),
+                    ub[:].rearrange("p t (c e) -> p c t e", e=2),
+                    gate[:, :, j0 : j0 + P].rearrange("p t (c e) -> p c t e", e=2),
+                    MULT,
+                )
+            nc.vector.quantize_mx(
+                out=h_w[rb][:, first : first + GROUP].bitcast(FP8X4),
+                scales=h_s[rb][:, first : first + GROUP],
+                in_=h[:].rearrange("p j t -> p (j t)"),
+            )
+
+        def down(piece, n, biased):
+            first, count = PIECES[piece]
+            step = count if count == PASS else P
+            y = psum_y.tile([P, count], F32, name="y")
+            for j0 in range(0, count, step):
+                tokens = slice(first + j0, first + j0 + step)
+                for rb in range(2):
+                    words, scales = h_w[rb][:, tokens].bitcast(FP8X4), h_s[rb][:, tokens]
+                    nc.tensor.matmul_mx(
+                        out=y[:, j0 : j0 + step],
+                        lhsT=wd4_w[:].bitcast(U8)[:, rb, 2 * P * n : 2 * P * (n + 1)].bitcast(FP4X4),
+                        lhsT_scale=wd4_s[:, rb, P * n : P * (n + 1)],
+                        rhs=words,
+                        rhs_scale=scales,
+                        start=(rb == 0),
+                        stop=False,
+                    )
+                    nc.tensor.matmul_mx(
+                        out=y[:, j0 : j0 + step],
+                        lhsT=wd8_w[:, rb, P * n : P * (n + 1)].bitcast(FP8X4),
+                        lhsT_scale=wd8_s[:, rb, P * n : P * (n + 1)],
+                        rhs=words,
+                        rhs_scale=scales,
+                        start=False,
+                        stop=(rb == 1),
+                    )
+            nc.scalar.activation(out=biased[:], in_=y[:], func=ACT.Identity, bias=bias[:, n : n + 1])
+            y_sb[piece, n] = biased
+
+        def down_held(piece, tiles):
+            for n in tiles:
+                down(piece, n, held(f"y_sb{piece}{n}", [P, PIECES[piece][1]], F32))
+
+        gather_words(0, held("tok_both0", [P, HALF], U32))
+        nc.vector.tensor_copy(
+            out=wg_s[:].rearrange("p a rb t m -> p (a rb) t m"),
+            in_=wg_s_raw[:].bitcast(U8).rearrange("p a (rb m t) -> p (a rb) t m", rb=2, t=4),
+        )
         quantize_wu(0, 0)
         quantize_wu(0, 1)
         hidden(0, 0)
-        gather_tokens(1)
-        permute_wg_words(1, held("wg_w1", [P, 2, 4, 2 * P], U8))
-        permute_wg_scales(1, held("wg_s1", [P, 2, 4, P], U8))
         quantize_wu(1, 0)
         quantize_wu(1, 1)
         hidden(0, 1)
+        gather_words(1, sharing("tok_both1", [P, HALF], U32, WG_SCALES_THEN_TOKEN_WORDS))
+        hidden(0, 2)
         hidden(1, 0)
         hidden(1, 1)
-        gather_tokens(2)
-        hidden(0, 2)
-        down(0)
+        down_held(0, range(N // P))
         hidden(1, 2)
-        down(1, (0, 1,))
-        gather_tokens(3)
+        down_held(1, (0, 1))
         hidden(0, 3)
         hidden(1, 3)
-        down(1, (2, 3,))
-        down(2)
-        for n in range(4):
-            placed[n] = held(f"placed{n}", [P, T], F32)
-            nc.vector.memset(placed[n][:].bitcast(I32), 0)
-        for c in range(len(CHUNKS)):
+        for n in (2, 3):
+            down(1, n, sharing(f"y_late{n}", [P, PIECES[1][1]], F32, LAST_GATE_THEN_Y + 4 * PIECES[1][1] * n))
+        down_held(2, range(N // P))
+
+        for n in range(N // P):
+            if n < 2:
+                rows[n] = held(f"rows{n}", [P, T], F32)
+            else:
+                rows[n] = sharing(f"rows{n}", [P, T], F32, WU_THEN_ROWS + ROW_BYTES * (n - 2))
+            nc.vector.memset(rows[n][:].bitcast(I32), 0)
+        for piece, (first, count) in enumerate(PIECES):
+            listed = offsets[:, first // LIST_COLUMN : (first + count) // LIST_COLUMN]
             for n in range(N // P):
-                scatter(n, c)
-                if c == len(CHUNKS) - 1:
-                    nc.sync.dma_start(out=out[P * n : P * (n + 1), :], in_=placed[n][:])
+                nc.vector.tensor_tensor(
+                    rows[n][:].indirect(listed), y_sb[piece, n][:], weight[:, first : first + count], MULT
+                )
+                if piece == len(PIECES) - 1:
+                    nc.sync.dma_start(out=out[P * n : P * (n + 1), :], in_=rows[n][:])

@@ -22,14 +22,13 @@ QUADRANT = 32
 LIST_COLUMN = 16
 HALF = J // 2
 GROUP = 256
-PIECES = ((0, 256), (256, 256), (512, 512))
 SHIFT_ROWS = 112
 
-TAB_SCALES_THEN_WG_WORDS = 0
-WG_SCALES_THEN_TOKEN_WORDS = 4096
-LAST_GATE_THEN_Y = 6144
-WU_THEN_ROWS = 10240
-ROW_BYTES = 4 * T
+LAST_GATE_THEN_Y = 0
+BOTH0_THEN_SCALES = 4096
+WG_THEN_ROWS = 8192
+WU_THEN_GATES = 16384
+AFTER_WU = {(0, 0): 0}
 
 
 def tile_list_modp_gsigm_res_noneb_kernel(
@@ -50,54 +49,67 @@ def tile_list_modp_gsigm_res_noneb_kernel(
         def sharing(name, shape, dtype, offset):
             return shared.tile(shape, dtype, name=name, align_bytes=64, offset=offset)
 
-        def load_scales(tile, src):
+        def load_scales(queue, tile, src):
             for q in range(P // QUADRANT):
-                nc.sync.dma_start(
+                queue.dma_start(
                     out=tile[QUADRANT * q : QUADRANT * q + 4, :, :],
                     in_=src[:, 4 * q : 4 * q + 4, :].rearrange("a r x -> r a x").bitcast(I32),
                 )
 
-        def load_wu(raw, rb, a):
+        def load_wu(rb, a):
+            raw = sharing(f"wu_raw{rb}{a}", [P, 4, PASS], F32, WU_THEN_GATES + 8192 * (2 * rb + a))
             block = wu[PASS * a : PASS * (a + 1), PASS * rb : PASS * (rb + 1)]
             nc.sync.dma_start(out=raw[:], in_=block.rearrange("(p i) c -> p i c", i=4))
             return raw
 
+        def load_wg(rb):
+            if rb == 0:
+                raw = sharing("wg_raw0", [P, 2, PASS // 2], I32, WG_THEN_ROWS)
+            else:
+                raw = held("wg_raw1", [P, 2, PASS // 2], I32)
+            block = wg_words[:, :, 2 * PASS * rb : 2 * PASS * (rb + 1)]
+            nc.sync.dma_start(out=raw[:], in_=block.rearrange("a p x -> p a x").bitcast(I32))
+            return raw
+
+        def listed(first, count):
+            return offsets[:, first // LIST_COLUMN : (first + count) // LIST_COLUMN]
+
+        tab_s = held("tab_s", [P, T // 4], I32)
+        nc.vector.memset(tab_s[:], 0)
+        rows = [held("rows0", [P, T], F32)]
+        nc.vector.memset(rows[0][:].bitcast(I32), 0)
+        wg_s_raw = held("wg_s_raw", [P, 2, R // 4], I32)
+        nc.vector.memset(wg_s_raw[:], 0)
+        tok_s = [held(f"tok_s{a}", [P, J], U8) for a in range(2)]
+        wd_s = held("wd_s", [P, 2, 2, N // 4], I32)
+        nc.vector.memset(tok_s[1][:].bitcast(I32), 0)
+        nc.vector.memset(wd_s[:], 0)
+        warm = held("warm", [P, 2], F32)
+        nc.gpsimd.memset(warm[:, 0:1], 0.0)
+        nc.scalar.activation(out=warm[:, 1:2], in_=warm[:, 0:1], func=ACT.Sigmoid)
+
         offsets = keep.tile([P, J // LIST_COLUMN], U16, name="offsets")
         nc.sync.dma_start(offsets[:], offs)
-        wg_raw = held("wg_raw", [P, 2, R // 2], I32)
-        nc.sync.dma_start(out=wg_raw[:], in_=wg_words.rearrange("a p x -> p a x").bitcast(I32))
-
-        tab_s = sharing("tab_s", [P, T // 4], I32, TAB_SCALES_THEN_WG_WORDS)
-        nc.gpsimd.memset(tab_s[:], 0)
+        wg_raw = {0: load_wg(0)}
         for q in range(P // QUADRANT):
             nc.sync.dma_start(
                 out=tab_s[QUADRANT * q : QUADRANT * q + 8, :], in_=tab_scales[:, 4 * q : 4 * q + 4, :].bitcast(I32)
             )
-        tok_s = [held(f"tok_s{a}", [P, J], U8) for a in range(2)]
-        nc.vector.memset(tok_s[1][:].bitcast(I32), 0)
-        nc.vector.tensor_copy(tok_s[0][:], tab_s[:].bitcast(U8).indirect(offsets[:]))
-
         tab_w = held("tab_w", [P, T], I32)
         nc.sync.dma_start(out=tab_w[:], in_=tab_words[0].rearrange("p t x -> p (t x)").bitcast(I32))
-        wg_s_raw = sharing("wg_s_raw", [P, 2, R // 4], I32, WG_SCALES_THEN_TOKEN_WORDS)
-        nc.vector.memset(wg_s_raw[:], 0)
-        load_scales(wg_s_raw, wg_scales)
-
+        load_scales(nc.scalar, wg_s_raw, wg_scales)
         wu_raw = {}
-        for a in range(2):
-            wu_raw[0, a] = load_wu(sharing(f"wu_raw0{a}", [P, 4, PASS], F32, WU_THEN_ROWS + ROW_BYTES * a), 0, a)
-        nc.sync.dma_start(out=tok_s[1][0:SHIFT_ROWS, :].bitcast(I32), in_=tok_s[0][4 : 4 + SHIFT_ROWS, :].bitcast(I32))
-        for a in range(2):
-            wu_raw[1, a] = load_wu(held(f"wu_raw1{a}", [P, 4, PASS], F32), 1, a)
-
+        wu_raw[0, 0] = load_wu(0, 0)
+        wu_raw[0, 1] = load_wu(0, 1)
+        wg_raw[1] = load_wg(1)
+        wu_raw[1, 0] = load_wu(1, 0)
+        wu_raw[1, 1] = load_wu(1, 1)
         wd4_w = held("wd4_w", [P, 2, N // 2], I32)
         nc.sync.dma_start(out=wd4_w[:], in_=wd4_words.rearrange("a p x -> p a x").bitcast(I32))
         wd8_w = held("wd8_w", [P, 2, N], I32)
         nc.sync.dma_start(out=wd8_w[:], in_=wd8_words.rearrange("a p n x -> p a (n x)").bitcast(I32))
-        wd_s = held("wd_s", [P, 2, 2, N // 4], I32)
-        nc.vector.memset(wd_s[:], 0)
-        load_scales(wd_s[:, 0], wd4_scales)
-        load_scales(wd_s[:, 1], wd8_scales)
+        load_scales(nc.sync, wd_s[:, 0], wd4_scales)
+        load_scales(nc.sync, wd_s[:, 1], wd8_scales)
         wd4_s, wd8_s = wd_s[:, 0].bitcast(U8), wd_s[:, 1].bitcast(U8)
         bias = held("bias", [P, N // P], F32)
         with nc.allow_non_contiguous_dma(reason="one bias value for each partition and output tile"):
@@ -105,36 +117,54 @@ def tile_list_modp_gsigm_res_noneb_kernel(
         weight = held("weight", [P, J], F32)
         nc.sync.dma_start(out=weight[:], in_=wgo)
 
-        wg_w = sharing("wg_w", [P, 2, 2, 4, 2 * P], U8, TAB_SCALES_THEN_WG_WORDS)
-        nc.vector.tensor_copy(
-            out=wg_w[:].bitcast(U16).rearrange("p a rb t m -> p (a rb) t m"),
-            in_=wg_raw[:].bitcast(U16).rearrange("p a (rb m t) -> p (a rb) t m", rb=2, t=4),
-        )
-        wg_s = held("wg_s", [P, 2, 2, 4, P], U8)
-
-        tok_w, wu_w, wu_s, y_sb, rows = {}, {}, {}, {}, {}
+        tok_w, wg_w, wg_s, wu_w, wu_s, gate = {}, {}, {}, {}, {}, {}
         h_w = [held(f"h_w{rb}", [P, J], U32) for rb in range(2)]
         h_s = [held(f"h_s{rb}", [P, J], U8) for rb in range(2)]
 
-        def gather_words(half, both):
-            listed = offsets[:, half * HALF // LIST_COLUMN : (half + 1) * HALF // LIST_COLUMN]
-            nc.vector.tensor_copy(both[:], tab_w[:].bitcast(U32).indirect(listed))
+        def gather_scales():
+            nc.vector.tensor_copy(tok_s[0][:], tab_s[:].bitcast(U8).indirect(offsets[:]))
+            nc.scalar.dma_start(
+                out=tok_s[1][0:SHIFT_ROWS, :].bitcast(I32), in_=tok_s[0][4 : 4 + SHIFT_ROWS, :].bitcast(I32)
+            )
+
+        def gather_words(half):
+            if half == 0:
+                both = sharing("tok_both0", [P, HALF], U32, BOTH0_THEN_SCALES)
+            else:
+                both = sharing("tok_both1", [P, HALF], U32, BOTH0_THEN_SCALES)
+            nc.vector.tensor_copy(both[:], tab_w[:].bitcast(U32).indirect(listed(half * HALF, HALF)))
             tok_w[half] = held(f"tok_w{half}", [P, 2, 2 * HALF], U8)
             nc.vector.tensor_copy(
                 out=tok_w[half][:].bitcast(U16), in_=both[:].bitcast(U16).rearrange("p (j a) -> p a j", a=2)
             )
 
+        def order_wg_words(rb):
+            wg_w[rb] = held(f"wg_w{rb}", [P, 2, 4, 2 * P], U8)
+            nc.vector.tensor_copy(
+                out=wg_w[rb][:].bitcast(U16), in_=wg_raw[rb][:].bitcast(U16).rearrange("p a (m t) -> p a t m", t=4)
+            )
+
+        def order_wg_scales(rb):
+            if rb == 0:
+                wg_s[rb] = held("wg_s0", [P, 2, 4, P], U8)
+            else:
+                wg_s[rb] = sharing("wg_s1", [P, 2, 4, P], U8, BOTH0_THEN_SCALES)
+            source = wg_s_raw[:].bitcast(U8)[:, :, PASS * rb : PASS * (rb + 1)]
+            nc.vector.tensor_copy(out=wg_s[rb][:], in_=source.rearrange("p a (m t) -> p a t m", t=4))
+
         def token_operand(a, first, count):
             half, j0 = divmod(first, HALF)
             return tok_w[half][:, a, 2 * j0 : 2 * (j0 + count)].bitcast(FP4X4), tok_s[a][:, first : first + count]
 
-        def quantize_wu(rb, a):
+        def quantize_wu(rb, a, split):
             grouped = ring.tile([P, 4, P, 4], BF16, name="wu_grouped", align_bytes=64)
             source = wu_raw[rb, a][:].rearrange("p i (m t) -> p m i t", t=4)
             for t0 in (0, 2):
-                nc.scalar.copy(
-                    out=grouped[:, t0 : t0 + 2, :, :].rearrange("p t m i -> p m i t"), in_=source[:, :, :, t0 : t0 + 2]
-                )
+                to = grouped[:, t0 : t0 + 2, :, :].rearrange("p t m i -> p m i t")
+                if t0 >= 4 - 2 * split:
+                    nc.vector.tensor_copy(out=to, in_=source[:, :, :, t0 : t0 + 2])
+                else:
+                    nc.scalar.copy(out=to, in_=source[:, :, :, t0 : t0 + 2])
             wu_w[rb, a] = held(f"wu_w{rb}{a}", [P, PASS], U32)
             wu_s[rb, a] = held(f"wu_s{rb}{a}", [P, PASS], U8)
             nc.vector.quantize_mx(
@@ -143,12 +173,14 @@ def tile_list_modp_gsigm_res_noneb_kernel(
                 in_=grouped[:].rearrange("p t m i -> p (t m i)"),
             )
 
-        def hidden(rb, g):
+        def gates(rb, g):
             first = g * GROUP
             if (rb, g) == (1, J // GROUP - 1):
-                gate = sharing("last_gate", [P, 4, GROUP], F32, LAST_GATE_THEN_Y)
+                gate[rb, g] = sharing("last_gate", [P, 4, GROUP], F32, LAST_GATE_THEN_Y)
+            elif (rb, g) in AFTER_WU:
+                gate[rb, g] = sharing(f"gate{rb}{g}", [P, 4, GROUP], F32, WU_THEN_GATES + 8192 * AFTER_WU[rb, g])
             else:
-                gate = held(f"gate{rb}{g}", [P, 4, GROUP], F32)
+                gate[rb, g] = held(f"gate{rb}{g}", [P, 4, GROUP], F32)
             for t0 in (0, 2):
                 ga = psum_ga.tile([P, 2, GROUP], F32, name="ga")
                 for t in range(2):
@@ -156,14 +188,17 @@ def tile_list_modp_gsigm_res_noneb_kernel(
                         words, scales = token_operand(a, first, GROUP)
                         nc.tensor.matmul_mx(
                             out=ga[:, t, :],
-                            lhsT=wg_w[:, a, rb, t0 + t, :].bitcast(FP4X4),
-                            lhsT_scale=wg_s[:, a, rb, t0 + t, :],
+                            lhsT=wg_w[rb][:, a, t0 + t, :].bitcast(FP4X4),
+                            lhsT_scale=wg_s[rb][:, a, t0 + t, :],
                             rhs=words,
                             rhs_scale=scales,
                             start=(a == 0),
                             stop=(a == 1),
                         )
-                nc.scalar.activation(out=gate[:, t0 : t0 + 2, :], in_=ga[:], func=ACT.Sigmoid)
+                nc.scalar.activation(out=gate[rb, g][:, t0 : t0 + 2, :], in_=ga[:], func=ACT.Sigmoid)
+
+        def hidden(rb, g):
+            first = g * GROUP
             h = ring.tile([P, GROUP, 4], BF16, name="h", align_bytes=64)
             for j0 in range(0, GROUP, P):
                 ub = psum_ub.tile([P, 4, P], F32, name="ub")
@@ -182,7 +217,7 @@ def tile_list_modp_gsigm_res_noneb_kernel(
                 nc.vector.tensor_tensor(
                     h[:, j0 : j0 + P, :].rearrange("p (c e) t -> p c t e", e=2),
                     ub[:].rearrange("p t (c e) -> p c t e", e=2),
-                    gate[:, :, j0 : j0 + P].rearrange("p t (c e) -> p c t e", e=2),
+                    gate[rb, g][:, :, j0 : j0 + P].rearrange("p t (c e) -> p c t e", e=2),
                     MULT,
                 )
             nc.vector.quantize_mx(
@@ -191,8 +226,7 @@ def tile_list_modp_gsigm_res_noneb_kernel(
                 in_=h[:].rearrange("p j t -> p (j t)"),
             )
 
-        def down(piece, n, biased):
-            first, count = PIECES[piece]
+        def down(n, first, count, biased):
             step = count if count == PASS else P
             y = psum_y.tile([P, count], F32, name="y")
             for j0 in range(0, count, step):
@@ -217,48 +251,63 @@ def tile_list_modp_gsigm_res_noneb_kernel(
                         start=False,
                         stop=(rb == 1),
                     )
-            nc.scalar.activation(out=biased[:], in_=y[:], func=ACT.Identity, bias=bias[:, n : n + 1])
-            y_sb[piece, n] = biased
+            nc.scalar.activation(out=biased, in_=y[:], func=ACT.Identity, bias=bias[:, n : n + 1])
 
-        def down_held(piece, tiles):
-            for n in tiles:
-                down(piece, n, held(f"y_sb{piece}{n}", [P, PIECES[piece][1]], F32))
+        def scatter(n, first, count, biased):
+            nc.vector.tensor_tensor(
+                rows[n % 2][:].indirect(listed(first, count)), biased, weight[:, first : first + count], MULT
+            )
 
-        gather_words(0, held("tok_both0", [P, HALF], U32))
-        nc.vector.tensor_copy(
-            out=wg_s[:].rearrange("p a rb t m -> p (a rb) t m"),
-            in_=wg_s_raw[:].bitcast(U8).rearrange("p a (rb m t) -> p (a rb) t m", rb=2, t=4),
-        )
-        quantize_wu(0, 0)
-        quantize_wu(0, 1)
+        def store(n):
+            nc.sync.dma_start(out=out[P * n : P * (n + 1), :], in_=rows[n % 2][:])
+
+        y_sb = [held(f"y_sb{n}", [P, J], F32) for n in range(N // P)]
+
+        def piece(n, first, count):
+            down(n, first, count, y_sb[n][:, first : first + count])
+            scatter(n, first, count, y_sb[n][:, first : first + count])
+
+        order_wg_words(0)
+        rows.append(sharing("rows1", [P, T], F32, WG_THEN_ROWS))
+        nc.gpsimd.memset(rows[1][:].bitcast(I32), 0)
+        gather_scales()
+        gather_words(0)
+        order_wg_scales(0)
+        quantize_wu(0, 0, 0)
+        gates(0, 0)
+        gather_words(1)
+        gates(0, 1)
+        quantize_wu(0, 1, 2)
+        gates(0, 2)
+        order_wg_words(1)
+        order_wg_scales(1)
+        gates(0, 3)
         hidden(0, 0)
-        quantize_wu(1, 0)
-        quantize_wu(1, 1)
+        quantize_wu(1, 0, 0)
         hidden(0, 1)
-        gather_words(1, sharing("tok_both1", [P, HALF], U32, WG_SCALES_THEN_TOKEN_WORDS))
+        gates(1, 0)
+        quantize_wu(1, 1, 0)
         hidden(0, 2)
-        hidden(1, 0)
-        hidden(1, 1)
-        down_held(0, range(N // P))
-        hidden(1, 2)
-        down_held(1, (0, 1))
+        gates(1, 1)
         hidden(0, 3)
+        gates(1, 2)
+        hidden(1, 0)
+        gates(1, 3)
+        hidden(1, 1)
+        hidden(1, 2)
+        piece(0, 0, GROUP)
+        piece(1, 0, GROUP)
         hidden(1, 3)
+        late = sharing("y_late", [P, 2 * GROUP], F32, LAST_GATE_THEN_Y)
+        down(0, GROUP, 2 * GROUP, late[:])
+        scatter(0, GROUP, 2 * GROUP, late[:])
+        piece(0, 3 * GROUP, GROUP)
+        store(0)
+        piece(1, GROUP, 2 * GROUP)
+        piece(1, 3 * GROUP, GROUP)
+        store(1)
         for n in (2, 3):
-            down(1, n, sharing(f"y_late{n}", [P, PIECES[1][1]], F32, LAST_GATE_THEN_Y + 4 * PIECES[1][1] * n))
-        down_held(2, range(N // P))
-
-        for n in range(N // P):
-            if n < 2:
-                rows[n] = held(f"rows{n}", [P, T], F32)
-            else:
-                rows[n] = sharing(f"rows{n}", [P, T], F32, WU_THEN_ROWS + ROW_BYTES * (n - 2))
-            nc.vector.memset(rows[n][:].bitcast(I32), 0)
-        for piece, (first, count) in enumerate(PIECES):
-            listed = offsets[:, first // LIST_COLUMN : (first + count) // LIST_COLUMN]
-            for n in range(N // P):
-                nc.vector.tensor_tensor(
-                    rows[n][:].indirect(listed), y_sb[piece, n][:], weight[:, first : first + count], MULT
-                )
-                if piece == len(PIECES) - 1:
-                    nc.sync.dma_start(out=out[P * n : P * (n + 1), :], in_=rows[n][:])
+            for first in (0, HALF):
+                down(n, first, HALF, y_sb[n][:, first : first + HALF])
+            scatter(n, 0, J, y_sb[n][:])
+            store(n)

@@ -26,6 +26,7 @@ SHIFT_ROWS = 112
 
 LAST_GATE_THEN_Y = 0
 BOTH0_THEN_SCALES = 4096
+WG_S_THEN_BOTH1 = 6144
 WG_THEN_ROWS = 8192
 WU_THEN_GATES = 16384
 AFTER_WU = {(0, 0): 0}
@@ -39,9 +40,8 @@ def tile_list_modp_gsigm_res_noneb_kernel(
         keep = ctx.enter_context(tc.tile_pool(name="keep", bufs=1))
         shared = ctx.enter_context(tc.tile_pool(name="shared", bufs=1))
         ring = ctx.enter_context(tc.tile_pool(name="ring", bufs=3))
-        psum_ga = ctx.enter_context(tc.psum_pool(name="psum_ga", bufs=3))
-        psum_ub = ctx.enter_context(tc.psum_pool(name="psum_ub", bufs=3))
-        psum_y = ctx.enter_context(tc.psum_pool(name="psum_y", bufs=2))
+        psum_ga = ctx.enter_context(tc.psum_pool(name="psum_ga", bufs=4))
+        psum_ub = ctx.enter_context(tc.psum_pool(name="psum_ub", bufs=4))
 
         def held(name, shape, dtype):
             return keep.tile(shape, dtype, name=name, align_bytes=64)
@@ -76,14 +76,15 @@ def tile_list_modp_gsigm_res_noneb_kernel(
 
         tab_s = held("tab_s", [P, T // 4], I32)
         nc.vector.memset(tab_s[:], 0)
-        rows = [held("rows0", [P, T], F32)]
+        rows = [held(f"rows{c}", [P, T], F32) for c in range(2)]
         nc.vector.memset(rows[0][:].bitcast(I32), 0)
-        wg_s_raw = held("wg_s_raw", [P, 2, R // 4], I32)
+        wg_s_raw = sharing("wg_s_raw", [P, 2, R // 4], I32, WG_S_THEN_BOTH1)
         nc.vector.memset(wg_s_raw[:], 0)
         tok_s = [held(f"tok_s{a}", [P, J], U8) for a in range(2)]
         wd_s = held("wd_s", [P, 2, 2, N // 4], I32)
         nc.vector.memset(tok_s[1][:].bitcast(I32), 0)
         nc.vector.memset(wd_s[:], 0)
+        nc.vector.memset(rows[1][:].bitcast(I32), 0)
         warm = held("warm", [P, 2], F32)
         nc.gpsimd.memset(warm[:, 0:1], 0.0)
         nc.scalar.activation(out=warm[:, 1:2], in_=warm[:, 0:1], func=ACT.Sigmoid)
@@ -97,9 +98,11 @@ def tile_list_modp_gsigm_res_noneb_kernel(
             )
         tab_w = held("tab_w", [P, T], I32)
         nc.sync.dma_start(out=tab_w[:], in_=tab_words[0].rearrange("p t x -> p (t x)").bitcast(I32))
-        load_scales(nc.scalar, wg_s_raw, wg_scales)
+        load_scales(nc.sync, wg_s_raw, wg_scales)
         wu_raw = {}
         wu_raw[0, 0] = load_wu(0, 0)
+        nc.vector.tensor_copy(tok_s[0][:], tab_s[:].bitcast(U8).indirect(offsets[:]))
+        nc.sync.dma_start(out=tok_s[1][0:SHIFT_ROWS, :].bitcast(I32), in_=tok_s[0][4 : 4 + SHIFT_ROWS, :].bitcast(I32))
         wu_raw[0, 1] = load_wu(0, 1)
         wg_raw[1] = load_wg(1)
         wu_raw[1, 0] = load_wu(1, 0)
@@ -121,17 +124,11 @@ def tile_list_modp_gsigm_res_noneb_kernel(
         h_w = [held(f"h_w{rb}", [P, J], U32) for rb in range(2)]
         h_s = [held(f"h_s{rb}", [P, J], U8) for rb in range(2)]
 
-        def gather_scales():
-            nc.vector.tensor_copy(tok_s[0][:], tab_s[:].bitcast(U8).indirect(offsets[:]))
-            nc.scalar.dma_start(
-                out=tok_s[1][0:SHIFT_ROWS, :].bitcast(I32), in_=tok_s[0][4 : 4 + SHIFT_ROWS, :].bitcast(I32)
-            )
-
         def gather_words(half):
             if half == 0:
                 both = sharing("tok_both0", [P, HALF], U32, BOTH0_THEN_SCALES)
             else:
-                both = sharing("tok_both1", [P, HALF], U32, BOTH0_THEN_SCALES)
+                both = sharing("tok_both1", [P, HALF], U32, WG_S_THEN_BOTH1)
             nc.vector.tensor_copy(both[:], tab_w[:].bitcast(U32).indirect(listed(half * HALF, HALF)))
             tok_w[half] = held(f"tok_w{half}", [P, 2, 2 * HALF], U8)
             nc.vector.tensor_copy(
@@ -148,7 +145,7 @@ def tile_list_modp_gsigm_res_noneb_kernel(
             if rb == 0:
                 wg_s[rb] = held("wg_s0", [P, 2, 4, P], U8)
             else:
-                wg_s[rb] = sharing("wg_s1", [P, 2, 4, P], U8, BOTH0_THEN_SCALES)
+                wg_s[rb] = held("wg_s1", [P, 2, 4, P], U8)
             source = wg_s_raw[:].bitcast(U8)[:, :, PASS * rb : PASS * (rb + 1)]
             nc.vector.tensor_copy(out=wg_s[rb][:], in_=source.rearrange("p a (m t) -> p a t m", t=4))
 
@@ -182,7 +179,7 @@ def tile_list_modp_gsigm_res_noneb_kernel(
             else:
                 gate[rb, g] = held(f"gate{rb}{g}", [P, 4, GROUP], F32)
             for t0 in (0, 2):
-                ga = psum_ga.tile([P, 2, GROUP], F32, name="ga")
+                ga = psum_ga.tile([P, 2, GROUP], F32, name="ga", tag="bank")
                 for t in range(2):
                     for a in range(2):
                         words, scales = token_operand(a, first, GROUP)
@@ -228,7 +225,7 @@ def tile_list_modp_gsigm_res_noneb_kernel(
 
         def down(n, first, count, biased):
             step = count if count == PASS else P
-            y = psum_y.tile([P, count], F32, name="y")
+            y = psum_ga.tile([P, count], F32, name="y", tag="bank")
             for j0 in range(0, count, step):
                 tokens = slice(first + j0, first + j0 + step)
                 for rb in range(2):
@@ -268,11 +265,9 @@ def tile_list_modp_gsigm_res_noneb_kernel(
             scatter(n, first, count, y_sb[n][:, first : first + count])
 
         order_wg_words(0)
-        rows.append(sharing("rows1", [P, T], F32, WG_THEN_ROWS))
-        nc.gpsimd.memset(rows[1][:].bitcast(I32), 0)
-        gather_scales()
         gather_words(0)
         order_wg_scales(0)
+        order_wg_scales(1)
         quantize_wu(0, 0, 0)
         gates(0, 0)
         gather_words(1)
@@ -280,7 +275,6 @@ def tile_list_modp_gsigm_res_noneb_kernel(
         quantize_wu(0, 1, 2)
         gates(0, 2)
         order_wg_words(1)
-        order_wg_scales(1)
         gates(0, 3)
         hidden(0, 0)
         quantize_wu(1, 0, 0)
@@ -295,18 +289,13 @@ def tile_list_modp_gsigm_res_noneb_kernel(
         gates(1, 3)
         hidden(1, 1)
         hidden(1, 2)
-        piece(0, 0, GROUP)
-        piece(1, 0, GROUP)
         hidden(1, 3)
         late = sharing("y_late", [P, 2 * GROUP], F32, LAST_GATE_THEN_Y)
-        down(0, GROUP, 2 * GROUP, late[:])
-        scatter(0, GROUP, 2 * GROUP, late[:])
-        piece(0, 3 * GROUP, GROUP)
+        piece(0, 0, HALF)
+        down(0, HALF, HALF, late[:])
+        scatter(0, HALF, HALF, late[:])
         store(0)
-        piece(1, GROUP, 2 * GROUP)
-        piece(1, 3 * GROUP, GROUP)
-        store(1)
-        for n in (2, 3):
+        for n in (1, 2, 3):
             for first in (0, HALF):
                 down(n, first, HALF, y_sb[n][:, first : first + HALF])
             scatter(n, 0, J, y_sb[n][:])

@@ -24,12 +24,12 @@ HALF = J // 2
 GROUP = 256
 SHIFT_ROWS = 112
 
-LAST_GATE_THEN_Y = 0
+LAST_GATE_THEN_Y = 81920
 BOTH0_THEN_SCALES = 4096
 WG_S_THEN_BOTH1 = 6144
 WG_THEN_ROWS = 8192
 WU_THEN_GATES = 16384
-AFTER_WU = {(0, 0): 0}
+AFTER_WU = {(0, 0): 2, (0, 1): 3, (1, 0): 6}
 
 
 def tile_list_modp_gsigm_res_noneb_kernel(
@@ -40,8 +40,7 @@ def tile_list_modp_gsigm_res_noneb_kernel(
         keep = ctx.enter_context(tc.tile_pool(name="keep", bufs=1))
         shared = ctx.enter_context(tc.tile_pool(name="shared", bufs=1))
         ring = ctx.enter_context(tc.tile_pool(name="ring", bufs=3))
-        psum_ga = ctx.enter_context(tc.psum_pool(name="psum_ga", bufs=4))
-        psum_ub = ctx.enter_context(tc.psum_pool(name="psum_ub", bufs=4))
+        psum_ga = ctx.enter_context(tc.psum_pool(name="psum_ga", bufs=8))
 
         def held(name, shape, dtype):
             return keep.tile(shape, dtype, name=name, align_bytes=64)
@@ -57,7 +56,7 @@ def tile_list_modp_gsigm_res_noneb_kernel(
                 )
 
         def load_wu(rb, a):
-            raw = sharing(f"wu_raw{rb}{a}", [P, 4, PASS], F32, WU_THEN_GATES + 8192 * (2 * rb + a))
+            raw = sharing(f"wu_raw{rb}{a}", [P, 4, PASS], F32, WU_THEN_GATES + 16384 * (2 * rb + a) + 4096)
             block = wu[PASS * a : PASS * (a + 1), PASS * rb : PASS * (rb + 1)]
             nc.sync.dma_start(out=raw[:], in_=block.rearrange("(p i) c -> p i c", i=4))
             return raw
@@ -73,6 +72,14 @@ def tile_list_modp_gsigm_res_noneb_kernel(
 
         def listed(first, count):
             return offsets[:, first // LIST_COLUMN : (first + count) // LIST_COLUMN]
+
+        wg_w = {}
+
+        def order_wg_words(rb):
+            wg_w[rb] = held(f"wg_w{rb}", [P, 2, 4, 2 * P], U8)
+            nc.vector.tensor_copy(
+                out=wg_w[rb][:].bitcast(U16), in_=wg_raw[rb][:].bitcast(U16).rearrange("p a (m t) -> p a t m", t=4)
+            )
 
         tab_s = held("tab_s", [P, T // 4], I32)
         nc.vector.memset(tab_s[:], 0)
@@ -101,6 +108,7 @@ def tile_list_modp_gsigm_res_noneb_kernel(
         load_scales(nc.sync, wg_s_raw, wg_scales)
         wu_raw = {}
         wu_raw[0, 0] = load_wu(0, 0)
+        order_wg_words(0)
         nc.vector.tensor_copy(tok_s[0][:], tab_s[:].bitcast(U8).indirect(offsets[:]))
         nc.sync.dma_start(out=tok_s[1][0:SHIFT_ROWS, :].bitcast(I32), in_=tok_s[0][4 : 4 + SHIFT_ROWS, :].bitcast(I32))
         wu_raw[0, 1] = load_wu(0, 1)
@@ -120,7 +128,7 @@ def tile_list_modp_gsigm_res_noneb_kernel(
         weight = held("weight", [P, J], F32)
         nc.sync.dma_start(out=weight[:], in_=wgo)
 
-        tok_w, wg_w, wg_s, wu_w, wu_s, gate = {}, {}, {}, {}, {}, {}
+        tok_w, wg_s, wu_w, wu_s, gate = {}, {}, {}, {}, {}
         h_w = [held(f"h_w{rb}", [P, J], U32) for rb in range(2)]
         h_s = [held(f"h_s{rb}", [P, J], U8) for rb in range(2)]
 
@@ -133,12 +141,6 @@ def tile_list_modp_gsigm_res_noneb_kernel(
             tok_w[half] = held(f"tok_w{half}", [P, 2, 2 * HALF], U8)
             nc.vector.tensor_copy(
                 out=tok_w[half][:].bitcast(U16), in_=both[:].bitcast(U16).rearrange("p (j a) -> p a j", a=2)
-            )
-
-        def order_wg_words(rb):
-            wg_w[rb] = held(f"wg_w{rb}", [P, 2, 4, 2 * P], U8)
-            nc.vector.tensor_copy(
-                out=wg_w[rb][:].bitcast(U16), in_=wg_raw[rb][:].bitcast(U16).rearrange("p a (m t) -> p a t m", t=4)
             )
 
         def order_wg_scales(rb):
@@ -156,11 +158,13 @@ def tile_list_modp_gsigm_res_noneb_kernel(
         def quantize_wu(rb, a, split):
             grouped = ring.tile([P, 4, P, 4], BF16, name="wu_grouped", align_bytes=64)
             source = wu_raw[rb, a][:].rearrange("p i (m t) -> p m i t", t=4)
-            for t0 in (0, 2):
-                to = grouped[:, t0 : t0 + 2, :, :].rearrange("p t m i -> p m i t")
-                if t0 >= 4 - 2 * split:
-                    nc.vector.tensor_copy(out=to, in_=source[:, :, :, t0 : t0 + 2])
-                else:
+            if split:
+                nc.vector.tensor_copy(
+                    out=grouped[:].rearrange("p t m i -> p m t i"), in_=source.rearrange("p m i t -> p m t i")
+                )
+            else:
+                for t0 in (0, 2):
+                    to = grouped[:, t0 : t0 + 2, :, :].rearrange("p t m i -> p m i t")
                     nc.scalar.copy(out=to, in_=source[:, :, :, t0 : t0 + 2])
             wu_w[rb, a] = held(f"wu_w{rb}{a}", [P, PASS], U32)
             wu_s[rb, a] = held(f"wu_s{rb}{a}", [P, PASS], U8)
@@ -170,37 +174,38 @@ def tile_list_modp_gsigm_res_noneb_kernel(
                 in_=grouped[:].rearrange("p t m i -> p (t m i)"),
             )
 
-        def gates(rb, g):
-            first = g * GROUP
-            if (rb, g) == (1, J // GROUP - 1):
-                gate[rb, g] = sharing("last_gate", [P, 4, GROUP], F32, LAST_GATE_THEN_Y)
-            elif (rb, g) in AFTER_WU:
-                gate[rb, g] = sharing(f"gate{rb}{g}", [P, 4, GROUP], F32, WU_THEN_GATES + 8192 * AFTER_WU[rb, g])
+        def gates(rb, half, places=range(4)):
+            first = half * HALF
+            if (rb, half) in gate:
+                pass
+            elif (rb, half) == (1, 1):
+                gate[rb, half] = sharing("last_gate", [P, 4, HALF], F32, LAST_GATE_THEN_Y)
+            elif (rb, half) in AFTER_WU:
+                gate[rb, half] = sharing(f"gate{rb}{half}", [P, 4, HALF], F32, WU_THEN_GATES + 8192 * AFTER_WU[rb, half])
             else:
-                gate[rb, g] = held(f"gate{rb}{g}", [P, 4, GROUP], F32)
-            for t0 in (0, 2):
-                ga = psum_ga.tile([P, 2, GROUP], F32, name="ga", tag="bank")
-                for t in range(2):
-                    for a in range(2):
-                        words, scales = token_operand(a, first, GROUP)
-                        nc.tensor.matmul_mx(
-                            out=ga[:, t, :],
-                            lhsT=wg_w[rb][:, a, t0 + t, :].bitcast(FP4X4),
-                            lhsT_scale=wg_s[rb][:, a, t0 + t, :],
-                            rhs=words,
-                            rhs_scale=scales,
-                            start=(a == 0),
-                            stop=(a == 1),
-                        )
-                nc.scalar.activation(out=gate[rb, g][:, t0 : t0 + 2, :], in_=ga[:], func=ACT.Sigmoid)
+                gate[rb, half] = held(f"gate{rb}{half}", [P, 4, HALF], F32)
+            for t in places:
+                ga = psum_ga.tile([P, HALF], F32, name="ga", tag="bank")
+                for a in (1, 0):
+                    words, scales = token_operand(a, first, HALF)
+                    nc.tensor.matmul_mx(
+                        out=ga[:],
+                        lhsT=wg_w[rb][:, a, t, :].bitcast(FP4X4),
+                        lhsT_scale=wg_s[rb][:, a, t, :],
+                        rhs=words,
+                        rhs_scale=scales,
+                        start=(a == 1),
+                        stop=(a == 0),
+                    )
+                nc.scalar.activation(out=gate[rb, half][:, t, :], in_=ga[:], func=ACT.Sigmoid)
 
         def hidden(rb, g):
             first = g * GROUP
             h = ring.tile([P, GROUP, 4], BF16, name="h", align_bytes=64)
             for j0 in range(0, GROUP, P):
-                ub = psum_ub.tile([P, 4, P], F32, name="ub")
+                ub = psum_ga.tile([P, 4, P], F32, name="ub", tag="bank")
                 for t in range(4):
-                    for a in range(2):
+                    for a in (1, 0):
                         words, scales = token_operand(a, first + j0, P)
                         nc.tensor.matmul_mx(
                             out=ub[:, t, :],
@@ -208,13 +213,13 @@ def tile_list_modp_gsigm_res_noneb_kernel(
                             lhsT_scale=wu_s[rb, a][:, P * t : P * (t + 1)],
                             rhs=words,
                             rhs_scale=scales,
-                            start=(a == 0),
-                            stop=(a == 1),
+                            start=(a == 1),
+                            stop=(a == 0),
                         )
                 nc.vector.tensor_tensor(
                     h[:, j0 : j0 + P, :].rearrange("p (c e) t -> p c t e", e=2),
                     ub[:].rearrange("p t (c e) -> p c t e", e=2),
-                    gate[rb, g][:, :, j0 : j0 + P].rearrange("p t (c e) -> p c t e", e=2),
+                    gate[rb, first // HALF][:, :, first % HALF + j0 : first % HALF + j0 + P].rearrange("p t (c e) -> p c t e", e=2),
                     MULT,
                 )
             nc.vector.quantize_mx(
@@ -264,29 +269,26 @@ def tile_list_modp_gsigm_res_noneb_kernel(
             down(n, first, count, y_sb[n][:, first : first + count])
             scatter(n, first, count, y_sb[n][:, first : first + count])
 
-        order_wg_words(0)
         gather_words(0)
         order_wg_scales(0)
         order_wg_scales(1)
         quantize_wu(0, 0, 0)
-        gates(0, 0)
         gather_words(1)
+        quantize_wu(0, 1, 0)
+        gates(0, 0)
         gates(0, 1)
-        quantize_wu(0, 1, 2)
-        gates(0, 2)
         order_wg_words(1)
-        gates(0, 3)
+        quantize_wu(1, 0, 2)
         hidden(0, 0)
-        quantize_wu(1, 0, 0)
-        hidden(0, 1)
-        gates(1, 0)
         quantize_wu(1, 1, 0)
+        hidden(0, 1)
         hidden(0, 2)
-        gates(1, 1)
+        gates(1, 0, (0, 1))
         hidden(0, 3)
-        gates(1, 2)
+        gates(1, 0, (2, 3))
+        gates(1, 1, (0, 1))
         hidden(1, 0)
-        gates(1, 3)
+        gates(1, 1, (2, 3))
         hidden(1, 1)
         hidden(1, 2)
         hidden(1, 3)

@@ -28,6 +28,7 @@ LAST_GATE_THEN_Y = 81920
 BOTH0_THEN_SCALES = 4096
 WG_S_THEN_BOTH1 = 6144
 WG_THEN_ROWS = 8192
+ROWS_AFTER = 7
 WU_THEN_GATES = 16384
 AFTER_WU = {(0, 0): 2, (0, 1): 3, (1, 0): 6}
 
@@ -83,15 +84,14 @@ def tile_list_modp_gsigm_res_noneb_kernel(
 
         tab_s = held("tab_s", [P, T // 4], I32)
         nc.vector.memset(tab_s[:], 0)
-        rows = [held(f"rows{c}", [P, T], F32) for c in range(2)]
+        rows = [held("rows0", [P, T], F32)]
         nc.vector.memset(rows[0][:].bitcast(I32), 0)
         wg_s_raw = sharing("wg_s_raw", [P, 2, R // 4], I32, WG_S_THEN_BOTH1)
         nc.vector.memset(wg_s_raw[:], 0)
-        tok_s = [held(f"tok_s{a}", [P, J], U8) for a in range(2)]
+        tok_s = held("tok_s", [P, 2, J], U8)
         wd_s = held("wd_s", [P, 2, 2, N // 4], I32)
-        nc.vector.memset(tok_s[1][:].bitcast(I32), 0)
+        nc.vector.memset(tok_s[:].bitcast(I32), 0)
         nc.vector.memset(wd_s[:], 0)
-        nc.vector.memset(rows[1][:].bitcast(I32), 0)
         warm = held("warm", [P, 2], F32)
         nc.gpsimd.memset(warm[:, 0:1], 0.0)
         nc.scalar.activation(out=warm[:, 1:2], in_=warm[:, 0:1], func=ACT.Sigmoid)
@@ -99,18 +99,20 @@ def tile_list_modp_gsigm_res_noneb_kernel(
         offsets = keep.tile([P, J // LIST_COLUMN], U16, name="offsets")
         nc.sync.dma_start(offsets[:], offs)
         wg_raw = {0: load_wg(0)}
-        for q in range(P // QUADRANT):
-            nc.sync.dma_start(
-                out=tab_s[QUADRANT * q : QUADRANT * q + 8, :], in_=tab_scales[:, 4 * q : 4 * q + 4, :].bitcast(I32)
-            )
+        nc.sync.dma_start(out=tab_s[0:QUADRANT, :], in_=tab_scales.rearrange("a b x -> b a x").bitcast(I32))
         tab_w = held("tab_w", [P, T], I32)
         nc.sync.dma_start(out=tab_w[:], in_=tab_words[0].rearrange("p t x -> p (t x)").bitcast(I32))
         load_scales(nc.sync, wg_s_raw, wg_scales)
         wu_raw = {}
         wu_raw[0, 0] = load_wu(0, 0)
         order_wg_words(0)
-        nc.vector.tensor_copy(tok_s[0][:], tab_s[:].bitcast(U8).indirect(offsets[:]))
-        nc.sync.dma_start(out=tok_s[1][0:SHIFT_ROWS, :].bitcast(I32), in_=tok_s[0][4 : 4 + SHIFT_ROWS, :].bitcast(I32))
+        tok_s_rows = held("tok_s_rows", [P, J], U8)
+        nc.vector.tensor_copy(tok_s_rows[:], tab_s[:].bitcast(U8).indirect(offsets[:]))
+        for q in range(P // QUADRANT):
+            nc.sync.dma_start(
+                out=tok_s[QUADRANT * q : QUADRANT * q + 4].bitcast(I32),
+                in_=tok_s_rows[8 * q : 8 * q + 8, :].bitcast(I32),
+            )
         wu_raw[0, 1] = load_wu(0, 1)
         wg_raw[1] = load_wg(1)
         wu_raw[1, 0] = load_wu(1, 0)
@@ -128,7 +130,7 @@ def tile_list_modp_gsigm_res_noneb_kernel(
         weight = held("weight", [P, J], F32)
         nc.sync.dma_start(out=weight[:], in_=wgo)
 
-        tok_w, wg_s, wu_w, wu_s, gate = {}, {}, {}, {}, {}
+        tok_w, wg_s, wu_w, wu_s, gate, rounded = {}, {}, {}, {}, {}, {}
         h_w = [held(f"h_w{rb}", [P, J], U32) for rb in range(2)]
         h_s = [held(f"h_s{rb}", [P, J], U8) for rb in range(2)]
 
@@ -151,21 +153,30 @@ def tile_list_modp_gsigm_res_noneb_kernel(
             source = wg_s_raw[:].bitcast(U8)[:, :, PASS * rb : PASS * (rb + 1)]
             nc.vector.tensor_copy(out=wg_s[rb][:], in_=source.rearrange("p a (m t) -> p a t m", t=4))
 
+        def clear_rows():
+            rows.append(sharing("rows1", [P, T], F32, WU_THEN_GATES + 8192 * ROWS_AFTER))
+            nc.vector.memset(rows[1][:].bitcast(I32), 0)
+
         def token_operand(a, first, count):
             half, j0 = divmod(first, HALF)
-            return tok_w[half][:, a, 2 * j0 : 2 * (j0 + count)].bitcast(FP4X4), tok_s[a][:, first : first + count]
+            return tok_w[half][:, a, 2 * j0 : 2 * (j0 + count)].bitcast(FP4X4), tok_s[:, a, first : first + count]
 
-        def quantize_wu(rb, a, split):
+        def round_wu(rb, a, split):
             grouped = ring.tile([P, 4, P, 4], BF16, name="wu_grouped", align_bytes=64)
             source = wu_raw[rb, a][:].rearrange("p i (m t) -> p m i t", t=4)
+            t1 = 4 - 2 * split
+            for t0 in range(0, t1, 2):
+                to = grouped[:, t0 : t0 + 2, :, :].rearrange("p t m i -> p m i t")
+                nc.scalar.copy(out=to, in_=source[:, :, :, t0 : t0 + 2])
             if split:
                 nc.vector.tensor_copy(
-                    out=grouped[:].rearrange("p t m i -> p m t i"), in_=source.rearrange("p m i t -> p m t i")
+                    out=grouped[:, t1:].rearrange("p t m i -> p m t i"),
+                    in_=source[:, :, :, t1:].rearrange("p m i t -> p m t i"),
                 )
-            else:
-                for t0 in (0, 2):
-                    to = grouped[:, t0 : t0 + 2, :, :].rearrange("p t m i -> p m i t")
-                    nc.scalar.copy(out=to, in_=source[:, :, :, t0 : t0 + 2])
+            rounded[rb, a] = grouped
+
+        def quantize_wu(rb, a):
+            grouped = rounded[rb, a]
             wu_w[rb, a] = held(f"wu_w{rb}{a}", [P, PASS], U32)
             wu_s[rb, a] = held(f"wu_s{rb}{a}", [P, PASS], U8)
             nc.vector.quantize_mx(
@@ -233,25 +244,25 @@ def tile_list_modp_gsigm_res_noneb_kernel(
             y = psum_ga.tile([P, count], F32, name="y", tag="bank")
             for j0 in range(0, count, step):
                 tokens = slice(first + j0, first + j0 + step)
-                for rb in range(2):
+                for rb in (1, 0):
                     words, scales = h_w[rb][:, tokens].bitcast(FP8X4), h_s[rb][:, tokens]
-                    nc.tensor.matmul_mx(
-                        out=y[:, j0 : j0 + step],
-                        lhsT=wd4_w[:].bitcast(U8)[:, rb, 2 * P * n : 2 * P * (n + 1)].bitcast(FP4X4),
-                        lhsT_scale=wd4_s[:, rb, P * n : P * (n + 1)],
-                        rhs=words,
-                        rhs_scale=scales,
-                        start=(rb == 0),
-                        stop=False,
-                    )
                     nc.tensor.matmul_mx(
                         out=y[:, j0 : j0 + step],
                         lhsT=wd8_w[:, rb, P * n : P * (n + 1)].bitcast(FP8X4),
                         lhsT_scale=wd8_s[:, rb, P * n : P * (n + 1)],
                         rhs=words,
                         rhs_scale=scales,
+                        start=(rb == 1),
+                        stop=False,
+                    )
+                    nc.tensor.matmul_mx(
+                        out=y[:, j0 : j0 + step],
+                        lhsT=wd4_w[:].bitcast(U8)[:, rb, 2 * P * n : 2 * P * (n + 1)].bitcast(FP4X4),
+                        lhsT_scale=wd4_s[:, rb, P * n : P * (n + 1)],
+                        rhs=words,
+                        rhs_scale=scales,
                         start=False,
-                        stop=(rb == 1),
+                        stop=(rb == 0),
                     )
             nc.scalar.activation(out=biased, in_=y[:], func=ACT.Identity, bias=bias[:, n : n + 1])
 
@@ -272,19 +283,24 @@ def tile_list_modp_gsigm_res_noneb_kernel(
         gather_words(0)
         order_wg_scales(0)
         order_wg_scales(1)
-        quantize_wu(0, 0, 0)
+        round_wu(0, 0, 0)
         gather_words(1)
-        quantize_wu(0, 1, 0)
+        quantize_wu(0, 0)
+        round_wu(0, 1, 1)
         gates(0, 0)
         gates(0, 1)
         order_wg_words(1)
-        quantize_wu(1, 0, 2)
+        quantize_wu(0, 1)
+        round_wu(1, 0, 2)
+        round_wu(1, 1, 0)
         hidden(0, 0)
-        quantize_wu(1, 1, 0)
         hidden(0, 1)
+        quantize_wu(1, 0)
         hidden(0, 2)
         gates(1, 0, (0, 1))
+        quantize_wu(1, 1)
         hidden(0, 3)
+        clear_rows()
         gates(1, 0, (2, 3))
         gates(1, 1, (0, 1))
         hidden(1, 0)
@@ -293,9 +309,9 @@ def tile_list_modp_gsigm_res_noneb_kernel(
         hidden(1, 2)
         hidden(1, 3)
         late = sharing("y_late", [P, 2 * GROUP], F32, LAST_GATE_THEN_Y)
-        piece(0, 0, HALF)
-        down(0, HALF, HALF, late[:])
-        scatter(0, HALF, HALF, late[:])
+        down(0, 0, HALF, late[:])
+        scatter(0, 0, HALF, late[:])
+        piece(0, HALF, HALF)
         store(0)
         for n in (1, 2, 3):
             for first in (0, HALF):

@@ -18,19 +18,21 @@ MULT = mybir.AluOpType.mult
 
 P = 128
 PASS = 512
+PLACES = 4
 QUADRANT = 32
 LIST_COLUMN = 16
 HALF = J // 2
 GROUP = 256
-SHIFT_ROWS = 112
+LAST_FIRST = (1, 0)
 
-LAST_GATE_THEN_Y = 81920
-BOTH0_THEN_SCALES = 4096
-WG_S_THEN_BOTH1 = 6144
-WG_THEN_ROWS = 8192
-ROWS_AFTER = 7
-WU_THEN_GATES = 16384
-AFTER_WU = {(0, 0): 2, (0, 1): 3, (1, 0): 6}
+BLOCK = 8192
+WG_SCALES_THEN_TOKEN_WORDS = 0
+FIRST_GATES = (BLOCK, 2 * BLOCK)
+WU_01 = BLOCK + BLOCK // 2
+THIRD_GATES = 3 * BLOCK
+SECOND_ROWS = 4 * BLOCK
+WU_11 = 3 * BLOCK + BLOCK // 2
+LAST_GATES_THEN_Y = 5 * BLOCK
 
 
 def tile_list_modp_gsigm_res_noneb_kernel(
@@ -41,7 +43,7 @@ def tile_list_modp_gsigm_res_noneb_kernel(
         keep = ctx.enter_context(tc.tile_pool(name="keep", bufs=1))
         shared = ctx.enter_context(tc.tile_pool(name="shared", bufs=1))
         ring = ctx.enter_context(tc.tile_pool(name="ring", bufs=3))
-        psum_ga = ctx.enter_context(tc.psum_pool(name="psum_ga", bufs=8))
+        psum = ctx.enter_context(tc.psum_pool(name="psum", bufs=8))
 
         def held(name, shape, dtype):
             return keep.tile(shape, dtype, name=name, align_bytes=64)
@@ -49,48 +51,43 @@ def tile_list_modp_gsigm_res_noneb_kernel(
         def sharing(name, shape, dtype, offset):
             return shared.tile(shape, dtype, name=name, align_bytes=64, offset=offset)
 
-        def load_scales(queue, tile, src):
+        def listed(first, count):
+            return offsets[:, first // LIST_COLUMN : (first + count) // LIST_COLUMN]
+
+        def load_scales(tile, src):
             for q in range(P // QUADRANT):
-                queue.dma_start(
+                nc.sync.dma_start(
                     out=tile[QUADRANT * q : QUADRANT * q + 4, :, :],
                     in_=src[:, 4 * q : 4 * q + 4, :].rearrange("a r x -> r a x").bitcast(I32),
                 )
 
-        def load_wu(rb, a):
-            raw = sharing(f"wu_raw{rb}{a}", [P, 4, PASS], F32, WU_THEN_GATES + 16384 * (2 * rb + a) + 4096)
-            block = wu[PASS * a : PASS * (a + 1), PASS * rb : PASS * (rb + 1)]
-            nc.sync.dma_start(out=raw[:], in_=block.rearrange("(p i) c -> p i c", i=4))
-            return raw
-
         def load_wg(rb):
-            if rb == 0:
-                raw = sharing("wg_raw0", [P, 2, PASS // 2], I32, WG_THEN_ROWS)
-            else:
-                raw = held("wg_raw1", [P, 2, PASS // 2], I32)
-            block = wg_words[:, :, 2 * PASS * rb : 2 * PASS * (rb + 1)]
-            nc.sync.dma_start(out=raw[:], in_=block.rearrange("a p x -> p a x").bitcast(I32))
+            raw = held(f"wg_raw{rb}", [P, 2, PASS // 2], I32)
+            columns = wg_words[:, :, 2 * PASS * rb : 2 * PASS * (rb + 1)]
+            nc.sync.dma_start(out=raw[:], in_=columns.rearrange("a p x -> p a x").bitcast(I32))
             return raw
 
-        def listed(first, count):
-            return offsets[:, first // LIST_COLUMN : (first + count) // LIST_COLUMN]
+        def load_wu(rb, a, raw):
+            block = wu[PASS * a : PASS * (a + 1), PASS * rb : PASS * (rb + 1)]
+            nc.sync.dma_start(out=raw[:], in_=block.rearrange("(p i) c -> p i c", i=PLACES))
+            return raw
 
-        wg_w = {}
-
-        def order_wg_words(rb):
-            wg_w[rb] = held(f"wg_w{rb}", [P, 2, 4, 2 * P], U8)
+        def order_wg_words(rb, raw):
+            ordered = held(f"wg_w{rb}", [P, 2, PLACES, 2 * P], U8)
             nc.vector.tensor_copy(
-                out=wg_w[rb][:].bitcast(U16), in_=wg_raw[rb][:].bitcast(U16).rearrange("p a (m t) -> p a t m", t=4)
+                out=ordered[:].bitcast(U16), in_=raw[:].bitcast(U16).rearrange("p a (m t) -> p a t m", t=PLACES)
             )
+            return ordered
 
         tab_s = held("tab_s", [P, T // 4], I32)
         nc.vector.memset(tab_s[:], 0)
         rows = [held("rows0", [P, T], F32)]
         nc.vector.memset(rows[0][:].bitcast(I32), 0)
-        wg_s_raw = sharing("wg_s_raw", [P, 2, R // 4], I32, WG_S_THEN_BOTH1)
+        wg_s_raw = sharing("wg_s_raw", [P, 2, R // 4], I32, WG_SCALES_THEN_TOKEN_WORDS)
         nc.vector.memset(wg_s_raw[:], 0)
         tok_s = held("tok_s", [P, 2, J], U8)
-        wd_s = held("wd_s", [P, 2, 2, N // 4], I32)
         nc.vector.memset(tok_s[:].bitcast(I32), 0)
+        wd_s = held("wd_s", [P, 2, 2, N // 4], I32)
         nc.vector.memset(wd_s[:], 0)
         warm = held("warm", [P, 2], F32)
         nc.gpsimd.memset(warm[:, 0:1], 0.0)
@@ -98,14 +95,14 @@ def tile_list_modp_gsigm_res_noneb_kernel(
 
         offsets = keep.tile([P, J // LIST_COLUMN], U16, name="offsets")
         nc.sync.dma_start(offsets[:], offs)
-        wg_raw = {0: load_wg(0)}
+        wg_raw0 = load_wg(0)
         nc.sync.dma_start(out=tab_s[0:QUADRANT, :], in_=tab_scales.rearrange("a b x -> b a x").bitcast(I32))
         tab_w = held("tab_w", [P, T], I32)
         nc.sync.dma_start(out=tab_w[:], in_=tab_words[0].rearrange("p t x -> p (t x)").bitcast(I32))
-        load_scales(nc.sync, wg_s_raw, wg_scales)
-        wu_raw = {}
-        wu_raw[0, 0] = load_wu(0, 0)
-        order_wg_words(0)
+        load_scales(wg_s_raw, wg_scales)
+        wu_shape = [P, PLACES, PASS]
+        wu_raw = {(0, 0): load_wu(0, 0, held("wu_raw00", wu_shape, F32))}
+        wg_w = {0: order_wg_words(0, wg_raw0)}
         tok_s_rows = held("tok_s_rows", [P, J], U8)
         nc.vector.tensor_copy(tok_s_rows[:], tab_s[:].bitcast(U8).indirect(offsets[:]))
         for q in range(P // QUADRANT):
@@ -113,16 +110,16 @@ def tile_list_modp_gsigm_res_noneb_kernel(
                 out=tok_s[QUADRANT * q : QUADRANT * q + 4].bitcast(I32),
                 in_=tok_s_rows[8 * q : 8 * q + 8, :].bitcast(I32),
             )
-        wu_raw[0, 1] = load_wu(0, 1)
-        wg_raw[1] = load_wg(1)
-        wu_raw[1, 0] = load_wu(1, 0)
-        wu_raw[1, 1] = load_wu(1, 1)
+        wu_raw[0, 1] = load_wu(0, 1, sharing("wu_raw01", wu_shape, F32, WU_01))
+        wg_raw1 = load_wg(1)
+        wu_raw[1, 0] = load_wu(1, 0, held("wu_raw10", wu_shape, F32))
+        wu_raw[1, 1] = load_wu(1, 1, sharing("wu_raw11", wu_shape, F32, WU_11))
         wd4_w = held("wd4_w", [P, 2, N // 2], I32)
         nc.sync.dma_start(out=wd4_w[:], in_=wd4_words.rearrange("a p x -> p a x").bitcast(I32))
         wd8_w = held("wd8_w", [P, 2, N], I32)
         nc.sync.dma_start(out=wd8_w[:], in_=wd8_words.rearrange("a p n x -> p a (n x)").bitcast(I32))
-        load_scales(nc.sync, wd_s[:, 0], wd4_scales)
-        load_scales(nc.sync, wd_s[:, 1], wd8_scales)
+        load_scales(wd_s[:, 0], wd4_scales)
+        load_scales(wd_s[:, 1], wd8_scales)
         wd4_s, wd8_s = wd_s[:, 0].bitcast(U8), wd_s[:, 1].bitcast(U8)
         bias = held("bias", [P, N // P], F32)
         with nc.allow_non_contiguous_dma(reason="one bias value for each partition and output tile"):
@@ -130,15 +127,11 @@ def tile_list_modp_gsigm_res_noneb_kernel(
         weight = held("weight", [P, J], F32)
         nc.sync.dma_start(out=weight[:], in_=wgo)
 
-        tok_w, wg_s, wu_w, wu_s, gate, rounded = {}, {}, {}, {}, {}, {}
+        tok_w, wg_s, rounded, wu_w, wu_s, gate = {}, {}, {}, {}, {}, {}
         h_w = [held(f"h_w{rb}", [P, J], U32) for rb in range(2)]
         h_s = [held(f"h_s{rb}", [P, J], U8) for rb in range(2)]
 
-        def gather_words(half):
-            if half == 0:
-                both = sharing("tok_both0", [P, HALF], U32, BOTH0_THEN_SCALES)
-            else:
-                both = sharing("tok_both1", [P, HALF], U32, WG_S_THEN_BOTH1)
+        def gather_words(half, both):
             nc.vector.tensor_copy(both[:], tab_w[:].bitcast(U32).indirect(listed(half * HALF, HALF)))
             tok_w[half] = held(f"tok_w{half}", [P, 2, 2 * HALF], U8)
             nc.vector.tensor_copy(
@@ -146,77 +139,63 @@ def tile_list_modp_gsigm_res_noneb_kernel(
             )
 
         def order_wg_scales(rb):
-            if rb == 0:
-                wg_s[rb] = held("wg_s0", [P, 2, 4, P], U8)
-            else:
-                wg_s[rb] = held("wg_s1", [P, 2, 4, P], U8)
-            source = wg_s_raw[:].bitcast(U8)[:, :, PASS * rb : PASS * (rb + 1)]
-            nc.vector.tensor_copy(out=wg_s[rb][:], in_=source.rearrange("p a (m t) -> p a t m", t=4))
-
-        def clear_rows():
-            rows.append(sharing("rows1", [P, T], F32, WU_THEN_GATES + 8192 * ROWS_AFTER))
-            nc.vector.memset(rows[1][:].bitcast(I32), 0)
+            wg_s[rb] = held(f"wg_s{rb}", [P, 2, PLACES, P], U8)
+            columns = wg_s_raw[:].bitcast(U8)[:, :, PASS * rb : PASS * (rb + 1)]
+            nc.vector.tensor_copy(out=wg_s[rb][:], in_=columns.rearrange("p a (m t) -> p a t m", t=PLACES))
 
         def token_operand(a, first, count):
             half, j0 = divmod(first, HALF)
             return tok_w[half][:, a, 2 * j0 : 2 * (j0 + count)].bitcast(FP4X4), tok_s[:, a, first : first + count]
 
-        def round_wu(rb, a, split):
-            grouped = ring.tile([P, 4, P, 4], BF16, name="wu_grouped", align_bytes=64)
-            source = wu_raw[rb, a][:].rearrange("p i (m t) -> p m i t", t=4)
-            t1 = 4 - 2 * split
-            for t0 in range(0, t1, 2):
-                to = grouped[:, t0 : t0 + 2, :, :].rearrange("p t m i -> p m i t")
-                nc.scalar.copy(out=to, in_=source[:, :, :, t0 : t0 + 2])
-            if split:
+        def round_wu(rb, a, on_scalar):
+            grouped = ring.tile([P, PLACES, P, PLACES], BF16, name="wu_grouped", align_bytes=64)
+            source = wu_raw[rb, a][:].rearrange("p i (m t) -> p m i t", t=PLACES)
+            for t0 in range(0, on_scalar, 2):
+                nc.scalar.copy(
+                    out=grouped[:, t0 : t0 + 2, :, :].rearrange("p t m i -> p m i t"), in_=source[:, :, :, t0 : t0 + 2]
+                )
+            if on_scalar < PLACES:
                 nc.vector.tensor_copy(
-                    out=grouped[:, t1:].rearrange("p t m i -> p m t i"),
-                    in_=source[:, :, :, t1:].rearrange("p m i t -> p m t i"),
+                    out=grouped[:, on_scalar:].rearrange("p t m i -> p m t i"),
+                    in_=source[:, :, :, on_scalar:].rearrange("p m i t -> p m t i"),
                 )
             rounded[rb, a] = grouped
 
         def quantize_wu(rb, a):
-            grouped = rounded[rb, a]
             wu_w[rb, a] = held(f"wu_w{rb}{a}", [P, PASS], U32)
             wu_s[rb, a] = held(f"wu_s{rb}{a}", [P, PASS], U8)
             nc.vector.quantize_mx(
                 out=wu_w[rb, a][:].bitcast(FP8X4),
                 scales=wu_s[rb, a][:],
-                in_=grouped[:].rearrange("p t m i -> p (t m i)"),
+                in_=rounded[rb, a][:].rearrange("p t m i -> p (t m i)"),
             )
 
-        def gates(rb, half, places=range(4)):
-            first = half * HALF
-            if (rb, half) in gate:
-                pass
-            elif (rb, half) == (1, 1):
-                gate[rb, half] = sharing("last_gate", [P, 4, HALF], F32, LAST_GATE_THEN_Y)
-            elif (rb, half) in AFTER_WU:
-                gate[rb, half] = sharing(f"gate{rb}{half}", [P, 4, HALF], F32, WU_THEN_GATES + 8192 * AFTER_WU[rb, half])
-            else:
-                gate[rb, half] = held(f"gate{rb}{half}", [P, 4, HALF], F32)
+        def gate_tile(rb, half, offset):
+            gate[rb, half] = sharing(f"gate{rb}{half}", [P, PLACES, HALF], F32, offset)
+
+        def gates(rb, half, places):
             for t in places:
-                ga = psum_ga.tile([P, HALF], F32, name="ga", tag="bank")
-                for a in (1, 0):
-                    words, scales = token_operand(a, first, HALF)
+                ga = psum.tile([P, HALF], F32, name="ga", tag="bank")
+                for a in LAST_FIRST:
+                    words, scales = token_operand(a, half * HALF, HALF)
                     nc.tensor.matmul_mx(
                         out=ga[:],
                         lhsT=wg_w[rb][:, a, t, :].bitcast(FP4X4),
                         lhsT_scale=wg_s[rb][:, a, t, :],
                         rhs=words,
                         rhs_scale=scales,
-                        start=(a == 1),
-                        stop=(a == 0),
+                        start=(a == LAST_FIRST[0]),
+                        stop=(a == LAST_FIRST[-1]),
                     )
                 nc.scalar.activation(out=gate[rb, half][:, t, :], in_=ga[:], func=ACT.Sigmoid)
 
         def hidden(rb, g):
             first = g * GROUP
-            h = ring.tile([P, GROUP, 4], BF16, name="h", align_bytes=64)
+            h = ring.tile([P, GROUP, PLACES], BF16, name="h", align_bytes=64)
             for j0 in range(0, GROUP, P):
-                ub = psum_ga.tile([P, 4, P], F32, name="ub", tag="bank")
-                for t in range(4):
-                    for a in (1, 0):
+                ub = psum.tile([P, PLACES, P], F32, name="ub", tag="bank")
+                for t in range(PLACES):
+                    for a in LAST_FIRST:
                         words, scales = token_operand(a, first + j0, P)
                         nc.tensor.matmul_mx(
                             out=ub[:, t, :],
@@ -224,13 +203,14 @@ def tile_list_modp_gsigm_res_noneb_kernel(
                             lhsT_scale=wu_s[rb, a][:, P * t : P * (t + 1)],
                             rhs=words,
                             rhs_scale=scales,
-                            start=(a == 1),
-                            stop=(a == 0),
+                            start=(a == LAST_FIRST[0]),
+                            stop=(a == LAST_FIRST[-1]),
                         )
+                half, in_half = divmod(first + j0, HALF)
                 nc.vector.tensor_tensor(
                     h[:, j0 : j0 + P, :].rearrange("p (c e) t -> p c t e", e=2),
                     ub[:].rearrange("p t (c e) -> p c t e", e=2),
-                    gate[rb, first // HALF][:, :, first % HALF + j0 : first % HALF + j0 + P].rearrange("p t (c e) -> p c t e", e=2),
+                    gate[rb, half][:, :, in_half : in_half + P].rearrange("p t (c e) -> p c t e", e=2),
                     MULT,
                 )
             nc.vector.quantize_mx(
@@ -239,31 +219,29 @@ def tile_list_modp_gsigm_res_noneb_kernel(
                 in_=h[:].rearrange("p j t -> p (j t)"),
             )
 
-        def down(n, first, count, biased):
-            step = count if count == PASS else P
-            y = psum_ga.tile([P, count], F32, name="y", tag="bank")
-            for j0 in range(0, count, step):
-                tokens = slice(first + j0, first + j0 + step)
-                for rb in (1, 0):
-                    words, scales = h_w[rb][:, tokens].bitcast(FP8X4), h_s[rb][:, tokens]
-                    nc.tensor.matmul_mx(
-                        out=y[:, j0 : j0 + step],
-                        lhsT=wd8_w[:, rb, P * n : P * (n + 1)].bitcast(FP8X4),
-                        lhsT_scale=wd8_s[:, rb, P * n : P * (n + 1)],
-                        rhs=words,
-                        rhs_scale=scales,
-                        start=(rb == 1),
-                        stop=False,
-                    )
-                    nc.tensor.matmul_mx(
-                        out=y[:, j0 : j0 + step],
-                        lhsT=wd4_w[:].bitcast(U8)[:, rb, 2 * P * n : 2 * P * (n + 1)].bitcast(FP4X4),
-                        lhsT_scale=wd4_s[:, rb, P * n : P * (n + 1)],
-                        rhs=words,
-                        rhs_scale=scales,
-                        start=False,
-                        stop=(rb == 0),
-                    )
+        def down(n, half, biased):
+            y = psum.tile([P, HALF], F32, name="y", tag="bank")
+            tokens = slice(half * HALF, (half + 1) * HALF)
+            for rb in LAST_FIRST:
+                words, scales = h_w[rb][:, tokens].bitcast(FP8X4), h_s[rb][:, tokens]
+                nc.tensor.matmul_mx(
+                    out=y[:],
+                    lhsT=wd8_w[:, rb, P * n : P * (n + 1)].bitcast(FP8X4),
+                    lhsT_scale=wd8_s[:, rb, P * n : P * (n + 1)],
+                    rhs=words,
+                    rhs_scale=scales,
+                    start=(rb == LAST_FIRST[0]),
+                    stop=False,
+                )
+                nc.tensor.matmul_mx(
+                    out=y[:],
+                    lhsT=wd4_w[:].bitcast(U8)[:, rb, 2 * P * n : 2 * P * (n + 1)].bitcast(FP4X4),
+                    lhsT_scale=wd4_s[:, rb, P * n : P * (n + 1)],
+                    rhs=words,
+                    rhs_scale=scales,
+                    start=False,
+                    stop=(rb == LAST_FIRST[-1]),
+                )
             nc.scalar.activation(out=biased, in_=y[:], func=ACT.Identity, bias=bias[:, n : n + 1])
 
         def scatter(n, first, count, biased):
@@ -274,47 +252,49 @@ def tile_list_modp_gsigm_res_noneb_kernel(
         def store(n):
             nc.sync.dma_start(out=out[P * n : P * (n + 1), :], in_=rows[n % 2][:])
 
-        y_sb = [held(f"y_sb{n}", [P, J], F32) for n in range(N // P)]
-
-        def piece(n, first, count):
-            down(n, first, count, y_sb[n][:, first : first + count])
-            scatter(n, first, count, y_sb[n][:, first : first + count])
-
-        gather_words(0)
+        gather_words(0, held("tok_both0", [P, HALF], U32))
         order_wg_scales(0)
         order_wg_scales(1)
-        round_wu(0, 0, 0)
-        gather_words(1)
+        round_wu(0, 0, on_scalar=PLACES)
+        gather_words(1, sharing("tok_both1", [P, HALF], U32, WG_SCALES_THEN_TOKEN_WORDS))
         quantize_wu(0, 0)
-        round_wu(0, 1, 1)
-        gates(0, 0)
-        gates(0, 1)
-        order_wg_words(1)
+        round_wu(0, 1, on_scalar=PLACES // 2)
+        for half in range(2):
+            gate_tile(0, half, FIRST_GATES[half])
+            gates(0, half, range(PLACES))
+        wg_w[1] = order_wg_words(1, wg_raw1)
         quantize_wu(0, 1)
-        round_wu(1, 0, 2)
-        round_wu(1, 1, 0)
+        round_wu(1, 0, on_scalar=PLACES // 2)
+        round_wu(1, 1, on_scalar=PLACES)
         hidden(0, 0)
         hidden(0, 1)
         quantize_wu(1, 0)
         hidden(0, 2)
+
+        gate_tile(1, 0, THIRD_GATES)
         gates(1, 0, (0, 1))
         quantize_wu(1, 1)
         hidden(0, 3)
-        clear_rows()
+        rows.append(sharing("rows1", [P, T], F32, SECOND_ROWS))
+        nc.vector.memset(rows[1][:].bitcast(I32), 0)
         gates(1, 0, (2, 3))
+        gate_tile(1, 1, LAST_GATES_THEN_Y)
         gates(1, 1, (0, 1))
         hidden(1, 0)
         gates(1, 1, (2, 3))
-        hidden(1, 1)
-        hidden(1, 2)
-        hidden(1, 3)
-        late = sharing("y_late", [P, 2 * GROUP], F32, LAST_GATE_THEN_Y)
-        down(0, 0, HALF, late[:])
-        scatter(0, 0, HALF, late[:])
-        piece(0, HALF, HALF)
+        for g in range(1, J // GROUP):
+            hidden(1, g)
+
+        first_half = sharing("y_first", [P, HALF], F32, LAST_GATES_THEN_Y)
+        down(0, 0, first_half[:])
+        scatter(0, 0, HALF, first_half[:])
+        second_half = held("y_second", [P, HALF], F32)
+        down(0, 1, second_half[:])
+        scatter(0, HALF, HALF, second_half[:])
         store(0)
-        for n in (1, 2, 3):
-            for first in (0, HALF):
-                down(n, first, HALF, y_sb[n][:, first : first + HALF])
-            scatter(n, 0, J, y_sb[n][:])
+        for n in range(1, N // P):
+            biased = held(f"y_biased{n}", [P, J], F32)
+            for half in range(2):
+                down(n, half, biased[:, half * HALF : (half + 1) * HALF])
+            scatter(n, 0, J, biased[:])
             store(n)

@@ -26,7 +26,8 @@ GROUP = 256
 LAST_FIRST = (1, 0)
 
 BLOCK = 8192
-WG_SCALES_THEN_TOKEN_WORDS = 0
+TOKEN_WORDS = 0
+ROUNDED_THEN_WG = BLOCK // 2
 FIRST_GATES = (BLOCK, 2 * BLOCK)
 WU_01 = BLOCK + BLOCK // 2
 THIRD_GATES = 3 * BLOCK
@@ -72,8 +73,7 @@ def tile_list_modp_gsigm_res_noneb_kernel(
             nc.sync.dma_start(out=raw[:], in_=block.rearrange("(p i) c -> p i c", i=PLACES))
             return raw
 
-        def order_wg_words(rb, raw):
-            ordered = held(f"wg_w{rb}", [P, 2, PLACES, 2 * P], U8)
+        def order_wg_words(ordered, raw):
             nc.vector.tensor_copy(
                 out=ordered[:].bitcast(U16), in_=raw[:].bitcast(U16).rearrange("p a (m t) -> p a t m", t=PLACES)
             )
@@ -81,10 +81,10 @@ def tile_list_modp_gsigm_res_noneb_kernel(
 
         tab_s = held("tab_s", [P, T // 4], I32)
         nc.vector.memset(tab_s[:], 0)
+        wg_s_raw = held("wg_s_raw", [P, 2, R // 4], I32)
+        nc.vector.memset(wg_s_raw[:], 0)
         rows = [held("rows0", [P, T], F32)]
         nc.vector.memset(rows[0][:].bitcast(I32), 0)
-        wg_s_raw = sharing("wg_s_raw", [P, 2, R // 4], I32, WG_SCALES_THEN_TOKEN_WORDS)
-        nc.vector.memset(wg_s_raw[:], 0)
         tok_s = held("tok_s", [P, 2, J], U8)
         nc.vector.memset(tok_s[:].bitcast(I32), 0)
         wd_s = held("wd_s", [P, 2, 2, N // 4], I32)
@@ -97,12 +97,13 @@ def tile_list_modp_gsigm_res_noneb_kernel(
         nc.sync.dma_start(offsets[:], offs)
         wg_raw0 = load_wg(0)
         nc.sync.dma_start(out=tab_s[0:QUADRANT, :], in_=tab_scales.rearrange("a b x -> b a x").bitcast(I32))
+        load_scales(wg_s_raw, wg_scales)
         tab_w = held("tab_w", [P, T], I32)
         nc.sync.dma_start(out=tab_w[:], in_=tab_words[0].rearrange("p t x -> p (t x)").bitcast(I32))
-        load_scales(wg_s_raw, wg_scales)
         wu_shape = [P, PLACES, PASS]
         wu_raw = {(0, 0): load_wu(0, 0, held("wu_raw00", wu_shape, F32))}
-        wg_w = {0: order_wg_words(0, wg_raw0)}
+        wg_w_shape, wg_s_shape = [P, 2, PLACES, 2 * P], [P, 2, PLACES, P]
+        wg_w = {0: order_wg_words(held("wg_w0", wg_w_shape, U8), wg_raw0)}
         tok_s_rows = held("tok_s_rows", [P, J], U8)
         nc.vector.tensor_copy(tok_s_rows[:], tab_s[:].bitcast(U8).indirect(offsets[:]))
         for q in range(P // QUADRANT):
@@ -128,18 +129,19 @@ def tile_list_modp_gsigm_res_noneb_kernel(
         nc.sync.dma_start(out=weight[:], in_=wgo)
 
         tok_w, wg_s, rounded, wu_w, wu_s, gate = {}, {}, {}, {}, {}, {}
+        rounded_shape = [P, PLACES, P, PLACES]
         h_w = [held(f"h_w{rb}", [P, J], U32) for rb in range(2)]
         h_s = [held(f"h_s{rb}", [P, J], U8) for rb in range(2)]
 
         def gather_words(half, both):
             nc.vector.tensor_copy(both[:], tab_w[:].bitcast(U32).indirect(listed(half * HALF, HALF)))
             tok_w[half] = held(f"tok_w{half}", [P, 2, 2 * HALF], U8)
-            nc.vector.tensor_copy(
-                out=tok_w[half][:].bitcast(U16), in_=both[:].bitcast(U16).rearrange("p (j a) -> p a j", a=2)
-            )
+            by_pass = both[:].bitcast(U16).rearrange("p (j a) -> p a j", a=2)
+            for a in LAST_FIRST:
+                nc.vector.tensor_copy(out=tok_w[half][:, a, :].bitcast(U16), in_=by_pass[:, a, :])
 
-        def order_wg_scales(rb):
-            wg_s[rb] = held(f"wg_s{rb}", [P, 2, PLACES, P], U8)
+        def order_wg_scales(rb, ordered):
+            wg_s[rb] = ordered
             columns = wg_s_raw[:].bitcast(U8)[:, :, PASS * rb : PASS * (rb + 1)]
             nc.vector.tensor_copy(out=wg_s[rb][:], in_=columns.rearrange("p a (m t) -> p a t m", t=PLACES))
 
@@ -147,8 +149,10 @@ def tile_list_modp_gsigm_res_noneb_kernel(
             half, j0 = divmod(first, HALF)
             return tok_w[half][:, a, 2 * j0 : 2 * (j0 + count)].bitcast(FP4X4), tok_s[:, a, first : first + count]
 
-        def round_wu(rb, a, on_scalar):
-            grouped = ring.tile([P, PLACES, P, PLACES], BF16, name="wu_grouped", align_bytes=64)
+        def ring_buffer():
+            return ring.tile(rounded_shape, BF16, name="wu_rounded", align_bytes=64)
+
+        def round_wu(rb, a, grouped, on_scalar):
             source = wu_raw[rb, a][:].rearrange("p i (m t) -> p m i t", t=PLACES)
             for t0 in range(0, on_scalar, 2):
                 nc.scalar.copy(
@@ -252,20 +256,20 @@ def tile_list_modp_gsigm_res_noneb_kernel(
         def store(n):
             nc.sync.dma_start(out=out[P * n : P * (n + 1), :], in_=rows[n % 2][:])
 
-        gather_words(0, held("tok_both0", [P, HALF], U32))
-        order_wg_scales(0)
-        order_wg_scales(1)
-        round_wu(0, 0, on_scalar=PLACES)
-        gather_words(1, sharing("tok_both1", [P, HALF], U32, WG_SCALES_THEN_TOKEN_WORDS))
+        order_wg_scales(0, held("wg_s0", wg_s_shape, U8))
+        gather_words(0, sharing("tok_both0", [P, HALF], U32, TOKEN_WORDS))
+        round_wu(0, 0, ring_buffer(), on_scalar=PLACES)
+        gather_words(1, sharing("tok_both1", [P, HALF], U32, TOKEN_WORDS))
         quantize_wu(0, 0)
-        round_wu(0, 1, on_scalar=PLACES // 2)
+        round_wu(0, 1, sharing("wu_rounded01", rounded_shape, BF16, ROUNDED_THEN_WG), on_scalar=PLACES // 2)
         for half in range(2):
             gate_tile(0, half, FIRST_GATES[half])
             gates(0, half, range(PLACES))
-        wg_w[1] = order_wg_words(1, wg_raw1)
         quantize_wu(0, 1)
-        round_wu(1, 0, on_scalar=PLACES // 2)
-        round_wu(1, 1, on_scalar=PLACES)
+        wg_w[1] = order_wg_words(sharing("wg_w1", wg_w_shape, U8, ROUNDED_THEN_WG), wg_raw1)
+        order_wg_scales(1, sharing("wg_s1", wg_s_shape, U8, ROUNDED_THEN_WG + BLOCK // 4))
+        round_wu(1, 0, ring_buffer(), on_scalar=PLACES // 2)
+        round_wu(1, 1, ring_buffer(), on_scalar=PLACES)
         hidden(0, 0)
         hidden(0, 1)
         quantize_wu(1, 0)
@@ -285,15 +289,14 @@ def tile_list_modp_gsigm_res_noneb_kernel(
         for g in range(1, J // GROUP):
             hidden(1, g)
 
-        first_half = sharing("y_first", [P, HALF], F32, LAST_GATES_THEN_Y)
-        down(0, 0, first_half[:])
-        scatter(0, 0, HALF, first_half[:])
-        second_half = held("y_second", [P, HALF], F32)
-        down(0, 1, second_half[:])
-        scatter(0, HALF, HALF, second_half[:])
+        for half in range(2):
+            biased = held(f"y_biased0{half}", [P, HALF], F32)
+            down(0, half, biased[:])
+            scatter(0, half * HALF, HALF, biased[:])
         store(0)
-        for n in range(1, N // P):
-            biased = held(f"y_biased{n}", [P, J], F32)
+        later = [sharing("y_biased1", [P, J], F32, LAST_GATES_THEN_Y)]
+        later.extend(held(f"y_biased{n}", [P, J], F32) for n in range(2, N // P))
+        for n, biased in enumerate(later, 1):
             for half in range(2):
                 down(n, half, biased[:, half * HALF : (half + 1) * HALF])
             scatter(n, 0, J, biased[:])

@@ -195,7 +195,10 @@ def tile_list_modp_gsigm_res_noneb_kernel(
 
         def hidden(rb, g):
             first = g * GROUP
-            h = ring.tile([P, GROUP, PLACES], BF16, name="h", align_bytes=64)
+            if (rb, g) == (1, J // GROUP - 1):
+                h = sharing("h_last", [P, GROUP, PLACES], BF16, SECOND_ROWS + BLOCK // 2)
+            else:
+                h = ring.tile([P, GROUP, PLACES], BF16, name="h", align_bytes=64)
             for j0 in range(0, GROUP, P):
                 ub = psum.tile([P, PLACES, P], F32, name="ub", tag="bank")
                 for t in range(PLACES):
@@ -279,8 +282,6 @@ def tile_list_modp_gsigm_res_noneb_kernel(
         gates(1, 0, (0, 1))
         quantize_wu(1, 1)
         hidden(0, 3)
-        rows.append(sharing("rows1", [P, T], F32, SECOND_ROWS))
-        nc.vector.memset(rows[1][:].bitcast(I32), 0)
         gates(1, 0, (2, 3))
         gate_tile(1, 1, LAST_GATES_THEN_Y)
         gates(1, 1, (0, 1))
@@ -288,6 +289,8 @@ def tile_list_modp_gsigm_res_noneb_kernel(
         gates(1, 1, (2, 3))
         for g in range(1, J // GROUP):
             hidden(1, g)
+        rows.append(sharing("rows1", [P, T], F32, SECOND_ROWS))
+        nc.gpsimd.memset(rows[1][:].bitcast(I32), 0)
 
         for half in range(2):
             biased = held(f"y_biased0{half}", [P, HALF], F32)

@@ -29,10 +29,11 @@ BLOCK = 8192
 TOKEN_WORDS = 0
 ROUNDED_THEN_WG = BLOCK // 2
 FIRST_GATES = (BLOCK, 2 * BLOCK)
-WU_01 = BLOCK + BLOCK // 2
+WU_01 = 2 * BLOCK - BLOCK // 4
 THIRD_GATES = 3 * BLOCK
 SECOND_ROWS = 4 * BLOCK
 WU_11 = 3 * BLOCK + BLOCK // 2
+THIRD_ROWS = 6 * BLOCK
 LAST_GATES_THEN_Y = 5 * BLOCK
 
 
@@ -68,8 +69,9 @@ def tile_list_modp_gsigm_res_noneb_kernel(
             nc.sync.dma_start(out=raw[:], in_=columns.rearrange("a p x -> p a x").bitcast(I32))
             return raw
 
-        def load_wu(rb, a, raw):
-            block = wu[PASS * a : PASS * (a + 1), PASS * rb : PASS * (rb + 1)]
+        def load_wu(rb, a, raw, first=0):
+            r0 = PASS * rb + first
+            block = wu[PASS * a : PASS * (a + 1), r0 : r0 + raw.shape[2]]
             nc.sync.dma_start(out=raw[:], in_=block.rearrange("(p i) c -> p i c", i=PLACES))
             return raw
 
@@ -79,10 +81,11 @@ def tile_list_modp_gsigm_res_noneb_kernel(
             )
             return ordered
 
-        tab_s = held("tab_s", [P, T // 4], I32)
-        nc.vector.memset(tab_s[:], 0)
         wg_s_raw = held("wg_s_raw", [P, 2, R // 4], I32)
         nc.vector.memset(wg_s_raw[:], 0)
+        tab_s = held("tab_s", [P, T // 4], I32)
+        nc.vector.memset(tab_s[QUADRANT : 2 * QUADRANT], 0)
+        nc.vector.memset(tab_s[2 * QUADRANT :], 0)
         rows = [held("rows0", [P, T], F32)]
         nc.vector.memset(rows[0][:].bitcast(I32), 0)
         tok_s = held("tok_s", [P, 2, J], U8)
@@ -95,15 +98,14 @@ def tile_list_modp_gsigm_res_noneb_kernel(
 
         offsets = keep.tile([P, J // LIST_COLUMN], U16, name="offsets")
         nc.sync.dma_start(offsets[:], offs)
-        wg_raw0 = load_wg(0)
         nc.sync.dma_start(out=tab_s[0:QUADRANT, :], in_=tab_scales.rearrange("a b x -> b a x").bitcast(I32))
+        wg_raw0 = load_wg(0)
         load_scales(wg_s_raw, wg_scales)
         tab_w = held("tab_w", [P, T], I32)
         nc.sync.dma_start(out=tab_w[:], in_=tab_words[0].rearrange("p t x -> p (t x)").bitcast(I32))
         wu_shape = [P, PLACES, PASS]
         wu_raw = {(0, 0): load_wu(0, 0, held("wu_raw00", wu_shape, F32))}
         wg_w_shape, wg_s_shape = [P, 2, PLACES, 2 * P], [P, 2, PLACES, P]
-        wg_w = {0: order_wg_words(held("wg_w0", wg_w_shape, U8), wg_raw0)}
         tok_s_rows = held("tok_s_rows", [P, J], U8)
         nc.vector.tensor_copy(tok_s_rows[:], tab_s[:].bitcast(U8).indirect(offsets[:]))
         for q in range(P // QUADRANT):
@@ -111,7 +113,10 @@ def tile_list_modp_gsigm_res_noneb_kernel(
                 out=tok_s[QUADRANT * q : QUADRANT * q + 4].bitcast(I32),
                 in_=tok_s_rows[8 * q : 8 * q + 8, :].bitcast(I32),
             )
-        wu_raw[0, 1] = load_wu(0, 1, sharing("wu_raw01", wu_shape, F32, WU_01))
+        wg_w = {0: order_wg_words(held("wg_w0", wg_w_shape, U8), wg_raw0)}
+        half_shape = [P, PLACES, PASS // 2]
+        wu_01 = [load_wu(0, 1, sharing("wu_raw01a", half_shape, F32, WU_01))]
+        wu_01.append(load_wu(0, 1, held("wu_raw01b", half_shape, F32), PASS // 2))
         wg_raw1 = load_wg(1)
         wu_raw[1, 0] = load_wu(1, 0, held("wu_raw10", wu_shape, F32))
         wu_raw[1, 1] = load_wu(1, 1, sharing("wu_raw11", wu_shape, F32, WU_11))
@@ -149,21 +154,21 @@ def tile_list_modp_gsigm_res_noneb_kernel(
             half, j0 = divmod(first, HALF)
             return tok_w[half][:, a, 2 * j0 : 2 * (j0 + count)].bitcast(FP4X4), tok_s[:, a, first : first + count]
 
-        def ring_buffer():
-            return ring.tile(rounded_shape, BF16, name="wu_rounded", align_bytes=64)
-
-        def round_wu(rb, a, grouped, on_scalar):
-            source = wu_raw[rb, a][:].rearrange("p i (m t) -> p m i t", t=PLACES)
+        def round_wu(raw, grouped, on_scalar):
+            source = raw[:].rearrange("p i (m t) -> p m i t", t=PLACES)
             for t0 in range(0, on_scalar, 2):
                 nc.scalar.copy(
-                    out=grouped[:, t0 : t0 + 2, :, :].rearrange("p t m i -> p m i t"), in_=source[:, :, :, t0 : t0 + 2]
+                    out=grouped[:, t0 : t0 + 2].rearrange("p t m i -> p m i t"), in_=source[:, :, :, t0 : t0 + 2]
                 )
             if on_scalar < PLACES:
                 nc.vector.tensor_copy(
                     out=grouped[:, on_scalar:].rearrange("p t m i -> p m t i"),
                     in_=source[:, :, :, on_scalar:].rearrange("p m i t -> p m t i"),
                 )
-            rounded[rb, a] = grouped
+
+        def round_block(rb, a, on_scalar):
+            rounded[rb, a] = ring.tile(rounded_shape, BF16, name="wu_rounded", align_bytes=64)
+            round_wu(wu_raw[rb, a], rounded[rb, a][:], on_scalar)
 
         def quantize_wu(rb, a):
             wu_w[rb, a] = held(f"wu_w{rb}{a}", [P, PASS], U32)
@@ -196,7 +201,7 @@ def tile_list_modp_gsigm_res_noneb_kernel(
         def hidden(rb, g):
             first = g * GROUP
             if (rb, g) == (1, J // GROUP - 1):
-                h = sharing("h_last", [P, GROUP, PLACES], BF16, SECOND_ROWS + BLOCK // 2)
+                h = sharing("h_last", [P, GROUP, PLACES], BF16, THIRD_ROWS)
             else:
                 h = ring.tile([P, GROUP, PLACES], BF16, name="h", align_bytes=64)
             for j0 in range(0, GROUP, P):
@@ -226,53 +231,68 @@ def tile_list_modp_gsigm_res_noneb_kernel(
                 in_=h[:].rearrange("p j t -> p (j t)"),
             )
 
-        def down(n, half, biased):
-            y = psum.tile([P, HALF], F32, name="y", tag="bank")
-            tokens = slice(half * HALF, (half + 1) * HALF)
-            for rb in LAST_FIRST:
-                words, scales = h_w[rb][:, tokens].bitcast(FP8X4), h_s[rb][:, tokens]
-                nc.tensor.matmul_mx(
-                    out=y[:],
-                    lhsT=wd8_w[:, rb, P * n : P * (n + 1)].bitcast(FP8X4),
-                    lhsT_scale=wd8_s[:, rb, P * n : P * (n + 1)],
-                    rhs=words,
-                    rhs_scale=scales,
-                    start=(rb == LAST_FIRST[0]),
-                    stop=False,
-                )
-                nc.tensor.matmul_mx(
-                    out=y[:],
-                    lhsT=wd4_w[:].bitcast(U8)[:, rb, 2 * P * n : 2 * P * (n + 1)].bitcast(FP4X4),
-                    lhsT_scale=wd4_s[:, rb, P * n : P * (n + 1)],
-                    rhs=words,
-                    rhs_scale=scales,
-                    start=False,
-                    stop=(rb == LAST_FIRST[-1]),
-                )
+        def down(n, first, count, biased):
+            y = psum.tile([P, count], F32, name="y", tag="bank")
+            width = HALF if count == HALF else P
+            for j0 in range(0, count, width):
+                for rb in LAST_FIRST:
+                    words = h_w[rb][:, first + j0 : first + j0 + width].bitcast(FP8X4)
+                    scales = h_s[rb][:, first + j0 : first + j0 + width]
+                    nc.tensor.matmul_mx(
+                        out=y[:, j0 : j0 + width],
+                        lhsT=wd8_w[:, rb, P * n : P * (n + 1)].bitcast(FP8X4),
+                        lhsT_scale=wd8_s[:, rb, P * n : P * (n + 1)],
+                        rhs=words,
+                        rhs_scale=scales,
+                        start=(rb == LAST_FIRST[0]),
+                        stop=False,
+                    )
+                    nc.tensor.matmul_mx(
+                        out=y[:, j0 : j0 + width],
+                        lhsT=wd4_w[:].bitcast(U8)[:, rb, 2 * P * n : 2 * P * (n + 1)].bitcast(FP4X4),
+                        lhsT_scale=wd4_s[:, rb, P * n : P * (n + 1)],
+                        rhs=words,
+                        rhs_scale=scales,
+                        start=False,
+                        stop=(rb == LAST_FIRST[-1]),
+                    )
             nc.scalar.activation(out=biased, in_=y[:], func=ACT.Identity, bias=bias[:, n : n + 1])
 
         def scatter(n, first, count, biased):
             nc.vector.tensor_tensor(
-                rows[n % 2][:].indirect(listed(first, count)), biased, weight[:, first : first + count], MULT
+                rows[n % 3][:].indirect(listed(first, count)), biased, weight[:, first : first + count], MULT
             )
 
         def store(n):
-            nc.sync.dma_start(out=out[P * n : P * (n + 1), :], in_=rows[n % 2][:])
+            nc.sync.dma_start(out=out[P * n : P * (n + 1), :], in_=rows[n % 3][:])
 
         order_wg_scales(0, held("wg_s0", wg_s_shape, U8))
+        idle = psum.tile([P, HALF], F32, name="idle", tag="bank")
+        for t in range(PLACES):
+            nc.tensor.matmul_mx(
+                out=idle[:],
+                lhsT=wg_w[0][:, 0, t, :].bitcast(FP4X4),
+                lhsT_scale=wg_s[0][:, 0, t, :],
+                rhs=wg_w[0][:, 0].rearrange("p t x -> p (t x)").bitcast(FP4X4),
+                rhs_scale=wg_s[0][:, 0].rearrange("p t m -> p (t m)"),
+                start=True,
+                stop=True,
+            )
         gather_words(0, sharing("tok_both0", [P, HALF], U32, TOKEN_WORDS))
-        round_wu(0, 0, ring_buffer(), on_scalar=PLACES)
+        round_block(0, 0, on_scalar=PLACES)
         gather_words(1, sharing("tok_both1", [P, HALF], U32, TOKEN_WORDS))
         quantize_wu(0, 0)
-        round_wu(0, 1, sharing("wu_rounded01", rounded_shape, BF16, ROUNDED_THEN_WG), on_scalar=PLACES // 2)
+        rounded[0, 1] = sharing("wu_rounded01", rounded_shape, BF16, ROUNDED_THEN_WG)
+        round_wu(wu_01[0], rounded[0, 1][:, :, : P // 2, :], on_scalar=PLACES)
+        round_wu(wu_01[1], rounded[0, 1][:, :, P // 2 :, :], on_scalar=0)
         for half in range(2):
             gate_tile(0, half, FIRST_GATES[half])
             gates(0, half, range(PLACES))
         quantize_wu(0, 1)
         wg_w[1] = order_wg_words(sharing("wg_w1", wg_w_shape, U8, ROUNDED_THEN_WG), wg_raw1)
         order_wg_scales(1, sharing("wg_s1", wg_s_shape, U8, ROUNDED_THEN_WG + BLOCK // 4))
-        round_wu(1, 0, ring_buffer(), on_scalar=PLACES // 2)
-        round_wu(1, 1, ring_buffer(), on_scalar=PLACES)
+        round_block(1, 0, on_scalar=PLACES // 2)
+        round_block(1, 1, on_scalar=PLACES)
         hidden(0, 0)
         hidden(0, 1)
         quantize_wu(1, 0)
@@ -286,21 +306,28 @@ def tile_list_modp_gsigm_res_noneb_kernel(
         gate_tile(1, 1, LAST_GATES_THEN_Y)
         gates(1, 1, (0, 1))
         hidden(1, 0)
-        gates(1, 1, (2, 3))
-        for g in range(1, J // GROUP):
-            hidden(1, g)
+        hidden(1, 1)
         rows.append(sharing("rows1", [P, T], F32, SECOND_ROWS))
-        nc.gpsimd.memset(rows[1][:].bitcast(I32), 0)
+        nc.vector.memset(rows[1][:].bitcast(I32), 0)
+        gates(1, 1, (2, 3))
+        for g in range(2, J // GROUP):
+            hidden(1, g)
+        rows.append(sharing("rows2", [P, T], F32, THIRD_ROWS))
+        nc.gpsimd.memset(rows[2][:].bitcast(I32), 0)
 
-        for half in range(2):
-            biased = held(f"y_biased0{half}", [P, HALF], F32)
-            down(0, half, biased[:])
-            scatter(0, half * HALF, HALF, biased[:])
-        store(0)
-        later = [sharing("y_biased1", [P, J], F32, LAST_GATES_THEN_Y)]
-        later.extend(held(f"y_biased{n}", [P, J], F32) for n in range(2, N // P))
-        for n, biased in enumerate(later, 1):
-            for half in range(2):
-                down(n, half, biased[:, half * HALF : (half + 1) * HALF])
-            scatter(n, 0, J, biased[:])
+        def down_and_scatter(n, first, count):
+            biased = held(f"y_biased{n}{first}", [P, count], F32)
+            for j0 in range(0, count, HALF):
+                width = min(count, HALF)
+                down(n, first + j0, width, biased[:, j0 : j0 + width])
+            scatter(n, first, count, biased[:])
+
+        down_and_scatter(0, 0, GROUP)
+        down_and_scatter(0, GROUP, GROUP)
+        down_and_scatter(1, 0, HALF)
+        for n in range(2):
+            down_and_scatter(n, HALF, HALF)
+            store(n)
+        for n in range(2, N // P):
+            down_and_scatter(n, 0, J)
             store(n)

@@ -116,7 +116,7 @@ def tile_list_modp_gsigm_res_noneb_kernel(
         wg_w = {0: order_wg_words(held("wg_w0", wg_w_shape, U8), wg_raw0)}
         half_shape = [P, PLACES, PASS // 2]
         wu_01 = [load_wu(0, 1, sharing("wu_raw01a", half_shape, F32, WU_01))]
-        wu_01.append(load_wu(0, 1, held("wu_raw01b", half_shape, F32), PASS // 2))
+        wu_01.append(load_wu(0, 1, sharing("wu_raw01b", half_shape, F32, ROUNDED_THEN_WG), PASS // 2))
         wg_raw1 = load_wg(1)
         wu_raw[1, 0] = load_wu(1, 0, held("wu_raw10", wu_shape, F32))
         wu_raw[1, 1] = load_wu(1, 1, sharing("wu_raw11", wu_shape, F32, WU_11))
@@ -156,28 +156,25 @@ def tile_list_modp_gsigm_res_noneb_kernel(
 
         def round_wu(raw, grouped, on_scalar):
             source = raw[:].rearrange("p i (m t) -> p m i t", t=PLACES)
-            for t0 in range(0, on_scalar, 2):
-                nc.scalar.copy(
-                    out=grouped[:, t0 : t0 + 2].rearrange("p t m i -> p m i t"), in_=source[:, :, :, t0 : t0 + 2]
-                )
-            if on_scalar < PLACES:
-                nc.vector.tensor_copy(
-                    out=grouped[:, on_scalar:].rearrange("p t m i -> p m t i"),
-                    in_=source[:, :, :, on_scalar:].rearrange("p m i t -> p m t i"),
-                )
+            for t0 in range(0, PLACES, 2):
+                copy = nc.scalar.copy if t0 < on_scalar else nc.vector.tensor_copy
+                copy(out=grouped[:, t0 : t0 + 2].rearrange("p t m i -> p m i t"), in_=source[:, :, :, t0 : t0 + 2])
 
         def round_block(rb, a, on_scalar):
             rounded[rb, a] = ring.tile(rounded_shape, BF16, name="wu_rounded", align_bytes=64)
             round_wu(wu_raw[rb, a], rounded[rb, a][:], on_scalar)
 
-        def quantize_wu(rb, a):
+        def quantize_wu(rb, a, pieces=1):
             wu_w[rb, a] = held(f"wu_w{rb}{a}", [P, PASS], U32)
             wu_s[rb, a] = held(f"wu_s{rb}{a}", [P, PASS], U8)
-            nc.vector.quantize_mx(
-                out=wu_w[rb, a][:].bitcast(FP8X4),
-                scales=wu_s[rb, a][:],
-                in_=rounded[rb, a][:].rearrange("p t m i -> p (t m i)"),
-            )
+            values = rounded[rb, a][:].rearrange("p t m i -> p (t m i)")
+            width = PASS // pieces
+            for c0 in range(0, PASS, width):
+                nc.vector.quantize_mx(
+                    out=wu_w[rb, a][:, c0 : c0 + width].bitcast(FP8X4),
+                    scales=wu_s[rb, a][:, c0 : c0 + width],
+                    in_=values[:, PLACES * c0 : PLACES * (c0 + width)],
+                )
 
         def gate_tile(rb, half, offset):
             gate[rb, half] = sharing(f"gate{rb}{half}", [P, PLACES, HALF], F32, offset)
@@ -282,13 +279,13 @@ def tile_list_modp_gsigm_res_noneb_kernel(
         round_block(0, 0, on_scalar=PLACES)
         gather_words(1, sharing("tok_both1", [P, HALF], U32, TOKEN_WORDS))
         quantize_wu(0, 0)
-        rounded[0, 1] = sharing("wu_rounded01", rounded_shape, BF16, ROUNDED_THEN_WG)
+        rounded[0, 1] = held("wu_rounded01", rounded_shape, BF16)
         round_wu(wu_01[0], rounded[0, 1][:, :, : P // 2, :], on_scalar=PLACES)
         round_wu(wu_01[1], rounded[0, 1][:, :, P // 2 :, :], on_scalar=0)
         for half in range(2):
             gate_tile(0, half, FIRST_GATES[half])
             gates(0, half, range(PLACES))
-        quantize_wu(0, 1)
+        quantize_wu(0, 1, pieces=2)
         wg_w[1] = order_wg_words(sharing("wg_w1", wg_w_shape, U8, ROUNDED_THEN_WG), wg_raw1)
         order_wg_scales(1, sharing("wg_s1", wg_s_shape, U8, ROUNDED_THEN_WG + BLOCK // 4))
         round_block(1, 0, on_scalar=PLACES // 2)

@@ -25,6 +25,7 @@ HALF = J // 2
 GROUP = 256
 LAST_FIRST = (1, 0)
 
+BANK = 2048
 BLOCK = 8192
 TOKEN_WORDS = 0
 ROUNDED_THEN_WG = BLOCK // 2
@@ -45,7 +46,7 @@ def tile_list_modp_gsigm_res_noneb_kernel(
         keep = ctx.enter_context(tc.tile_pool(name="keep", bufs=1))
         shared = ctx.enter_context(tc.tile_pool(name="shared", bufs=1))
         ring = ctx.enter_context(tc.tile_pool(name="ring", bufs=3))
-        psum = ctx.enter_context(tc.psum_pool(name="psum", bufs=8))
+        psum = ctx.enter_context(tc.psum_pool(name="psum", bufs=1))
 
         def held(name, shape, dtype):
             return keep.tile(shape, dtype, name=name, align_bytes=64)
@@ -55,6 +56,9 @@ def tile_list_modp_gsigm_res_noneb_kernel(
 
         def listed(first, count):
             return offsets[:, first // LIST_COLUMN : (first + count) // LIST_COLUMN]
+
+        def bank(name, shape, number):
+            return psum.tile(shape, F32, name=name, offset=number * BANK)
 
         def load_scales(tile, src):
             for q in range(P // QUADRANT):
@@ -156,9 +160,13 @@ def tile_list_modp_gsigm_res_noneb_kernel(
 
         def round_wu(raw, grouped, on_scalar):
             source = raw[:].rearrange("p i (m t) -> p m i t", t=PLACES)
+            if on_scalar == PLACES:
+                nc.scalar.copy(out=grouped.rearrange("p t m i -> p m i t"), in_=source)
+                return
             for t0 in range(0, PLACES, 2):
-                copy = nc.scalar.copy if t0 < on_scalar else nc.vector.tensor_copy
-                copy(out=grouped[:, t0 : t0 + 2].rearrange("p t m i -> p m i t"), in_=source[:, :, :, t0 : t0 + 2])
+                nc.vector.tensor_copy(
+                    out=grouped[:, t0 : t0 + 2].rearrange("p t m i -> p m i t"), in_=source[:, :, :, t0 : t0 + 2]
+                )
 
         def round_block(rb, a, on_scalar):
             rounded[rb, a] = ring.tile(rounded_shape, BF16, name="wu_rounded", align_bytes=64)
@@ -179,9 +187,9 @@ def tile_list_modp_gsigm_res_noneb_kernel(
         def gate_tile(rb, half, offset):
             gate[rb, half] = sharing(f"gate{rb}{half}", [P, PLACES, HALF], F32, offset)
 
-        def gates(rb, half, places):
-            for t in places:
-                ga = psum.tile([P, HALF], F32, name="ga", tag="bank")
+        def gates(rb, half, places, banks):
+            for t, number in zip(places, banks):
+                ga = bank(f"ga{rb}{half}{t}", [P, HALF], number)
                 for a in LAST_FIRST:
                     words, scales = token_operand(a, half * HALF, HALF)
                     nc.tensor.matmul_mx(
@@ -195,14 +203,14 @@ def tile_list_modp_gsigm_res_noneb_kernel(
                     )
                 nc.scalar.activation(out=gate[rb, half][:, t, :], in_=ga[:], func=ACT.Sigmoid)
 
-        def hidden(rb, g):
+        def hidden(rb, g, banks, offset=None):
             first = g * GROUP
-            if (rb, g) == (1, J // GROUP - 1):
-                h = sharing("h_last", [P, GROUP, PLACES], BF16, THIRD_ROWS)
+            if offset is not None:
+                h = sharing(f"h{rb}{g}", [P, GROUP, PLACES], BF16, offset)
             else:
                 h = ring.tile([P, GROUP, PLACES], BF16, name="h", align_bytes=64)
-            for j0 in range(0, GROUP, P):
-                ub = psum.tile([P, PLACES, P], F32, name="ub", tag="bank")
+            for j0, number in zip(range(0, GROUP, P), banks):
+                ub = bank(f"ub{rb}{g}{j0}", [P, PLACES, P], number)
                 for t in range(PLACES):
                     for a in LAST_FIRST:
                         words, scales = token_operand(a, first + j0, P)
@@ -228,8 +236,8 @@ def tile_list_modp_gsigm_res_noneb_kernel(
                 in_=h[:].rearrange("p j t -> p (j t)"),
             )
 
-        def down(n, first, count, biased):
-            y = psum.tile([P, count], F32, name="y", tag="bank")
+        def down(n, first, count, biased, number):
+            y = bank(f"y{n}{first}", [P, count], number)
             width = HALF if count == HALF else P
             for j0 in range(0, count, width):
                 for rb in LAST_FIRST:
@@ -264,7 +272,7 @@ def tile_list_modp_gsigm_res_noneb_kernel(
             nc.sync.dma_start(out=out[P * n : P * (n + 1), :], in_=rows[n % 3][:])
 
         order_wg_scales(0, held("wg_s0", wg_s_shape, U8))
-        idle = psum.tile([P, HALF], F32, name="idle", tag="bank")
+        idle = bank("idle", [P, HALF], 0)
         for t in range(PLACES):
             nc.tensor.matmul_mx(
                 out=idle[:],
@@ -284,47 +292,46 @@ def tile_list_modp_gsigm_res_noneb_kernel(
         round_wu(wu_01[1], rounded[0, 1][:, :, P // 2 :, :], on_scalar=0)
         for half in range(2):
             gate_tile(0, half, FIRST_GATES[half])
-            gates(0, half, range(PLACES))
+            gates(0, half, range(PLACES), ((1, 2, 3, 4), (5, 6, 7, 0))[half])
         quantize_wu(0, 1, pieces=2)
         wg_w[1] = order_wg_words(sharing("wg_w1", wg_w_shape, U8, ROUNDED_THEN_WG), wg_raw1)
         order_wg_scales(1, sharing("wg_s1", wg_s_shape, U8, ROUNDED_THEN_WG + BLOCK // 4))
-        round_block(1, 0, on_scalar=PLACES // 2)
+        round_block(1, 0, on_scalar=0)
         round_block(1, 1, on_scalar=PLACES)
-        hidden(0, 0)
-        hidden(0, 1)
+        hidden(0, 0, (1, 2))
+        hidden(0, 1, (3, 4))
         quantize_wu(1, 0)
-        hidden(0, 2)
+        hidden(0, 2, (5, 6))
 
-        gate_tile(1, 0, THIRD_GATES)
-        gates(1, 0, (0, 1))
-        quantize_wu(1, 1)
-        hidden(0, 3)
-        gates(1, 0, (2, 3))
-        gate_tile(1, 1, LAST_GATES_THEN_Y)
-        gates(1, 1, (0, 1))
-        hidden(1, 0)
-        hidden(1, 1)
-        rows.append(sharing("rows1", [P, T], F32, SECOND_ROWS))
-        nc.vector.memset(rows[1][:].bitcast(I32), 0)
-        gates(1, 1, (2, 3))
-        for g in range(2, J // GROUP):
-            hidden(1, g)
-        rows.append(sharing("rows2", [P, T], F32, THIRD_ROWS))
-        nc.gpsimd.memset(rows[2][:].bitcast(I32), 0)
-
-        def down_and_scatter(n, first, count):
+        def down_and_scatter(n, first, count, banks):
             biased = held(f"y_biased{n}{first}", [P, count], F32)
-            for j0 in range(0, count, HALF):
-                width = min(count, HALF)
-                down(n, first + j0, width, biased[:, j0 : j0 + width])
+            width = count // len(banks)
+            for j0, number in zip(range(0, count, width), banks):
+                down(n, first + j0, width, biased[:, j0 : j0 + width], number)
             scatter(n, first, count, biased[:])
 
-        down_and_scatter(0, 0, GROUP)
-        down_and_scatter(0, GROUP, GROUP)
-        down_and_scatter(1, 0, HALF)
+        gate_tile(1, 0, THIRD_GATES)
+        gates(1, 0, (0, 1), (7, 0))
+        quantize_wu(1, 1)
+        hidden(0, 3, (1, 2))
+        gates(1, 0, (2, 3), (3, 4))
+        gate_tile(1, 1, LAST_GATES_THEN_Y)
+        gates(1, 1, (0, 1), (5, 6))
+        hidden(1, 0, (7, 0), SECOND_ROWS + BLOCK // 2)
+        hidden(1, 1, (1, 2), SECOND_ROWS + BLOCK // 2)
+        down_and_scatter(0, 0, GROUP, (3, 4))
+        rows.append(sharing("rows1", [P, T], F32, SECOND_ROWS))
+        nc.gpsimd.memset(rows[1][:].bitcast(I32), 0)
+        gates(1, 1, (2, 3), (3, 4))
+        hidden(1, 2, (1, 2))
+        hidden(1, 3, (3, 4), THIRD_ROWS)
+        rows.append(sharing("rows2", [P, T], F32, THIRD_ROWS))
+        nc.gpsimd.memset(rows[2][:].bitcast(I32), 0)
+        down_and_scatter(0, GROUP, GROUP, (5,))
+        down_and_scatter(1, 0, HALF, (6,))
         for n in range(2):
-            down_and_scatter(n, HALF, HALF)
+            down_and_scatter(n, HALF, HALF, ((7,), (0,))[n])
             store(n)
         for n in range(2, N // P):
-            down_and_scatter(n, 0, J)
+            down_and_scatter(n, 0, J, ((5, 6), (7, 0))[n - 2])
             store(n)

@@ -160,13 +160,9 @@ def tile_list_modp_gsigm_res_noneb_kernel(
 
         def round_wu(raw, grouped, on_scalar):
             source = raw[:].rearrange("p i (m t) -> p m i t", t=PLACES)
-            if on_scalar == PLACES:
-                nc.scalar.copy(out=grouped.rearrange("p t m i -> p m i t"), in_=source)
-                return
             for t0 in range(0, PLACES, 2):
-                nc.vector.tensor_copy(
-                    out=grouped[:, t0 : t0 + 2].rearrange("p t m i -> p m i t"), in_=source[:, :, :, t0 : t0 + 2]
-                )
+                copy = nc.scalar.copy if t0 < on_scalar else nc.vector.tensor_copy
+                copy(out=grouped[:, t0 : t0 + 2].rearrange("p t m i -> p m i t"), in_=source[:, :, :, t0 : t0 + 2])
 
         def round_block(rb, a, on_scalar):
             rounded[rb, a] = ring.tile(rounded_shape, BF16, name="wu_rounded", align_bytes=64)

@@ -292,7 +292,7 @@ def tile_list_modp_gsigm_res_noneb_kernel(
         quantize_wu(0, 1, pieces=2)
         wg_w[1] = order_wg_words(sharing("wg_w1", wg_w_shape, U8, ROUNDED_THEN_WG), wg_raw1)
         order_wg_scales(1, sharing("wg_s1", wg_s_shape, U8, ROUNDED_THEN_WG + BLOCK // 4))
-        round_block(1, 0, on_scalar=0)
+        round_block(1, 0, on_scalar=PLACES // 2)
         round_block(1, 1, on_scalar=PLACES)
         hidden(0, 0, (1, 2))
         hidden(0, 1, (3, 4))

@@ -15,6 +15,7 @@ FP8X4 = mybir.dt.float8_e4m3fn_x4
 FP4X4 = mybir.dt.float4_e2m1fn_x4
 ACT = mybir.ActivationFunctionType
 MULT = mybir.AluOpType.mult
+ADD = mybir.AluOpType.add
 
 P = 128
 PASS = 512
@@ -27,15 +28,12 @@ LAST_FIRST = (1, 0)
 
 BANK = 2048
 BLOCK = 8192
-TOKEN_WORDS = 0
-ROUNDED_THEN_WG = BLOCK // 2
-FIRST_GATES = (BLOCK, 2 * BLOCK)
-WU_01 = 2 * BLOCK - BLOCK // 4
-THIRD_GATES = 3 * BLOCK
-SECOND_ROWS = 4 * BLOCK
-WU_11 = 3 * BLOCK + BLOCK // 2
-THIRD_ROWS = 6 * BLOCK
-LAST_GATES_THEN_Y = 5 * BLOCK
+SCALES_THEN_WORDS = 0
+ROUNDED_THEN_WG = BLOCK
+WU_THEN_GATES = 3 * BLOCK
+WARM_THEN_ROWS = 5 * BLOCK
+UB_THEN_Y = 6 * BLOCK
+H_THEN_ROWS = 2 * BLOCK
 
 
 def tile_list_modp_gsigm_res_noneb_kernel(
@@ -67,25 +65,24 @@ def tile_list_modp_gsigm_res_noneb_kernel(
                     in_=src[:, 4 * q : 4 * q + 4, :].rearrange("a r x -> r a x").bitcast(I32),
                 )
 
-        def load_wg(rb):
-            raw = held(f"wg_raw{rb}", [P, 2, PASS // 2], I32)
+        def load_wg(rb, raw):
             columns = wg_words[:, :, 2 * PASS * rb : 2 * PASS * (rb + 1)]
             nc.sync.dma_start(out=raw[:], in_=columns.rearrange("a p x -> p a x").bitcast(I32))
             return raw
 
-        def load_wu(rb, a, raw, first=0):
-            r0 = PASS * rb + first
-            block = wu[PASS * a : PASS * (a + 1), r0 : r0 + raw.shape[2]]
+        def load_wu(rb, a, offset=None):
+            name, shape = f"wu_raw{rb}{a}", [P, PLACES, PASS]
+            raw = held(name, shape, F32) if offset is None else sharing(name, shape, F32, offset)
+            block = wu[PASS * a : PASS * (a + 1), PASS * rb : PASS * (rb + 1)]
             nc.sync.dma_start(out=raw[:], in_=block.rearrange("(p i) c -> p i c", i=PLACES))
             return raw
 
-        def order_wg_words(ordered, raw):
-            nc.vector.tensor_copy(
-                out=ordered[:].bitcast(U16), in_=raw[:].bitcast(U16).rearrange("p a (m t) -> p a t m", t=PLACES)
-            )
-            return ordered
+        def order_wg_words(rb, ordered):
+            wg_w[rb] = ordered
+            columns = wg_raw[rb][:].bitcast(U16)
+            nc.vector.tensor_copy(out=ordered[:].bitcast(U16), in_=columns.rearrange("p a (m t) -> p a t m", t=PLACES))
 
-        wg_s_raw = held("wg_s_raw", [P, 2, R // 4], I32)
+        wg_s_raw = sharing("wg_s_raw", [P, 2, R // 4], I32, SCALES_THEN_WORDS)
         nc.vector.memset(wg_s_raw[:], 0)
         tab_s = held("tab_s", [P, T // 4], I32)
         nc.vector.memset(tab_s[QUADRANT : 2 * QUADRANT], 0)
@@ -96,34 +93,34 @@ def tile_list_modp_gsigm_res_noneb_kernel(
         nc.vector.memset(tok_s[:].bitcast(I32), 0)
         wd_s = held("wd_s", [P, 2, 2, N // 4], I32)
         nc.vector.memset(wd_s[:], 0)
-        warm = held("warm", [P, 2], F32)
-        nc.gpsimd.memset(warm[:, 0:1], 0.0)
+        warm = sharing("warm", [P, 32], F32, WARM_THEN_ROWS - 64)
+        nc.vector.memset(warm[:, 0:1], 0.0)
         nc.scalar.activation(out=warm[:, 1:2], in_=warm[:, 0:1], func=ACT.Sigmoid)
+
+        for n in (1, 2):
+            rows.append(sharing(f"rows{n}", [P, T], F32, WARM_THEN_ROWS + (n - 2) * BLOCK))
+            nc.gpsimd.memset(rows[n][:].bitcast(I32), 0)
 
         offsets = keep.tile([P, J // LIST_COLUMN], U16, name="offsets")
         nc.sync.dma_start(offsets[:], offs)
         nc.sync.dma_start(out=tab_s[0:QUADRANT, :], in_=tab_scales.rearrange("a b x -> b a x").bitcast(I32))
-        wg_raw0 = load_wg(0)
-        load_scales(wg_s_raw, wg_scales)
         tab_w = held("tab_w", [P, T], I32)
         nc.sync.dma_start(out=tab_w[:], in_=tab_words[0].rearrange("p t x -> p (t x)").bitcast(I32))
-        wu_shape = [P, PLACES, PASS]
-        wu_raw = {(0, 0): load_wu(0, 0, held("wu_raw00", wu_shape, F32))}
+        wg_raw = [load_wg(0, held("wg_raw0", [P, 2, PASS // 2], I32))]
+        load_scales(wg_s_raw, wg_scales)
+        wu_raw = {(0, 0): load_wu(0, 0)}
         wg_w_shape, wg_s_shape = [P, 2, PLACES, 2 * P], [P, 2, PLACES, P]
         tok_s_rows = held("tok_s_rows", [P, J], U8)
         nc.vector.tensor_copy(tok_s_rows[:], tab_s[:].bitcast(U8).indirect(offsets[:]))
         for q in range(P // QUADRANT):
-            nc.sync.dma_start(
+            nc.scalar.dma_start(
                 out=tok_s[QUADRANT * q : QUADRANT * q + 4].bitcast(I32),
                 in_=tok_s_rows[8 * q : 8 * q + 8, :].bitcast(I32),
             )
-        wg_w = {0: order_wg_words(held("wg_w0", wg_w_shape, U8), wg_raw0)}
-        half_shape = [P, PLACES, PASS // 2]
-        wu_01 = [load_wu(0, 1, sharing("wu_raw01a", half_shape, F32, WU_01))]
-        wu_01.append(load_wu(0, 1, sharing("wu_raw01b", half_shape, F32, ROUNDED_THEN_WG), PASS // 2))
-        wg_raw1 = load_wg(1)
-        wu_raw[1, 0] = load_wu(1, 0, held("wu_raw10", wu_shape, F32))
-        wu_raw[1, 1] = load_wu(1, 1, sharing("wu_raw11", wu_shape, F32, WU_11))
+        wu_raw[0, 1] = load_wu(0, 1)
+        wg_raw.append(load_wg(1, held("wg_raw1", [P, 2, PASS // 2], I32)))
+        wu_raw[1, 0] = load_wu(1, 0)
+        wu_raw[1, 1] = load_wu(1, 1, WU_THEN_GATES)
         wd4_w = held("wd4_w", [P, 2, N // 2], I32)
         nc.sync.dma_start(out=wd4_w[:], in_=wd4_words.rearrange("a p x -> p a x").bitcast(I32))
         wd8_w = held("wd8_w", [P, 2, N], I32)
@@ -137,17 +134,15 @@ def tile_list_modp_gsigm_res_noneb_kernel(
         weight = held("weight", [P, J], F32)
         nc.sync.dma_start(out=weight[:], in_=wgo)
 
-        tok_w, wg_s, rounded, wu_w, wu_s, gate = {}, {}, {}, {}, {}, {}
+        tok_w, wg_w, wg_s, rounded, wu_w, wu_s, gate = {}, {}, {}, {}, {}, {}, {}
         rounded_shape = [P, PLACES, P, PLACES]
         h_w = [held(f"h_w{rb}", [P, J], U32) for rb in range(2)]
         h_s = [held(f"h_s{rb}", [P, J], U8) for rb in range(2)]
 
-        def gather_words(half, both):
-            nc.vector.tensor_copy(both[:], tab_w[:].bitcast(U32).indirect(listed(half * HALF, HALF)))
-            tok_w[half] = held(f"tok_w{half}", [P, 2, 2 * HALF], U8)
-            by_pass = both[:].bitcast(U16).rearrange("p (j a) -> p a j", a=2)
-            for a in LAST_FIRST:
-                nc.vector.tensor_copy(out=tok_w[half][:, a, :].bitcast(U16), in_=by_pass[:, a, :])
+        def part_words(half, both, parted):
+            tok_w[half] = parted
+            by_pass = both[:, half * HALF : (half + 1) * HALF].bitcast(U16).rearrange("p (j a) -> p a j", a=2)
+            nc.vector.tensor_copy(out=tok_w[half][:].bitcast(U16), in_=by_pass)
 
         def order_wg_scales(rb, ordered):
             wg_s[rb] = ordered
@@ -161,11 +156,14 @@ def tile_list_modp_gsigm_res_noneb_kernel(
         def round_wu(raw, grouped, on_scalar):
             source = raw[:].rearrange("p i (m t) -> p m i t", t=PLACES)
             for t0 in range(0, PLACES, 2):
-                copy = nc.scalar.copy if t0 < on_scalar else nc.vector.tensor_copy
+                copy = nc.scalar.copy if t0 >= PLACES - on_scalar else nc.vector.tensor_copy
                 copy(out=grouped[:, t0 : t0 + 2].rearrange("p t m i -> p m i t"), in_=source[:, :, :, t0 : t0 + 2])
 
-        def round_block(rb, a, on_scalar):
-            rounded[rb, a] = ring.tile(rounded_shape, BF16, name="wu_rounded", align_bytes=64)
+        def round_block(rb, a, on_scalar, offset=None):
+            if offset is None:
+                rounded[rb, a] = held(f"wu_rounded{rb}{a}", rounded_shape, BF16)
+            else:
+                rounded[rb, a] = sharing(f"wu_rounded{rb}{a}", rounded_shape, BF16, offset)
             round_wu(wu_raw[rb, a], rounded[rb, a][:], on_scalar)
 
         def quantize_wu(rb, a, pieces=1):
@@ -180,8 +178,9 @@ def tile_list_modp_gsigm_res_noneb_kernel(
                     in_=values[:, PLACES * c0 : PLACES * (c0 + width)],
                 )
 
-        def gate_tile(rb, half, offset):
-            gate[rb, half] = sharing(f"gate{rb}{half}", [P, PLACES, HALF], F32, offset)
+        def gate_tile(rb, half, offset=None):
+            name, shape = f"gate{rb}{half}", [P, PLACES, HALF]
+            gate[rb, half] = held(name, shape, F32) if offset is None else sharing(name, shape, F32, offset)
 
         def gates(rb, half, places, banks):
             for t, number in zip(places, banks):
@@ -207,7 +206,7 @@ def tile_list_modp_gsigm_res_noneb_kernel(
                 h = ring.tile([P, GROUP, PLACES], BF16, name="h", align_bytes=64)
             for j0, number in zip(range(0, GROUP, P), banks):
                 ub = bank(f"ub{rb}{g}{j0}", [P, PLACES, P], number)
-                for t in range(PLACES):
+                for t in reversed(range(PLACES)):
                     for a in LAST_FIRST:
                         words, scales = token_operand(a, first + j0, P)
                         nc.tensor.matmul_mx(
@@ -232,7 +231,7 @@ def tile_list_modp_gsigm_res_noneb_kernel(
                 in_=h[:].rearrange("p j t -> p (j t)"),
             )
 
-        def down(n, first, count, biased, number):
+        def down(n, first, count, number):
             y = bank(f"y{n}{first}", [P, count], number)
             width = HALF if count == HALF else P
             for j0 in range(0, count, width):
@@ -257,77 +256,134 @@ def tile_list_modp_gsigm_res_noneb_kernel(
                         start=False,
                         stop=(rb == LAST_FIRST[-1]),
                     )
-            nc.scalar.activation(out=biased, in_=y[:], func=ACT.Identity, bias=bias[:, n : n + 1])
+            return y
 
-        def scatter(n, first, count, biased):
+        def add_bias(n, first, count, banks, offset=None):
+            name, shape = f"y_biased{n}{first}", [P, count]
+            biased = held(name, shape, F32) if offset is None else sharing(name, shape, F32, offset)
+            width = count // len(banks)
+            for j0, number in zip(range(0, count, width), banks):
+                y = down(n, first + j0, width, number)
+                nc.scalar.activation(
+                    out=biased[:, j0 : j0 + width], in_=y[:], func=ACT.Identity, bias=bias[:, n : n + 1]
+                )
+            return biased
+
+        def scatter_times_weight(n, first, biased):
+            count = biased.shape[1]
             nc.vector.tensor_tensor(
-                rows[n % 3][:].indirect(listed(first, count)), biased, weight[:, first : first + count], MULT
+                rows[n][:].indirect(listed(first, count)), biased[:], weight[:, first : first + count], MULT
             )
 
-        def store(n):
-            nc.sync.dma_start(out=out[P * n : P * (n + 1), :], in_=rows[n % 3][:])
+        def times_weight(n, first, biased):
+            count = biased.shape[1]
+            weighted = held(f"y_weighted{n}{first}", [P, count], F32)
+            nc.gpsimd.tensor_tensor(weighted[:], biased[:], weight[:, first : first + count], MULT)
+            return weighted
 
-        order_wg_scales(0, held("wg_s0", wg_s_shape, U8))
+        def scatter(n, first, weighted):
+            nc.vector.tensor_copy(rows[n][:].indirect(listed(first, weighted.shape[1])), weighted[:])
+
+        def factor(g, which, banks, offset=None):
+            name, shape = f"factor{g}{which}", [P, GROUP, PLACES]
+            tile = held(name, shape, F32) if offset is None else sharing(name, shape, F32, offset)
+            for j0, number in zip(range(0, GROUP, P), banks):
+                acc = bank(f"acc{g}{which}{j0}", [P, PLACES, P], number)
+                for t in range(PLACES):
+                    for a in LAST_FIRST:
+                        words, scales = token_operand(a, g * GROUP + j0, P)
+                        if which == 0:
+                            lhs, lhs_scales = wg_w[1][:, a, t, :].bitcast(FP4X4), wg_s[1][:, a, t, :]
+                        else:
+                            columns = slice(P * t, P * (t + 1))
+                            lhs, lhs_scales = wu_w[1, a][:, columns].bitcast(FP8X4), wu_s[1, a][:, columns]
+                        nc.tensor.matmul_mx(
+                            out=acc[:, t, :],
+                            lhsT=lhs,
+                            lhsT_scale=lhs_scales,
+                            rhs=words,
+                            rhs_scale=scales,
+                            start=(a == LAST_FIRST[0]),
+                            stop=(a == LAST_FIRST[-1]),
+                        )
+                nc.scalar.activation(
+                    out=tile[:, j0 : j0 + P, :],
+                    in_=acc[:].rearrange("p t j -> p j t"),
+                    func=(ACT.Sigmoid, ACT.Copy)[which],
+                )
+            return tile
+
+        def product(h, gates, ub):
+            flat = "p j t -> p (j t)"
+            nc.gpsimd.tensor_tensor(h.rearrange(flat), gates[:].rearrange(flat), ub[:].rearrange(flat), MULT)
+
+        def store(n):
+            nc.sync.dma_start(out=out[P * n : P * (n + 1), :], in_=rows[n][:])
+
+        both = held("tok_both", [P, J], U32)
+        nc.vector.tensor_copy(both[:], tab_w[:].bitcast(U32).indirect(offsets[:]))
+        order_wg_words(0, held("wg_w0", wg_w_shape, U8))
         idle = bank("idle", [P, HALF], 0)
-        for t in range(PLACES):
+        for t in range(2):
             nc.tensor.matmul_mx(
                 out=idle[:],
                 lhsT=wg_w[0][:, 0, t, :].bitcast(FP4X4),
-                lhsT_scale=wg_s[0][:, 0, t, :],
+                lhsT_scale=wg_s_raw[:, 0, : P // 4].bitcast(U8),
                 rhs=wg_w[0][:, 0].rearrange("p t x -> p (t x)").bitcast(FP4X4),
-                rhs_scale=wg_s[0][:, 0].rearrange("p t m -> p (t m)"),
+                rhs_scale=wg_s_raw[:, 0, : HALF // 4].bitcast(U8),
                 start=True,
                 stop=True,
             )
-        gather_words(0, sharing("tok_both0", [P, HALF], U32, TOKEN_WORDS))
-        round_block(0, 0, on_scalar=PLACES)
-        gather_words(1, sharing("tok_both1", [P, HALF], U32, TOKEN_WORDS))
+        part_words(0, both, held("tok_w0", [P, 2, 2 * HALF], U8))
+        for rb in range(2):
+            order_wg_scales(rb, held(f"wg_s{rb}", wg_s_shape, U8))
+        part_words(1, both, sharing("tok_w1", [P, 2, 2 * HALF], U8, SCALES_THEN_WORDS))
+        round_block(0, 0, on_scalar=PLACES // 2)
         quantize_wu(0, 0)
-        rounded[0, 1] = held("wu_rounded01", rounded_shape, BF16)
-        round_wu(wu_01[0], rounded[0, 1][:, :, : P // 2, :], on_scalar=PLACES)
-        round_wu(wu_01[1], rounded[0, 1][:, :, P // 2 :, :], on_scalar=0)
-        for half in range(2):
-            gate_tile(0, half, FIRST_GATES[half])
-            gates(0, half, range(PLACES), ((1, 2, 3, 4), (5, 6, 7, 0))[half])
+        round_block(0, 1, on_scalar=0, offset=ROUNDED_THEN_WG)
+        gate_tile(0, 0)
+        gates(0, 0, range(PLACES), (1, 2, 3, 4))
+        gate_tile(0, 1)
+        gates(0, 1, range(PLACES), (5, 6, 7, 0))
         quantize_wu(0, 1, pieces=2)
-        wg_w[1] = order_wg_words(sharing("wg_w1", wg_w_shape, U8, ROUNDED_THEN_WG), wg_raw1)
-        order_wg_scales(1, sharing("wg_s1", wg_s_shape, U8, ROUNDED_THEN_WG + BLOCK // 4))
-        round_block(1, 0, on_scalar=PLACES // 2)
-        round_block(1, 1, on_scalar=PLACES)
+        order_wg_words(1, sharing("wg_w1", wg_w_shape, U8, ROUNDED_THEN_WG))
+        round_block(1, 0, on_scalar=PLACES)
+        round_block(1, 1, on_scalar=PLACES // 2)
         hidden(0, 0, (1, 2))
         hidden(0, 1, (3, 4))
         quantize_wu(1, 0)
+        quantize_wu(1, 1, pieces=2)
         hidden(0, 2, (5, 6))
-
-        def down_and_scatter(n, first, count, banks):
-            biased = held(f"y_biased{n}{first}", [P, count], F32)
-            width = count // len(banks)
-            for j0, number in zip(range(0, count, width), banks):
-                down(n, first + j0, width, biased[:, j0 : j0 + width], number)
-            scatter(n, first, count, biased[:])
-
-        gate_tile(1, 0, THIRD_GATES)
-        gates(1, 0, (0, 1), (7, 0))
-        quantize_wu(1, 1)
-        hidden(0, 3, (1, 2))
-        gates(1, 0, (2, 3), (3, 4))
-        gate_tile(1, 1, LAST_GATES_THEN_Y)
-        gates(1, 1, (0, 1), (5, 6))
-        hidden(1, 0, (7, 0), SECOND_ROWS + BLOCK // 2)
-        hidden(1, 1, (1, 2), SECOND_ROWS + BLOCK // 2)
-        down_and_scatter(0, 0, GROUP, (3, 4))
-        rows.append(sharing("rows1", [P, T], F32, SECOND_ROWS))
-        nc.gpsimd.memset(rows[1][:].bitcast(I32), 0)
-        gates(1, 1, (2, 3), (3, 4))
-        hidden(1, 2, (1, 2))
-        hidden(1, 3, (3, 4), THIRD_ROWS)
-        rows.append(sharing("rows2", [P, T], F32, THIRD_ROWS))
-        nc.gpsimd.memset(rows[2][:].bitcast(I32), 0)
-        down_and_scatter(0, GROUP, GROUP, (5,))
-        down_and_scatter(1, 0, HALF, (6,))
+        gate_tile(1, 0, WU_THEN_GATES)
+        gates(1, 0, range(PLACES), (7, 0, 1, 2))
+        hidden(1, 0, (3, 4))
+        hidden(1, 1, (5, 6))
+        hidden(0, 3, (3, 4), H_THEN_ROWS)
+        rows.append(sharing("rows3", [P, T], F32, H_THEN_ROWS))
+        nc.gpsimd.memset(rows[3][:].bitcast(I32), 0)
+        biased = add_bias(0, 0, GROUP, (7, 0))
+        weighted = held("y_weighted10", [P, GROUP], F32)
+        nc.vector.scalar_tensor_tensor(
+            weighted[:], down(1, 0, GROUP, 1)[:], bias[:, 1:2], weight[:, :GROUP], ADD, MULT
+        )
+        scatter_times_weight(0, 0, biased)
+        scatter(1, 0, weighted)
+        scatter(2, 0, times_weight(2, 0, add_bias(2, 0, HALF, (2,))))
+        last_h = held("last_h", [P, HALF, PLACES], BF16)
+        gates2 = factor(2, 0, (7, 0))
+        scatter(3, 0, times_weight(3, 0, add_bias(3, 0, HALF, (5,))))
+        product(last_h[:, :GROUP], gates2, factor(2, 1, (1, 2)))
+        product(last_h[:, GROUP:], factor(3, 0, (7, 0)), factor(3, 1, (5, 1), UB_THEN_Y))
+        nc.vector.quantize_mx(
+            out=h_w[1][:, HALF:].bitcast(FP8X4), scales=h_s[1][:, HALF:], in_=last_h[:].rearrange("p j t -> p (j t)")
+        )
         for n in range(2):
-            down_and_scatter(n, HALF, HALF, ((7,), (0,))[n])
-            store(n)
-        for n in range(2, N // P):
-            down_and_scatter(n, 0, J, ((5, 6), (7, 0))[n - 2])
+            scatter_times_weight(n, GROUP, add_bias(n, GROUP, GROUP, ((6,), (3,))[n], UB_THEN_Y + 1024 * n))
+        scatter_times_weight(0, HALF, add_bias(0, HALF, GROUP, (4,)))
+        scatter_times_weight(1, HALF, add_bias(1, HALF, HALF, (2,)))
+        store(1)
+        scatter_times_weight(0, HALF + GROUP, add_bias(0, HALF + GROUP, GROUP, (7,)))
+        store(0)
+        for n in (2, 3):
+            scatter_times_weight(n, HALF, add_bias(n, HALF, HALF, ((0,), (5,))[n - 2]))
             store(n)

@@ -33,7 +33,8 @@ ROUNDED_THEN_WG = BLOCK
 WU_THEN_GATES = 3 * BLOCK
 WARM_THEN_ROWS = 5 * BLOCK
 UB_THEN_Y = 6 * BLOCK
-H_THEN_ROWS = 2 * BLOCK
+LAST_H = 7 * BLOCK
+H_THEN_ROWS = 9 * BLOCK
 
 
 def tile_list_modp_gsigm_res_noneb_kernel(
@@ -93,13 +94,12 @@ def tile_list_modp_gsigm_res_noneb_kernel(
         nc.vector.memset(tok_s[:].bitcast(I32), 0)
         wd_s = held("wd_s", [P, 2, 2, N // 4], I32)
         nc.vector.memset(wd_s[:], 0)
-        warm = sharing("warm", [P, 32], F32, WARM_THEN_ROWS - 64)
+        warm = sharing("warm", [P, 2], F32, WARM_THEN_ROWS)
         nc.vector.memset(warm[:, 0:1], 0.0)
         nc.scalar.activation(out=warm[:, 1:2], in_=warm[:, 0:1], func=ACT.Sigmoid)
 
-        for n in (1, 2):
-            rows.append(sharing(f"rows{n}", [P, T], F32, WARM_THEN_ROWS + (n - 2) * BLOCK))
-            nc.gpsimd.memset(rows[n][:].bitcast(I32), 0)
+        rows.append(sharing("rows1", [P, T], F32, WARM_THEN_ROWS))
+        nc.gpsimd.memset(rows[1][:].bitcast(I32), 0)
 
         offsets = keep.tile([P, J // LIST_COLUMN], U16, name="offsets")
         nc.sync.dma_start(offsets[:], offs)
@@ -113,7 +113,7 @@ def tile_list_modp_gsigm_res_noneb_kernel(
         tok_s_rows = held("tok_s_rows", [P, J], U8)
         nc.vector.tensor_copy(tok_s_rows[:], tab_s[:].bitcast(U8).indirect(offsets[:]))
         for q in range(P // QUADRANT):
-            nc.scalar.dma_start(
+            nc.sync.dma_start(
                 out=tok_s[QUADRANT * q : QUADRANT * q + 4].bitcast(I32),
                 in_=tok_s_rows[8 * q : 8 * q + 8, :].bitcast(I32),
             )
@@ -153,18 +153,17 @@ def tile_list_modp_gsigm_res_noneb_kernel(
             half, j0 = divmod(first, HALF)
             return tok_w[half][:, a, 2 * j0 : 2 * (j0 + count)].bitcast(FP4X4), tok_s[:, a, first : first + count]
 
-        def round_wu(raw, grouped, on_scalar):
-            source = raw[:].rearrange("p i (m t) -> p m i t", t=PLACES)
-            for t0 in range(0, PLACES, 2):
-                copy = nc.scalar.copy if t0 >= PLACES - on_scalar else nc.vector.tensor_copy
-                copy(out=grouped[:, t0 : t0 + 2].rearrange("p t m i -> p m i t"), in_=source[:, :, :, t0 : t0 + 2])
+        def round_wu(rb, a, copy, places, m0=0, m1=P):
+            source = wu_raw[rb, a][:].rearrange("p i (m t) -> p m i t", t=PLACES)
+            for t0 in places:
+                target = rounded[rb, a][:, t0 : t0 + 2, m0:m1].rearrange("p t m i -> p m i t")
+                copy(out=target, in_=source[:, m0:m1, :, t0 : t0 + 2])
 
-        def round_block(rb, a, on_scalar, offset=None):
-            if offset is None:
-                rounded[rb, a] = held(f"wu_rounded{rb}{a}", rounded_shape, BF16)
-            else:
-                rounded[rb, a] = sharing(f"wu_rounded{rb}{a}", rounded_shape, BF16, offset)
-            round_wu(wu_raw[rb, a], rounded[rb, a][:], on_scalar)
+        def rounded_tile(rb, a, offset=None):
+            name = f"wu_rounded{rb}{a}"
+            rounded[rb, a] = (
+                held(name, rounded_shape, BF16) if offset is None else sharing(name, rounded_shape, BF16, offset)
+            )
 
         def quantize_wu(rb, a, pieces=1):
             wu_w[rb, a] = held(f"wu_w{rb}{a}", [P, PASS], U32)
@@ -198,7 +197,7 @@ def tile_list_modp_gsigm_res_noneb_kernel(
                     )
                 nc.scalar.activation(out=gate[rb, half][:, t, :], in_=ga[:], func=ACT.Sigmoid)
 
-        def hidden(rb, g, banks, offset=None):
+        def hidden(rb, g, banks, offset=None, places=(3, 2, 1, 0)):
             first = g * GROUP
             if offset is not None:
                 h = sharing(f"h{rb}{g}", [P, GROUP, PLACES], BF16, offset)
@@ -206,7 +205,7 @@ def tile_list_modp_gsigm_res_noneb_kernel(
                 h = ring.tile([P, GROUP, PLACES], BF16, name="h", align_bytes=64)
             for j0, number in zip(range(0, GROUP, P), banks):
                 ub = bank(f"ub{rb}{g}{j0}", [P, PLACES, P], number)
-                for t in reversed(range(PLACES)):
+                for t in places:
                     for a in LAST_FIRST:
                         words, scales = token_operand(a, first + j0, P)
                         nc.tensor.matmul_mx(
@@ -225,6 +224,10 @@ def tile_list_modp_gsigm_res_noneb_kernel(
                     gate[rb, half][:, :, in_half : in_half + P].rearrange("p t (c e) -> p c t e", e=2),
                     MULT,
                 )
+            quantize_h(rb, g, h)
+
+        def quantize_h(rb, g, h):
+            first = g * GROUP
             nc.vector.quantize_mx(
                 out=h_w[rb][:, first : first + GROUP].bitcast(FP8X4),
                 scales=h_s[rb][:, first : first + GROUP],
@@ -313,9 +316,11 @@ def tile_list_modp_gsigm_res_noneb_kernel(
                 )
             return tile
 
-        def product(h, gates, ub):
+        def hidden_on_gpsimd(g, gates, ub):
+            h = sharing(f"h1{g}", [P, GROUP, PLACES], BF16, LAST_H)
             flat = "p j t -> p (j t)"
-            nc.gpsimd.tensor_tensor(h.rearrange(flat), gates[:].rearrange(flat), ub[:].rearrange(flat), MULT)
+            nc.gpsimd.tensor_tensor(h[:].rearrange(flat), gates[:].rearrange(flat), ub[:].rearrange(flat), MULT)
+            return h
 
         def store(n):
             nc.sync.dma_start(out=out[P * n : P * (n + 1), :], in_=rows[n][:])
@@ -338,18 +343,25 @@ def tile_list_modp_gsigm_res_noneb_kernel(
         for rb in range(2):
             order_wg_scales(rb, held(f"wg_s{rb}", wg_s_shape, U8))
         part_words(1, both, sharing("tok_w1", [P, 2, 2 * HALF], U8, SCALES_THEN_WORDS))
-        round_block(0, 0, on_scalar=PLACES // 2)
+        on_scalar, on_vector = nc.scalar.copy, nc.vector.tensor_copy
+        rounded_tile(0, 0)
+        round_wu(0, 0, on_vector, (0,))
+        round_wu(0, 0, on_scalar, (2,))
         quantize_wu(0, 0)
-        round_block(0, 1, on_scalar=0, offset=ROUNDED_THEN_WG)
+        rounded_tile(0, 1, ROUNDED_THEN_WG)
+        round_wu(0, 1, on_vector, (0, 2))
         gate_tile(0, 0)
         gates(0, 0, range(PLACES), (1, 2, 3, 4))
         gate_tile(0, 1)
         gates(0, 1, range(PLACES), (5, 6, 7, 0))
         quantize_wu(0, 1, pieces=2)
         order_wg_words(1, sharing("wg_w1", wg_w_shape, U8, ROUNDED_THEN_WG))
-        round_block(1, 0, on_scalar=PLACES)
-        round_block(1, 1, on_scalar=PLACES // 2)
-        hidden(0, 0, (1, 2))
+        rounded_tile(1, 0)
+        round_wu(1, 0, on_scalar, (0, 2))
+        rounded_tile(1, 1)
+        round_wu(1, 1, on_vector, (0,))
+        round_wu(1, 1, on_scalar, (2,))
+        hidden(0, 0, (1, 2), places=range(PLACES))
         hidden(0, 1, (3, 4))
         quantize_wu(1, 0)
         quantize_wu(1, 1, pieces=2)
@@ -358,32 +370,27 @@ def tile_list_modp_gsigm_res_noneb_kernel(
         gates(1, 0, range(PLACES), (7, 0, 1, 2))
         hidden(1, 0, (3, 4))
         hidden(1, 1, (5, 6))
-        hidden(0, 3, (3, 4), H_THEN_ROWS)
-        rows.append(sharing("rows3", [P, T], F32, H_THEN_ROWS))
-        nc.gpsimd.memset(rows[3][:].bitcast(I32), 0)
-        biased = add_bias(0, 0, GROUP, (7, 0))
-        weighted = held("y_weighted10", [P, GROUP], F32)
-        nc.vector.scalar_tensor_tensor(
-            weighted[:], down(1, 0, GROUP, 1)[:], bias[:, 1:2], weight[:, :GROUP], ADD, MULT
-        )
-        scatter_times_weight(0, 0, biased)
-        scatter(1, 0, weighted)
-        scatter(2, 0, times_weight(2, 0, add_bias(2, 0, HALF, (2,))))
-        last_h = held("last_h", [P, HALF, PLACES], BF16)
-        gates2 = factor(2, 0, (7, 0))
-        scatter(3, 0, times_weight(3, 0, add_bias(3, 0, HALF, (5,))))
-        product(last_h[:, :GROUP], gates2, factor(2, 1, (1, 2)))
-        product(last_h[:, GROUP:], factor(3, 0, (7, 0)), factor(3, 1, (5, 1), UB_THEN_Y))
-        nc.vector.quantize_mx(
-            out=h_w[1][:, HALF:].bitcast(FP8X4), scales=h_s[1][:, HALF:], in_=last_h[:].rearrange("p j t -> p (j t)")
-        )
-        for n in range(2):
-            scatter_times_weight(n, GROUP, add_bias(n, GROUP, GROUP, ((6,), (3,))[n], UB_THEN_Y + 1024 * n))
-        scatter_times_weight(0, HALF, add_bias(0, HALF, GROUP, (4,)))
-        scatter_times_weight(1, HALF, add_bias(1, HALF, HALF, (2,)))
-        store(1)
-        scatter_times_weight(0, HALF + GROUP, add_bias(0, HALF + GROUP, GROUP, (7,)))
-        store(0)
+        hidden(0, 3, (3, 4), H_THEN_ROWS - 1024)
         for n in (2, 3):
-            scatter_times_weight(n, HALF, add_bias(n, HALF, HALF, ((0,), (5,))[n - 2]))
+            rows.append(sharing(f"rows{n}", [P, T], F32, H_THEN_ROWS + (n - 3) * BLOCK))
+        for n in (3, 2):
+            nc.gpsimd.memset(rows[n][:].bitcast(I32), 0)
+        scatter_times_weight(0, 0, add_bias(0, 0, GROUP, (7, 0)))
+        weighted = held("y_weighted20", [P, HALF], F32)
+        nc.vector.scalar_tensor_tensor(
+            weighted[:], down(2, 0, HALF, 1)[:], bias[:, 2:3], weight[:, :HALF], ADD, MULT
+        )
+        scatter_times_weight(1, 0, add_bias(1, 0, HALF, (2,), LAST_H))
+        scatter(2, 0, weighted)
+        quantize_h(1, 2, hidden_on_gpsimd(2, factor(2, 0, (7, 0)), factor(2, 1, (1, 2))))
+        scatter(3, 0, times_weight(3, 0, add_bias(3, 0, HALF, (5,))))
+        quantize_h(1, 3, hidden_on_gpsimd(3, factor(3, 0, (7, 0)), factor(3, 1, (1, 2), UB_THEN_Y)))
+        scatter_times_weight(0, GROUP, add_bias(0, GROUP, GROUP, (6,), UB_THEN_Y))
+        scatter_times_weight(1, HALF, add_bias(1, HALF, GROUP, (3,), UB_THEN_Y + 1024))
+        scatter_times_weight(0, HALF, add_bias(0, HALF, GROUP, (4,), UB_THEN_Y + 2048))
+        for n in (1, 0):
+            scatter_times_weight(n, HALF + GROUP, add_bias(n, HALF + GROUP, GROUP, ((7,), (5,))[n]))
+            store(n)
+        for n in (2, 3):
+            scatter_times_weight(n, HALF, add_bias(n, HALF, HALF, ((0,), (1,))[n - 2]))
             store(n)

@@ -26,6 +26,7 @@ HALF = J // 2
 GROUP = 256
 LAST_FIRST = (1, 0)
 
+LATE = 64
 BANK = 2048
 BLOCK = 8192
 SCALES_THEN_WORDS = 0
@@ -278,10 +279,11 @@ def tile_list_modp_gsigm_res_noneb_kernel(
                 rows[n][:].indirect(listed(first, count)), biased[:], weight[:, first : first + count], MULT
             )
 
-        def times_weight(n, first, biased):
-            count = biased.shape[1]
-            weighted = held(f"y_weighted{n}{first}", [P, count], F32)
-            nc.gpsimd.tensor_tensor(weighted[:], biased[:], weight[:, first : first + count], MULT)
+        def weigh_in_bank(n, y, count=HALF):
+            weighted = held(f"y_weighted{n}", [P, HALF], F32)
+            nc.vector.scalar_tensor_tensor(
+                weighted[:, :count], y[:, :count], bias[:, n : n + 1], weight[:, :count], ADD, MULT
+            )
             return weighted
 
         def scatter(n, first, weighted):
@@ -317,7 +319,7 @@ def tile_list_modp_gsigm_res_noneb_kernel(
             return tile
 
         def hidden_on_gpsimd(g, gates, ub):
-            h = sharing(f"h1{g}", [P, GROUP, PLACES], BF16, LAST_H)
+            h = sharing(f"h1{g}", [P, GROUP, PLACES], BF16, LAST_H - 1024 * (g - 2))
             flat = "p j t -> p (j t)"
             nc.gpsimd.tensor_tensor(h[:].rearrange(flat), gates[:].rearrange(flat), ub[:].rearrange(flat), MULT)
             return h
@@ -376,16 +378,21 @@ def tile_list_modp_gsigm_res_noneb_kernel(
         for n in (3, 2):
             nc.gpsimd.memset(rows[n][:].bitcast(I32), 0)
         scatter_times_weight(0, 0, add_bias(0, 0, GROUP, (7, 0)))
-        weighted = held("y_weighted20", [P, HALF], F32)
-        nc.vector.scalar_tensor_tensor(
-            weighted[:], down(2, 0, HALF, 1)[:], bias[:, 2:3], weight[:, :HALF], ADD, MULT
-        )
+        weighted = weigh_in_bank(2, down(2, 0, HALF, 1))
         scatter_times_weight(1, 0, add_bias(1, 0, HALF, (2,), LAST_H))
         scatter(2, 0, weighted)
-        quantize_h(1, 2, hidden_on_gpsimd(2, factor(2, 0, (7, 0)), factor(2, 1, (1, 2))))
-        scatter(3, 0, times_weight(3, 0, add_bias(3, 0, HALF, (5,))))
-        quantize_h(1, 3, hidden_on_gpsimd(3, factor(3, 0, (7, 0)), factor(3, 1, (1, 2), UB_THEN_Y)))
-        scatter_times_weight(0, GROUP, add_bias(0, GROUP, GROUP, (6,), UB_THEN_Y))
+        h = hidden_on_gpsimd(2, factor(2, 0, (7, 0)), factor(2, 1, (1, 2)))
+        gates3 = factor(3, 0, (7, 0))
+        y = down(3, 0, HALF, 5)
+        late = slice(HALF - LATE, HALF)
+        biased = held("y_biased3", [P, LATE], F32)
+        nc.scalar.activation(out=biased[:], in_=y[:, late], func=ACT.Identity, bias=bias[:, 3:4])
+        weighted = weigh_in_bank(3, y, HALF - LATE)
+        nc.gpsimd.tensor_tensor(weighted[:, late], biased[:], weight[:, late], MULT)
+        quantize_h(1, 2, h)
+        scatter(3, 0, weighted)
+        quantize_h(1, 3, hidden_on_gpsimd(3, gates3, factor(3, 1, (1, 2), UB_THEN_Y)))
+        scatter_times_weight(0, GROUP, add_bias(0, GROUP, GROUP, (6,), LAST_H + 1024))
         scatter_times_weight(1, HALF, add_bias(1, HALF, GROUP, (3,), UB_THEN_Y + 1024))
         scatter_times_weight(0, HALF, add_bias(0, HALF, GROUP, (4,), UB_THEN_Y + 2048))
         for n in (1, 0):

@@ -27,6 +27,7 @@ GROUP = 256
 LAST_FIRST = (1, 0)
 
 LATE = 64
+VECTOR_SHARE = 96
 BANK = 2048
 BLOCK = 8192
 SCALES_THEN_WORDS = 0
@@ -95,12 +96,10 @@ def tile_list_modp_gsigm_res_noneb_kernel(
         nc.vector.memset(tok_s[:].bitcast(I32), 0)
         wd_s = held("wd_s", [P, 2, 2, N // 4], I32)
         nc.vector.memset(wd_s[:], 0)
-        warm = sharing("warm", [P, 2], F32, WARM_THEN_ROWS)
-        nc.vector.memset(warm[:, 0:1], 0.0)
+        warm = held("warm", [P, 2], F32)
+        nc.gpsimd.memset(warm[:, 0:1], 0.0)
         nc.scalar.activation(out=warm[:, 1:2], in_=warm[:, 0:1], func=ACT.Sigmoid)
 
-        rows.append(sharing("rows1", [P, T], F32, WARM_THEN_ROWS))
-        nc.gpsimd.memset(rows[1][:].bitcast(I32), 0)
 
         offsets = keep.tile([P, J // LIST_COLUMN], U16, name="offsets")
         nc.sync.dma_start(offsets[:], offs)
@@ -351,7 +350,8 @@ def tile_list_modp_gsigm_res_noneb_kernel(
         round_wu(0, 0, on_scalar, (2,))
         quantize_wu(0, 0)
         rounded_tile(0, 1, ROUNDED_THEN_WG)
-        round_wu(0, 1, on_vector, (0, 2))
+        round_wu(0, 1, on_vector, (0, 2), 0, VECTOR_SHARE)
+        round_wu(0, 1, on_scalar, (0, 2), VECTOR_SHARE, P)
         gate_tile(0, 0)
         gates(0, 0, range(PLACES), (1, 2, 3, 4))
         gate_tile(0, 1)
@@ -373,11 +373,13 @@ def tile_list_modp_gsigm_res_noneb_kernel(
         hidden(1, 0, (3, 4))
         hidden(1, 1, (5, 6))
         hidden(0, 3, (3, 4), H_THEN_ROWS - 1024)
-        for n in (2, 3):
-            rows.append(sharing(f"rows{n}", [P, T], F32, H_THEN_ROWS + (n - 3) * BLOCK))
-        for n in (3, 2):
+        rows.append(sharing("rows1", [P, T], F32, H_THEN_ROWS - BLOCK))
+        rows.append(sharing("rows2", [P, T], F32, H_THEN_ROWS))
+        for n in (1, 2):
             nc.gpsimd.memset(rows[n][:].bitcast(I32), 0)
-        scatter_times_weight(0, 0, add_bias(0, 0, GROUP, (7, 0)))
+        scatter_times_weight(0, 0, add_bias(0, 0, GROUP, (7, 0), H_THEN_ROWS + BLOCK))
+        rows.append(sharing("rows3", [P, T], F32, H_THEN_ROWS + BLOCK))
+        nc.gpsimd.memset(rows[3][:].bitcast(I32), 0)
         weighted = weigh_in_bank(2, down(2, 0, HALF, 1))
         scatter_times_weight(1, 0, add_bias(1, 0, HALF, (2,), LAST_H))
         scatter(2, 0, weighted)

@@ -25,18 +25,18 @@ LIST_COLUMN = 16
 HALF = J // 2
 GROUP = 256
 LAST_FIRST = (1, 0)
-
 LATE = 64
-VECTOR_SHARE = 96
+
 BANK = 2048
 BLOCK = 8192
-SCALES_THEN_WORDS = 0
-ROUNDED_THEN_WG = BLOCK
-WU_THEN_GATES = 3 * BLOCK
-WARM_THEN_ROWS = 5 * BLOCK
-UB_THEN_Y = 6 * BLOCK
-LAST_H = 7 * BLOCK
-H_THEN_ROWS = 9 * BLOCK
+QUARTER = 1024
+SCALES_THEN_ROWS = 0
+WU_THEN_WG = BLOCK
+WU_THEN_GATES = 2 * BLOCK
+TOKEN_WORDS = 3 * BLOCK
+UB_THEN_Y = 3 * BLOCK + BLOCK // 2
+Y_THEN_H = 4 * BLOCK + QUARTER
+LATER_ROWS = (5 * BLOCK, 6 * BLOCK, 7 * BLOCK)
 
 
 def tile_list_modp_gsigm_res_noneb_kernel(
@@ -49,10 +49,9 @@ def tile_list_modp_gsigm_res_noneb_kernel(
         ring = ctx.enter_context(tc.tile_pool(name="ring", bufs=3))
         psum = ctx.enter_context(tc.psum_pool(name="psum", bufs=1))
 
-        def held(name, shape, dtype):
-            return keep.tile(shape, dtype, name=name, align_bytes=64)
-
-        def sharing(name, shape, dtype, offset):
+        def sbuf(name, shape, dtype, offset=None):
+            if offset is None:
+                return keep.tile(shape, dtype, name=name, align_bytes=64)
             return shared.tile(shape, dtype, name=name, align_bytes=64, offset=offset)
 
         def listed(first, count):
@@ -68,106 +67,109 @@ def tile_list_modp_gsigm_res_noneb_kernel(
                     in_=src[:, 4 * q : 4 * q + 4, :].rearrange("a r x -> r a x").bitcast(I32),
                 )
 
-        def load_wg(rb, raw):
+        def load_wg(rb):
+            raw = sbuf(f"wg_raw{rb}", [P, 2, PASS // 2], I32)
             columns = wg_words[:, :, 2 * PASS * rb : 2 * PASS * (rb + 1)]
             nc.sync.dma_start(out=raw[:], in_=columns.rearrange("a p x -> p a x").bitcast(I32))
             return raw
 
         def load_wu(rb, a, offset=None):
-            name, shape = f"wu_raw{rb}{a}", [P, PLACES, PASS]
-            raw = held(name, shape, F32) if offset is None else sharing(name, shape, F32, offset)
+            raw = sbuf(f"wu_raw{rb}{a}", [P, PLACES, PASS], F32, offset)
             block = wu[PASS * a : PASS * (a + 1), PASS * rb : PASS * (rb + 1)]
             nc.sync.dma_start(out=raw[:], in_=block.rearrange("(p i) c -> p i c", i=PLACES))
             return raw
 
-        def order_wg_words(rb, ordered):
-            wg_w[rb] = ordered
-            columns = wg_raw[rb][:].bitcast(U16)
-            nc.vector.tensor_copy(out=ordered[:].bitcast(U16), in_=columns.rearrange("p a (m t) -> p a t m", t=PLACES))
+        def order_wg_words(rb, offset=None):
+            wg_w[rb] = sbuf(f"wg_w{rb}", [P, 2, PLACES, 2 * P], U8, offset)
+            columns = wg_raw[rb][:].bitcast(U16).rearrange("p a (m t) -> p a t m", t=PLACES)
+            nc.vector.tensor_copy(out=wg_w[rb][:].bitcast(U16), in_=columns)
 
-        wg_s_raw = sharing("wg_s_raw", [P, 2, R // 4], I32, SCALES_THEN_WORDS)
-        nc.vector.memset(wg_s_raw[:], 0)
-        tab_s = held("tab_s", [P, T // 4], I32)
+        wg_s = sbuf("wg_s", [P, 2, 2, PLACES, P], U8)
+        nc.vector.memset(wg_s[:].rearrange("p r a t m -> p (r a t m)").bitcast(I32), 0)
+        wg_s_rows = sbuf("wg_s_rows", [P, PASS // 4], I32, SCALES_THEN_ROWS)
+        nc.vector.memset(wg_s_rows[2 * QUADRANT :], 0)
+        tab_s = sbuf("tab_s", [P, T // 4], I32)
         nc.vector.memset(tab_s[QUADRANT : 2 * QUADRANT], 0)
         nc.vector.memset(tab_s[2 * QUADRANT :], 0)
-        rows = [held("rows0", [P, T], F32)]
-        nc.vector.memset(rows[0][:].bitcast(I32), 0)
-        tok_s = held("tok_s", [P, 2, J], U8)
-        nc.vector.memset(tok_s[:].bitcast(I32), 0)
-        wd_s = held("wd_s", [P, 2, 2, N // 4], I32)
-        nc.vector.memset(wd_s[:], 0)
-        warm = held("warm", [P, 2], F32)
+        warm = sbuf("warm", [P, 2], F32)
         nc.gpsimd.memset(warm[:, 0:1], 0.0)
         nc.scalar.activation(out=warm[:, 1:2], in_=warm[:, 0:1], func=ACT.Sigmoid)
 
-
         offsets = keep.tile([P, J // LIST_COLUMN], U16, name="offsets")
         nc.sync.dma_start(offsets[:], offs)
+        for a in range(2):
+            nc.sync.dma_start(
+                out=wg_s_rows[a : 2 * QUADRANT : 2, :],
+                in_=wg_scales[a].rearrange("b (r x) -> (b r) x", r=2).bitcast(I32),
+            )
         nc.sync.dma_start(out=tab_s[0:QUADRANT, :], in_=tab_scales.rearrange("a b x -> b a x").bitcast(I32))
-        tab_w = held("tab_w", [P, T], I32)
+        wg_raw = [load_wg(0)]
+        tab_w = sbuf("tab_w", [P, T], I32)
         nc.sync.dma_start(out=tab_w[:], in_=tab_words[0].rearrange("p t x -> p (t x)").bitcast(I32))
-        wg_raw = [load_wg(0, held("wg_raw0", [P, 2, PASS // 2], I32))]
-        load_scales(wg_s_raw, wg_scales)
+        wg_s_ordered = sbuf("wg_s_ordered", [P, PLACES, P], U8)
+        by_place = wg_s_rows[:].bitcast(U8).rearrange("p (m t) -> p t m", t=PLACES)
+        nc.vector.tensor_copy(out=wg_s_ordered[:], in_=by_place)
+        for q in range(P // QUADRANT):
+            nc.sync.dma_start(
+                out=wg_s[QUADRANT * q : QUADRANT * q + 4].rearrange("p r a t m -> p (r a t m)").bitcast(I32),
+                in_=wg_s_ordered[16 * q : 16 * q + 16].rearrange("p t m -> p (t m)").bitcast(I32),
+            )
+        rows = [sbuf("rows0", [P, T], F32, SCALES_THEN_ROWS)]
+        nc.gpsimd.memset(rows[0][:].bitcast(I32), 0)
+        tok_s = sbuf("tok_s", [P, 2, J], U8)
+        nc.vector.memset(tok_s[:].bitcast(I32), 0)
+        wd_s = sbuf("wd_s", [P, 2, 2, N // 4], I32)
+        nc.vector.memset(wd_s[:], 0)
         wu_raw = {(0, 0): load_wu(0, 0)}
-        wg_w_shape, wg_s_shape = [P, 2, PLACES, 2 * P], [P, 2, PLACES, P]
-        tok_s_rows = held("tok_s_rows", [P, J], U8)
+        tok_s_rows = sbuf("tok_s_rows", [P, J], U8)
         nc.vector.tensor_copy(tok_s_rows[:], tab_s[:].bitcast(U8).indirect(offsets[:]))
         for q in range(P // QUADRANT):
             nc.sync.dma_start(
                 out=tok_s[QUADRANT * q : QUADRANT * q + 4].bitcast(I32),
                 in_=tok_s_rows[8 * q : 8 * q + 8, :].bitcast(I32),
             )
-        wu_raw[0, 1] = load_wu(0, 1)
-        wg_raw.append(load_wg(1, held("wg_raw1", [P, 2, PASS // 2], I32)))
+        wu_raw[0, 1] = load_wu(0, 1, WU_THEN_WG)
+        wg_raw.append(load_wg(1))
         wu_raw[1, 0] = load_wu(1, 0)
         wu_raw[1, 1] = load_wu(1, 1, WU_THEN_GATES)
-        wd4_w = held("wd4_w", [P, 2, N // 2], I32)
+        wd4_w = sbuf("wd4_w", [P, 2, N // 2], I32)
         nc.sync.dma_start(out=wd4_w[:], in_=wd4_words.rearrange("a p x -> p a x").bitcast(I32))
-        wd8_w = held("wd8_w", [P, 2, N], I32)
+        wd8_w = sbuf("wd8_w", [P, 2, N], I32)
         nc.sync.dma_start(out=wd8_w[:], in_=wd8_words.rearrange("a p n x -> p a (n x)").bitcast(I32))
         load_scales(wd_s[:, 0], wd4_scales)
         load_scales(wd_s[:, 1], wd8_scales)
         wd4_s, wd8_s = wd_s[:, 0].bitcast(U8), wd_s[:, 1].bitcast(U8)
-        bias = held("bias", [P, N // P], F32)
+        bias = sbuf("bias", [P, N // P], F32)
         with nc.allow_non_contiguous_dma(reason="one bias value for each partition and output tile"):
             nc.sync.dma_start(out=bias[:], in_=b.rearrange("(c p) -> p c", p=P))
-        weight = held("weight", [P, J], F32)
+        weight = sbuf("weight", [P, J], F32)
         nc.sync.dma_start(out=weight[:], in_=wgo)
 
-        tok_w, wg_w, wg_s, rounded, wu_w, wu_s, gate = {}, {}, {}, {}, {}, {}, {}
-        rounded_shape = [P, PLACES, P, PLACES]
-        h_w = [held(f"h_w{rb}", [P, J], U32) for rb in range(2)]
-        h_s = [held(f"h_s{rb}", [P, J], U8) for rb in range(2)]
+        tok_w, wg_w, rounded, wu_w, wu_s, gate = {}, {}, {}, {}, {}, {}
+        h_w = [sbuf(f"h_w{rb}", [P, J], U32) for rb in range(2)]
+        h_s = [sbuf(f"h_s{rb}", [P, J], U8) for rb in range(2)]
 
-        def part_words(half, both, parted):
-            tok_w[half] = parted
-            by_pass = both[:, half * HALF : (half + 1) * HALF].bitcast(U16).rearrange("p (j a) -> p a j", a=2)
+        def gather_words(half):
+            both = sbuf(f"tok_both{half}", [P, HALF], U32, TOKEN_WORDS)
+            nc.vector.tensor_copy(both[:], tab_w[:].bitcast(U32).indirect(listed(half * HALF, HALF)))
+            tok_w[half] = sbuf(f"tok_w{half}", [P, 2, 2 * HALF], U8)
+            by_pass = both[:].bitcast(U16).rearrange("p (j a) -> p a j", a=2)
             nc.vector.tensor_copy(out=tok_w[half][:].bitcast(U16), in_=by_pass)
-
-        def order_wg_scales(rb, ordered):
-            wg_s[rb] = ordered
-            columns = wg_s_raw[:].bitcast(U8)[:, :, PASS * rb : PASS * (rb + 1)]
-            nc.vector.tensor_copy(out=wg_s[rb][:], in_=columns.rearrange("p a (m t) -> p a t m", t=PLACES))
 
         def token_operand(a, first, count):
             half, j0 = divmod(first, HALF)
             return tok_w[half][:, a, 2 * j0 : 2 * (j0 + count)].bitcast(FP4X4), tok_s[:, a, first : first + count]
 
-        def round_wu(rb, a, copy, places, m0=0, m1=P):
+        def round_wu(rb, a, copies):
+            rounded[rb, a] = sbuf(f"wu_rounded{rb}{a}", [P, PLACES, P, PLACES], BF16)
             source = wu_raw[rb, a][:].rearrange("p i (m t) -> p m i t", t=PLACES)
-            for t0 in places:
-                target = rounded[rb, a][:, t0 : t0 + 2, m0:m1].rearrange("p t m i -> p m i t")
-                copy(out=target, in_=source[:, m0:m1, :, t0 : t0 + 2])
-
-        def rounded_tile(rb, a, offset=None):
-            name = f"wu_rounded{rb}{a}"
-            rounded[rb, a] = (
-                held(name, rounded_shape, BF16) if offset is None else sharing(name, rounded_shape, BF16, offset)
-            )
+            for t0, copy in zip((0, 2), copies):
+                target = rounded[rb, a][:, t0 : t0 + 2].rearrange("p t m i -> p m i t")
+                copy(out=target, in_=source[:, :, :, t0 : t0 + 2])
 
         def quantize_wu(rb, a, pieces=1):
-            wu_w[rb, a] = held(f"wu_w{rb}{a}", [P, PASS], U32)
-            wu_s[rb, a] = held(f"wu_s{rb}{a}", [P, PASS], U8)
+            wu_w[rb, a] = sbuf(f"wu_w{rb}{a}", [P, PASS], U32)
+            wu_s[rb, a] = sbuf(f"wu_s{rb}{a}", [P, PASS], U8)
             values = rounded[rb, a][:].rearrange("p t m i -> p (t m i)")
             width = PASS // pieces
             for c0 in range(0, PASS, width):
@@ -177,19 +179,16 @@ def tile_list_modp_gsigm_res_noneb_kernel(
                     in_=values[:, PLACES * c0 : PLACES * (c0 + width)],
                 )
 
-        def gate_tile(rb, half, offset=None):
-            name, shape = f"gate{rb}{half}", [P, PLACES, HALF]
-            gate[rb, half] = held(name, shape, F32) if offset is None else sharing(name, shape, F32, offset)
-
-        def gates(rb, half, places, banks):
-            for t, number in zip(places, banks):
+        def gates(rb, half, banks, offset=None):
+            gate[rb, half] = sbuf(f"gate{rb}{half}", [P, PLACES, HALF], F32, offset)
+            for t, number in enumerate(banks):
                 ga = bank(f"ga{rb}{half}{t}", [P, HALF], number)
                 for a in LAST_FIRST:
                     words, scales = token_operand(a, half * HALF, HALF)
                     nc.tensor.matmul_mx(
                         out=ga[:],
                         lhsT=wg_w[rb][:, a, t, :].bitcast(FP4X4),
-                        lhsT_scale=wg_s[rb][:, a, t, :],
+                        lhsT_scale=wg_s[:, rb, a, t, :],
                         rhs=words,
                         rhs_scale=scales,
                         start=(a == LAST_FIRST[0]),
@@ -200,7 +199,7 @@ def tile_list_modp_gsigm_res_noneb_kernel(
         def hidden(rb, g, banks, offset=None, places=(3, 2, 1, 0)):
             first = g * GROUP
             if offset is not None:
-                h = sharing(f"h{rb}{g}", [P, GROUP, PLACES], BF16, offset)
+                h = sbuf(f"h{rb}{g}", [P, GROUP, PLACES], BF16, offset)
             else:
                 h = ring.tile([P, GROUP, PLACES], BF16, name="h", align_bytes=64)
             for j0, number in zip(range(0, GROUP, P), banks):
@@ -262,8 +261,7 @@ def tile_list_modp_gsigm_res_noneb_kernel(
             return y
 
         def add_bias(n, first, count, banks, offset=None):
-            name, shape = f"y_biased{n}{first}", [P, count]
-            biased = held(name, shape, F32) if offset is None else sharing(name, shape, F32, offset)
+            biased = sbuf(f"y_biased{n}{first}", [P, count], F32, offset)
             width = count // len(banks)
             for j0, number in zip(range(0, count, width), banks):
                 y = down(n, first + j0, width, number)
@@ -272,134 +270,128 @@ def tile_list_modp_gsigm_res_noneb_kernel(
                 )
             return biased
 
-        def scatter_times_weight(n, first, biased):
-            count = biased.shape[1]
+        def down_and_scatter(n, first, count, banks, offset=None):
+            biased = add_bias(n, first, count, banks, offset)
             nc.vector.tensor_tensor(
                 rows[n][:].indirect(listed(first, count)), biased[:], weight[:, first : first + count], MULT
             )
 
         def weigh_in_bank(n, y, count=HALF):
-            weighted = held(f"y_weighted{n}", [P, HALF], F32)
+            weighted = sbuf(f"y_weighted{n}", [P, HALF], F32)
             nc.vector.scalar_tensor_tensor(
                 weighted[:, :count], y[:, :count], bias[:, n : n + 1], weight[:, :count], ADD, MULT
             )
             return weighted
 
-        def scatter(n, first, weighted):
-            nc.vector.tensor_copy(rows[n][:].indirect(listed(first, weighted.shape[1])), weighted[:])
+        def scatter_first_half(n, weighted):
+            nc.vector.tensor_copy(rows[n][:].indirect(listed(0, HALF)), weighted[:])
 
-        def factor(g, which, banks, offset=None):
-            name, shape = f"factor{g}{which}", [P, GROUP, PLACES]
-            tile = held(name, shape, F32) if offset is None else sharing(name, shape, F32, offset)
+        def factor(name, g, stationary, func, banks, offset=None):
+            values = sbuf(name, [P, GROUP, PLACES], F32, offset)
             for j0, number in zip(range(0, GROUP, P), banks):
-                acc = bank(f"acc{g}{which}{j0}", [P, PLACES, P], number)
+                acc = bank(f"acc_{name}{j0}", [P, PLACES, P], number)
                 for t in range(PLACES):
                     for a in LAST_FIRST:
                         words, scales = token_operand(a, g * GROUP + j0, P)
-                        if which == 0:
-                            lhs, lhs_scales = wg_w[1][:, a, t, :].bitcast(FP4X4), wg_s[1][:, a, t, :]
-                        else:
-                            columns = slice(P * t, P * (t + 1))
-                            lhs, lhs_scales = wu_w[1, a][:, columns].bitcast(FP8X4), wu_s[1, a][:, columns]
+                        lhs_words, lhs_scales = stationary(a, t)
                         nc.tensor.matmul_mx(
                             out=acc[:, t, :],
-                            lhsT=lhs,
+                            lhsT=lhs_words,
                             lhsT_scale=lhs_scales,
                             rhs=words,
                             rhs_scale=scales,
                             start=(a == LAST_FIRST[0]),
                             stop=(a == LAST_FIRST[-1]),
                         )
-                nc.scalar.activation(
-                    out=tile[:, j0 : j0 + P, :],
-                    in_=acc[:].rearrange("p t j -> p j t"),
-                    func=(ACT.Sigmoid, ACT.Copy)[which],
-                )
-            return tile
+                nc.scalar.activation(out=values[:, j0 : j0 + P, :], in_=acc[:].rearrange("p t j -> p j t"), func=func)
+            return values
 
-        def hidden_on_gpsimd(g, gates, ub):
-            h = sharing(f"h1{g}", [P, GROUP, PLACES], BF16, LAST_H - 1024 * (g - 2))
+        def gate_factor(g, banks):
+            def wg_columns(a, t):
+                return wg_w[1][:, a, t, :].bitcast(FP4X4), wg_s[:, 1, a, t, :]
+
+            return factor(f"gates{g}", g, wg_columns, ACT.Sigmoid, banks)
+
+        def up_factor(g, banks, offset=None):
+            def wu_columns(a, t):
+                return wu_w[1, a][:, P * t : P * (t + 1)].bitcast(FP8X4), wu_s[1, a][:, P * t : P * (t + 1)]
+
+            return factor(f"up{g}", g, wu_columns, ACT.Copy, banks, offset)
+
+        def product_on_gpsimd(g, gated, up, offset):
+            h = sbuf(f"h1{g}", [P, GROUP, PLACES], BF16, offset)
             flat = "p j t -> p (j t)"
-            nc.gpsimd.tensor_tensor(h[:].rearrange(flat), gates[:].rearrange(flat), ub[:].rearrange(flat), MULT)
+            nc.gpsimd.tensor_tensor(h[:].rearrange(flat), gated[:].rearrange(flat), up[:].rearrange(flat), MULT)
             return h
+
+        def zeroed_rows(n):
+            rows.append(sbuf(f"rows{n}", [P, T], F32, LATER_ROWS[n - 1]))
+            nc.gpsimd.memset(rows[n][:].bitcast(I32), 0)
 
         def store(n):
             nc.sync.dma_start(out=out[P * n : P * (n + 1), :], in_=rows[n][:])
 
-        both = held("tok_both", [P, J], U32)
-        nc.vector.tensor_copy(both[:], tab_w[:].bitcast(U32).indirect(offsets[:]))
-        order_wg_words(0, held("wg_w0", wg_w_shape, U8))
+        order_wg_words(0)
         idle = bank("idle", [P, HALF], 0)
-        for t in range(2):
+        for t in range(PLACES):
             nc.tensor.matmul_mx(
                 out=idle[:],
                 lhsT=wg_w[0][:, 0, t, :].bitcast(FP4X4),
-                lhsT_scale=wg_s_raw[:, 0, : P // 4].bitcast(U8),
+                lhsT_scale=wg_s[:, 0, 0, t, :],
                 rhs=wg_w[0][:, 0].rearrange("p t x -> p (t x)").bitcast(FP4X4),
-                rhs_scale=wg_s_raw[:, 0, : HALF // 4].bitcast(U8),
+                rhs_scale=wg_s[:, 0, 0].rearrange("p t m -> p (t m)"),
                 start=True,
                 stop=True,
             )
-        part_words(0, both, held("tok_w0", [P, 2, 2 * HALF], U8))
-        for rb in range(2):
-            order_wg_scales(rb, held(f"wg_s{rb}", wg_s_shape, U8))
-        part_words(1, both, sharing("tok_w1", [P, 2, 2 * HALF], U8, SCALES_THEN_WORDS))
+        gather_words(0)
+        gather_words(1)
         on_scalar, on_vector = nc.scalar.copy, nc.vector.tensor_copy
-        rounded_tile(0, 0)
-        round_wu(0, 0, on_vector, (0,))
-        round_wu(0, 0, on_scalar, (2,))
+        round_wu(0, 0, (on_scalar, on_scalar))
         quantize_wu(0, 0)
-        rounded_tile(0, 1, ROUNDED_THEN_WG)
-        round_wu(0, 1, on_vector, (0, 2), 0, VECTOR_SHARE)
-        round_wu(0, 1, on_scalar, (0, 2), VECTOR_SHARE, P)
-        gate_tile(0, 0)
-        gates(0, 0, range(PLACES), (1, 2, 3, 4))
-        gate_tile(0, 1)
-        gates(0, 1, range(PLACES), (5, 6, 7, 0))
+        round_wu(0, 1, (on_vector, on_vector))
+        gates(0, 0, (1, 2, 3, 4))
+        gates(0, 1, (5, 6, 7, 0))
         quantize_wu(0, 1, pieces=2)
-        order_wg_words(1, sharing("wg_w1", wg_w_shape, U8, ROUNDED_THEN_WG))
-        rounded_tile(1, 0)
-        round_wu(1, 0, on_scalar, (0, 2))
-        rounded_tile(1, 1)
-        round_wu(1, 1, on_vector, (0,))
-        round_wu(1, 1, on_scalar, (2,))
+        order_wg_words(1, WU_THEN_WG)
+        round_wu(1, 0, (on_scalar, on_scalar))
+        round_wu(1, 1, (on_vector, on_scalar))
         hidden(0, 0, (1, 2), places=range(PLACES))
         hidden(0, 1, (3, 4))
         quantize_wu(1, 0)
         quantize_wu(1, 1, pieces=2)
         hidden(0, 2, (5, 6))
-        gate_tile(1, 0, WU_THEN_GATES)
-        gates(1, 0, range(PLACES), (7, 0, 1, 2))
+
+        gates(1, 0, (7, 0, 1, 2), WU_THEN_GATES)
         hidden(1, 0, (3, 4))
         hidden(1, 1, (5, 6))
-        hidden(0, 3, (3, 4), H_THEN_ROWS - 1024)
-        rows.append(sharing("rows1", [P, T], F32, H_THEN_ROWS - BLOCK))
-        rows.append(sharing("rows2", [P, T], F32, H_THEN_ROWS))
-        for n in (1, 2):
-            nc.gpsimd.memset(rows[n][:].bitcast(I32), 0)
-        scatter_times_weight(0, 0, add_bias(0, 0, GROUP, (7, 0), H_THEN_ROWS + BLOCK))
-        rows.append(sharing("rows3", [P, T], F32, H_THEN_ROWS + BLOCK))
-        nc.gpsimd.memset(rows[3][:].bitcast(I32), 0)
+        hidden(0, 3, (3, 4), LATER_ROWS[1] - QUARTER)
+
+        zeroed_rows(1)
+        zeroed_rows(2)
+        down_and_scatter(0, 0, GROUP, (7, 0), LATER_ROWS[2])
+        zeroed_rows(3)
         weighted = weigh_in_bank(2, down(2, 0, HALF, 1))
-        scatter_times_weight(1, 0, add_bias(1, 0, HALF, (2,), LAST_H))
-        scatter(2, 0, weighted)
-        h = hidden_on_gpsimd(2, factor(2, 0, (7, 0)), factor(2, 1, (1, 2)))
-        gates3 = factor(3, 0, (7, 0))
+        down_and_scatter(1, 0, HALF, (2,), Y_THEN_H)
+        scatter_first_half(2, weighted)
+        third_h = product_on_gpsimd(2, gate_factor(2, (7, 0)), up_factor(2, (1, 2)), Y_THEN_H)
+        last_gates = gate_factor(3, (7, 0))
         y = down(3, 0, HALF, 5)
         late = slice(HALF - LATE, HALF)
-        biased = held("y_biased3", [P, LATE], F32)
-        nc.scalar.activation(out=biased[:], in_=y[:, late], func=ACT.Identity, bias=bias[:, 3:4])
+        late_biased = sbuf("late_biased", [P, LATE], F32)
+        nc.scalar.activation(out=late_biased[:], in_=y[:, late], func=ACT.Identity, bias=bias[:, 3:4])
         weighted = weigh_in_bank(3, y, HALF - LATE)
-        nc.gpsimd.tensor_tensor(weighted[:, late], biased[:], weight[:, late], MULT)
-        quantize_h(1, 2, h)
-        scatter(3, 0, weighted)
-        quantize_h(1, 3, hidden_on_gpsimd(3, gates3, factor(3, 1, (1, 2), UB_THEN_Y)))
-        scatter_times_weight(0, GROUP, add_bias(0, GROUP, GROUP, (6,), LAST_H + 1024))
-        scatter_times_weight(1, HALF, add_bias(1, HALF, GROUP, (3,), UB_THEN_Y + 1024))
-        scatter_times_weight(0, HALF, add_bias(0, HALF, GROUP, (4,), UB_THEN_Y + 2048))
-        for n in (1, 0):
-            scatter_times_weight(n, HALF + GROUP, add_bias(n, HALF + GROUP, GROUP, ((7,), (5,))[n]))
+        nc.gpsimd.tensor_tensor(weighted[:, late], late_biased[:], weight[:, late], MULT)
+        quantize_h(1, 2, third_h)
+        scatter_first_half(3, weighted)
+        last_up = up_factor(3, (1, 2), UB_THEN_Y)
+        quantize_h(1, 3, product_on_gpsimd(3, last_gates, last_up, Y_THEN_H - QUARTER))
+        down_and_scatter(0, GROUP, GROUP, (6,), Y_THEN_H + QUARTER)
+
+        down_and_scatter(1, HALF, GROUP, (3,), UB_THEN_Y)
+        down_and_scatter(0, HALF, GROUP, (4,), UB_THEN_Y + QUARTER)
+        for n, number in ((1, 5), (0, 7)):
+            down_and_scatter(n, HALF + GROUP, GROUP, (number,))
             store(n)
-        for n in (2, 3):
-            scatter_times_weight(n, HALF, add_bias(n, HALF, HALF, ((0,), (1,))[n - 2]))
+        for n, number in ((2, 0), (3, 1)):
+            down_and_scatter(n, HALF, HALF, (number,))
             store(n)

@@ -25,7 +25,7 @@ LIST_COLUMN = 16
 HALF = J // 2
 GROUP = 256
 LAST_FIRST = (1, 0)
-LATE = 64
+LATE = 192
 
 BANK = 2048
 BLOCK = 8192
@@ -36,7 +36,7 @@ WU_THEN_GATES = 2 * BLOCK
 TOKEN_WORDS = 3 * BLOCK
 UB_THEN_Y = 3 * BLOCK + BLOCK // 2
 Y_THEN_H = 4 * BLOCK + QUARTER
-LATER_ROWS = (5 * BLOCK, 6 * BLOCK, 7 * BLOCK)
+LATER_ROWS = {1: 5 * BLOCK, 3: 6 * BLOCK, 2: 7 * BLOCK}
 
 
 def tile_list_modp_gsigm_res_noneb_kernel(
@@ -114,7 +114,7 @@ def tile_list_modp_gsigm_res_noneb_kernel(
                 out=wg_s[QUADRANT * q : QUADRANT * q + 4].rearrange("p r a t m -> p (r a t m)").bitcast(I32),
                 in_=wg_s_ordered[16 * q : 16 * q + 16].rearrange("p t m -> p (t m)").bitcast(I32),
             )
-        rows = [sbuf("rows0", [P, T], F32, SCALES_THEN_ROWS)]
+        rows = {0: sbuf("rows0", [P, T], F32, SCALES_THEN_ROWS)}
         nc.gpsimd.memset(rows[0][:].bitcast(I32), 0)
         tok_s = sbuf("tok_s", [P, 2, J], U8)
         nc.vector.memset(tok_s[:].bitcast(I32), 0)
@@ -179,22 +179,29 @@ def tile_list_modp_gsigm_res_noneb_kernel(
                     in_=values[:, PLACES * c0 : PLACES * (c0 + width)],
                 )
 
-        def gates(rb, half, banks, offset=None):
+        def gate_tile(rb, half, offset=None):
             gate[rb, half] = sbuf(f"gate{rb}{half}", [P, PLACES, HALF], F32, offset)
-            for t, number in enumerate(banks):
-                ga = bank(f"ga{rb}{half}{t}", [P, HALF], number)
-                for a in LAST_FIRST:
-                    words, scales = token_operand(a, half * HALF, HALF)
-                    nc.tensor.matmul_mx(
-                        out=ga[:],
-                        lhsT=wg_w[rb][:, a, t, :].bitcast(FP4X4),
-                        lhsT_scale=wg_s[:, rb, a, t, :],
-                        rhs=words,
-                        rhs_scale=scales,
-                        start=(a == LAST_FIRST[0]),
-                        stop=(a == LAST_FIRST[-1]),
-                    )
-                nc.scalar.activation(out=gate[rb, half][:, t, :], in_=ga[:], func=ACT.Sigmoid)
+
+        def gates(rb, first, count, banks):
+            half, j0 = divmod(first, HALF)
+            places = HALF // count
+            for t0, number in zip(range(0, PLACES, places), banks):
+                ga = bank(f"ga{rb}{first}{t0}", [P, places, count], number)
+                for t in range(t0, t0 + places):
+                    for a in LAST_FIRST:
+                        words, scales = token_operand(a, first, count)
+                        nc.tensor.matmul_mx(
+                            out=ga[:, t - t0, :],
+                            lhsT=wg_w[rb][:, a, t, :].bitcast(FP4X4),
+                            lhsT_scale=wg_s[:, rb, a, t, :],
+                            rhs=words,
+                            rhs_scale=scales,
+                            start=(a == LAST_FIRST[0]),
+                            stop=(a == LAST_FIRST[-1]),
+                        )
+                nc.scalar.activation(
+                    out=gate[rb, half][:, t0 : t0 + places, j0 : j0 + count], in_=ga[:], func=ACT.Sigmoid
+                )
 
         def hidden(rb, g, banks, offset=None, places=(3, 2, 1, 0)):
             first = g * GROUP
@@ -325,7 +332,7 @@ def tile_list_modp_gsigm_res_noneb_kernel(
             return h
 
         def zeroed_rows(n):
-            rows.append(sbuf(f"rows{n}", [P, T], F32, LATER_ROWS[n - 1]))
+            rows[n] = sbuf(f"rows{n}", [P, T], F32, LATER_ROWS[n])
             nc.gpsimd.memset(rows[n][:].bitcast(I32), 0)
 
         def store(n):
@@ -349,8 +356,10 @@ def tile_list_modp_gsigm_res_noneb_kernel(
         round_wu(0, 0, (on_scalar, on_scalar))
         quantize_wu(0, 0)
         round_wu(0, 1, (on_vector, on_vector))
-        gates(0, 0, (1, 2, 3, 4))
-        gates(0, 1, (5, 6, 7, 0))
+        gate_tile(0, 0)
+        gates(0, 0, HALF, (1, 2, 3, 4))
+        gate_tile(0, 1)
+        gates(0, HALF, HALF, (5, 6, 7, 0))
         quantize_wu(0, 1, pieces=2)
         order_wg_words(1, WU_THEN_WG)
         round_wu(1, 0, (on_scalar, on_scalar))
@@ -361,16 +370,19 @@ def tile_list_modp_gsigm_res_noneb_kernel(
         quantize_wu(1, 1, pieces=2)
         hidden(0, 2, (5, 6))
 
-        gates(1, 0, (7, 0, 1, 2), WU_THEN_GATES)
+        gate_tile(1, 0, WU_THEN_GATES)
+        gates(1, 0, GROUP, (7, 0))
+        gates(1, GROUP, GROUP, (1, 2))
         hidden(1, 0, (3, 4))
         hidden(1, 1, (5, 6))
-        hidden(0, 3, (3, 4), LATER_ROWS[1] - QUARTER)
+        hidden(0, 3, (3, 4), LATER_ROWS[3] - QUARTER)
 
         zeroed_rows(1)
-        zeroed_rows(2)
-        down_and_scatter(0, 0, GROUP, (7, 0), LATER_ROWS[2])
         zeroed_rows(3)
+        down_and_scatter(0, 0, GROUP, (7, 0), LATER_ROWS[2])
+        zeroed_rows(2)
         weighted = weigh_in_bank(2, down(2, 0, HALF, 1))
+        down_and_scatter(0, GROUP, GROUP, (6,))
         down_and_scatter(1, 0, HALF, (2,), Y_THEN_H)
         scatter_first_half(2, weighted)
         third_h = product_on_gpsimd(2, gate_factor(2, (7, 0)), up_factor(2, (1, 2)), Y_THEN_H)
@@ -384,8 +396,7 @@ def tile_list_modp_gsigm_res_noneb_kernel(
         quantize_h(1, 2, third_h)
         scatter_first_half(3, weighted)
         last_up = up_factor(3, (1, 2), UB_THEN_Y)
-        quantize_h(1, 3, product_on_gpsimd(3, last_gates, last_up, Y_THEN_H - QUARTER))
-        down_and_scatter(0, GROUP, GROUP, (6,), Y_THEN_H + QUARTER)
+        quantize_h(1, 3, product_on_gpsimd(3, last_gates, last_up, Y_THEN_H))
 
         down_and_scatter(1, HALF, GROUP, (3,), UB_THEN_Y)
         down_and_scatter(0, HALF, GROUP, (4,), UB_THEN_Y + QUARTER)

@@ -25,7 +25,7 @@ LIST_COLUMN = 16
 HALF = J // 2
 GROUP = 256
 LAST_FIRST = (1, 0)
-LATE = 192
+LATE = 320
 
 BANK = 2048
 BLOCK = 8192

@@ -25,18 +25,21 @@ LIST_COLUMN = 16
 HALF = J // 2
 GROUP = 256
 LAST_FIRST = (1, 0)
-LATE = 320
+SHARE = 160
 
 BANK = 2048
 BLOCK = 8192
-QUARTER = 1024
-SCALES_THEN_ROWS = 0
-WU_THEN_WG = BLOCK
-WU_THEN_GATES = 2 * BLOCK
-TOKEN_WORDS = 3 * BLOCK
-UB_THEN_Y = 3 * BLOCK + BLOCK // 2
-Y_THEN_H = 4 * BLOCK + QUARTER
-LATER_ROWS = {1: 5 * BLOCK, 3: 6 * BLOCK, 2: 7 * BLOCK}
+KIB = 1024
+ROWS = [n * BLOCK for n in range(4)]
+TOKEN_WORDS = 4 * BLOCK + 2 * KIB
+H_LOW = 5 * BLOCK + KIB
+H_HIGH = 5 * BLOCK + 2 * KIB
+LATE_HIGH = 5 * BLOCK + 3 * KIB
+UP_THEN_Y = 6 * BLOCK
+LAST_WU = 7 * BLOCK
+FIRST_WU = 9 * BLOCK
+WU_THEN_WG = 10 * BLOCK + 2 * KIB
+Y_THEN_CODES = 11 * BLOCK + 2 * KIB
 
 
 def tile_list_modp_gsigm_res_noneb_kernel(
@@ -46,7 +49,6 @@ def tile_list_modp_gsigm_res_noneb_kernel(
     with ExitStack() as ctx:
         keep = ctx.enter_context(tc.tile_pool(name="keep", bufs=1))
         shared = ctx.enter_context(tc.tile_pool(name="shared", bufs=1))
-        ring = ctx.enter_context(tc.tile_pool(name="ring", bufs=3))
         psum = ctx.enter_context(tc.psum_pool(name="psum", bufs=1))
 
         def sbuf(name, shape, dtype, offset=None):
@@ -61,21 +63,25 @@ def tile_list_modp_gsigm_res_noneb_kernel(
             return psum.tile(shape, F32, name=name, offset=number * BANK)
 
         def load_scales(tile, src):
-            for q in range(P // QUADRANT):
+            for r in range(4):
                 nc.sync.dma_start(
-                    out=tile[QUADRANT * q : QUADRANT * q + 4, :, :],
-                    in_=src[:, 4 * q : 4 * q + 4, :].rearrange("a r x -> r a x").bitcast(I32),
+                    out=tile[r:P:QUADRANT],
+                    in_=src[:, r:16:4, :].rearrange("a q x -> q a x").bitcast(I32),
                 )
 
-        def load_wg(rb):
-            raw = sbuf(f"wg_raw{rb}", [P, 2, PASS // 2], I32)
+        def zeroed_rows(n):
+            rows[n] = sbuf(f"rows{n}", [P, T], F32, ROWS[n])
+            nc.gpsimd.memset(rows[n][:].bitcast(I32), 0)
+
+        def load_wg(rb, offset=None):
+            raw = sbuf(f"wg_raw{rb}", [P, 2, PASS // 2], I32, offset)
             columns = wg_words[:, :, 2 * PASS * rb : 2 * PASS * (rb + 1)]
             nc.sync.dma_start(out=raw[:], in_=columns.rearrange("a p x -> p a x").bitcast(I32))
             return raw
 
-        def load_wu(rb, a, offset=None):
-            raw = sbuf(f"wu_raw{rb}{a}", [P, PLACES, PASS], F32, offset)
-            block = wu[PASS * a : PASS * (a + 1), PASS * rb : PASS * (rb + 1)]
+        def load_wu(rb, a, offset=None, c0=0, width=PASS):
+            raw = sbuf(f"wu_raw{rb}{a}{c0}", [P, PLACES, width], F32, offset)
+            block = wu[PASS * a : PASS * (a + 1), PASS * rb + c0 : PASS * rb + c0 + width]
             nc.sync.dma_start(out=raw[:], in_=block.rearrange("(p i) c -> p i c", i=PLACES))
             return raw
 
@@ -84,43 +90,36 @@ def tile_list_modp_gsigm_res_noneb_kernel(
             columns = wg_raw[rb][:].bitcast(U16).rearrange("p a (m t) -> p a t m", t=PLACES)
             nc.vector.tensor_copy(out=wg_w[rb][:].bitcast(U16), in_=columns)
 
-        wg_s = sbuf("wg_s", [P, 2, 2, PLACES, P], U8)
-        nc.vector.memset(wg_s[:].rearrange("p r a t m -> p (r a t m)").bitcast(I32), 0)
-        wg_s_rows = sbuf("wg_s_rows", [P, PASS // 4], I32, SCALES_THEN_ROWS)
-        nc.vector.memset(wg_s_rows[2 * QUADRANT :], 0)
+        wg_s_raw = sbuf("wg_s_raw", [P, 2, R // 4], I32)
+        nc.vector.memset(wg_s_raw[:], 0)
         tab_s = sbuf("tab_s", [P, T // 4], I32)
         nc.vector.memset(tab_s[QUADRANT : 2 * QUADRANT], 0)
         nc.vector.memset(tab_s[2 * QUADRANT :], 0)
-        warm = sbuf("warm", [P, 2], F32)
+        tok_s = sbuf("tok_s", [P, 2, J], U8)
+        nc.vector.memset(tok_s[:].bitcast(I32), 0)
+        wd_s = sbuf("wd_s", [P, 2, 2, N // 4], I32)
+        nc.vector.memset(wd_s[:], 0)
+        rows = {}
+        warm = sbuf("warm", [P, 2], F32, ROWS[0])
         nc.gpsimd.memset(warm[:, 0:1], 0.0)
         nc.scalar.activation(out=warm[:, 1:2], in_=warm[:, 0:1], func=ACT.Sigmoid)
 
         offsets = keep.tile([P, J // LIST_COLUMN], U16, name="offsets")
         nc.sync.dma_start(offsets[:], offs)
-        for a in range(2):
-            nc.sync.dma_start(
-                out=wg_s_rows[a : 2 * QUADRANT : 2, :],
-                in_=wg_scales[a].rearrange("b (r x) -> (b r) x", r=2).bitcast(I32),
-            )
         nc.sync.dma_start(out=tab_s[0:QUADRANT, :], in_=tab_scales.rearrange("a b x -> b a x").bitcast(I32))
-        wg_raw = [load_wg(0)]
+        load_scales(wg_s_raw, wg_scales)
+        wg_raw = [load_wg(0, ROWS[1])]
         tab_w = sbuf("tab_w", [P, T], I32)
         nc.sync.dma_start(out=tab_w[:], in_=tab_words[0].rearrange("p t x -> p (t x)").bitcast(I32))
-        wg_s_ordered = sbuf("wg_s_ordered", [P, PLACES, P], U8)
-        by_place = wg_s_rows[:].bitcast(U8).rearrange("p (m t) -> p t m", t=PLACES)
-        nc.vector.tensor_copy(out=wg_s_ordered[:], in_=by_place)
-        for q in range(P // QUADRANT):
-            nc.sync.dma_start(
-                out=wg_s[QUADRANT * q : QUADRANT * q + 4].rearrange("p r a t m -> p (r a t m)").bitcast(I32),
-                in_=wg_s_ordered[16 * q : 16 * q + 16].rearrange("p t m -> p (t m)").bitcast(I32),
-            )
-        rows = {0: sbuf("rows0", [P, T], F32, SCALES_THEN_ROWS)}
-        nc.gpsimd.memset(rows[0][:].bitcast(I32), 0)
-        tok_s = sbuf("tok_s", [P, 2, J], U8)
-        nc.vector.memset(tok_s[:].bitcast(I32), 0)
-        wd_s = sbuf("wd_s", [P, 2, 2, N // 4], I32)
-        nc.vector.memset(wd_s[:], 0)
-        wu_raw = {(0, 0): load_wu(0, 0)}
+        wu_raw = {(0, 0): load_wu(0, 0, FIRST_WU)}
+        wg_s = {}
+
+        def order_wg_scales(rb, offset=None):
+            wg_s[rb] = sbuf(f"wg_s{rb}", [P, 2, PLACES, P], U8, offset)
+            columns = wg_s_raw[:].bitcast(U8)[:, :, PASS * rb : PASS * (rb + 1)]
+            nc.vector.tensor_copy(out=wg_s[rb][:], in_=columns.rearrange("p a (m t) -> p a t m", t=PLACES))
+
+        zeroed_rows(0)
         tok_s_rows = sbuf("tok_s_rows", [P, J], U8)
         nc.vector.tensor_copy(tok_s_rows[:], tab_s[:].bitcast(U8).indirect(offsets[:]))
         for q in range(P // QUADRANT):
@@ -129,29 +128,23 @@ def tile_list_modp_gsigm_res_noneb_kernel(
                 in_=tok_s_rows[8 * q : 8 * q + 8, :].bitcast(I32),
             )
         wu_raw[0, 1] = load_wu(0, 1, WU_THEN_WG)
-        wg_raw.append(load_wg(1))
+        wg_raw.append(load_wg(1, ROWS[2]))
         wu_raw[1, 0] = load_wu(1, 0)
-        wu_raw[1, 1] = load_wu(1, 1, WU_THEN_GATES)
-        wd4_w = sbuf("wd4_w", [P, 2, N // 2], I32)
-        nc.sync.dma_start(out=wd4_w[:], in_=wd4_words.rearrange("a p x -> p a x").bitcast(I32))
-        wd8_w = sbuf("wd8_w", [P, 2, N], I32)
-        nc.sync.dma_start(out=wd8_w[:], in_=wd8_words.rearrange("a p n x -> p a (n x)").bitcast(I32))
-        load_scales(wd_s[:, 0], wd4_scales)
-        load_scales(wd_s[:, 1], wd8_scales)
-        wd4_s, wd8_s = wd_s[:, 0].bitcast(U8), wd_s[:, 1].bitcast(U8)
-        bias = sbuf("bias", [P, N // P], F32)
-        with nc.allow_non_contiguous_dma(reason="one bias value for each partition and output tile"):
-            nc.sync.dma_start(out=bias[:], in_=b.rearrange("(c p) -> p c", p=P))
-        weight = sbuf("weight", [P, J], F32)
-        nc.sync.dma_start(out=weight[:], in_=wgo)
+        last_raw = [load_wu(1, 1, LAST_WU + half * BLOCK // 2, half * PASS // 2, PASS // 2) for half in range(2)]
 
         tok_w, wg_w, rounded, wu_w, wu_s, gate = {}, {}, {}, {}, {}, {}
-        h_w = [sbuf(f"h_w{rb}", [P, J], U32) for rb in range(2)]
-        h_s = [sbuf(f"h_s{rb}", [P, J], U8) for rb in range(2)]
+        h_w, h_s = {}, {}
+
+        def codes_of_h(rb, first, count):
+            start = min(first // GROUP * GROUP, HALF)
+            return h_w[rb, start][:, first - start : first - start + count], h_s[rb, start][:, first - start : first - start + count]
 
         def gather_words(half):
-            both = sbuf(f"tok_both{half}", [P, HALF], U32, TOKEN_WORDS)
+            both = sbuf(f"tok_both{half}", [P, HALF], U32, TOKEN_WORDS + 2 * KIB * half)
             nc.vector.tensor_copy(both[:], tab_w[:].bitcast(U32).indirect(listed(half * HALF, HALF)))
+            return both
+
+        def part_words(half, both):
             tok_w[half] = sbuf(f"tok_w{half}", [P, 2, 2 * HALF], U8)
             by_pass = both[:].bitcast(U16).rearrange("p (j a) -> p a j", a=2)
             nc.vector.tensor_copy(out=tok_w[half][:].bitcast(U16), in_=by_pass)
@@ -160,12 +153,28 @@ def tile_list_modp_gsigm_res_noneb_kernel(
             half, j0 = divmod(first, HALF)
             return tok_w[half][:, a, 2 * j0 : 2 * (j0 + count)].bitcast(FP4X4), tok_s[:, a, first : first + count]
 
-        def round_wu(rb, a, copies):
-            rounded[rb, a] = sbuf(f"wu_rounded{rb}{a}", [P, PLACES, P, PLACES], BF16)
+        def round_wu(rb, a, copies, offset=None):
+            rounded[rb, a] = sbuf(f"wu_rounded{rb}{a}", [P, PLACES, P, PLACES], BF16, offset)
             source = wu_raw[rb, a][:].rearrange("p i (m t) -> p m i t", t=PLACES)
             for t0, copy in zip((0, 2), copies):
                 target = rounded[rb, a][:, t0 : t0 + 2].rearrange("p t m i -> p m i t")
                 copy(out=target, in_=source[:, :, :, t0 : t0 + 2])
+
+        def round_last(half, copies, offset=None):
+            last = sbuf(f"last_rounded{half}", [P, PLACES, P // 2, PLACES], BF16, offset)
+            source = last_raw[half][:].rearrange("p i (m t) -> p m i t", t=PLACES)
+            for t0, copy in zip((0, 2), copies):
+                copy(out=last[:, t0 : t0 + 2].rearrange("p t m i -> p m i t"), in_=source[:, :, :, t0 : t0 + 2])
+            return last
+
+        def quantize_last(half, last):
+            for t in range(PLACES):
+                columns = slice(P * t + half * P // 2, P * t + (half + 1) * P // 2)
+                nc.vector.quantize_mx(
+                    out=wu_w[1, 1][:, columns].bitcast(FP8X4),
+                    scales=wu_s[1, 1][:, columns],
+                    in_=last[:, t].rearrange("p m i -> p (m i)"),
+                )
 
         def quantize_wu(rb, a, pieces=1):
             wu_w[rb, a] = sbuf(f"wu_w{rb}{a}", [P, PASS], U32)
@@ -179,12 +188,11 @@ def tile_list_modp_gsigm_res_noneb_kernel(
                     in_=values[:, PLACES * c0 : PLACES * (c0 + width)],
                 )
 
-        def gate_tile(rb, half, offset=None):
-            gate[rb, half] = sbuf(f"gate{rb}{half}", [P, PLACES, HALF], F32, offset)
-
-        def gates(rb, first, count, banks):
-            half, j0 = divmod(first, HALF)
+        def gates(rb, first, count, banks, offset=None):
             places = HALF // count
+            tile = sbuf(f"gate{rb}{first}", [P, PLACES, count], F32, offset)
+            for j0 in range(0, count, P):
+                gate[rb, first + j0] = tile[:, :, j0 : j0 + P]
             for t0, number in zip(range(0, PLACES, places), banks):
                 ga = bank(f"ga{rb}{first}{t0}", [P, places, count], number)
                 for t in range(t0, t0 + places):
@@ -193,25 +201,20 @@ def tile_list_modp_gsigm_res_noneb_kernel(
                         nc.tensor.matmul_mx(
                             out=ga[:, t - t0, :],
                             lhsT=wg_w[rb][:, a, t, :].bitcast(FP4X4),
-                            lhsT_scale=wg_s[:, rb, a, t, :],
+                            lhsT_scale=wg_s[rb][:, a, t, :],
                             rhs=words,
                             rhs_scale=scales,
                             start=(a == LAST_FIRST[0]),
                             stop=(a == LAST_FIRST[-1]),
                         )
-                nc.scalar.activation(
-                    out=gate[rb, half][:, t0 : t0 + places, j0 : j0 + count], in_=ga[:], func=ACT.Sigmoid
-                )
+                nc.scalar.activation(out=tile[:, t0 : t0 + places, :], in_=ga[:], func=ACT.Sigmoid)
 
-        def hidden(rb, g, banks, offset=None, places=(3, 2, 1, 0)):
-            first = g * GROUP
-            if offset is not None:
-                h = sbuf(f"h{rb}{g}", [P, GROUP, PLACES], BF16, offset)
-            else:
-                h = ring.tile([P, GROUP, PLACES], BF16, name="h", align_bytes=64)
-            for j0, number in zip(range(0, GROUP, P), banks):
-                ub = bank(f"ub{rb}{g}{j0}", [P, PLACES, P], number)
-                for t in places:
+        def hidden(rb, first, banks, offset=None, first_places=(3, 2, 1, 0)):
+            count = P * len(banks)
+            h = sbuf(f"h{rb}{first}", [P, count, PLACES], BF16, offset)
+            for j0, number in zip(range(0, count, P), banks):
+                ub = bank(f"ub{rb}{first}{j0}", [P, PLACES, P], number)
+                for t in first_places if j0 == 0 else (3, 2, 1, 0):
                     for a in LAST_FIRST:
                         words, scales = token_operand(a, first + j0, P)
                         nc.tensor.matmul_mx(
@@ -223,20 +226,24 @@ def tile_list_modp_gsigm_res_noneb_kernel(
                             start=(a == LAST_FIRST[0]),
                             stop=(a == LAST_FIRST[-1]),
                         )
-                half, in_half = divmod(first + j0, HALF)
                 nc.vector.tensor_tensor(
                     h[:, j0 : j0 + P, :].rearrange("p (c e) t -> p c t e", e=2),
                     ub[:].rearrange("p t (c e) -> p c t e", e=2),
-                    gate[rb, half][:, :, in_half : in_half + P].rearrange("p t (c e) -> p c t e", e=2),
+                    gate[rb, first + j0].rearrange("p t (c e) -> p c t e", e=2),
                     MULT,
                 )
-            quantize_h(rb, g, h)
+            quantize_h(rb, first, h, count=count)
 
-        def quantize_h(rb, g, h):
-            first = g * GROUP
+        def quantize_h(rb, first, h, offset=None, count=GROUP):
+            start = min(first // GROUP * GROUP, HALF)
+            if (rb, start) not in h_w:
+                width = HALF if start == HALF else GROUP
+                h_w[rb, start] = sbuf(f"h_w{rb}{start}", [P, width], U32, offset)
+                h_s[rb, start] = sbuf(f"h_s{rb}{start}", [P, width], U8)
+            words, scales = codes_of_h(rb, first, count)
             nc.vector.quantize_mx(
-                out=h_w[rb][:, first : first + GROUP].bitcast(FP8X4),
-                scales=h_s[rb][:, first : first + GROUP],
+                out=words.bitcast(FP8X4),
+                scales=scales,
                 in_=h[:].rearrange("p j t -> p (j t)"),
             )
 
@@ -245,12 +252,12 @@ def tile_list_modp_gsigm_res_noneb_kernel(
             width = HALF if count == HALF else P
             for j0 in range(0, count, width):
                 for rb in LAST_FIRST:
-                    words = h_w[rb][:, first + j0 : first + j0 + width].bitcast(FP8X4)
-                    scales = h_s[rb][:, first + j0 : first + j0 + width]
+                    words, scales = codes_of_h(rb, first + j0, width)
+                    words = words.bitcast(FP8X4)
                     nc.tensor.matmul_mx(
                         out=y[:, j0 : j0 + width],
-                        lhsT=wd8_w[:, rb, P * n : P * (n + 1)].bitcast(FP8X4),
-                        lhsT_scale=wd8_s[:, rb, P * n : P * (n + 1)],
+                        lhsT=wd4_w[:].bitcast(U8)[:, rb, 2 * P * n : 2 * P * (n + 1)].bitcast(FP4X4),
+                        lhsT_scale=wd4_s[:, rb, P * n : P * (n + 1)],
                         rhs=words,
                         rhs_scale=scales,
                         start=(rb == LAST_FIRST[0]),
@@ -258,8 +265,8 @@ def tile_list_modp_gsigm_res_noneb_kernel(
                     )
                     nc.tensor.matmul_mx(
                         out=y[:, j0 : j0 + width],
-                        lhsT=wd4_w[:].bitcast(U8)[:, rb, 2 * P * n : 2 * P * (n + 1)].bitcast(FP4X4),
-                        lhsT_scale=wd4_s[:, rb, P * n : P * (n + 1)],
+                        lhsT=wd8_w[:, rb, P * n : P * (n + 1)].bitcast(FP8X4),
+                        lhsT_scale=wd8_s[:, rb, P * n : P * (n + 1)],
                         rhs=words,
                         rhs_scale=scales,
                         start=False,
@@ -283,21 +290,40 @@ def tile_list_modp_gsigm_res_noneb_kernel(
                 rows[n][:].indirect(listed(first, count)), biased[:], weight[:, first : first + count], MULT
             )
 
-        def weigh_in_bank(n, y, count=HALF):
-            weighted = sbuf(f"y_weighted{n}", [P, HALF], F32)
+        def weighed_on_vector(g, n, number, offset=None):
+            first = g * GROUP
+            y = down(n, first, GROUP, number)
+            weighted = sbuf(f"y_weighted{g}{n}", [P, GROUP], F32, offset)
             nc.vector.scalar_tensor_tensor(
-                weighted[:, :count], y[:, :count], bias[:, n : n + 1], weight[:, :count], ADD, MULT
+                weighted[:], y[:], bias[:, n : n + 1], weight[:, first : first + GROUP], ADD, MULT
             )
-            return weighted
+            return weighted[:]
 
-        def scatter_first_half(n, weighted):
-            nc.vector.tensor_copy(rows[n][:].indirect(listed(0, HALF)), weighted[:])
+        def weighed_pair(g, n0, share, banks, offset):
+            first, own = g * GROUP, GROUP - share
+            weighted = sbuf(f"y_weighted{g}{n0}", [P, 2, GROUP], F32)
+            biased = sbuf(f"y_late{g}{n0}", [P, 2, share], F32, offset)
+            for i, number in enumerate(banks):
+                n = n0 + i
+                y = down(n, first, GROUP, number)
+                nc.scalar.activation(out=biased[:, i, :], in_=y[:, own:], func=ACT.Identity, bias=bias[:, n : n + 1])
+                if own:
+                    nc.vector.scalar_tensor_tensor(
+                        weighted[:, i, :own], y[:, :own], bias[:, n : n + 1], weight[:, first : first + own], ADD, MULT
+                    )
+            late = weight[:, first + own : first + GROUP].unsqueeze(1).to_broadcast([P, 2, share])
+            nc.gpsimd.tensor_tensor(weighted[:, :, own:], biased[:], late, MULT)
+            return weighted[:, 0, :], weighted[:, 1, :]
+
+        def scatter_pair(g, n0, weighted):
+            for i in range(2):
+                nc.vector.tensor_copy(rows[n0 + i][:].indirect(listed(g * GROUP, GROUP)), weighted[i])
 
         def factor(name, g, stationary, func, banks, offset=None):
             values = sbuf(name, [P, GROUP, PLACES], F32, offset)
             for j0, number in zip(range(0, GROUP, P), banks):
                 acc = bank(f"acc_{name}{j0}", [P, PLACES, P], number)
-                for t in range(PLACES):
+                for t in reversed(range(PLACES)):
                     for a in LAST_FIRST:
                         words, scales = token_operand(a, g * GROUP + j0, P)
                         lhs_words, lhs_scales = stationary(a, t)
@@ -313,96 +339,113 @@ def tile_list_modp_gsigm_res_noneb_kernel(
                 nc.scalar.activation(out=values[:, j0 : j0 + P, :], in_=acc[:].rearrange("p t j -> p j t"), func=func)
             return values
 
-        def gate_factor(g, banks):
+        def gate_factor(rb, g, banks, offset=None):
             def wg_columns(a, t):
-                return wg_w[1][:, a, t, :].bitcast(FP4X4), wg_s[:, 1, a, t, :]
+                return wg_w[rb][:, a, t, :].bitcast(FP4X4), wg_s[rb][:, a, t, :]
 
-            return factor(f"gates{g}", g, wg_columns, ACT.Sigmoid, banks)
+            return factor(f"gates{rb}{g}", g, wg_columns, ACT.Sigmoid, banks, offset)
 
-        def up_factor(g, banks, offset=None):
+        def up_factor(rb, g, banks, offset=None):
             def wu_columns(a, t):
-                return wu_w[1, a][:, P * t : P * (t + 1)].bitcast(FP8X4), wu_s[1, a][:, P * t : P * (t + 1)]
+                return wu_w[rb, a][:, P * t : P * (t + 1)].bitcast(FP8X4), wu_s[rb, a][:, P * t : P * (t + 1)]
 
-            return factor(f"up{g}", g, wu_columns, ACT.Copy, banks, offset)
+            return factor(f"up{rb}{g}", g, wu_columns, ACT.Copy, banks, offset)
 
-        def product_on_gpsimd(g, gated, up, offset):
-            h = sbuf(f"h1{g}", [P, GROUP, PLACES], BF16, offset)
+        def product_on_gpsimd(rb, g, gated, up, offset):
+            h = sbuf(f"h{rb}{g}", [P, GROUP, PLACES], BF16, offset)
             flat = "p j t -> p (j t)"
             nc.gpsimd.tensor_tensor(h[:].rearrange(flat), gated[:].rearrange(flat), up[:].rearrange(flat), MULT)
             return h
 
-        def zeroed_rows(n):
-            rows[n] = sbuf(f"rows{n}", [P, T], F32, LATER_ROWS[n])
-            nc.gpsimd.memset(rows[n][:].bitcast(I32), 0)
-
         def store(n):
             nc.sync.dma_start(out=out[P * n : P * (n + 1), :], in_=rows[n][:])
 
+        order_wg_scales(0)
         order_wg_words(0)
         idle = bank("idle", [P, HALF], 0)
         for t in range(PLACES):
             nc.tensor.matmul_mx(
                 out=idle[:],
                 lhsT=wg_w[0][:, 0, t, :].bitcast(FP4X4),
-                lhsT_scale=wg_s[:, 0, 0, t, :],
+                lhsT_scale=wg_s[0][:, 0, t, :],
                 rhs=wg_w[0][:, 0].rearrange("p t x -> p (t x)").bitcast(FP4X4),
-                rhs_scale=wg_s[:, 0, 0].rearrange("p t m -> p (t m)"),
+                rhs_scale=wg_s[0][:, 0].rearrange("p t m -> p (t m)"),
                 start=True,
                 stop=True,
             )
-        gather_words(0)
-        gather_words(1)
+        zeroed_rows(1)
+        both = [gather_words(half) for half in range(2)]
+        for half in range(2):
+            part_words(half, both[half])
+        order_wg_scales(1, TOKEN_WORDS)
+        wd8_w = sbuf("wd8_w", [P, 2, N], I32)
+        nc.sync.dma_start(out=wd8_w[:], in_=wd8_words.rearrange("a p n x -> p a (n x)").bitcast(I32))
+        load_scales(wd_s[:, 1], wd8_scales)
+        wd4_w = sbuf("wd4_w", [P, 2, N // 2], I32)
+        nc.sync.dma_start(out=wd4_w[:], in_=wd4_words.rearrange("a p x -> p a x").bitcast(I32))
+        load_scales(wd_s[:, 0], wd4_scales)
+        wd4_s, wd8_s = wd_s[:, 0].bitcast(U8), wd_s[:, 1].bitcast(U8)
+        weight = sbuf("weight", [P, J], F32)
+        nc.sync.dma_start(out=weight[:, :GROUP], in_=wgo[:, :GROUP])
+        bias = sbuf("bias", [P, N // P], F32)
+        with nc.allow_non_contiguous_dma(reason="one bias value for each partition and output tile"):
+            nc.sync.dma_start(out=bias[:], in_=b.rearrange("(c p) -> p c", p=P))
+        nc.sync.dma_start(out=weight[:, GROUP:], in_=wgo[:, GROUP:])
+
         on_scalar, on_vector = nc.scalar.copy, nc.vector.tensor_copy
-        round_wu(0, 0, (on_scalar, on_scalar))
+        round_wu(0, 0, (on_scalar, on_vector))
         quantize_wu(0, 0)
         round_wu(0, 1, (on_vector, on_vector))
-        gate_tile(0, 0)
-        gates(0, 0, HALF, (1, 2, 3, 4))
-        gate_tile(0, 1)
-        gates(0, HALF, HALF, (5, 6, 7, 0))
+        gates(0, 0, HALF, (1, 2, 3, 4), FIRST_WU - 6 * KIB)
+        gates(0, HALF, GROUP, (5, 6), FIRST_WU + 2 * KIB)
+        gated = {(0, 3): gate_factor(0, 3, (7, 0), FIRST_WU + 6 * KIB)}
         quantize_wu(0, 1, pieces=2)
         order_wg_words(1, WU_THEN_WG)
-        round_wu(1, 0, (on_scalar, on_scalar))
-        round_wu(1, 1, (on_vector, on_scalar))
-        hidden(0, 0, (1, 2), places=range(PLACES))
-        hidden(0, 1, (3, 4))
-        quantize_wu(1, 0)
-        quantize_wu(1, 1, pieces=2)
-        hidden(0, 2, (5, 6))
-
-        gate_tile(1, 0, WU_THEN_GATES)
-        gates(1, 0, GROUP, (7, 0))
-        gates(1, GROUP, GROUP, (1, 2))
-        hidden(1, 0, (3, 4))
-        hidden(1, 1, (5, 6))
-        hidden(0, 3, (3, 4), LATER_ROWS[3] - QUARTER)
-
-        zeroed_rows(1)
-        zeroed_rows(3)
-        down_and_scatter(0, 0, GROUP, (7, 0), LATER_ROWS[2])
         zeroed_rows(2)
-        weighted = weigh_in_bank(2, down(2, 0, HALF, 1))
-        down_and_scatter(0, GROUP, GROUP, (6,))
-        down_and_scatter(1, 0, HALF, (2,), Y_THEN_H)
-        scatter_first_half(2, weighted)
-        third_h = product_on_gpsimd(2, gate_factor(2, (7, 0)), up_factor(2, (1, 2)), Y_THEN_H)
-        last_gates = gate_factor(3, (7, 0))
-        y = down(3, 0, HALF, 5)
-        late = slice(HALF - LATE, HALF)
-        late_biased = sbuf("late_biased", [P, LATE], F32)
-        nc.scalar.activation(out=late_biased[:], in_=y[:, late], func=ACT.Identity, bias=bias[:, 3:4])
-        weighted = weigh_in_bank(3, y, HALF - LATE)
-        nc.gpsimd.tensor_tensor(weighted[:, late], late_biased[:], weight[:, late], MULT)
-        quantize_h(1, 2, third_h)
-        scatter_first_half(3, weighted)
-        last_up = up_factor(3, (1, 2), UB_THEN_Y)
-        quantize_h(1, 3, product_on_gpsimd(3, last_gates, last_up, Y_THEN_H))
+        round_wu(1, 0, (on_scalar, on_scalar))
+        hidden(0, 0, (1, 2), first_places=range(PLACES))
+        hidden(0, GROUP, (3, 4))
+        last = [round_last(0, (on_vector, on_scalar)), round_last(1, (on_vector, on_scalar), 4 * BLOCK - KIB)]
+        quantize_wu(1, 0)
+        wu_w[1, 1], wu_s[1, 1] = sbuf("wu_w11", [P, PASS], U32), sbuf("wu_s11", [P, PASS], U8)
+        for half in range(2):
+            quantize_last(half, last[half])
+        zeroed_rows(3)
+        gates(1, 0, GROUP, (5, 6), LAST_WU + 2 * KIB)
+        gated[1, 1] = gate_factor(1, 1, (7, 0), LAST_WU + 6 * KIB)
+        hidden(1, 0, (3,), None, first_places=range(PLACES))
+        hidden(1, P, (4,), H_LOW)
+        hidden(0, HALF, (1,), 4 * BLOCK)
+        hidden(0, HALF + P, (2,), H_LOW + KIB // 2)
 
-        down_and_scatter(1, HALF, GROUP, (3,), UB_THEN_Y)
-        down_and_scatter(0, HALF, GROUP, (4,), UB_THEN_Y + QUARTER)
-        for n, number in ((1, 5), (0, 7)):
+        up = up_factor(1, 1, (5, 6))
+        weighted = weighed_on_vector(0, 0, 7, Y_THEN_CODES), weighed_on_vector(0, 1, 0)
+        h = product_on_gpsimd(1, 1, gated[1, 1], up, H_LOW)
+        scatter_pair(0, 0, weighted)
+        weighted = weighed_pair(0, 2, GROUP, (1, 2), LATE_HIGH)
+        up = up_factor(0, 3, (7, 0))
+        quantize_h(1, GROUP, h, Y_THEN_CODES)
+        h = product_on_gpsimd(0, 3, gated[0, 3], up, H_HIGH)
+        scatter_pair(0, 2, weighted)
+        gated[1, 2] = gate_factor(1, 2, (1, 2))
+        weighted = weighed_pair(1, 0, SHARE, (5, 6), H_HIGH - 2 * SHARE * 4)
+        up = up_factor(1, 2, (7, 0))
+        quantize_h(0, 3 * GROUP, h)
+        h = product_on_gpsimd(1, 2, gated[1, 2], up, H_LOW)
+        scatter_pair(1, 0, weighted)
+        gated[1, 3] = gate_factor(1, 3, (1, 2))
+        weighted = weighed_pair(1, 2, SHARE, (3, 4), LATE_HIGH)
+        up = up_factor(1, 3, (7, 0), UP_THEN_Y)
+        quantize_h(1, 2 * GROUP, h)
+        h = product_on_gpsimd(1, 3, gated[1, 3], up, H_HIGH)
+        scatter_pair(1, 2, weighted)
+        quantize_h(1, 3 * GROUP, h)
+
+        down_and_scatter(1, HALF, GROUP, (5,), UP_THEN_Y)
+        down_and_scatter(0, HALF, GROUP, (6,), UP_THEN_Y + KIB)
+        for n, number in ((1, 1), (0, 2)):
             down_and_scatter(n, HALF + GROUP, GROUP, (number,))
             store(n)
-        for n, number in ((2, 0), (3, 1)):
+        for n, number in ((2, 7), (3, 0)):
             down_and_scatter(n, HALF, HALF, (number,))
             store(n)

@@ -25,7 +25,9 @@ LIST_COLUMN = 16
 HALF = J // 2
 GROUP = 256
 LAST_FIRST = (1, 0)
-SHARE = 160
+SHARE = 80
+FIRST_SHARE = 256
+WARM_UP = 3
 
 BANK = 2048
 BLOCK = 8192
@@ -39,7 +41,7 @@ UP_THEN_Y = 6 * BLOCK
 LAST_WU = 7 * BLOCK
 FIRST_WU = 9 * BLOCK
 WU_THEN_WG = 10 * BLOCK + 2 * KIB
-Y_THEN_CODES = 11 * BLOCK + 2 * KIB
+Y_THEN_CODES = 11 * BLOCK + 3 * KIB
 
 
 def tile_list_modp_gsigm_res_noneb_kernel(
@@ -135,8 +137,11 @@ def tile_list_modp_gsigm_res_noneb_kernel(
         tok_w, wg_w, rounded, wu_w, wu_s, gate = {}, {}, {}, {}, {}, {}
         h_w, h_s = {}, {}
 
+        def codes_start(rb, first):
+            return first // HALF * HALF if rb == 0 else min(first // GROUP * GROUP, HALF)
+
         def codes_of_h(rb, first, count):
-            start = min(first // GROUP * GROUP, HALF)
+            start = codes_start(rb, first)
             return h_w[rb, start][:, first - start : first - start + count], h_s[rb, start][:, first - start : first - start + count]
 
         def gather_words(half):
@@ -232,12 +237,12 @@ def tile_list_modp_gsigm_res_noneb_kernel(
                     gate[rb, first + j0].rearrange("p t (c e) -> p c t e", e=2),
                     MULT,
                 )
-            quantize_h(rb, first, h, count=count)
+            return h
 
         def quantize_h(rb, first, h, offset=None, count=GROUP):
-            start = min(first // GROUP * GROUP, HALF)
+            start = codes_start(rb, first)
             if (rb, start) not in h_w:
-                width = HALF if start == HALF else GROUP
+                width = HALF if start == HALF or rb == 0 else GROUP
                 h_w[rb, start] = sbuf(f"h_w{rb}{start}", [P, width], U32, offset)
                 h_s[rb, start] = sbuf(f"h_s{rb}{start}", [P, width], U8)
             words, scales = codes_of_h(rb, first, count)
@@ -362,19 +367,19 @@ def tile_list_modp_gsigm_res_noneb_kernel(
 
         order_wg_scales(0)
         order_wg_words(0)
+        zeroed_rows(1)
+        both = [gather_words(half) for half in range(2)]
         idle = bank("idle", [P, HALF], 0)
-        for t in range(PLACES):
+        for t in range(WARM_UP):
             nc.tensor.matmul_mx(
                 out=idle[:],
                 lhsT=wg_w[0][:, 0, t, :].bitcast(FP4X4),
                 lhsT_scale=wg_s[0][:, 0, t, :],
-                rhs=wg_w[0][:, 0].rearrange("p t x -> p (t x)").bitcast(FP4X4),
+                rhs=both[0][:, : HALF // 2].bitcast(U8).bitcast(FP4X4),
                 rhs_scale=wg_s[0][:, 0].rearrange("p t m -> p (t m)"),
                 start=True,
                 stop=True,
             )
-        zeroed_rows(1)
-        both = [gather_words(half) for half in range(2)]
         for half in range(2):
             part_words(half, both[half])
         order_wg_scales(1, TOKEN_WORDS)
@@ -403,28 +408,31 @@ def tile_list_modp_gsigm_res_noneb_kernel(
         order_wg_words(1, WU_THEN_WG)
         zeroed_rows(2)
         round_wu(1, 0, (on_scalar, on_scalar))
-        hidden(0, 0, (1, 2), first_places=range(PLACES))
-        hidden(0, GROUP, (3, 4))
-        last = [round_last(0, (on_vector, on_scalar)), round_last(1, (on_vector, on_scalar), 4 * BLOCK - KIB)]
+        h = hidden(0, 0, (1, 2, 3, 4), first_places=range(PLACES))
+        last = [round_last(0, (on_vector, on_scalar))]
+        quantize_h(0, 0, h, count=HALF)
         quantize_wu(1, 0)
+        last.append(round_last(1, (on_vector, on_scalar), 4 * BLOCK - KIB))
         wu_w[1, 1], wu_s[1, 1] = sbuf("wu_w11", [P, PASS], U32), sbuf("wu_s11", [P, PASS], U8)
         for half in range(2):
             quantize_last(half, last[half])
         zeroed_rows(3)
-        gates(1, 0, GROUP, (5, 6), LAST_WU + 2 * KIB)
-        gated[1, 1] = gate_factor(1, 1, (7, 0), LAST_WU + 6 * KIB)
-        hidden(1, 0, (3,), None, first_places=range(PLACES))
-        hidden(1, P, (4,), H_LOW)
-        hidden(0, HALF, (1,), 4 * BLOCK)
-        hidden(0, HALF + P, (2,), H_LOW + KIB // 2)
+        gates(1, 0, GROUP, (5, 6), LAST_WU)
+        gated[1, 1] = gate_factor(1, 1, (7, 0), LAST_WU + 4 * KIB)
+        h = [hidden(1, 0, (3,), None, first_places=range(PLACES)), hidden(1, P, (4,), H_LOW - KIB // 2)]
+        quantize_h(1, 0, h[0], count=P)
+        quantize_h(1, P, h[1], count=P)
+        fillers = [hidden(0, HALF, (1,), 4 * BLOCK), hidden(0, HALF + P, (2,), H_LOW - KIB - KIB // 4)]
 
         up = up_factor(1, 1, (5, 6))
         weighted = weighed_on_vector(0, 0, 7, Y_THEN_CODES), weighed_on_vector(0, 1, 0)
         h = product_on_gpsimd(1, 1, gated[1, 1], up, H_LOW)
         scatter_pair(0, 0, weighted)
-        weighted = weighed_pair(0, 2, GROUP, (1, 2), LATE_HIGH)
+        weighted = weighed_pair(0, 2, FIRST_SHARE, (1, 2), LATE_HIGH)
         up = up_factor(0, 3, (7, 0))
-        quantize_h(1, GROUP, h, Y_THEN_CODES)
+        quantize_h(0, HALF, fillers[0], Y_THEN_CODES + KIB // 2, count=P)
+        quantize_h(0, HALF + P, fillers[1], count=P)
+        quantize_h(1, GROUP, h, Y_THEN_CODES - KIB // 2)
         h = product_on_gpsimd(0, 3, gated[0, 3], up, H_HIGH)
         scatter_pair(0, 2, weighted)
         gated[1, 2] = gate_factor(1, 2, (1, 2))

@@ -25,23 +25,22 @@ LIST_COLUMN = 16
 HALF = J // 2
 GROUP = 256
 LAST_FIRST = (1, 0)
-SHARE = 80
-FIRST_SHARE = 256
+SHARE = 256
 WARM_UP = 3
 
 BANK = 2048
 BLOCK = 8192
 KIB = 1024
 ROWS = [n * BLOCK for n in range(4)]
-TOKEN_WORDS = 4 * BLOCK + 2 * KIB
-H_LOW = 5 * BLOCK + KIB
-H_HIGH = 5 * BLOCK + 2 * KIB
-LATE_HIGH = 5 * BLOCK + 3 * KIB
+TOKEN_WORDS = 4 * BLOCK + 4 * KIB
+H_LOW = 5 * BLOCK + 4 * KIB
+H_HIGH = 5 * BLOCK + 5 * KIB
+LATE_HIGH = 5 * BLOCK + 6 * KIB
 UP_THEN_Y = 6 * BLOCK
 LAST_WU = 7 * BLOCK
-FIRST_WU = 9 * BLOCK
-WU_THEN_WG = 10 * BLOCK + 2 * KIB
-Y_THEN_CODES = 11 * BLOCK + 3 * KIB
+FIRST_WU = 9 * BLOCK + 2 * KIB
+WU_THEN_WG = 10 * BLOCK + 4 * KIB
+Y_THEN_CODES = 11 * BLOCK + 4 * KIB
 
 
 def tile_list_modp_gsigm_res_noneb_kernel(
@@ -138,7 +137,7 @@ def tile_list_modp_gsigm_res_noneb_kernel(
         h_w, h_s = {}, {}
 
         def codes_start(rb, first):
-            return first // HALF * HALF if rb == 0 else min(first // GROUP * GROUP, HALF)
+            return first // HALF * HALF
 
         def codes_of_h(rb, first, count):
             start = codes_start(rb, first)
@@ -242,7 +241,7 @@ def tile_list_modp_gsigm_res_noneb_kernel(
         def quantize_h(rb, first, h, offset=None, count=GROUP):
             start = codes_start(rb, first)
             if (rb, start) not in h_w:
-                width = HALF if start == HALF or rb == 0 else GROUP
+                width = HALF
                 h_w[rb, start] = sbuf(f"h_w{rb}{start}", [P, width], U32, offset)
                 h_s[rb, start] = sbuf(f"h_s{rb}{start}", [P, width], U8)
             words, scales = codes_of_h(rb, first, count)
@@ -254,29 +253,29 @@ def tile_list_modp_gsigm_res_noneb_kernel(
 
         def down(n, first, count, number):
             y = bank(f"y{n}{first}", [P, count], number)
-            width = HALF if count == HALF else P
-            for j0 in range(0, count, width):
-                for rb in LAST_FIRST:
-                    words, scales = codes_of_h(rb, first + j0, width)
-                    words = words.bitcast(FP8X4)
+            narrow = HALF if count == HALF else P
+            for rb in LAST_FIRST:
+                for j0 in range(0, count, narrow):
+                    words, scales = codes_of_h(rb, first + j0, narrow)
                     nc.tensor.matmul_mx(
-                        out=y[:, j0 : j0 + width],
+                        out=y[:, j0 : j0 + narrow],
                         lhsT=wd4_w[:].bitcast(U8)[:, rb, 2 * P * n : 2 * P * (n + 1)].bitcast(FP4X4),
                         lhsT_scale=wd4_s[:, rb, P * n : P * (n + 1)],
-                        rhs=words,
+                        rhs=words.bitcast(FP8X4),
                         rhs_scale=scales,
-                        start=(rb == LAST_FIRST[0]),
+                        start=(rb == LAST_FIRST[0] and j0 == 0),
                         stop=False,
                     )
-                    nc.tensor.matmul_mx(
-                        out=y[:, j0 : j0 + width],
-                        lhsT=wd8_w[:, rb, P * n : P * (n + 1)].bitcast(FP8X4),
-                        lhsT_scale=wd8_s[:, rb, P * n : P * (n + 1)],
-                        rhs=words,
-                        rhs_scale=scales,
-                        start=False,
-                        stop=(rb == LAST_FIRST[-1]),
-                    )
+                words, scales = codes_of_h(rb, first, count)
+                nc.tensor.matmul_mx(
+                    out=y[:],
+                    lhsT=wd8_w[:, rb, P * n : P * (n + 1)].bitcast(FP8X4),
+                    lhsT_scale=wd8_s[:, rb, P * n : P * (n + 1)],
+                    rhs=words.bitcast(FP8X4),
+                    rhs_scale=scales,
+                    start=False,
+                    stop=(rb == LAST_FIRST[-1]),
+                )
             return y
 
         def add_bias(n, first, count, banks, offset=None):
@@ -295,38 +294,29 @@ def tile_list_modp_gsigm_res_noneb_kernel(
                 rows[n][:].indirect(listed(first, count)), biased[:], weight[:, first : first + count], MULT
             )
 
-        def weighed_on_vector(g, n, number, offset=None):
-            first = g * GROUP
-            y = down(n, first, GROUP, number)
-            weighted = sbuf(f"y_weighted{g}{n}", [P, GROUP], F32, offset)
-            nc.vector.scalar_tensor_tensor(
-                weighted[:], y[:], bias[:, n : n + 1], weight[:, first : first + GROUP], ADD, MULT
-            )
-            return weighted[:]
+        def weigh_in_bank(y, n, first, out):
+            count = out.shape[-1]
+            nc.vector.scalar_tensor_tensor(out, y, bias[:, n : n + 1], weight[:, first : first + count], ADD, MULT)
 
-        def weighed_pair(g, n0, share, banks, offset):
-            first, own = g * GROUP, GROUP - share
-            weighted = sbuf(f"y_weighted{g}{n0}", [P, 2, GROUP], F32)
-            biased = sbuf(f"y_late{g}{n0}", [P, 2, share], F32, offset)
-            for i, number in enumerate(banks):
-                n = n0 + i
-                y = down(n, first, GROUP, number)
-                nc.scalar.activation(out=biased[:, i, :], in_=y[:, own:], func=ACT.Identity, bias=bias[:, n : n + 1])
-                if own:
-                    nc.vector.scalar_tensor_tensor(
-                        weighted[:, i, :own], y[:, :own], bias[:, n : n + 1], weight[:, first : first + own], ADD, MULT
-                    )
-            late = weight[:, first + own : first + GROUP].unsqueeze(1).to_broadcast([P, 2, share])
-            nc.gpsimd.tensor_tensor(weighted[:, :, own:], biased[:], late, MULT)
-            return weighted[:, 0, :], weighted[:, 1, :]
+        def weighed_by_both(n, number, offset):
+            own = HALF - SHARE
+            y = down(n, 0, HALF, number)
+            weighted = sbuf(f"y_weighted{n}", [P, HALF], F32)
+            biased = sbuf(f"y_late{n}", [P, SHARE], F32, offset)
+            nc.scalar.activation(out=biased[:], in_=y[:, own:], func=ACT.Identity, bias=bias[:, n : n + 1])
+            weigh_in_bank(y[:, :own], n, 0, weighted[:, :own])
+            nc.gpsimd.tensor_tensor(weighted[:, own:], biased[:], weight[:, own:HALF], MULT)
+            return weighted
 
-        def scatter_pair(g, n0, weighted):
-            for i in range(2):
-                nc.vector.tensor_copy(rows[n0 + i][:].indirect(listed(g * GROUP, GROUP)), weighted[i])
+        def scatter(n, first, count, weighted):
+            nc.vector.tensor_copy(rows[n][:].indirect(listed(first, count)), weighted)
 
-        def factor(name, g, stationary, func, banks, offset=None):
-            values = sbuf(name, [P, GROUP, PLACES], F32, offset)
+        def factor(name, g, stationary, func, banks, offset=None, values=None):
+            if values is None:
+                values = sbuf(name, [P, GROUP, PLACES], F32, offset)
             for j0, number in zip(range(0, GROUP, P), banks):
+                if number is None:
+                    continue
                 acc = bank(f"acc_{name}{j0}", [P, PLACES, P], number)
                 for t in reversed(range(PLACES)):
                     for a in LAST_FIRST:
@@ -344,11 +334,11 @@ def tile_list_modp_gsigm_res_noneb_kernel(
                 nc.scalar.activation(out=values[:, j0 : j0 + P, :], in_=acc[:].rearrange("p t j -> p j t"), func=func)
             return values
 
-        def gate_factor(rb, g, banks, offset=None):
+        def gate_factor(rb, g, banks, offset=None, values=None):
             def wg_columns(a, t):
                 return wg_w[rb][:, a, t, :].bitcast(FP4X4), wg_s[rb][:, a, t, :]
 
-            return factor(f"gates{rb}{g}", g, wg_columns, ACT.Sigmoid, banks, offset)
+            return factor(f"gates{rb}{g}", g, wg_columns, ACT.Sigmoid, banks, offset, values)
 
         def up_factor(rb, g, banks, offset=None):
             def wu_columns(a, t):
@@ -391,69 +381,72 @@ def tile_list_modp_gsigm_res_noneb_kernel(
         load_scales(wd_s[:, 0], wd4_scales)
         wd4_s, wd8_s = wd_s[:, 0].bitcast(U8), wd_s[:, 1].bitcast(U8)
         weight = sbuf("weight", [P, J], F32)
-        nc.sync.dma_start(out=weight[:, :GROUP], in_=wgo[:, :GROUP])
+        nc.sync.dma_start(out=weight[:, :HALF], in_=wgo[:, :HALF])
         bias = sbuf("bias", [P, N // P], F32)
         with nc.allow_non_contiguous_dma(reason="one bias value for each partition and output tile"):
             nc.sync.dma_start(out=bias[:], in_=b.rearrange("(c p) -> p c", p=P))
-        nc.sync.dma_start(out=weight[:, GROUP:], in_=wgo[:, GROUP:])
+        nc.sync.dma_start(out=weight[:, HALF:], in_=wgo[:, HALF:])
 
         on_scalar, on_vector = nc.scalar.copy, nc.vector.tensor_copy
-        round_wu(0, 0, (on_scalar, on_vector))
+        round_wu(0, 0, (on_scalar, on_scalar))
         quantize_wu(0, 0)
         round_wu(0, 1, (on_vector, on_vector))
         gates(0, 0, HALF, (1, 2, 3, 4), FIRST_WU - 6 * KIB)
         gates(0, HALF, GROUP, (5, 6), FIRST_WU + 2 * KIB)
-        gated = {(0, 3): gate_factor(0, 3, (7, 0), FIRST_WU + 6 * KIB)}
+        gated = gate_factor(0, 3, (7, None), FIRST_WU + 6 * KIB)
         quantize_wu(0, 1, pieces=2)
         order_wg_words(1, WU_THEN_WG)
         zeroed_rows(2)
         round_wu(1, 0, (on_scalar, on_scalar))
-        h = hidden(0, 0, (1, 2, 3, 4), first_places=range(PLACES))
+        h = hidden(0, 0, (0, 1, 2, 3), first_places=range(PLACES))
         last = [round_last(0, (on_vector, on_scalar))]
         quantize_h(0, 0, h, count=HALF)
         quantize_wu(1, 0)
-        last.append(round_last(1, (on_vector, on_scalar), 4 * BLOCK - KIB))
+        last.append(round_last(1, (on_vector, on_scalar), 4 * BLOCK))
         wu_w[1, 1], wu_s[1, 1] = sbuf("wu_w11", [P, PASS], U32), sbuf("wu_s11", [P, PASS], U8)
         for half in range(2):
             quantize_last(half, last[half])
+        gates(1, 0, GROUP, (4, 5), LAST_WU)
+        gates(1, GROUP, GROUP, (6, 7), LAST_WU + 4 * KIB)
+        h = hidden(1, 0, (2, 3), None, first_places=range(PLACES))
+        filler = hidden(0, HALF, (0, 1), 4 * BLOCK)
+        quantize_h(1, 0, h)
+        h = hidden(1, GROUP, (4, 5), ROWS[3])
+        quantize_h(0, HALF, filler)
+        quantize_h(1, GROUP, h)
         zeroed_rows(3)
-        gates(1, 0, GROUP, (5, 6), LAST_WU)
-        gated[1, 1] = gate_factor(1, 1, (7, 0), LAST_WU + 4 * KIB)
-        h = [hidden(1, 0, (3,), None, first_places=range(PLACES)), hidden(1, P, (4,), H_LOW - KIB // 2)]
-        quantize_h(1, 0, h[0], count=P)
-        quantize_h(1, P, h[1], count=P)
-        fillers = [hidden(0, HALF, (1,), 4 * BLOCK), hidden(0, HALF + P, (2,), H_LOW - KIB - KIB // 4)]
 
-        up = up_factor(1, 1, (5, 6))
-        weighted = weighed_on_vector(0, 0, 7, Y_THEN_CODES), weighed_on_vector(0, 1, 0)
-        h = product_on_gpsimd(1, 1, gated[1, 1], up, H_LOW)
-        scatter_pair(0, 0, weighted)
-        weighted = weighed_pair(0, 2, FIRST_SHARE, (1, 2), LATE_HIGH)
-        up = up_factor(0, 3, (7, 0))
-        quantize_h(0, HALF, fillers[0], Y_THEN_CODES + KIB // 2, count=P)
-        quantize_h(0, HALF + P, fillers[1], count=P)
-        quantize_h(1, GROUP, h, Y_THEN_CODES - KIB // 2)
-        h = product_on_gpsimd(0, 3, gated[0, 3], up, H_HIGH)
-        scatter_pair(0, 2, weighted)
-        gated[1, 2] = gate_factor(1, 2, (1, 2))
-        weighted = weighed_pair(1, 0, SHARE, (5, 6), H_HIGH - 2 * SHARE * 4)
-        up = up_factor(1, 2, (7, 0))
+        gate_factor(0, 3, (None, 3), values=gated)
+        down_and_scatter(0, 0, GROUP, (6, 7))
+        down_and_scatter(1, 0, GROUP, (2,))
+        weighted = [sbuf(f"y_weighted{n}", [P, GROUP], F32) for n in range(2)]
+        for n, number in enumerate((3, 0)):
+            weigh_in_bank(down(n, GROUP, GROUP, number)[:], n, GROUP, weighted[n][:])
+        up = up_factor(0, 3, (6, 7))
+        h = product_on_gpsimd(0, 3, gated, up, H_LOW)
+        for n in range(2):
+            scatter(n, GROUP, GROUP, weighted[n][:])
+        gated = gate_factor(1, 2, (2, 6))
+        weighted = weighed_by_both(2, 1, LATE_HIGH)
+        up = up_factor(1, 2, (7, 2))
         quantize_h(0, 3 * GROUP, h)
-        h = product_on_gpsimd(1, 2, gated[1, 2], up, H_LOW)
-        scatter_pair(1, 0, weighted)
-        gated[1, 3] = gate_factor(1, 3, (1, 2))
-        weighted = weighed_pair(1, 2, SHARE, (3, 4), LATE_HIGH)
-        up = up_factor(1, 3, (7, 0), UP_THEN_Y)
+
+        h = product_on_gpsimd(1, 2, gated, up, H_HIGH)
+        scatter(2, 0, HALF, weighted[:])
+        gated = gate_factor(1, 3, (6, 7))
+        weighted = weighed_by_both(3, 3, H_HIGH - SHARE * 4)
+        up = up_factor(1, 3, (2, 6), UP_THEN_Y)
         quantize_h(1, 2 * GROUP, h)
-        h = product_on_gpsimd(1, 3, gated[1, 3], up, H_HIGH)
-        scatter_pair(1, 2, weighted)
+
+        h = product_on_gpsimd(1, 3, gated, up, H_LOW)
+        scatter(3, 0, HALF, weighted[:])
         quantize_h(1, 3 * GROUP, h)
 
-        down_and_scatter(1, HALF, GROUP, (5,), UP_THEN_Y)
-        down_and_scatter(0, HALF, GROUP, (6,), UP_THEN_Y + KIB)
-        for n, number in ((1, 1), (0, 2)):
+        down_and_scatter(1, HALF, GROUP, (7,), UP_THEN_Y)
+        down_and_scatter(0, HALF, GROUP, (2,), UP_THEN_Y + KIB)
+        for n, number in ((1, 4), (0, 5)):
             down_and_scatter(n, HALF + GROUP, GROUP, (number,))
             store(n)
-        for n, number in ((2, 7), (3, 0)):
+        for n, number in ((2, 0), (3, 1)):
             down_and_scatter(n, HALF, HALF, (number,))
             store(n)

@@ -26,7 +26,7 @@ HALF = J // 2
 GROUP = 256
 LAST_FIRST = (1, 0)
 SHARE = 256
-WARM_UP = 3
+FIRST_SHARE = 256
 
 BANK = 2048
 BLOCK = 8192
@@ -91,8 +91,10 @@ def tile_list_modp_gsigm_res_noneb_kernel(
             columns = wg_raw[rb][:].bitcast(U16).rearrange("p a (m t) -> p a t m", t=PLACES)
             nc.vector.tensor_copy(out=wg_w[rb][:].bitcast(U16), in_=columns)
 
-        wg_s_raw = sbuf("wg_s_raw", [P, 2, R // 4], I32)
-        nc.vector.memset(wg_s_raw[:], 0)
+        wg_s = sbuf("wg_s", [P, 2, 2, PLACES, P], U8)
+        nc.vector.memset(wg_s[:].rearrange("p r a t m -> p (r a t m)").bitcast(I32), 0)
+        wg_s_rows = sbuf("wg_s_rows", [P, PASS // 4], I32, ROWS[0])
+        nc.vector.memset(wg_s_rows[2 * QUADRANT :], 0)
         tab_s = sbuf("tab_s", [P, T // 4], I32)
         nc.vector.memset(tab_s[QUADRANT : 2 * QUADRANT], 0)
         nc.vector.memset(tab_s[2 * QUADRANT :], 0)
@@ -101,26 +103,31 @@ def tile_list_modp_gsigm_res_noneb_kernel(
         wd_s = sbuf("wd_s", [P, 2, 2, N // 4], I32)
         nc.vector.memset(wd_s[:], 0)
         rows = {}
-        warm = sbuf("warm", [P, 2], F32, ROWS[0])
+        warm = sbuf("warm", [P, 2], F32)
         nc.gpsimd.memset(warm[:, 0:1], 0.0)
         nc.scalar.activation(out=warm[:, 1:2], in_=warm[:, 0:1], func=ACT.Sigmoid)
 
         offsets = keep.tile([P, J // LIST_COLUMN], U16, name="offsets")
         nc.sync.dma_start(offsets[:], offs)
+        for a in range(2):
+            nc.sync.dma_start(
+                out=wg_s_rows[a : 2 * QUADRANT : 2, :],
+                in_=wg_scales[a].rearrange("b (r x) -> (b r) x", r=2).bitcast(I32),
+            )
         nc.sync.dma_start(out=tab_s[0:QUADRANT, :], in_=tab_scales.rearrange("a b x -> b a x").bitcast(I32))
-        load_scales(wg_s_raw, wg_scales)
-        wg_raw = [load_wg(0, ROWS[1])]
+        wg_raw = [load_wg(0)]
         tab_w = sbuf("tab_w", [P, T], I32)
         nc.sync.dma_start(out=tab_w[:], in_=tab_words[0].rearrange("p t x -> p (t x)").bitcast(I32))
-        wu_raw = {(0, 0): load_wu(0, 0, FIRST_WU)}
-        wg_s = {}
-
-        def order_wg_scales(rb, offset=None):
-            wg_s[rb] = sbuf(f"wg_s{rb}", [P, 2, PLACES, P], U8, offset)
-            columns = wg_s_raw[:].bitcast(U8)[:, :, PASS * rb : PASS * (rb + 1)]
-            nc.vector.tensor_copy(out=wg_s[rb][:], in_=columns.rearrange("p a (m t) -> p a t m", t=PLACES))
-
+        wg_s_ordered = sbuf("wg_s_ordered", [P, PLACES, P], U8)
+        by_place = wg_s_rows[:].bitcast(U8).rearrange("p (m t) -> p t m", t=PLACES)
+        nc.vector.tensor_copy(out=wg_s_ordered[:], in_=by_place)
+        for q in range(P // QUADRANT):
+            nc.sync.dma_start(
+                out=wg_s[QUADRANT * q : QUADRANT * q + 4].rearrange("p r a t m -> p (r a t m)").bitcast(I32),
+                in_=wg_s_ordered[16 * q : 16 * q + 16].rearrange("p t m -> p (t m)").bitcast(I32),
+            )
         zeroed_rows(0)
+        wu_raw = {(0, 0): load_wu(0, 0, FIRST_WU)}
         tok_s_rows = sbuf("tok_s_rows", [P, J], U8)
         nc.vector.tensor_copy(tok_s_rows[:], tab_s[:].bitcast(U8).indirect(offsets[:]))
         for q in range(P // QUADRANT):
@@ -129,7 +136,7 @@ def tile_list_modp_gsigm_res_noneb_kernel(
                 in_=tok_s_rows[8 * q : 8 * q + 8, :].bitcast(I32),
             )
         wu_raw[0, 1] = load_wu(0, 1, WU_THEN_WG)
-        wg_raw.append(load_wg(1, ROWS[2]))
+        wg_raw.append(load_wg(1, ROWS[1]))
         wu_raw[1, 0] = load_wu(1, 0)
         last_raw = [load_wu(1, 1, LAST_WU + half * BLOCK // 2, half * PASS // 2, PASS // 2) for half in range(2)]
 
@@ -144,7 +151,7 @@ def tile_list_modp_gsigm_res_noneb_kernel(
             return h_w[rb, start][:, first - start : first - start + count], h_s[rb, start][:, first - start : first - start + count]
 
         def gather_words(half):
-            both = sbuf(f"tok_both{half}", [P, HALF], U32, TOKEN_WORDS + 2 * KIB * half)
+            both = sbuf(f"tok_both{half}", [P, HALF], U32, TOKEN_WORDS)
             nc.vector.tensor_copy(both[:], tab_w[:].bitcast(U32).indirect(listed(half * HALF, HALF)))
             return both
 
@@ -205,7 +212,7 @@ def tile_list_modp_gsigm_res_noneb_kernel(
                         nc.tensor.matmul_mx(
                             out=ga[:, t - t0, :],
                             lhsT=wg_w[rb][:, a, t, :].bitcast(FP4X4),
-                            lhsT_scale=wg_s[rb][:, a, t, :],
+                            lhsT_scale=wg_s[:, rb, a, t, :],
                             rhs=words,
                             rhs_scale=scales,
                             start=(a == LAST_FIRST[0]),
@@ -298,11 +305,11 @@ def tile_list_modp_gsigm_res_noneb_kernel(
             count = out.shape[-1]
             nc.vector.scalar_tensor_tensor(out, y, bias[:, n : n + 1], weight[:, first : first + count], ADD, MULT)
 
-        def weighed_by_both(n, number, offset):
-            own = HALF - SHARE
+        def weighed_by_both(n, number, offset, share):
+            own = HALF - share
             y = down(n, 0, HALF, number)
             weighted = sbuf(f"y_weighted{n}", [P, HALF], F32)
-            biased = sbuf(f"y_late{n}", [P, SHARE], F32, offset)
+            biased = sbuf(f"y_late{n}", [P, share], F32, offset)
             nc.scalar.activation(out=biased[:], in_=y[:, own:], func=ACT.Identity, bias=bias[:, n : n + 1])
             weigh_in_bank(y[:, :own], n, 0, weighted[:, :own])
             nc.gpsimd.tensor_tensor(weighted[:, own:], biased[:], weight[:, own:HALF], MULT)
@@ -336,7 +343,7 @@ def tile_list_modp_gsigm_res_noneb_kernel(
 
         def gate_factor(rb, g, banks, offset=None, values=None):
             def wg_columns(a, t):
-                return wg_w[rb][:, a, t, :].bitcast(FP4X4), wg_s[rb][:, a, t, :]
+                return wg_w[rb][:, a, t, :].bitcast(FP4X4), wg_s[:, rb, a, t, :]
 
             return factor(f"gates{rb}{g}", g, wg_columns, ACT.Sigmoid, banks, offset, values)
 
@@ -355,24 +362,20 @@ def tile_list_modp_gsigm_res_noneb_kernel(
         def store(n):
             nc.sync.dma_start(out=out[P * n : P * (n + 1), :], in_=rows[n][:])
 
-        order_wg_scales(0)
         order_wg_words(0)
-        zeroed_rows(1)
-        both = [gather_words(half) for half in range(2)]
         idle = bank("idle", [P, HALF], 0)
-        for t in range(WARM_UP):
+        for t in range(PLACES):
             nc.tensor.matmul_mx(
                 out=idle[:],
                 lhsT=wg_w[0][:, 0, t, :].bitcast(FP4X4),
-                lhsT_scale=wg_s[0][:, 0, t, :],
-                rhs=both[0][:, : HALF // 2].bitcast(U8).bitcast(FP4X4),
-                rhs_scale=wg_s[0][:, 0].rearrange("p t m -> p (t m)"),
+                lhsT_scale=wg_s[:, 0, 0, t, :],
+                rhs=wg_w[0][:, 0].rearrange("p t x -> p (t x)").bitcast(FP4X4),
+                rhs_scale=wg_s[:, 0, 0].rearrange("p t m -> p (t m)"),
                 start=True,
                 stop=True,
             )
         for half in range(2):
-            part_words(half, both[half])
-        order_wg_scales(1, TOKEN_WORDS)
+            part_words(half, gather_words(half))
         wd8_w = sbuf("wd8_w", [P, 2, N], I32)
         nc.sync.dma_start(out=wd8_w[:], in_=wd8_words.rearrange("a p n x -> p a (n x)").bitcast(I32))
         load_scales(wd_s[:, 1], wd8_scales)
@@ -396,22 +399,23 @@ def tile_list_modp_gsigm_res_noneb_kernel(
         gated = gate_factor(0, 3, (7, None), FIRST_WU + 6 * KIB)
         quantize_wu(0, 1, pieces=2)
         order_wg_words(1, WU_THEN_WG)
-        zeroed_rows(2)
+        zeroed_rows(1)
         round_wu(1, 0, (on_scalar, on_scalar))
         h = hidden(0, 0, (0, 1, 2, 3), first_places=range(PLACES))
         last = [round_last(0, (on_vector, on_scalar))]
         quantize_h(0, 0, h, count=HALF)
         quantize_wu(1, 0)
-        last.append(round_last(1, (on_vector, on_scalar), 4 * BLOCK))
+        last.append(round_last(1, (on_vector, on_scalar), ROWS[3] - KIB))
         wu_w[1, 1], wu_s[1, 1] = sbuf("wu_w11", [P, PASS], U32), sbuf("wu_s11", [P, PASS], U8)
         for half in range(2):
             quantize_last(half, last[half])
+        zeroed_rows(2)
         gates(1, 0, GROUP, (4, 5), LAST_WU)
         gates(1, GROUP, GROUP, (6, 7), LAST_WU + 4 * KIB)
         h = hidden(1, 0, (2, 3), None, first_places=range(PLACES))
-        filler = hidden(0, HALF, (0, 1), 4 * BLOCK)
+        filler = hidden(0, HALF, (0, 1), ROWS[3])
         quantize_h(1, 0, h)
-        h = hidden(1, GROUP, (4, 5), ROWS[3])
+        h = hidden(1, GROUP, (4, 5), ROWS[3] + 2 * KIB)
         quantize_h(0, HALF, filler)
         quantize_h(1, GROUP, h)
         zeroed_rows(3)
@@ -427,14 +431,14 @@ def tile_list_modp_gsigm_res_noneb_kernel(
         for n in range(2):
             scatter(n, GROUP, GROUP, weighted[n][:])
         gated = gate_factor(1, 2, (2, 6))
-        weighted = weighed_by_both(2, 1, LATE_HIGH)
+        weighted = weighed_by_both(2, 1, LATE_HIGH, FIRST_SHARE)
         up = up_factor(1, 2, (7, 2))
         quantize_h(0, 3 * GROUP, h)
 
         h = product_on_gpsimd(1, 2, gated, up, H_HIGH)
         scatter(2, 0, HALF, weighted[:])
         gated = gate_factor(1, 3, (6, 7))
-        weighted = weighed_by_both(3, 3, H_HIGH - SHARE * 4)
+        weighted = weighed_by_both(3, 3, H_HIGH - SHARE * 4, SHARE)
         up = up_factor(1, 3, (2, 6), UP_THEN_Y)
         quantize_h(1, 2 * GROUP, h)
 

@@ -24,23 +24,18 @@ QUADRANT = 32
 LIST_COLUMN = 16
 HALF = J // 2
 GROUP = 256
-LAST_FIRST = (1, 0)
-SHARE = 256
-FIRST_SHARE = 256
-
 BANK = 2048
-BLOCK = 8192
 KIB = 1024
+BLOCK = 8 * KIB
+TABLE_ROWS = 96
+
 ROWS = [n * BLOCK for n in range(4)]
-TOKEN_WORDS = 4 * BLOCK + 4 * KIB
-H_LOW = 5 * BLOCK + 4 * KIB
-H_HIGH = 5 * BLOCK + 5 * KIB
-LATE_HIGH = 5 * BLOCK + 6 * KIB
-UP_THEN_Y = 6 * BLOCK
-LAST_WU = 7 * BLOCK
-FIRST_WU = 9 * BLOCK + 2 * KIB
-WU_THEN_WG = 10 * BLOCK + 4 * KIB
-Y_THEN_CODES = 11 * BLOCK + 4 * KIB
+LATE_H = 4 * BLOCK
+LATE_GATE = LATE_H + 4 * KIB
+LATE_UP = LATE_GATE + 4 * KIB
+RAW_11 = 48 * KIB
+WG_SCALES = 56 * KIB
+EARLY_H = 58 * KIB
 
 
 def tile_list_modp_gsigm_res_noneb_kernel(
@@ -57,101 +52,97 @@ def tile_list_modp_gsigm_res_noneb_kernel(
                 return keep.tile(shape, dtype, name=name, align_bytes=64)
             return shared.tile(shape, dtype, name=name, align_bytes=64, offset=offset)
 
-        def listed(first, count):
-            return offsets[:, first // LIST_COLUMN : (first + count) // LIST_COLUMN]
-
         def bank(name, shape, number):
             return psum.tile(shape, F32, name=name, offset=number * BANK)
 
+        def listed(first, count):
+            return offsets[:, first // LIST_COLUMN : (first + count) // LIST_COLUMN]
+
         def load_scales(tile, src):
             for r in range(4):
-                nc.sync.dma_start(
-                    out=tile[r:P:QUADRANT],
-                    in_=src[:, r:16:4, :].rearrange("a q x -> q a x").bitcast(I32),
-                )
+                nc.sync.dma_start(out=tile[r:P:QUADRANT], in_=src[:, r:16:4, :].rearrange("a q x -> q a x").bitcast(I32))
 
         def zeroed_rows(n):
             rows[n] = sbuf(f"rows{n}", [P, T], F32, ROWS[n])
             nc.gpsimd.memset(rows[n][:].bitcast(I32), 0)
 
-        def load_wg(rb, offset=None):
-            raw = sbuf(f"wg_raw{rb}", [P, 2, PASS // 2], I32, offset)
+        def load_wg(rb):
+            raw = sbuf(f"wg_raw{rb}", [P, 2, PASS // 2], I32)
             columns = wg_words[:, :, 2 * PASS * rb : 2 * PASS * (rb + 1)]
             nc.sync.dma_start(out=raw[:], in_=columns.rearrange("a p x -> p a x").bitcast(I32))
             return raw
 
-        def load_wu(rb, a, offset=None, c0=0, width=PASS):
-            raw = sbuf(f"wu_raw{rb}{a}{c0}", [P, PLACES, width], F32, offset)
-            block = wu[PASS * a : PASS * (a + 1), PASS * rb + c0 : PASS * rb + c0 + width]
+        def load_wu(rb, a, offset=None):
+            raw = sbuf(f"wu_raw{rb}{a}", [P, PLACES, PASS], F32, offset)
+            block = wu[PASS * a : PASS * (a + 1), PASS * rb : PASS * (rb + 1)]
             nc.sync.dma_start(out=raw[:], in_=block.rearrange("(p i) c -> p i c", i=PLACES))
             return raw
 
-        def order_wg_words(rb, offset=None):
-            wg_w[rb] = sbuf(f"wg_w{rb}", [P, 2, PLACES, 2 * P], U8, offset)
-            columns = wg_raw[rb][:].bitcast(U16).rearrange("p a (m t) -> p a t m", t=PLACES)
-            nc.vector.tensor_copy(out=wg_w[rb][:].bitcast(U16), in_=columns)
-
-        wg_s = sbuf("wg_s", [P, 2, 2, PLACES, P], U8)
-        nc.vector.memset(wg_s[:].rearrange("p r a t m -> p (r a t m)").bitcast(I32), 0)
-        wg_s_rows = sbuf("wg_s_rows", [P, PASS // 4], I32, ROWS[0])
-        nc.vector.memset(wg_s_rows[2 * QUADRANT :], 0)
-        tab_s = sbuf("tab_s", [P, T // 4], I32)
-        nc.vector.memset(tab_s[QUADRANT : 2 * QUADRANT], 0)
-        nc.vector.memset(tab_s[2 * QUADRANT :], 0)
-        tok_s = sbuf("tok_s", [P, 2, J], U8)
-        nc.vector.memset(tok_s[:].bitcast(I32), 0)
-        wd_s = sbuf("wd_s", [P, 2, 2, N // 4], I32)
-        nc.vector.memset(wd_s[:], 0)
         rows = {}
         warm = sbuf("warm", [P, 2], F32)
-        nc.gpsimd.memset(warm[:, 0:1], 0.0)
+        nc.vector.memset(warm[:, 0:1], 0.0)
         nc.scalar.activation(out=warm[:, 1:2], in_=warm[:, 0:1], func=ACT.Sigmoid)
+        tab_s = sbuf("tab_s", [P, T // 4], I32)
+        nc.vector.memset(tab_s[:TABLE_ROWS], 0)
+        wg_s_raw = sbuf("wg_s_raw", [P, 2, R // 4], I32, WG_SCALES)
+        nc.gpsimd.memset(wg_s_raw[:], 0)
+        tok_s = sbuf("tok_s", [P, 2, J], U8)
+        nc.gpsimd.memset(tok_s[:].bitcast(I32), 0)
+        wd_s = sbuf("wd_s", [P, 2, 2, N // 4], I32)
+        nc.gpsimd.memset(wd_s[:], 0)
+        zeroed_rows(0)
 
         offsets = keep.tile([P, J // LIST_COLUMN], U16, name="offsets")
         nc.sync.dma_start(offsets[:], offs)
-        for a in range(2):
+        for r in range(4):
             nc.sync.dma_start(
-                out=wg_s_rows[a : 2 * QUADRANT : 2, :],
-                in_=wg_scales[a].rearrange("b (r x) -> (b r) x", r=2).bitcast(I32),
+                out=tab_s[TABLE_ROWS + r : P : 4, :],
+                in_=tab_scales[:, r:16:4, :].rearrange("a q x -> q a x").bitcast(I32),
             )
-        nc.sync.dma_start(out=tab_s[0:QUADRANT, :], in_=tab_scales.rearrange("a b x -> b a x").bitcast(I32))
-        wg_raw = [load_wg(0)]
         tab_w = sbuf("tab_w", [P, T], I32)
         nc.sync.dma_start(out=tab_w[:], in_=tab_words[0].rearrange("p t x -> p (t x)").bitcast(I32))
-        wg_s_ordered = sbuf("wg_s_ordered", [P, PLACES, P], U8)
-        by_place = wg_s_rows[:].bitcast(U8).rearrange("p (m t) -> p t m", t=PLACES)
-        nc.vector.tensor_copy(out=wg_s_ordered[:], in_=by_place)
-        for q in range(P // QUADRANT):
-            nc.sync.dma_start(
-                out=wg_s[QUADRANT * q : QUADRANT * q + 4].rearrange("p r a t m -> p (r a t m)").bitcast(I32),
-                in_=wg_s_ordered[16 * q : 16 * q + 16].rearrange("p t m -> p (t m)").bitcast(I32),
-            )
-        zeroed_rows(0)
-        wu_raw = {(0, 0): load_wu(0, 0, FIRST_WU)}
+        wg_raw = [load_wg(0)]
+        load_scales(wg_s_raw, wg_scales)
+        wu_raw = {(0, 0): load_wu(0, 0)}
         tok_s_rows = sbuf("tok_s_rows", [P, J], U8)
         nc.vector.tensor_copy(tok_s_rows[:], tab_s[:].bitcast(U8).indirect(offsets[:]))
-        for q in range(P // QUADRANT):
+        for r in range(4):
             nc.sync.dma_start(
-                out=tok_s[QUADRANT * q : QUADRANT * q + 4].bitcast(I32),
-                in_=tok_s_rows[8 * q : 8 * q + 8, :].bitcast(I32),
+                out=tok_s[r:P:QUADRANT].bitcast(I32),
+                in_=tok_s_rows[TABLE_ROWS + r : P : 4, :].bitcast(I32),
             )
-        wu_raw[0, 1] = load_wu(0, 1, WU_THEN_WG)
-        wg_raw.append(load_wg(1, ROWS[1]))
+        wu_raw[0, 1] = load_wu(0, 1)
+        wg_raw.append(load_wg(1))
         wu_raw[1, 0] = load_wu(1, 0)
-        last_raw = [load_wu(1, 1, LAST_WU + half * BLOCK // 2, half * PASS // 2, PASS // 2) for half in range(2)]
+        wu_raw[1, 1] = load_wu(1, 1, RAW_11)
+        wd8_w = sbuf("wd8_w", [P, 2, N], I32)
+        nc.sync.dma_start(out=wd8_w[:], in_=wd8_words.rearrange("a p n x -> p a (n x)").bitcast(I32))
+        load_scales(wd_s[:, 1], wd8_scales)
+        wd4_w = sbuf("wd4_w", [P, 2, N // 2], I32)
+        nc.sync.dma_start(out=wd4_w[:], in_=wd4_words.rearrange("a p x -> p a x").bitcast(I32))
+        load_scales(wd_s[:, 0], wd4_scales)
+        wd4_s, wd8_s = wd_s[:, 0].bitcast(U8), wd_s[:, 1].bitcast(U8)
+        bias = sbuf("bias", [P, N // P], F32)
+        with nc.allow_non_contiguous_dma(reason="one bias value for each partition and output tile"):
+            nc.sync.dma_start(out=bias[:], in_=b.rearrange("(c p) -> p c", p=P))
+        weight = sbuf("weight", [P, J], F32)
+        nc.sync.dma_start(out=weight[:, :HALF], in_=wgo[:, :HALF])
+        nc.sync.dma_start(out=weight[:, HALF:], in_=wgo[:, HALF:])
 
-        tok_w, wg_w, rounded, wu_w, wu_s, gate = {}, {}, {}, {}, {}, {}
-        h_w, h_s = {}, {}
+        tok_w, wg_w, wg_s, rounded, wu_w, wu_s, gate, codes = {}, {}, {}, {}, {}, {}, {}, {}
 
-        def codes_start(rb, first):
-            return first // HALF * HALF
+        def order_wg_words(rb):
+            wg_w[rb] = sbuf(f"wg_w{rb}", [P, 2, PLACES, 2 * P], U8)
+            columns = wg_raw[rb][:].bitcast(U16).rearrange("p a (m t) -> p a t m", t=PLACES)
+            nc.scalar.copy(out=wg_w[rb][:].bitcast(U16), in_=columns)
 
-        def codes_of_h(rb, first, count):
-            start = codes_start(rb, first)
-            return h_w[rb, start][:, first - start : first - start + count], h_s[rb, start][:, first - start : first - start + count]
+        def order_wg_scales(rb):
+            wg_s[rb] = sbuf(f"wg_s{rb}", [P, 2, PLACES, P], U8)
+            columns = wg_s_raw[:].bitcast(U8)[:, :, PASS * rb : PASS * (rb + 1)]
+            nc.vector.tensor_copy(out=wg_s[rb][:], in_=columns.rearrange("p a (m t) -> p a t m", t=PLACES))
 
-        def gather_words(half):
-            both = sbuf(f"tok_both{half}", [P, HALF], U32, TOKEN_WORDS)
+        def gather_words(half, offset=None):
+            both = sbuf(f"tok_both{half}", [P, HALF], U32, offset)
             nc.vector.tensor_copy(both[:], tab_w[:].bitcast(U32).indirect(listed(half * HALF, HALF)))
             return both
 
@@ -164,40 +155,31 @@ def tile_list_modp_gsigm_res_noneb_kernel(
             half, j0 = divmod(first, HALF)
             return tok_w[half][:, a, 2 * j0 : 2 * (j0 + count)].bitcast(FP4X4), tok_s[:, a, first : first + count]
 
-        def round_wu(rb, a, copies, offset=None):
-            rounded[rb, a] = sbuf(f"wu_rounded{rb}{a}", [P, PLACES, P, PLACES], BF16, offset)
+        def round_wu(rb, a, t0, copy, offset=None):
+            rounded[rb, a, t0] = sbuf(f"wu_rounded{rb}{a}{t0}", [P, 2, P, PLACES], BF16, offset)
             source = wu_raw[rb, a][:].rearrange("p i (m t) -> p m i t", t=PLACES)
-            for t0, copy in zip((0, 2), copies):
-                target = rounded[rb, a][:, t0 : t0 + 2].rearrange("p t m i -> p m i t")
-                copy(out=target, in_=source[:, :, :, t0 : t0 + 2])
+            copy(out=rounded[rb, a, t0][:].rearrange("p t m i -> p m i t"), in_=source[:, :, :, t0 : t0 + 2])
 
-        def round_last(half, copies, offset=None):
-            last = sbuf(f"last_rounded{half}", [P, PLACES, P // 2, PLACES], BF16, offset)
-            source = last_raw[half][:].rearrange("p i (m t) -> p m i t", t=PLACES)
-            for t0, copy in zip((0, 2), copies):
-                copy(out=last[:, t0 : t0 + 2].rearrange("p t m i -> p m i t"), in_=source[:, :, :, t0 : t0 + 2])
-            return last
+        def quantize_wu(rb, a, t0):
+            wu_w[rb, a, t0] = sbuf(f"wu_w{rb}{a}{t0}", [P, 2 * P], U32)
+            wu_s[rb, a, t0] = sbuf(f"wu_s{rb}{a}{t0}", [P, 2 * P], U8)
+            nc.vector.quantize_mx(
+                out=wu_w[rb, a, t0][:].bitcast(FP8X4),
+                scales=wu_s[rb, a, t0][:],
+                in_=rounded[rb, a, t0][:].rearrange("p t m i -> p (t m i)"),
+            )
 
-        def quantize_last(half, last):
-            for t in range(PLACES):
-                columns = slice(P * t + half * P // 2, P * t + (half + 1) * P // 2)
-                nc.vector.quantize_mx(
-                    out=wu_w[1, 1][:, columns].bitcast(FP8X4),
-                    scales=wu_s[1, 1][:, columns],
-                    in_=last[:, t].rearrange("p m i -> p (m i)"),
-                )
+        def wg_columns(rb, a, t):
+            return wg_w[rb][:, a, t, :].bitcast(FP4X4), wg_s[rb][:, a, t, :]
 
-        def quantize_wu(rb, a, pieces=1):
-            wu_w[rb, a] = sbuf(f"wu_w{rb}{a}", [P, PASS], U32)
-            wu_s[rb, a] = sbuf(f"wu_s{rb}{a}", [P, PASS], U8)
-            values = rounded[rb, a][:].rearrange("p t m i -> p (t m i)")
-            width = PASS // pieces
-            for c0 in range(0, PASS, width):
-                nc.vector.quantize_mx(
-                    out=wu_w[rb, a][:, c0 : c0 + width].bitcast(FP8X4),
-                    scales=wu_s[rb, a][:, c0 : c0 + width],
-                    in_=values[:, PLACES * c0 : PLACES * (c0 + width)],
-                )
+        def wu_columns(rb, a, t):
+            key, columns = (rb, a, t - t % 2), slice(P * (t % 2), P * (t % 2 + 1))
+            return wu_w[key][:, columns].bitcast(FP8X4), wu_s[key][:, columns]
+
+        def multiply(acc, stationary, moving, start, stop):
+            nc.tensor.matmul_mx(
+                out=acc, lhsT=stationary[0], lhsT_scale=stationary[1], rhs=moving[0], rhs_scale=moving[1], start=start, stop=stop
+            )
 
         def gates(rb, first, count, banks, offset=None):
             places = HALF // count
@@ -207,250 +189,176 @@ def tile_list_modp_gsigm_res_noneb_kernel(
             for t0, number in zip(range(0, PLACES, places), banks):
                 ga = bank(f"ga{rb}{first}{t0}", [P, places, count], number)
                 for t in range(t0, t0 + places):
-                    for a in LAST_FIRST:
-                        words, scales = token_operand(a, first, count)
-                        nc.tensor.matmul_mx(
-                            out=ga[:, t - t0, :],
-                            lhsT=wg_w[rb][:, a, t, :].bitcast(FP4X4),
-                            lhsT_scale=wg_s[:, rb, a, t, :],
-                            rhs=words,
-                            rhs_scale=scales,
-                            start=(a == LAST_FIRST[0]),
-                            stop=(a == LAST_FIRST[-1]),
-                        )
+                    for a in range(2):
+                        multiply(ga[:, t - t0, :], wg_columns(rb, a, t), token_operand(a, first, count), a == 0, a == 1)
                 nc.scalar.activation(out=tile[:, t0 : t0 + places, :], in_=ga[:], func=ACT.Sigmoid)
 
-        def hidden(rb, first, banks, offset=None, first_places=(3, 2, 1, 0)):
-            count = P * len(banks)
-            h = sbuf(f"h{rb}{first}", [P, count, PLACES], BF16, offset)
-            for j0, number in zip(range(0, count, P), banks):
-                ub = bank(f"ub{rb}{first}{j0}", [P, PLACES, P], number)
-                for t in first_places if j0 == 0 else (3, 2, 1, 0):
-                    for a in LAST_FIRST:
-                        words, scales = token_operand(a, first + j0, P)
-                        nc.tensor.matmul_mx(
-                            out=ub[:, t, :],
-                            lhsT=wu_w[rb, a][:, P * t : P * (t + 1)].bitcast(FP8X4),
-                            lhsT_scale=wu_s[rb, a][:, P * t : P * (t + 1)],
-                            rhs=words,
-                            rhs_scale=scales,
-                            start=(a == LAST_FIRST[0]),
-                            stop=(a == LAST_FIRST[-1]),
-                        )
-                nc.vector.tensor_tensor(
-                    h[:, j0 : j0 + P, :].rearrange("p (c e) t -> p c t e", e=2),
-                    ub[:].rearrange("p t (c e) -> p c t e", e=2),
-                    gate[rb, first + j0].rearrange("p t (c e) -> p c t e", e=2),
-                    MULT,
-                )
-            return h
+        def four_places(name, columns, rb, firsts, banks, places=(0, 1, 2, 3)):
+            accs = [bank(f"{name}{rb}{first}", [P, PLACES, P], number) for first, number in zip(firsts, banks)]
+            for a in range(2):
+                for acc, first in zip(accs, firsts):
+                    for t in places:
+                        start, stop = (a, t) == (0, places[0]), (a, t) == (1, places[-1])
+                        multiply(acc[:, t, :], columns(rb, a, t), token_operand(a, first, P), start, stop)
+            return accs
 
-        def quantize_h(rb, first, h, offset=None, count=GROUP):
-            start = codes_start(rb, first)
-            if (rb, start) not in h_w:
-                width = HALF
-                h_w[rb, start] = sbuf(f"h_w{rb}{start}", [P, width], U32, offset)
-                h_s[rb, start] = sbuf(f"h_s{rb}{start}", [P, width], U8)
-            words, scales = codes_of_h(rb, first, count)
-            nc.vector.quantize_mx(
-                out=words.bitcast(FP8X4),
-                scales=scales,
-                in_=h[:].rearrange("p j t -> p (j t)"),
+        def product(rb, first, ub, h):
+            nc.vector.tensor_tensor(
+                h.rearrange("p (c e) t -> p c t e", e=2),
+                ub[:].rearrange("p t (c e) -> p c t e", e=2),
+                gate[rb, first].rearrange("p t (c e) -> p c t e", e=2),
+                MULT,
             )
 
-        def down(n, first, count, number):
-            y = bank(f"y{n}{first}", [P, count], number)
-            narrow = HALF if count == HALF else P
-            for rb in LAST_FIRST:
-                for j0 in range(0, count, narrow):
-                    words, scales = codes_of_h(rb, first + j0, narrow)
-                    nc.tensor.matmul_mx(
-                        out=y[:, j0 : j0 + narrow],
-                        lhsT=wd4_w[:].bitcast(U8)[:, rb, 2 * P * n : 2 * P * (n + 1)].bitcast(FP4X4),
-                        lhsT_scale=wd4_s[:, rb, P * n : P * (n + 1)],
-                        rhs=words.bitcast(FP8X4),
-                        rhs_scale=scales,
-                        start=(rb == LAST_FIRST[0] and j0 == 0),
-                        stop=False,
-                    )
-                words, scales = codes_of_h(rb, first, count)
-                nc.tensor.matmul_mx(
-                    out=y[:],
-                    lhsT=wd8_w[:, rb, P * n : P * (n + 1)].bitcast(FP8X4),
-                    lhsT_scale=wd8_s[:, rb, P * n : P * (n + 1)],
-                    rhs=words.bitcast(FP8X4),
-                    rhs_scale=scales,
-                    start=False,
-                    stop=(rb == LAST_FIRST[-1]),
-                )
-            return y
+        def quantize_h(keys, h):
+            name = "_".join(f"{rb}{g}" for rb, g in keys)
+            words = sbuf(f"h_w{name}", [P, GROUP * len(keys)], U32)
+            scales = sbuf(f"h_s{name}", [P, GROUP * len(keys)], U8)
+            nc.vector.quantize_mx(out=words[:].bitcast(FP8X4), scales=scales[:], in_=h[:].rearrange("p j t -> p (j t)"))
+            for c, key in enumerate(keys):
+                codes[key] = words[:, GROUP * c : GROUP * (c + 1)].bitcast(FP8X4), scales[:, GROUP * c : GROUP * (c + 1)]
 
-        def add_bias(n, first, count, banks, offset=None):
-            biased = sbuf(f"y_biased{n}{first}", [P, count], F32, offset)
-            width = count // len(banks)
-            for j0, number in zip(range(0, count, width), banks):
-                y = down(n, first + j0, width, number)
-                nc.scalar.activation(
-                    out=biased[:, j0 : j0 + width], in_=y[:], func=ACT.Identity, bias=bias[:, n : n + 1]
-                )
+        def down(n, groups, number):
+            y = bank(f"y{n}{groups[0]}", [P, len(groups), GROUP], number)
+            wd4 = [(wd4_w[:].bitcast(U8)[:, rb, 2 * P * n : 2 * P * (n + 1)].bitcast(FP4X4), wd4_s[:, rb, P * n : P * (n + 1)]) for rb in range(2)]
+            wd8 = [(wd8_w[:, rb, P * n : P * (n + 1)].bitcast(FP8X4), wd8_s[:, rb, P * n : P * (n + 1)]) for rb in range(2)]
+            for c, g in enumerate(groups):
+                for rb in range(2):
+                    multiply(y[:, c, :], wd4[rb], codes[rb, g], rb == 0, False)
+                    multiply(y[:, c, :], wd8[rb], codes[rb, g], False, rb == 1)
+            return y[:].rearrange("p c j -> p (c j)")
+
+        def add_bias(n, groups, banks, offset=None):
+            biased = sbuf(f"y_biased{n}{groups[0]}", [P, GROUP * len(groups)], F32, offset)
+            share = len(groups) // len(banks)
+            for c, number in zip(range(0, len(groups), share), banks):
+                y = down(n, groups[c : c + share], number)
+                target = biased[:, GROUP * c : GROUP * (c + share)]
+                nc.scalar.activation(out=target, in_=y, func=ACT.Identity, bias=bias[:, n : n + 1])
             return biased
 
-        def down_and_scatter(n, first, count, banks, offset=None):
-            biased = add_bias(n, first, count, banks, offset)
-            nc.vector.tensor_tensor(
-                rows[n][:].indirect(listed(first, count)), biased[:], weight[:, first : first + count], MULT
-            )
+        def weights(groups):
+            return weight[:, GROUP * groups[0] : GROUP * (groups[-1] + 1)]
 
-        def weigh_in_bank(y, n, first, out):
-            count = out.shape[-1]
-            nc.vector.scalar_tensor_tensor(out, y, bias[:, n : n + 1], weight[:, first : first + count], ADD, MULT)
+        def window(n, groups):
+            return rows[n][:].indirect(listed(GROUP * groups[0], GROUP * len(groups)))
 
-        def weighed_by_both(n, number, offset, share):
-            own = HALF - share
-            y = down(n, 0, HALF, number)
-            weighted = sbuf(f"y_weighted{n}", [P, HALF], F32)
-            biased = sbuf(f"y_late{n}", [P, share], F32, offset)
-            nc.scalar.activation(out=biased[:], in_=y[:, own:], func=ACT.Identity, bias=bias[:, n : n + 1])
-            weigh_in_bank(y[:, :own], n, 0, weighted[:, :own])
-            nc.gpsimd.tensor_tensor(weighted[:, own:], biased[:], weight[:, own:HALF], MULT)
+        def weigh_and_scatter(n, groups, biased):
+            nc.vector.tensor_tensor(window(n, groups), biased[:], weights(groups), MULT)
+
+        def weigh_in_bank(n, groups, y):
+            weighted = sbuf(f"y_weighted{n}{groups[0]}", [P, GROUP * len(groups)], F32)
+            nc.vector.scalar_tensor_tensor(weighted[:], y, bias[:, n : n + 1], weights(groups), ADD, MULT)
             return weighted
 
-        def scatter(n, first, count, weighted):
-            nc.vector.tensor_copy(rows[n][:].indirect(listed(first, count)), weighted)
+        def weigh_on_gpsimd(n, groups, biased, offset=None):
+            weighted = sbuf(f"y_weighted{n}{groups[0]}", [P, GROUP * len(groups)], F32, offset)
+            nc.gpsimd.tensor_tensor(weighted[:], biased[:], weights(groups), MULT)
+            return weighted
 
-        def factor(name, g, stationary, func, banks, offset=None, values=None):
-            if values is None:
-                values = sbuf(name, [P, GROUP, PLACES], F32, offset)
+        def scatter(n, groups, weighted):
+            nc.vector.tensor_copy(window(n, groups), weighted)
+
+        def factor(name, columns, rb, g, func, banks, offset=None):
+            values = sbuf(f"{name}{rb}{g}", [P, GROUP, PLACES], F32, offset)
             for j0, number in zip(range(0, GROUP, P), banks):
-                if number is None:
-                    continue
-                acc = bank(f"acc_{name}{j0}", [P, PLACES, P], number)
-                for t in reversed(range(PLACES)):
-                    for a in LAST_FIRST:
-                        words, scales = token_operand(a, g * GROUP + j0, P)
-                        lhs_words, lhs_scales = stationary(a, t)
-                        nc.tensor.matmul_mx(
-                            out=acc[:, t, :],
-                            lhsT=lhs_words,
-                            lhsT_scale=lhs_scales,
-                            rhs=words,
-                            rhs_scale=scales,
-                            start=(a == LAST_FIRST[0]),
-                            stop=(a == LAST_FIRST[-1]),
-                        )
+                (acc,) = four_places(name, columns, rb, [g * GROUP + j0], [number])
                 nc.scalar.activation(out=values[:, j0 : j0 + P, :], in_=acc[:].rearrange("p t j -> p j t"), func=func)
             return values
 
-        def gate_factor(rb, g, banks, offset=None, values=None):
-            def wg_columns(a, t):
-                return wg_w[rb][:, a, t, :].bitcast(FP4X4), wg_s[:, rb, a, t, :]
-
-            return factor(f"gates{rb}{g}", g, wg_columns, ACT.Sigmoid, banks, offset, values)
-
-        def up_factor(rb, g, banks, offset=None):
-            def wu_columns(a, t):
-                return wu_w[rb, a][:, P * t : P * (t + 1)].bitcast(FP8X4), wu_s[rb, a][:, P * t : P * (t + 1)]
-
-            return factor(f"up{rb}{g}", g, wu_columns, ACT.Copy, banks, offset)
-
-        def product_on_gpsimd(rb, g, gated, up, offset):
-            h = sbuf(f"h{rb}{g}", [P, GROUP, PLACES], BF16, offset)
+        def product_on_gpsimd(gated, up, h):
             flat = "p j t -> p (j t)"
-            nc.gpsimd.tensor_tensor(h[:].rearrange(flat), gated[:].rearrange(flat), up[:].rearrange(flat), MULT)
-            return h
+            nc.gpsimd.tensor_tensor(h.rearrange(flat), gated[:].rearrange(flat), up[:].rearrange(flat), MULT)
 
         def store(n):
             nc.sync.dma_start(out=out[P * n : P * (n + 1), :], in_=rows[n][:])
 
+        on_scalar, on_vector = nc.scalar.copy, nc.vector.tensor_copy
+
         order_wg_words(0)
         idle = bank("idle", [P, HALF], 0)
-        for t in range(PLACES):
-            nc.tensor.matmul_mx(
-                out=idle[:],
-                lhsT=wg_w[0][:, 0, t, :].bitcast(FP4X4),
-                lhsT_scale=wg_s[:, 0, 0, t, :],
-                rhs=wg_w[0][:, 0].rearrange("p t x -> p (t x)").bitcast(FP4X4),
-                rhs_scale=wg_s[:, 0, 0].rearrange("p t m -> p (t m)"),
-                start=True,
-                stop=True,
-            )
-        for half in range(2):
-            part_words(half, gather_words(half))
-        wd8_w = sbuf("wd8_w", [P, 2, N], I32)
-        nc.sync.dma_start(out=wd8_w[:], in_=wd8_words.rearrange("a p n x -> p a (n x)").bitcast(I32))
-        load_scales(wd_s[:, 1], wd8_scales)
-        wd4_w = sbuf("wd4_w", [P, 2, N // 2], I32)
-        nc.sync.dma_start(out=wd4_w[:], in_=wd4_words.rearrange("a p x -> p a x").bitcast(I32))
-        load_scales(wd_s[:, 0], wd4_scales)
-        wd4_s, wd8_s = wd_s[:, 0].bitcast(U8), wd_s[:, 1].bitcast(U8)
-        weight = sbuf("weight", [P, J], F32)
-        nc.sync.dma_start(out=weight[:, :HALF], in_=wgo[:, :HALF])
-        bias = sbuf("bias", [P, N // P], F32)
-        with nc.allow_non_contiguous_dma(reason="one bias value for each partition and output tile"):
-            nc.sync.dma_start(out=bias[:], in_=b.rearrange("(c p) -> p c", p=P))
-        nc.sync.dma_start(out=weight[:, HALF:], in_=wgo[:, HALF:])
-
-        on_scalar, on_vector = nc.scalar.copy, nc.vector.tensor_copy
-        round_wu(0, 0, (on_scalar, on_scalar))
-        quantize_wu(0, 0)
-        round_wu(0, 1, (on_vector, on_vector))
-        gates(0, 0, HALF, (1, 2, 3, 4), FIRST_WU - 6 * KIB)
-        gates(0, HALF, GROUP, (5, 6), FIRST_WU + 2 * KIB)
-        gated = gate_factor(0, 3, (7, None), FIRST_WU + 6 * KIB)
-        quantize_wu(0, 1, pieces=2)
-        order_wg_words(1, WU_THEN_WG)
+        raw_words, raw_scales = wg_raw[0][:].bitcast(U8), wg_s_raw[:].bitcast(U8)
+        for t in range(3):
+            stationary = raw_words[:, 0, : 2 * P].bitcast(FP4X4), raw_scales[:, 0, :P]
+            multiply(idle[:], stationary, (raw_words[:, 0].bitcast(FP4X4), raw_scales[:, 0, :PASS]), True, True)
+        part_words(0, gather_words(0))
+        order_wg_scales(0)
+        order_wg_scales(1)
+        part_words(1, gather_words(1, WG_SCALES))
+        round_wu(0, 0, 0, on_scalar)
+        round_wu(0, 0, 2, on_scalar)
+        gates(0, 0, GROUP, (1, 2))
+        gates(0, GROUP, GROUP, (3, 4))
+        gates(0, HALF, GROUP, (5, 6))
+        quantize_wu(0, 0, 0)
+        round_wu(0, 1, 0, on_vector)
+        quantize_wu(0, 0, 2)
+        round_wu(0, 1, 2, on_vector, ROWS[1])
+        quantize_wu(0, 1, 0)
+        quantize_wu(0, 1, 2)
         zeroed_rows(1)
-        round_wu(1, 0, (on_scalar, on_scalar))
-        h = hidden(0, 0, (0, 1, 2, 3), first_places=range(PLACES))
-        last = [round_last(0, (on_vector, on_scalar))]
-        quantize_h(0, 0, h, count=HALF)
-        quantize_wu(1, 0)
-        last.append(round_last(1, (on_vector, on_scalar), ROWS[3] - KIB))
-        wu_w[1, 1], wu_s[1, 1] = sbuf("wu_w11", [P, PASS], U32), sbuf("wu_s11", [P, PASS], U8)
-        for half in range(2):
-            quantize_last(half, last[half])
+        order_wg_words(1)
+
+        h = sbuf("h00", [P, HALF, PLACES], BF16)
+        firsts = range(0, HALF, P)
+        for first, ub in zip(firsts, four_places("ub", wu_columns, 0, firsts, (7, 0, 1, 2))):
+            product(0, first, ub, h[:, first : first + P])
+        round_wu(1, 0, 2, on_scalar)
+        round_wu(1, 0, 0, on_vector)
+        quantize_h([(0, 0), (0, 1)], h)
+        quantize_wu(1, 0, 2)
+        quantize_wu(1, 0, 0)
+        round_wu(1, 1, 2, on_scalar, EARLY_H)
+        round_wu(1, 1, 0, on_vector, ROWS[2])
+        gates(1, 0, GROUP, (3, 4), RAW_11)
+        filler = four_places("ub", wu_columns, 0, (HALF, HALF + P), (5, 6))
+        quantize_wu(1, 1, 2)
+        quantize_wu(1, 1, 0)
         zeroed_rows(2)
-        gates(1, 0, GROUP, (4, 5), LAST_WU)
-        gates(1, GROUP, GROUP, (6, 7), LAST_WU + 4 * KIB)
-        h = hidden(1, 0, (2, 3), None, first_places=range(PLACES))
-        filler = hidden(0, HALF, (0, 1), ROWS[3])
-        quantize_h(1, 0, h)
-        h = hidden(1, GROUP, (4, 5), ROWS[3] + 2 * KIB)
-        quantize_h(0, HALF, filler)
-        quantize_h(1, GROUP, h)
+        gates(1, GROUP, GROUP, (7, 0), RAW_11 + 4 * KIB)
+        h = sbuf("h02_10", [P, HALF, PLACES], BF16, EARLY_H)
+        for j0, ub in zip((0, P), filler):
+            product(0, HALF + j0, ub, h[:, j0 : j0 + P])
+        for first, ub in zip((0, P), four_places("ub", wu_columns, 1, (0, P), (1, 2), (2, 3, 0, 1))):
+            product(1, first, ub, h[:, GROUP + first : GROUP + first + P])
+        h11 = sbuf("h11", [P, GROUP, PLACES], BF16, ROWS[3])
+        ubs = four_places("ub", wu_columns, 1, (GROUP, GROUP + P), (3, 4))
+        gated = factor("late_gate", wg_columns, 1, 2, ACT.Sigmoid, (5, 6), LATE_GATE)
+        product(1, GROUP, ubs[0], h11[:, :P])
+        quantize_h([(0, 2), (1, 0)], h)
+        product(1, GROUP + P, ubs[1], h11[:, P:])
+        quantize_h([(1, 1)], h11)
         zeroed_rows(3)
 
-        gate_factor(0, 3, (None, 3), values=gated)
-        down_and_scatter(0, 0, GROUP, (6, 7))
-        down_and_scatter(1, 0, GROUP, (2,))
-        weighted = [sbuf(f"y_weighted{n}", [P, GROUP], F32) for n in range(2)]
-        for n, number in enumerate((3, 0)):
-            weigh_in_bank(down(n, GROUP, GROUP, number)[:], n, GROUP, weighted[n][:])
-        up = up_factor(0, 3, (6, 7))
-        h = product_on_gpsimd(0, 3, gated, up, H_LOW)
-        for n in range(2):
-            scatter(n, GROUP, GROUP, weighted[n][:])
-        gated = gate_factor(1, 2, (2, 6))
-        weighted = weighed_by_both(2, 1, LATE_HIGH, FIRST_SHARE)
-        up = up_factor(1, 2, (7, 2))
-        quantize_h(0, 3 * GROUP, h)
+        weigh_and_scatter(0, [0], add_bias(0, [0], [1]))
+        first = weigh_in_bank(0, [1], down(0, [1], 7))
+        weigh_and_scatter(1, [0], add_bias(1, [0], [2]))
+        second = weigh_on_gpsimd(1, [1], add_bias(1, [1], [0]))
+        third = weigh_on_gpsimd(2, [0, 1], add_bias(2, [0, 1], [3, 4]))
+        up = factor("late_up", wu_columns, 1, 2, ACT.Copy, (1, 7))
+        scatter(0, [1], first[:])
+        scatter(1, [1], second[:])
+        h12 = sbuf("h12", [P, GROUP, PLACES], BF16, LATE_H)
+        product_on_gpsimd(gated, up, h12[:])
+        fourth = weigh_on_gpsimd(3, [0, 1], add_bias(3, [0, 1], [5, 6]), LATE_GATE)
+        scatter(2, [0, 1], third[:])
+        quantize_h([(1, 2)], h12)
 
-        h = product_on_gpsimd(1, 2, gated, up, H_HIGH)
-        scatter(2, 0, HALF, weighted[:])
-        gated = gate_factor(1, 3, (6, 7))
-        weighted = weighed_by_both(3, 3, H_HIGH - SHARE * 4, SHARE)
-        up = up_factor(1, 3, (2, 6), UP_THEN_Y)
-        quantize_h(1, 2 * GROUP, h)
+        h3 = sbuf("h3", [P, HALF, PLACES], BF16, LATE_H)
+        for rb, gate_banks, up_banks in ((0, (2, 0), (3, 4)), (1, (1, 7), (5, 6))):
+            gated = factor("late_gate", wg_columns, rb, 3, ACT.Sigmoid, gate_banks)
+            up = factor("late_up", wu_columns, rb, 3, ACT.Copy, up_banks, LATE_UP + rb * 4 * KIB)
+            product_on_gpsimd(gated, up, h3[:, rb * GROUP : (rb + 1) * GROUP])
+        scatter(3, [0], fourth[:, :GROUP])
+        first = weigh_in_bank(0, [2], down(0, [2], 2))
+        scatter(3, [1], fourth[:, GROUP:])
+        scatter(0, [2], first[:])
+        quantize_h([(0, 3), (1, 3)], h3)
 
-        h = product_on_gpsimd(1, 3, gated, up, H_LOW)
-        scatter(3, 0, HALF, weighted[:])
-        quantize_h(1, 3 * GROUP, h)
-
-        down_and_scatter(1, HALF, GROUP, (7,), UP_THEN_Y)
-        down_and_scatter(0, HALF, GROUP, (2,), UP_THEN_Y + KIB)
-        for n, number in ((1, 4), (0, 5)):
-            down_and_scatter(n, HALF + GROUP, GROUP, (number,))
+        for n, number in ((1, 0), (2, 3)):
+            weigh_and_scatter(n, [2], add_bias(n, [2], [number], LATE_UP + 3 * KIB + n * KIB))
+        for n, number in ((0, 4), (1, 1), (2, 7)):
+            weigh_and_scatter(n, [3], add_bias(n, [3], [number]))
             store(n)
-        for n, number in ((2, 0), (3, 1)):
-            down_and_scatter(n, HALF, HALF, (number,))
-            store(n)
+        weigh_and_scatter(3, [2, 3], add_bias(3, [2, 3], [5]))
+        store(3)

@@ -34,8 +34,8 @@ LATE_H = 4 * BLOCK
 LATE_GATE = LATE_H + 4 * KIB
 LATE_UP = LATE_GATE + 4 * KIB
 RAW_11 = 48 * KIB
-WG_SCALES = 56 * KIB
 EARLY_H = 58 * KIB
+WG_SCALES = 62 * KIB
 
 
 def tile_list_modp_gsigm_res_noneb_kernel(
@@ -82,15 +82,14 @@ def tile_list_modp_gsigm_res_noneb_kernel(
         warm = sbuf("warm", [P, 2], F32)
         nc.vector.memset(warm[:, 0:1], 0.0)
         nc.scalar.activation(out=warm[:, 1:2], in_=warm[:, 0:1], func=ACT.Sigmoid)
-        tab_s = sbuf("tab_s", [P, T // 4], I32)
+        tab_s = sbuf("tab_s", [P, T // 4], I32, ROWS[0])
         nc.vector.memset(tab_s[:TABLE_ROWS], 0)
         wg_s_raw = sbuf("wg_s_raw", [P, 2, R // 4], I32, WG_SCALES)
-        nc.gpsimd.memset(wg_s_raw[:], 0)
+        nc.vector.memset(wg_s_raw[:], 0)
         tok_s = sbuf("tok_s", [P, 2, J], U8)
-        nc.gpsimd.memset(tok_s[:].bitcast(I32), 0)
+        nc.vector.memset(tok_s[:].bitcast(I32), 0)
         wd_s = sbuf("wd_s", [P, 2, 2, N // 4], I32)
-        nc.gpsimd.memset(wd_s[:], 0)
-        zeroed_rows(0)
+        nc.vector.memset(wd_s[:], 0)
 
         offsets = keep.tile([P, J // LIST_COLUMN], U16, name="offsets")
         nc.sync.dma_start(offsets[:], offs)
@@ -106,6 +105,7 @@ def tile_list_modp_gsigm_res_noneb_kernel(
         wu_raw = {(0, 0): load_wu(0, 0)}
         tok_s_rows = sbuf("tok_s_rows", [P, J], U8)
         nc.vector.tensor_copy(tok_s_rows[:], tab_s[:].bitcast(U8).indirect(offsets[:]))
+        zeroed_rows(0)
         for r in range(4):
             nc.sync.dma_start(
                 out=tok_s[r:P:QUADRANT].bitcast(I32),
@@ -141,13 +141,13 @@ def tile_list_modp_gsigm_res_noneb_kernel(
             columns = wg_s_raw[:].bitcast(U8)[:, :, PASS * rb : PASS * (rb + 1)]
             nc.vector.tensor_copy(out=wg_s[rb][:], in_=columns.rearrange("p a (m t) -> p a t m", t=PLACES))
 
-        def gather_words(half, offset=None):
-            both = sbuf(f"tok_both{half}", [P, HALF], U32, offset)
+        def gather_words(half):
+            both = sbuf(f"tok_both{half}", [P, HALF], U32)
             nc.vector.tensor_copy(both[:], tab_w[:].bitcast(U32).indirect(listed(half * HALF, HALF)))
             return both
 
-        def part_words(half, both):
-            tok_w[half] = sbuf(f"tok_w{half}", [P, 2, 2 * HALF], U8)
+        def part_words(half, both, offset=None):
+            tok_w[half] = sbuf(f"tok_w{half}", [P, 2, 2 * HALF], U8, offset)
             by_pass = both[:].bitcast(U16).rearrange("p (j a) -> p a j", a=2)
             nc.vector.tensor_copy(out=tok_w[half][:].bitcast(U16), in_=by_pass)
 
@@ -246,8 +246,8 @@ def tile_list_modp_gsigm_res_noneb_kernel(
         def weigh_and_scatter(n, groups, biased):
             nc.vector.tensor_tensor(window(n, groups), biased[:], weights(groups), MULT)
 
-        def weigh_in_bank(n, groups, y):
-            weighted = sbuf(f"y_weighted{n}{groups[0]}", [P, GROUP * len(groups)], F32)
+        def weigh_in_bank(n, groups, y, offset=None):
+            weighted = sbuf(f"y_weighted{n}{groups[0]}", [P, GROUP * len(groups)], F32, offset)
             nc.vector.scalar_tensor_tensor(weighted[:], y, bias[:, n : n + 1], weights(groups), ADD, MULT)
             return weighted
 
@@ -281,18 +281,19 @@ def tile_list_modp_gsigm_res_noneb_kernel(
         for t in range(3):
             stationary = raw_words[:, 0, : 2 * P].bitcast(FP4X4), raw_scales[:, 0, :P]
             multiply(idle[:], stationary, (raw_words[:, 0].bitcast(FP4X4), raw_scales[:, 0, :PASS]), True, True)
-        part_words(0, gather_words(0))
-        order_wg_scales(0)
-        order_wg_scales(1)
-        part_words(1, gather_words(1, WG_SCALES))
+        both = [gather_words(half) for half in range(2)]
+        part_words(0, both[0])
+        for rb in range(2):
+            order_wg_scales(rb)
+        part_words(1, both[1], WG_SCALES)
         round_wu(0, 0, 0, on_scalar)
-        round_wu(0, 0, 2, on_scalar)
+        round_wu(0, 0, 2, on_vector)
         gates(0, 0, GROUP, (1, 2))
         gates(0, GROUP, GROUP, (3, 4))
         gates(0, HALF, GROUP, (5, 6))
         quantize_wu(0, 0, 0)
-        round_wu(0, 1, 0, on_vector)
         quantize_wu(0, 0, 2)
+        round_wu(0, 1, 0, on_vector)
         round_wu(0, 1, 2, on_vector, ROWS[1])
         quantize_wu(0, 1, 0)
         quantize_wu(0, 1, 2)
@@ -300,9 +301,9 @@ def tile_list_modp_gsigm_res_noneb_kernel(
         order_wg_words(1)
 
         h = sbuf("h00", [P, HALF, PLACES], BF16)
-        firsts = range(0, HALF, P)
-        for first, ub in zip(firsts, four_places("ub", wu_columns, 0, firsts, (7, 0, 1, 2))):
-            product(0, first, ub, h[:, first : first + P])
+        for firsts, banks in (((0, P), (7, 0)), ((2 * P, 3 * P), (5, 6))):
+            for first, ub in zip(firsts, four_places("ub", wu_columns, 0, firsts, banks)):
+                product(0, first, ub, h[:, first : first + P])
         round_wu(1, 0, 2, on_scalar)
         round_wu(1, 0, 0, on_vector)
         quantize_h([(0, 0), (0, 1)], h)
@@ -310,55 +311,59 @@ def tile_list_modp_gsigm_res_noneb_kernel(
         quantize_wu(1, 0, 0)
         round_wu(1, 1, 2, on_scalar, EARLY_H)
         round_wu(1, 1, 0, on_vector, ROWS[2])
-        gates(1, 0, GROUP, (3, 4), RAW_11)
-        filler = four_places("ub", wu_columns, 0, (HALF, HALF + P), (5, 6))
+        gates(1, 0, GROUP, (1, 2), RAW_11)
+        filler = four_places("ub", wu_columns, 0, (HALF, HALF + P), (7, 0))
         quantize_wu(1, 1, 2)
         quantize_wu(1, 1, 0)
         zeroed_rows(2)
-        gates(1, GROUP, GROUP, (7, 0), RAW_11 + 4 * KIB)
+        gates(1, GROUP, GROUP, (3, 4), RAW_11 + 4 * KIB)
         h = sbuf("h02_10", [P, HALF, PLACES], BF16, EARLY_H)
         for j0, ub in zip((0, P), filler):
             product(0, HALF + j0, ub, h[:, j0 : j0 + P])
-        for first, ub in zip((0, P), four_places("ub", wu_columns, 1, (0, P), (1, 2), (2, 3, 0, 1))):
+        for first, ub in zip((0, P), four_places("ub", wu_columns, 1, (0, P), (5, 6), (2, 3, 0, 1))):
             product(1, first, ub, h[:, GROUP + first : GROUP + first + P])
         h11 = sbuf("h11", [P, GROUP, PLACES], BF16, ROWS[3])
-        ubs = four_places("ub", wu_columns, 1, (GROUP, GROUP + P), (3, 4))
-        gated = factor("late_gate", wg_columns, 1, 2, ACT.Sigmoid, (5, 6), LATE_GATE)
+        ubs = four_places("ub", wu_columns, 1, (GROUP, GROUP + P), (1, 2))
+        gated = factor("late_gate", wg_columns, 1, 2, ACT.Sigmoid, (7, 0), LATE_GATE)
         product(1, GROUP, ubs[0], h11[:, :P])
         quantize_h([(0, 2), (1, 0)], h)
         product(1, GROUP + P, ubs[1], h11[:, P:])
         quantize_h([(1, 1)], h11)
         zeroed_rows(3)
 
-        weigh_and_scatter(0, [0], add_bias(0, [0], [1]))
-        first = weigh_in_bank(0, [1], down(0, [1], 7))
-        weigh_and_scatter(1, [0], add_bias(1, [0], [2]))
-        second = weigh_on_gpsimd(1, [1], add_bias(1, [1], [0]))
-        third = weigh_on_gpsimd(2, [0, 1], add_bias(2, [0, 1], [3, 4]))
-        up = factor("late_up", wu_columns, 1, 2, ACT.Copy, (1, 7))
+        weigh_and_scatter(0, [0], add_bias(0, [0], [5]))
+        first = weigh_in_bank(0, [1], down(0, [1], 3))
+        weigh_and_scatter(1, [0], add_bias(1, [0], [6]))
+        second = weigh_on_gpsimd(1, [1], add_bias(1, [1], [4]))
+        third = weigh_on_gpsimd(2, [0, 1], add_bias(2, [0, 1], [1, 2]))
+        up = factor("late_up", wu_columns, 1, 2, ACT.Copy, (5, 3))
         scatter(0, [1], first[:])
         scatter(1, [1], second[:])
         h12 = sbuf("h12", [P, GROUP, PLACES], BF16, LATE_H)
         product_on_gpsimd(gated, up, h12[:])
-        fourth = weigh_on_gpsimd(3, [0, 1], add_bias(3, [0, 1], [5, 6]), LATE_GATE)
+        fourth = weigh_on_gpsimd(3, [0, 1], add_bias(3, [0, 1], [7, 0]), LATE_GATE)
         scatter(2, [0, 1], third[:])
         quantize_h([(1, 2)], h12)
 
-        h3 = sbuf("h3", [P, HALF, PLACES], BF16, LATE_H)
-        for rb, gate_banks, up_banks in ((0, (2, 0), (3, 4)), (1, (1, 7), (5, 6))):
-            gated = factor("late_gate", wg_columns, rb, 3, ACT.Sigmoid, gate_banks)
-            up = factor("late_up", wu_columns, rb, 3, ACT.Copy, up_banks, LATE_UP + rb * 4 * KIB)
-            product_on_gpsimd(gated, up, h3[:, rb * GROUP : (rb + 1) * GROUP])
-        scatter(3, [0], fourth[:, :GROUP])
-        first = weigh_in_bank(0, [2], down(0, [2], 2))
-        scatter(3, [1], fourth[:, GROUP:])
-        scatter(0, [2], first[:])
-        quantize_h([(0, 3), (1, 3)], h3)
+        gated = factor("late_gate", wg_columns, 0, 3, ACT.Sigmoid, (6, 4))
+        up = factor("late_up", wu_columns, 0, 3, ACT.Copy, (1, 2), LATE_UP)
+        h = sbuf("h03", [P, GROUP, PLACES], BF16, LATE_H)
+        product_on_gpsimd(gated, up, h[:])
+        scatter(3, [0, 1], fourth[:])
+        gated = factor("late_gate", wg_columns, 1, 3, ACT.Sigmoid, (5, 3))
+        up = factor("late_up", wu_columns, 1, 3, ACT.Copy, (7, 0), LATE_UP + 4 * KIB)
+        weighted = [weigh_in_bank(n, [2], down(n, [2], number), LATE_UP + n * KIB) for n, number in ((0, 6), (1, 4))]
+        quantize_h([(0, 3)], h)
 
-        for n, number in ((1, 0), (2, 3)):
-            weigh_and_scatter(n, [2], add_bias(n, [2], [number], LATE_UP + 3 * KIB + n * KIB))
-        for n, number in ((0, 4), (1, 1), (2, 7)):
+        h = sbuf("h13", [P, GROUP, PLACES], BF16, LATE_H)
+        product_on_gpsimd(gated, up, h[:])
+        for n in range(2):
+            scatter(n, [2], weighted[n][:])
+        quantize_h([(1, 3)], h)
+
+        weigh_and_scatter(2, [2], add_bias(2, [2], [1], LATE_UP + 4 * KIB))
+        for n, number in ((0, 2), (1, 5), (2, 3)):
             weigh_and_scatter(n, [3], add_bias(n, [3], [number]))
             store(n)
-        weigh_and_scatter(3, [2, 3], add_bias(3, [2, 3], [5]))
+        weigh_and_scatter(3, [2, 3], add_bias(3, [2, 3], [7]))
         store(3)

@@ -29,13 +29,14 @@ KIB = 1024
 BLOCK = 8 * KIB
 TABLE_ROWS = 96
 
-ROWS = [n * BLOCK for n in range(4)]
-LATE_H = 4 * BLOCK
-LATE_GATE = LATE_H + 4 * KIB
-LATE_UP = LATE_GATE + 4 * KIB
-RAW_11 = 48 * KIB
-EARLY_H = 58 * KIB
-WG_SCALES = 62 * KIB
+ROWS = {3: 0, 0: BLOCK, 1: 2 * BLOCK, 2: 3 * BLOCK}
+RAW_11 = 32 * KIB
+EARLY_H = 40 * KIB
+WG_SCALES = 42 * KIB
+FIRST_Y = 44 * KIB
+WEIGHED_0 = 46 * KIB
+BIASED_1 = 48 * KIB
+UP = [50 * KIB, 54 * KIB, 58 * KIB]
 
 
 def tile_list_modp_gsigm_res_noneb_kernel(
@@ -82,7 +83,7 @@ def tile_list_modp_gsigm_res_noneb_kernel(
         warm = sbuf("warm", [P, 2], F32)
         nc.vector.memset(warm[:, 0:1], 0.0)
         nc.scalar.activation(out=warm[:, 1:2], in_=warm[:, 0:1], func=ACT.Sigmoid)
-        tab_s = sbuf("tab_s", [P, T // 4], I32, ROWS[0])
+        tab_s = sbuf("tab_s", [P, T // 4], I32, ROWS[3])
         nc.vector.memset(tab_s[:TABLE_ROWS], 0)
         wg_s_raw = sbuf("wg_s_raw", [P, 2, R // 4], I32, WG_SCALES)
         nc.vector.memset(wg_s_raw[:], 0)
@@ -105,7 +106,7 @@ def tile_list_modp_gsigm_res_noneb_kernel(
         wu_raw = {(0, 0): load_wu(0, 0)}
         tok_s_rows = sbuf("tok_s_rows", [P, J], U8)
         nc.vector.tensor_copy(tok_s_rows[:], tab_s[:].bitcast(U8).indirect(offsets[:]))
-        zeroed_rows(0)
+        zeroed_rows(3)
         for r in range(4):
             nc.sync.dma_start(
                 out=tok_s[r:P:QUADRANT].bitcast(I32),
@@ -126,8 +127,8 @@ def tile_list_modp_gsigm_res_noneb_kernel(
         with nc.allow_non_contiguous_dma(reason="one bias value for each partition and output tile"):
             nc.sync.dma_start(out=bias[:], in_=b.rearrange("(c p) -> p c", p=P))
         weight = sbuf("weight", [P, J], F32)
-        nc.sync.dma_start(out=weight[:, :HALF], in_=wgo[:, :HALF])
         nc.sync.dma_start(out=weight[:, HALF:], in_=wgo[:, HALF:])
+        nc.sync.dma_start(out=weight[:, :HALF], in_=wgo[:, :HALF])
 
         tok_w, wg_w, wg_s, rounded, wu_w, wu_s, gate, codes = {}, {}, {}, {}, {}, {}, {}, {}
 
@@ -210,11 +211,17 @@ def tile_list_modp_gsigm_res_noneb_kernel(
                 MULT,
             )
 
-        def quantize_h(keys, h):
+        def quantize_h(keys, pieces, offset=None):
             name = "_".join(f"{rb}{g}" for rb, g in keys)
-            words = sbuf(f"h_w{name}", [P, GROUP * len(keys)], U32)
+            words = sbuf(f"h_w{name}", [P, GROUP * len(keys)], U32, offset)
             scales = sbuf(f"h_s{name}", [P, GROUP * len(keys)], U8)
-            nc.vector.quantize_mx(out=words[:].bitcast(FP8X4), scales=scales[:], in_=h[:].rearrange("p j t -> p (j t)"))
+            width = GROUP * len(keys) // len(pieces)
+            for c0, h in zip(range(0, GROUP * len(keys), width), pieces):
+                nc.vector.quantize_mx(
+                    out=words[:, c0 : c0 + width].bitcast(FP8X4),
+                    scales=scales[:, c0 : c0 + width],
+                    in_=h[:].rearrange("p j t -> p (j t)"),
+                )
             for c, key in enumerate(keys):
                 codes[key] = words[:, GROUP * c : GROUP * (c + 1)].bitcast(FP8X4), scales[:, GROUP * c : GROUP * (c + 1)]
 
@@ -259,16 +266,16 @@ def tile_list_modp_gsigm_res_noneb_kernel(
         def scatter(n, groups, weighted):
             nc.vector.tensor_copy(window(n, groups), weighted)
 
-        def factor(name, columns, rb, g, func, banks, offset=None):
-            values = sbuf(f"{name}{rb}{g}", [P, GROUP, PLACES], F32, offset)
-            for j0, number in zip(range(0, GROUP, P), banks):
-                (acc,) = four_places(name, columns, rb, [g * GROUP + j0], [number])
+        def factor(name, columns, rb, first, func, banks, offset=None):
+            values = sbuf(f"{name}{rb}{first}", [P, P * len(banks), PLACES], F32, offset)
+            for j0, number in zip(range(0, P * len(banks), P), banks):
+                (acc,) = four_places(name, columns, rb, [first + j0], [number])
                 nc.scalar.activation(out=values[:, j0 : j0 + P, :], in_=acc[:].rearrange("p t j -> p j t"), func=func)
             return values
 
         def product_on_gpsimd(gated, up, h):
             flat = "p j t -> p (j t)"
-            nc.gpsimd.tensor_tensor(h.rearrange(flat), gated[:].rearrange(flat), up[:].rearrange(flat), MULT)
+            nc.gpsimd.tensor_tensor(h.rearrange(flat), gated.rearrange(flat), up.rearrange(flat), MULT)
 
         def store(n):
             nc.sync.dma_start(out=out[P * n : P * (n + 1), :], in_=rows[n][:])
@@ -294,10 +301,10 @@ def tile_list_modp_gsigm_res_noneb_kernel(
         quantize_wu(0, 0, 0)
         quantize_wu(0, 0, 2)
         round_wu(0, 1, 0, on_vector)
-        round_wu(0, 1, 2, on_vector, ROWS[1])
+        round_wu(0, 1, 2, on_vector, ROWS[0])
         quantize_wu(0, 1, 0)
         quantize_wu(0, 1, 2)
-        zeroed_rows(1)
+        zeroed_rows(0)
         order_wg_words(1)
 
         h = sbuf("h00", [P, HALF, PLACES], BF16)
@@ -306,64 +313,69 @@ def tile_list_modp_gsigm_res_noneb_kernel(
                 product(0, first, ub, h[:, first : first + P])
         round_wu(1, 0, 2, on_scalar)
         round_wu(1, 0, 0, on_vector)
-        quantize_h([(0, 0), (0, 1)], h)
+        quantize_h([(0, 0), (0, 1)], [h])
         quantize_wu(1, 0, 2)
         quantize_wu(1, 0, 0)
         round_wu(1, 1, 2, on_scalar, EARLY_H)
-        round_wu(1, 1, 0, on_vector, ROWS[2])
+        round_wu(1, 1, 0, on_vector, ROWS[1])
         gates(1, 0, GROUP, (1, 2), RAW_11)
         filler = four_places("ub", wu_columns, 0, (HALF, HALF + P), (7, 0))
         quantize_wu(1, 1, 2)
         quantize_wu(1, 1, 0)
-        zeroed_rows(2)
+        zeroed_rows(1)
         gates(1, GROUP, GROUP, (3, 4), RAW_11 + 4 * KIB)
-        h = sbuf("h02_10", [P, HALF, PLACES], BF16, EARLY_H)
+        h02 = sbuf("h02", [P, GROUP, PLACES], BF16, EARLY_H)
         for j0, ub in zip((0, P), filler):
-            product(0, HALF + j0, ub, h[:, j0 : j0 + P])
+            product(0, HALF + j0, ub, h02[:, j0 : j0 + P])
+        h10 = sbuf("h10", [P, GROUP, PLACES], BF16)
         for first, ub in zip((0, P), four_places("ub", wu_columns, 1, (0, P), (5, 6), (2, 3, 0, 1))):
-            product(1, first, ub, h[:, GROUP + first : GROUP + first + P])
-        h11 = sbuf("h11", [P, GROUP, PLACES], BF16, ROWS[3])
+            product(1, first, ub, h10[:, first : first + P])
+        h11 = sbuf("h11", [P, GROUP, PLACES], BF16, ROWS[2])
         ubs = four_places("ub", wu_columns, 1, (GROUP, GROUP + P), (1, 2))
-        gated = factor("late_gate", wg_columns, 1, 2, ACT.Sigmoid, (7, 0), LATE_GATE)
+        gated = factor("late_gate", wg_columns, 1, HALF, ACT.Sigmoid, [0])
         product(1, GROUP, ubs[0], h11[:, :P])
-        quantize_h([(0, 2), (1, 0)], h)
+        quantize_h([(1, 0)], [h10])
         product(1, GROUP + P, ubs[1], h11[:, P:])
-        quantize_h([(1, 1)], h11)
-        zeroed_rows(3)
+        quantize_h([(1, 1)], [h11])
+        zeroed_rows(2)
 
-        weigh_and_scatter(0, [0], add_bias(0, [0], [5]))
-        first = weigh_in_bank(0, [1], down(0, [1], 3))
-        weigh_and_scatter(1, [0], add_bias(1, [0], [6]))
-        second = weigh_on_gpsimd(1, [1], add_bias(1, [1], [4]))
-        third = weigh_on_gpsimd(2, [0, 1], add_bias(2, [0, 1], [1, 2]))
-        up = factor("late_up", wu_columns, 1, 2, ACT.Copy, (5, 3))
-        scatter(0, [1], first[:])
-        scatter(1, [1], second[:])
-        h12 = sbuf("h12", [P, GROUP, PLACES], BF16, LATE_H)
-        product_on_gpsimd(gated, up, h12[:])
-        fourth = weigh_on_gpsimd(3, [0, 1], add_bias(3, [0, 1], [7, 0]), LATE_GATE)
-        scatter(2, [0, 1], third[:])
-        quantize_h([(1, 2)], h12)
+        weigh_and_scatter(3, [0], add_bias(3, [0], [5], FIRST_Y))
+        weighted = {0: weigh_in_bank(0, [0, 1], down(0, [0, 1], 3), WEIGHED_0)}
+        quantize_h([(0, 2)], [h02], FIRST_Y)
 
-        gated = factor("late_gate", wg_columns, 0, 3, ACT.Sigmoid, (6, 4))
-        up = factor("late_up", wu_columns, 0, 3, ACT.Copy, (1, 2), LATE_UP)
-        h = sbuf("h03", [P, GROUP, PLACES], BF16, LATE_H)
-        product_on_gpsimd(gated, up, h[:])
-        scatter(3, [0, 1], fourth[:])
-        gated = factor("late_gate", wg_columns, 1, 3, ACT.Sigmoid, (5, 3))
-        up = factor("late_up", wu_columns, 1, 3, ACT.Copy, (7, 0), LATE_UP + 4 * KIB)
-        weighted = [weigh_in_bank(n, [2], down(n, [2], number), LATE_UP + n * KIB) for n, number in ((0, 6), (1, 4))]
-        quantize_h([(0, 3)], h)
+        scatter(0, [0, 1], weighted[0][:])
+        weighted[1] = weigh_on_gpsimd(1, [0, 1], add_bias(1, [0, 1], [6, 4], BIASED_1), EARLY_H)
+        up = factor("late_up", wu_columns, 1, HALF, ACT.Copy, [5])
+        h = [sbuf("h12a", [P, P, PLACES], BF16, BIASED_1), sbuf("h12b", [P, P, PLACES], BF16, WEIGHED_0)]
+        product_on_gpsimd(gated[:], up[:], h[0][:])
 
-        h = sbuf("h13", [P, GROUP, PLACES], BF16, LATE_H)
-        product_on_gpsimd(gated, up, h[:])
-        for n in range(2):
-            scatter(n, [2], weighted[n][:])
-        quantize_h([(1, 3)], h)
+        scatter(1, [0, 1], weighted[1][:])
+        gated = factor("late_gate", wg_columns, 1, HALF + P, ACT.Sigmoid, [6])
+        up = factor("late_up", wu_columns, 1, HALF + P, ACT.Copy, [4], UP[0])
+        product_on_gpsimd(gated[:], up[:], h[1][:])
+        weighted[2] = weigh_on_gpsimd(2, [0, 1], add_bias(2, [0, 1], [1, 2]), UP[0])
+        y = down(3, [1], 7)
+        quantize_h([(1, 2)], h)
 
-        weigh_and_scatter(2, [2], add_bias(2, [2], [1], LATE_UP + 4 * KIB))
-        for n, number in ((0, 2), (1, 5), (2, 3)):
-            weigh_and_scatter(n, [3], add_bias(n, [3], [number]))
+        scatter(2, [0, 1], weighted[2][:])
+        gated = factor("late_gate", wg_columns, 0, 3 * GROUP, ACT.Sigmoid, (5, 3))
+        up = factor("late_up", wu_columns, 0, 3 * GROUP, ACT.Copy, (1, 2), UP[1])
+        h = sbuf("h03", [P, GROUP, PLACES], BF16, WEIGHED_0)
+        product_on_gpsimd(gated[:], up[:], h[:])
+        weighted[3] = sbuf("y_weighted3", [P, HALF], F32, UP[1])
+        gated = factor("late_gate", wg_columns, 1, 3 * GROUP, ACT.Sigmoid, (6, 4))
+        up = factor("late_up", wu_columns, 1, 3 * GROUP, ACT.Copy, (5, 3), UP[2])
+        for c, y in enumerate((y, down(3, [2], 0))):
+            target = weighted[3][:, GROUP * c : GROUP * (c + 1)]
+            nc.vector.scalar_tensor_tensor(target, y, bias[:, 3:4], weights([1 + c]), ADD, MULT)
+        quantize_h([(0, 3)], [h])
+
+        scatter(3, [1, 2], weighted[3][:])
+        h = sbuf("h13", [P, GROUP, PLACES], BF16, WEIGHED_0)
+        product_on_gpsimd(gated[:], up[:], h[:])
+        quantize_h([(1, 3)], [h])
+
+        weigh_and_scatter(0, [2], add_bias(0, [2], [1], UP[2]))
+        for n, groups, number in ((3, [3], 2), (0, [3], 6), (1, [2, 3], 4), (2, [2, 3], 7)):
+            weigh_and_scatter(n, groups, add_bias(n, groups, [number]))
             store(n)
-        weigh_and_scatter(3, [2, 3], add_bias(3, [2, 3], [7]))
-        store(3)

@@ -27,12 +27,13 @@ GROUP = 256
 BANK = 2048
 KIB = 1024
 BLOCK = 8 * KIB
+WARM_UPS = 4
 TABLE_ROWS = 96
 
 ROWS = {3: 0, 0: BLOCK, 1: 2 * BLOCK, 2: 3 * BLOCK}
 RAW_11 = 32 * KIB
 EARLY_H = 40 * KIB
-WG_SCALES = 42 * KIB
+TOKEN_WORDS = 42 * KIB
 FIRST_Y = 44 * KIB
 WEIGHED_0 = 46 * KIB
 BIASED_1 = 48 * KIB
@@ -82,11 +83,12 @@ def tile_list_modp_gsigm_res_noneb_kernel(
         rows = {}
         warm = sbuf("warm", [P, 2], F32)
         nc.vector.memset(warm[:, 0:1], 0.0)
-        nc.scalar.activation(out=warm[:, 1:2], in_=warm[:, 0:1], func=ACT.Sigmoid)
-        tab_s = sbuf("tab_s", [P, T // 4], I32, ROWS[3])
+        wg_s_rows = sbuf("wg_s_rows", [P, PASS // 4], I32, ROWS[3])
+        nc.vector.memset(wg_s_rows[2 * QUADRANT :], 0)
+        wg_s = sbuf("wg_s", [P, 2, 2, PLACES, P], U8)
+        nc.vector.memset(wg_s[:].bitcast(I32), 0)
+        tab_s = sbuf("tab_s", [P, T // 4], I32)
         nc.vector.memset(tab_s[:TABLE_ROWS], 0)
-        wg_s_raw = sbuf("wg_s_raw", [P, 2, R // 4], I32, WG_SCALES)
-        nc.vector.memset(wg_s_raw[:], 0)
         tok_s = sbuf("tok_s", [P, 2, J], U8)
         nc.vector.memset(tok_s[:].bitcast(I32), 0)
         wd_s = sbuf("wd_s", [P, 2, 2, N // 4], I32)
@@ -94,23 +96,33 @@ def tile_list_modp_gsigm_res_noneb_kernel(
 
         offsets = keep.tile([P, J // LIST_COLUMN], U16, name="offsets")
         nc.sync.dma_start(offsets[:], offs)
-        for r in range(4):
+        for a in range(2):
             nc.sync.dma_start(
-                out=tab_s[TABLE_ROWS + r : P : 4, :],
-                in_=tab_scales[:, r:16:4, :].rearrange("a q x -> q a x").bitcast(I32),
+                out=wg_s_rows[a : 2 * QUADRANT : 2, :],
+                in_=wg_scales[a].rearrange("b (r x) -> (b r) x", r=2).bitcast(I32),
             )
+        nc.scalar.activation(out=warm[:, 1:2], in_=warm[:, 0:1], func=ACT.Sigmoid)
+        nc.sync.dma_start(out=tab_s[TABLE_ROWS:, :], in_=tab_scales.rearrange("a b x -> b a x").bitcast(I32))
+        wg_raw = [load_wg(0)]
         tab_w = sbuf("tab_w", [P, T], I32)
         nc.sync.dma_start(out=tab_w[:], in_=tab_words[0].rearrange("p t x -> p (t x)").bitcast(I32))
-        wg_raw = [load_wg(0)]
-        load_scales(wg_s_raw, wg_scales)
+        wg_s_ordered = sbuf("wg_s_ordered", [P, PLACES, P], U8)
+        by_place = wg_s_rows[:].bitcast(U8).rearrange("p (m t) -> p t m", t=PLACES)
+        nc.vector.tensor_copy(out=wg_s_ordered[:], in_=by_place)
+
+        for q in range(P // QUADRANT):
+            nc.sync.dma_start(
+                out=wg_s[QUADRANT * q : QUADRANT * q + 4].rearrange("p r a t m -> p (r a t m)").bitcast(I32),
+                in_=wg_s_ordered[16 * q : 16 * q + 16].rearrange("p t m -> p (t m)").bitcast(I32),
+            )
+        zeroed_rows(3)
         wu_raw = {(0, 0): load_wu(0, 0)}
         tok_s_rows = sbuf("tok_s_rows", [P, J], U8)
         nc.vector.tensor_copy(tok_s_rows[:], tab_s[:].bitcast(U8).indirect(offsets[:]))
-        zeroed_rows(3)
-        for r in range(4):
+        for q in range(P // QUADRANT):
             nc.sync.dma_start(
-                out=tok_s[r:P:QUADRANT].bitcast(I32),
-                in_=tok_s_rows[TABLE_ROWS + r : P : 4, :].bitcast(I32),
+                out=tok_s[QUADRANT * q : QUADRANT * q + 4].bitcast(I32),
+                in_=tok_s_rows[TABLE_ROWS + 8 * q : TABLE_ROWS + 8 * q + 8, :].bitcast(I32),
             )
         wu_raw[0, 1] = load_wu(0, 1)
         wg_raw.append(load_wg(1))
@@ -130,25 +142,20 @@ def tile_list_modp_gsigm_res_noneb_kernel(
         nc.sync.dma_start(out=weight[:, HALF:], in_=wgo[:, HALF:])
         nc.sync.dma_start(out=weight[:, :HALF], in_=wgo[:, :HALF])
 
-        tok_w, wg_w, wg_s, rounded, wu_w, wu_s, gate, codes = {}, {}, {}, {}, {}, {}, {}, {}
+        tok_w, wg_w, rounded, wu_w, wu_s, gate, codes = {}, {}, {}, {}, {}, {}, {}
 
         def order_wg_words(rb):
             wg_w[rb] = sbuf(f"wg_w{rb}", [P, 2, PLACES, 2 * P], U8)
             columns = wg_raw[rb][:].bitcast(U16).rearrange("p a (m t) -> p a t m", t=PLACES)
-            nc.scalar.copy(out=wg_w[rb][:].bitcast(U16), in_=columns)
-
-        def order_wg_scales(rb):
-            wg_s[rb] = sbuf(f"wg_s{rb}", [P, 2, PLACES, P], U8)
-            columns = wg_s_raw[:].bitcast(U8)[:, :, PASS * rb : PASS * (rb + 1)]
-            nc.vector.tensor_copy(out=wg_s[rb][:], in_=columns.rearrange("p a (m t) -> p a t m", t=PLACES))
+            nc.vector.tensor_copy(out=wg_w[rb][:].bitcast(U16), in_=columns)
 
         def gather_words(half):
-            both = sbuf(f"tok_both{half}", [P, HALF], U32)
+            both = sbuf(f"tok_both{half}", [P, HALF], U32, TOKEN_WORDS)
             nc.vector.tensor_copy(both[:], tab_w[:].bitcast(U32).indirect(listed(half * HALF, HALF)))
             return both
 
-        def part_words(half, both, offset=None):
-            tok_w[half] = sbuf(f"tok_w{half}", [P, 2, 2 * HALF], U8, offset)
+        def part_words(half, both):
+            tok_w[half] = sbuf(f"tok_w{half}", [P, 2, 2 * HALF], U8)
             by_pass = both[:].bitcast(U16).rearrange("p (j a) -> p a j", a=2)
             nc.vector.tensor_copy(out=tok_w[half][:].bitcast(U16), in_=by_pass)
 
@@ -171,7 +178,7 @@ def tile_list_modp_gsigm_res_noneb_kernel(
             )
 
         def wg_columns(rb, a, t):
-            return wg_w[rb][:, a, t, :].bitcast(FP4X4), wg_s[rb][:, a, t, :]
+            return wg_w[rb][:, a, t, :].bitcast(FP4X4), wg_s[:, rb, a, t, :]
 
         def wu_columns(rb, a, t):
             key, columns = (rb, a, t - t % 2), slice(P * (t % 2), P * (t % 2 + 1))
@@ -284,19 +291,14 @@ def tile_list_modp_gsigm_res_noneb_kernel(
 
         order_wg_words(0)
         idle = bank("idle", [P, HALF], 0)
-        raw_words, raw_scales = wg_raw[0][:].bitcast(U8), wg_s_raw[:].bitcast(U8)
-        for t in range(3):
-            stationary = raw_words[:, 0, : 2 * P].bitcast(FP4X4), raw_scales[:, 0, :P]
-            multiply(idle[:], stationary, (raw_words[:, 0].bitcast(FP4X4), raw_scales[:, 0, :PASS]), True, True)
-        both = [gather_words(half) for half in range(2)]
-        part_words(0, both[0])
-        for rb in range(2):
-            order_wg_scales(rb)
-        part_words(1, both[1], WG_SCALES)
+        all_columns = wg_w[0][:, 0].rearrange("p t x -> p (t x)").bitcast(FP4X4), wg_s[:, 0, 0].rearrange("p t m -> p (t m)")
+        for t in range(WARM_UPS):
+            multiply(idle[:], wg_columns(0, 0, t % PLACES), all_columns, True, True)
+        for half in range(2):
+            part_words(half, gather_words(half))
         round_wu(0, 0, 0, on_scalar)
-        round_wu(0, 0, 2, on_vector)
-        gates(0, 0, GROUP, (1, 2))
-        gates(0, GROUP, GROUP, (3, 4))
+        round_wu(0, 0, 2, on_scalar)
+        gates(0, 0, HALF, (1, 2, 3, 4))
         gates(0, HALF, GROUP, (5, 6))
         quantize_wu(0, 0, 0)
         quantize_wu(0, 0, 2)
@@ -304,38 +306,38 @@ def tile_list_modp_gsigm_res_noneb_kernel(
         round_wu(0, 1, 2, on_vector, ROWS[0])
         quantize_wu(0, 1, 0)
         quantize_wu(0, 1, 2)
-        zeroed_rows(0)
         order_wg_words(1)
+        zeroed_rows(0)
 
         h = sbuf("h00", [P, HALF, PLACES], BF16)
         for firsts, banks in (((0, P), (7, 0)), ((2 * P, 3 * P), (5, 6))):
             for first, ub in zip(firsts, four_places("ub", wu_columns, 0, firsts, banks)):
                 product(0, first, ub, h[:, first : first + P])
+        round_wu(1, 0, 0, on_scalar)
         round_wu(1, 0, 2, on_scalar)
-        round_wu(1, 0, 0, on_vector)
+        quantize_wu(1, 0, 0)
         quantize_h([(0, 0), (0, 1)], [h])
         quantize_wu(1, 0, 2)
-        quantize_wu(1, 0, 0)
         round_wu(1, 1, 2, on_scalar, EARLY_H)
         round_wu(1, 1, 0, on_vector, ROWS[1])
         gates(1, 0, GROUP, (1, 2), RAW_11)
-        filler = four_places("ub", wu_columns, 0, (HALF, HALF + P), (7, 0))
+        (filler,) = four_places("ub", wu_columns, 0, [HALF], [7])
         quantize_wu(1, 1, 2)
         quantize_wu(1, 1, 0)
         zeroed_rows(1)
         gates(1, GROUP, GROUP, (3, 4), RAW_11 + 4 * KIB)
         h02 = sbuf("h02", [P, GROUP, PLACES], BF16, EARLY_H)
-        for j0, ub in zip((0, P), filler):
-            product(0, HALF + j0, ub, h02[:, j0 : j0 + P])
+        product(0, HALF, filler, h02[:, :P])
         h10 = sbuf("h10", [P, GROUP, PLACES], BF16)
         for first, ub in zip((0, P), four_places("ub", wu_columns, 1, (0, P), (5, 6), (2, 3, 0, 1))):
             product(1, first, ub, h10[:, first : first + P])
         h11 = sbuf("h11", [P, GROUP, PLACES], BF16, ROWS[2])
         ubs = four_places("ub", wu_columns, 1, (GROUP, GROUP + P), (1, 2))
-        gated = factor("late_gate", wg_columns, 1, HALF, ACT.Sigmoid, [0])
+        (filler,) = four_places("ub", wu_columns, 0, [HALF + P], [6])
         product(1, GROUP, ubs[0], h11[:, :P])
         quantize_h([(1, 0)], [h10])
         product(1, GROUP + P, ubs[1], h11[:, P:])
+        product(0, HALF + P, filler, h02[:, P:])
         quantize_h([(1, 1)], [h11])
         zeroed_rows(2)
 
@@ -344,28 +346,29 @@ def tile_list_modp_gsigm_res_noneb_kernel(
         quantize_h([(0, 2)], [h02], FIRST_Y)
 
         scatter(0, [0, 1], weighted[0][:])
-        weighted[1] = weigh_on_gpsimd(1, [0, 1], add_bias(1, [0, 1], [6, 4], BIASED_1), EARLY_H)
-        up = factor("late_up", wu_columns, 1, HALF, ACT.Copy, [5])
+        weighted[1] = weigh_on_gpsimd(1, [0, 1], add_bias(1, [0, 1], [7, 0], BIASED_1), EARLY_H)
+        gated = factor("late_gate", wg_columns, 1, HALF, ACT.Sigmoid, [5])
+        up = factor("late_up", wu_columns, 1, HALF, ACT.Copy, [7])
         h = [sbuf("h12a", [P, P, PLACES], BF16, BIASED_1), sbuf("h12b", [P, P, PLACES], BF16, WEIGHED_0)]
         product_on_gpsimd(gated[:], up[:], h[0][:])
 
         scatter(1, [0, 1], weighted[1][:])
-        gated = factor("late_gate", wg_columns, 1, HALF + P, ACT.Sigmoid, [6])
-        up = factor("late_up", wu_columns, 1, HALF + P, ACT.Copy, [4], UP[0])
+        gated = factor("late_gate", wg_columns, 1, HALF + P, ACT.Sigmoid, [0])
+        up = factor("late_up", wu_columns, 1, HALF + P, ACT.Copy, [5], UP[0])
         product_on_gpsimd(gated[:], up[:], h[1][:])
         weighted[2] = weigh_on_gpsimd(2, [0, 1], add_bias(2, [0, 1], [1, 2]), UP[0])
-        y = down(3, [1], 7)
+        y = down(3, [1], 4)
         quantize_h([(1, 2)], h)
 
         scatter(2, [0, 1], weighted[2][:])
-        gated = factor("late_gate", wg_columns, 0, 3 * GROUP, ACT.Sigmoid, (5, 3))
+        gated = factor("late_gate", wg_columns, 0, 3 * GROUP, ACT.Sigmoid, (3, 7))
         up = factor("late_up", wu_columns, 0, 3 * GROUP, ACT.Copy, (1, 2), UP[1])
         h = sbuf("h03", [P, GROUP, PLACES], BF16, WEIGHED_0)
         product_on_gpsimd(gated[:], up[:], h[:])
         weighted[3] = sbuf("y_weighted3", [P, HALF], F32, UP[1])
-        gated = factor("late_gate", wg_columns, 1, 3 * GROUP, ACT.Sigmoid, (6, 4))
-        up = factor("late_up", wu_columns, 1, 3 * GROUP, ACT.Copy, (5, 3), UP[2])
-        for c, y in enumerate((y, down(3, [2], 0))):
+        gated = factor("late_gate", wg_columns, 1, 3 * GROUP, ACT.Sigmoid, (0, 5))
+        up = factor("late_up", wu_columns, 1, 3 * GROUP, ACT.Copy, (3, 7), UP[2])
+        for c, y in enumerate((y, down(3, [2], 6))):
             target = weighted[3][:, GROUP * c : GROUP * (c + 1)]
             nc.vector.scalar_tensor_tensor(target, y, bias[:, 3:4], weights([1 + c]), ADD, MULT)
         quantize_h([(0, 3)], [h])
@@ -376,6 +379,6 @@ def tile_list_modp_gsigm_res_noneb_kernel(
         quantize_h([(1, 3)], [h])
 
         weigh_and_scatter(0, [2], add_bias(0, [2], [1], UP[2]))
-        for n, groups, number in ((3, [3], 2), (0, [3], 6), (1, [2, 3], 4), (2, [2, 3], 7)):
+        for n, groups, number in ((3, [3], 2), (0, [3], 0), (1, [2, 3], 5), (2, [2, 3], 4)):
             weigh_and_scatter(n, groups, add_bias(n, groups, [number]))
             store(n)

@@ -31,13 +31,11 @@ WARM_UPS = 4
 TABLE_ROWS = 96
 
 ROWS = {3: 0, 0: BLOCK, 1: 2 * BLOCK, 2: 3 * BLOCK}
-RAW_11 = 32 * KIB
-EARLY_H = 40 * KIB
+RAW_11 = 34 * KIB
+EARLY_H = 62 * KIB
 TOKEN_WORDS = 42 * KIB
 FIRST_Y = 44 * KIB
-WEIGHED_0 = 46 * KIB
-BIASED_1 = 48 * KIB
-UP = [50 * KIB, 54 * KIB, 58 * KIB]
+UP = [46 * KIB, 50 * KIB, 54 * KIB, 58 * KIB]
 
 
 def tile_list_modp_gsigm_res_noneb_kernel(
@@ -144,10 +142,10 @@ def tile_list_modp_gsigm_res_noneb_kernel(
 
         tok_w, wg_w, rounded, wu_w, wu_s, gate, codes = {}, {}, {}, {}, {}, {}, {}
 
-        def order_wg_words(rb):
+        def order_wg_words(rb, copy):
             wg_w[rb] = sbuf(f"wg_w{rb}", [P, 2, PLACES, 2 * P], U8)
             columns = wg_raw[rb][:].bitcast(U16).rearrange("p a (m t) -> p a t m", t=PLACES)
-            nc.vector.tensor_copy(out=wg_w[rb][:].bitcast(U16), in_=columns)
+            copy(out=wg_w[rb][:].bitcast(U16), in_=columns)
 
         def gather_words(half):
             both = sbuf(f"tok_both{half}", [P, HALF], U32, TOKEN_WORDS)
@@ -218,19 +216,20 @@ def tile_list_modp_gsigm_res_noneb_kernel(
                 MULT,
             )
 
-        def quantize_h(keys, pieces, offset=None):
+        def codes_of(keys, offset=None):
             name = "_".join(f"{rb}{g}" for rb, g in keys)
             words = sbuf(f"h_w{name}", [P, GROUP * len(keys)], U32, offset)
             scales = sbuf(f"h_s{name}", [P, GROUP * len(keys)], U8)
-            width = GROUP * len(keys) // len(pieces)
-            for c0, h in zip(range(0, GROUP * len(keys), width), pieces):
-                nc.vector.quantize_mx(
-                    out=words[:, c0 : c0 + width].bitcast(FP8X4),
-                    scales=scales[:, c0 : c0 + width],
-                    in_=h[:].rearrange("p j t -> p (j t)"),
-                )
             for c, key in enumerate(keys):
                 codes[key] = words[:, GROUP * c : GROUP * (c + 1)].bitcast(FP8X4), scales[:, GROUP * c : GROUP * (c + 1)]
+            return words, scales
+
+        def quantize_h(target, first, h):
+            words, scales = target
+            tokens = slice(first, first + h[:].shape[1])
+            nc.vector.quantize_mx(
+                out=words[:, tokens].bitcast(FP8X4), scales=scales[:, tokens], in_=h[:].rearrange("p j t -> p (j t)")
+            )
 
         def down(n, groups, number):
             y = bank(f"y{n}{groups[0]}", [P, len(groups), GROUP], number)
@@ -289,7 +288,7 @@ def tile_list_modp_gsigm_res_noneb_kernel(
 
         on_scalar, on_vector = nc.scalar.copy, nc.vector.tensor_copy
 
-        order_wg_words(0)
+        order_wg_words(0, on_scalar)
         idle = bank("idle", [P, HALF], 0)
         all_columns = wg_w[0][:, 0].rearrange("p t x -> p (t x)").bitcast(FP4X4), wg_s[:, 0, 0].rearrange("p t m -> p (t m)")
         for t in range(WARM_UPS):
@@ -306,7 +305,7 @@ def tile_list_modp_gsigm_res_noneb_kernel(
         round_wu(0, 1, 2, on_vector, ROWS[0])
         quantize_wu(0, 1, 0)
         quantize_wu(0, 1, 2)
-        order_wg_words(1)
+        order_wg_words(1, on_vector)
         zeroed_rows(0)
 
         h = sbuf("h00", [P, HALF, PLACES], BF16)
@@ -316,16 +315,17 @@ def tile_list_modp_gsigm_res_noneb_kernel(
         round_wu(1, 0, 0, on_scalar)
         round_wu(1, 0, 2, on_scalar)
         quantize_wu(1, 0, 0)
-        quantize_h([(0, 0), (0, 1)], [h])
+        quantize_h(codes_of([(0, 0), (0, 1)]), 0, h)
         quantize_wu(1, 0, 2)
         round_wu(1, 1, 2, on_scalar, EARLY_H)
         round_wu(1, 1, 0, on_vector, ROWS[1])
-        gates(1, 0, GROUP, (1, 2), RAW_11)
+        gates(1, 0, GROUP, (1, 2), RAW_11 - 2 * KIB)
         (filler,) = four_places("ub", wu_columns, 0, [HALF], [7])
         quantize_wu(1, 1, 2)
         quantize_wu(1, 1, 0)
         zeroed_rows(1)
-        gates(1, GROUP, GROUP, (3, 4), RAW_11 + 4 * KIB)
+        gates(1, GROUP, GROUP, (3, 4), RAW_11 + 2 * KIB)
+        gated = factor("late_gate", wg_columns, 1, HALF, ACT.Sigmoid, [0], RAW_11 + 6 * KIB)
         h02 = sbuf("h02", [P, GROUP, PLACES], BF16, EARLY_H)
         product(0, HALF, filler, h02[:, :P])
         h10 = sbuf("h10", [P, GROUP, PLACES], BF16)
@@ -335,50 +335,52 @@ def tile_list_modp_gsigm_res_noneb_kernel(
         ubs = four_places("ub", wu_columns, 1, (GROUP, GROUP + P), (1, 2))
         (filler,) = four_places("ub", wu_columns, 0, [HALF + P], [6])
         product(1, GROUP, ubs[0], h11[:, :P])
-        quantize_h([(1, 0)], [h10])
+        quantize_h(codes_of([(1, 0)]), 0, h10)
         product(1, GROUP + P, ubs[1], h11[:, P:])
         product(0, HALF + P, filler, h02[:, P:])
-        quantize_h([(1, 1)], [h11])
+        quantize_h(codes_of([(1, 1)]), 0, h11)
         zeroed_rows(2)
 
         weigh_and_scatter(3, [0], add_bias(3, [0], [5], FIRST_Y))
-        weighted = {0: weigh_in_bank(0, [0, 1], down(0, [0, 1], 3), WEIGHED_0)}
-        quantize_h([(0, 2)], [h02], FIRST_Y)
+        weighted = {0: weigh_in_bank(0, [0, 1], down(0, [0, 1], 3))}
+        quantize_h(codes_of([(0, 2)], FIRST_Y), 0, h02)
 
         scatter(0, [0, 1], weighted[0][:])
-        weighted[1] = weigh_on_gpsimd(1, [0, 1], add_bias(1, [0, 1], [7, 0], BIASED_1), EARLY_H)
-        gated = factor("late_gate", wg_columns, 1, HALF, ACT.Sigmoid, [5])
-        up = factor("late_up", wu_columns, 1, HALF, ACT.Copy, [7])
-        h = [sbuf("h12a", [P, P, PLACES], BF16, BIASED_1), sbuf("h12b", [P, P, PLACES], BF16, WEIGHED_0)]
-        product_on_gpsimd(gated[:], up[:], h[0][:])
+        up = factor("late_up", wu_columns, 1, HALF, ACT.Copy, [5], UP[0])
+        h = sbuf("h12a", [P, P, PLACES], BF16, EARLY_H)
+        product_on_gpsimd(gated[:], up[:], h[:])
+        weighted[1] = weigh_on_gpsimd(1, [0, 1], add_bias(1, [0, 1], [0, 4]), UP[0])
+        target = codes_of([(1, 2)])
+        quantize_h(target, 0, h)
 
         scatter(1, [0, 1], weighted[1][:])
-        gated = factor("late_gate", wg_columns, 1, HALF + P, ACT.Sigmoid, [0])
-        up = factor("late_up", wu_columns, 1, HALF + P, ACT.Copy, [5], UP[0])
-        product_on_gpsimd(gated[:], up[:], h[1][:])
-        weighted[2] = weigh_on_gpsimd(2, [0, 1], add_bias(2, [0, 1], [1, 2]), UP[0])
-        y = down(3, [1], 4)
-        quantize_h([(1, 2)], h)
+        gated = factor("late_gate", wg_columns, 1, HALF + P, ACT.Sigmoid, [5])
+        up = factor("late_up", wu_columns, 1, HALF + P, ACT.Copy, [0], UP[3])
+        h = sbuf("h12b", [P, P, PLACES], BF16, EARLY_H)
+        product_on_gpsimd(gated[:], up[:], h[:])
+        weighted[2] = weigh_on_gpsimd(2, [0, 1], add_bias(2, [0, 1], [1, 2]), UP[3])
+        y = down(3, [1], 7)
+        quantize_h(target, P, h)
 
         scatter(2, [0, 1], weighted[2][:])
-        gated = factor("late_gate", wg_columns, 0, 3 * GROUP, ACT.Sigmoid, (3, 7))
+        gated = factor("late_gate", wg_columns, 0, 3 * GROUP, ACT.Sigmoid, (3, 4))
         up = factor("late_up", wu_columns, 0, 3 * GROUP, ACT.Copy, (1, 2), UP[1])
-        h = sbuf("h03", [P, GROUP, PLACES], BF16, WEIGHED_0)
+        h = sbuf("h03", [P, GROUP, PLACES], BF16, EARLY_H)
         product_on_gpsimd(gated[:], up[:], h[:])
         weighted[3] = sbuf("y_weighted3", [P, HALF], F32, UP[1])
-        gated = factor("late_gate", wg_columns, 1, 3 * GROUP, ACT.Sigmoid, (0, 5))
-        up = factor("late_up", wu_columns, 1, 3 * GROUP, ACT.Copy, (3, 7), UP[2])
+        gated = factor("late_gate", wg_columns, 1, 3 * GROUP, ACT.Sigmoid, (5, 0))
+        up = factor("late_up", wu_columns, 1, 3 * GROUP, ACT.Copy, (3, 4), UP[2])
         for c, y in enumerate((y, down(3, [2], 6))):
             target = weighted[3][:, GROUP * c : GROUP * (c + 1)]
             nc.vector.scalar_tensor_tensor(target, y, bias[:, 3:4], weights([1 + c]), ADD, MULT)
-        quantize_h([(0, 3)], [h])
+        quantize_h(codes_of([(0, 3)]), 0, h)
 
         scatter(3, [1, 2], weighted[3][:])
-        h = sbuf("h13", [P, GROUP, PLACES], BF16, WEIGHED_0)
+        h = sbuf("h13", [P, GROUP, PLACES], BF16, EARLY_H)
         product_on_gpsimd(gated[:], up[:], h[:])
-        quantize_h([(1, 3)], [h])
+        quantize_h(codes_of([(1, 3)]), 0, h)
 
         weigh_and_scatter(0, [2], add_bias(0, [2], [1], UP[2]))
-        for n, groups, number in ((3, [3], 2), (0, [3], 0), (1, [2, 3], 5), (2, [2, 3], 4)):
+        for n, groups, number in ((3, [3], 2), (0, [3], 0), (1, [2, 3], 5), (2, [2, 3], 7)):
             weigh_and_scatter(n, groups, add_bias(n, groups, [number]))
             store(n)

@@ -32,10 +32,10 @@ TABLE_ROWS = 96
 
 ROWS = {3: 0, 0: BLOCK, 1: 2 * BLOCK, 2: 3 * BLOCK}
 RAW_11 = 34 * KIB
-EARLY_H = 62 * KIB
+EARLY_H = 54 * KIB
 TOKEN_WORDS = 42 * KIB
 FIRST_Y = 44 * KIB
-UP = [46 * KIB, 50 * KIB, 54 * KIB, 58 * KIB]
+UP = [46 * KIB, 50 * KIB]
 
 
 def tile_list_modp_gsigm_res_noneb_kernel(
@@ -216,10 +216,10 @@ def tile_list_modp_gsigm_res_noneb_kernel(
                 MULT,
             )
 
-        def codes_of(keys, offset=None):
+        def codes_of(keys, offset=None, scales_offset=None):
             name = "_".join(f"{rb}{g}" for rb, g in keys)
             words = sbuf(f"h_w{name}", [P, GROUP * len(keys)], U32, offset)
-            scales = sbuf(f"h_s{name}", [P, GROUP * len(keys)], U8)
+            scales = sbuf(f"h_s{name}", [P, GROUP * len(keys)], U8, scales_offset)
             for c, key in enumerate(keys):
                 codes[key] = words[:, GROUP * c : GROUP * (c + 1)].bitcast(FP8X4), scales[:, GROUP * c : GROUP * (c + 1)]
             return words, scales
@@ -259,15 +259,11 @@ def tile_list_modp_gsigm_res_noneb_kernel(
         def weigh_and_scatter(n, groups, biased):
             nc.vector.tensor_tensor(window(n, groups), biased[:], weights(groups), MULT)
 
-        def weigh_in_bank(n, groups, y, offset=None):
-            weighted = sbuf(f"y_weighted{n}{groups[0]}", [P, GROUP * len(groups)], F32, offset)
-            nc.vector.scalar_tensor_tensor(weighted[:], y, bias[:, n : n + 1], weights(groups), ADD, MULT)
-            return weighted
+        def weigh_in_bank(n, groups, y, target):
+            nc.vector.scalar_tensor_tensor(target, y, bias[:, n : n + 1], weights(groups), ADD, MULT)
 
-        def weigh_on_gpsimd(n, groups, biased, offset=None):
-            weighted = sbuf(f"y_weighted{n}{groups[0]}", [P, GROUP * len(groups)], F32, offset)
-            nc.gpsimd.tensor_tensor(weighted[:], biased[:], weights(groups), MULT)
-            return weighted
+        def weigh_on_gpsimd(groups, biased, target):
+            nc.gpsimd.tensor_tensor(target, biased[:], weights(groups), MULT)
 
         def scatter(n, groups, weighted):
             nc.vector.tensor_copy(window(n, groups), weighted)
@@ -342,37 +338,40 @@ def tile_list_modp_gsigm_res_noneb_kernel(
         zeroed_rows(2)
 
         weigh_and_scatter(3, [0], add_bias(3, [0], [5], FIRST_Y))
-        weighted = {0: weigh_in_bank(0, [0, 1], down(0, [0, 1], 3))}
+        weighted = {n: sbuf(f"y_weighted{n}", [P, HALF], F32) for n in range(2)}
+        weigh_in_bank(0, [0, 1], down(0, [0, 1], 3), weighted[0][:])
+        weigh_in_bank(1, [0], down(1, [0], 4), weighted[1][:, :GROUP])
         quantize_h(codes_of([(0, 2)], FIRST_Y), 0, h02)
 
         scatter(0, [0, 1], weighted[0][:])
-        up = factor("late_up", wu_columns, 1, HALF, ACT.Copy, [5], UP[0])
-        h = sbuf("h12a", [P, P, PLACES], BF16, EARLY_H)
+        up = factor("late_up", wu_columns, 1, HALF, ACT.Copy, [5])
+        h = sbuf("h12a", [P, P, PLACES], BF16, EARLY_H + 512)
         product_on_gpsimd(gated[:], up[:], h[:])
-        weighted[1] = weigh_on_gpsimd(1, [0, 1], add_bias(1, [0, 1], [0, 4]), UP[0])
-        target = codes_of([(1, 2)])
+        weigh_on_gpsimd([1], add_bias(1, [1], [0], EARLY_H + 1536), weighted[1][:, GROUP:])
+        weighted[2] = sbuf("y_weighted2", [P, HALF], F32, EARLY_H + 2432)
+        weigh_in_bank(2, [0], down(2, [0], 1), weighted[2][:, :GROUP])
+        target = codes_of([(1, 2)], scales_offset=EARLY_H + 2048)
         quantize_h(target, 0, h)
 
         scatter(1, [0, 1], weighted[1][:])
         gated = factor("late_gate", wg_columns, 1, HALF + P, ACT.Sigmoid, [5])
-        up = factor("late_up", wu_columns, 1, HALF + P, ACT.Copy, [0], UP[3])
+        up = factor("late_up", wu_columns, 1, HALF + P, ACT.Copy, [4])
         h = sbuf("h12b", [P, P, PLACES], BF16, EARLY_H)
         product_on_gpsimd(gated[:], up[:], h[:])
-        weighted[2] = weigh_on_gpsimd(2, [0, 1], add_bias(2, [0, 1], [1, 2]), UP[3])
+        weigh_on_gpsimd([1], add_bias(2, [1], [2], EARLY_H + 1024), weighted[2][:, GROUP:])
         y = down(3, [1], 7)
         quantize_h(target, P, h)
 
         scatter(2, [0, 1], weighted[2][:])
-        gated = factor("late_gate", wg_columns, 0, 3 * GROUP, ACT.Sigmoid, (3, 4))
-        up = factor("late_up", wu_columns, 0, 3 * GROUP, ACT.Copy, (1, 2), UP[1])
+        gated = factor("late_gate", wg_columns, 0, 3 * GROUP, ACT.Sigmoid, (3, 0))
+        up = factor("late_up", wu_columns, 0, 3 * GROUP, ACT.Copy, (5, 4), UP[0])
         h = sbuf("h03", [P, GROUP, PLACES], BF16, EARLY_H)
         product_on_gpsimd(gated[:], up[:], h[:])
-        weighted[3] = sbuf("y_weighted3", [P, HALF], F32, UP[1])
-        gated = factor("late_gate", wg_columns, 1, 3 * GROUP, ACT.Sigmoid, (5, 0))
-        up = factor("late_up", wu_columns, 1, 3 * GROUP, ACT.Copy, (3, 4), UP[2])
+        weighted[3] = sbuf("y_weighted3", [P, HALF], F32, UP[0])
+        gated = factor("late_gate", wg_columns, 1, 3 * GROUP, ACT.Sigmoid, (1, 2))
+        up = factor("late_up", wu_columns, 1, 3 * GROUP, ACT.Copy, (3, 0), UP[1])
         for c, y in enumerate((y, down(3, [2], 6))):
-            target = weighted[3][:, GROUP * c : GROUP * (c + 1)]
-            nc.vector.scalar_tensor_tensor(target, y, bias[:, 3:4], weights([1 + c]), ADD, MULT)
+            weigh_in_bank(3, [1 + c], y, weighted[3][:, GROUP * c : GROUP * (c + 1)])
         quantize_h(codes_of([(0, 3)]), 0, h)
 
         scatter(3, [1, 2], weighted[3][:])
@@ -380,7 +379,7 @@ def tile_list_modp_gsigm_res_noneb_kernel(
         product_on_gpsimd(gated[:], up[:], h[:])
         quantize_h(codes_of([(1, 3)]), 0, h)
 
-        weigh_and_scatter(0, [2], add_bias(0, [2], [1], UP[2]))
-        for n, groups, number in ((3, [3], 2), (0, [3], 0), (1, [2, 3], 5), (2, [2, 3], 7)):
+        weigh_and_scatter(0, [2], add_bias(0, [2], [5], UP[1]))
+        for n, groups, number in ((3, [3], 4), (0, [3], 1), (1, [2, 3], 2), (2, [2, 3], 7)):
             weigh_and_scatter(n, groups, add_bias(n, groups, [number]))
             store(n)

@@ -27,15 +27,17 @@ GROUP = 256
 BANK = 2048
 KIB = 1024
 BLOCK = 8 * KIB
+DENSE_ROWS = 96
 WARM_UPS = 4
-TABLE_ROWS = 96
 
 ROWS = {3: 0, 0: BLOCK, 1: 2 * BLOCK, 2: 3 * BLOCK}
-RAW_11 = 34 * KIB
-EARLY_H = 54 * KIB
+LAST_WU = 34 * KIB
 TOKEN_WORDS = 42 * KIB
 FIRST_Y = 44 * KIB
-UP = [46 * KIB, 50 * KIB]
+LATE_UP = [46 * KIB, 50 * KIB]
+EARLY_H = 54 * KIB
+HALF_GATE, HALF_UP = 56 * KIB, 58 * KIB
+LATE_H = 60 * KIB
 
 
 def tile_list_modp_gsigm_res_noneb_kernel(
@@ -60,7 +62,8 @@ def tile_list_modp_gsigm_res_noneb_kernel(
 
         def load_scales(tile, src):
             for r in range(4):
-                nc.sync.dma_start(out=tile[r:P:QUADRANT], in_=src[:, r:16:4, :].rearrange("a q x -> q a x").bitcast(I32))
+                rows_r = src[:, r:16:4, :].rearrange("a q x -> q a x")
+                nc.sync.dma_start(out=tile[r:P:QUADRANT], in_=rows_r.bitcast(I32))
 
         def zeroed_rows(n):
             rows[n] = sbuf(f"rows{n}", [P, T], F32, ROWS[n])
@@ -86,7 +89,7 @@ def tile_list_modp_gsigm_res_noneb_kernel(
         wg_s = sbuf("wg_s", [P, 2, 2, PLACES, P], U8)
         nc.vector.memset(wg_s[:].bitcast(I32), 0)
         tab_s = sbuf("tab_s", [P, T // 4], I32)
-        nc.vector.memset(tab_s[:TABLE_ROWS], 0)
+        nc.vector.memset(tab_s[:DENSE_ROWS], 0)
         tok_s = sbuf("tok_s", [P, 2, J], U8)
         nc.vector.memset(tok_s[:].bitcast(I32), 0)
         wd_s = sbuf("wd_s", [P, 2, 2, N // 4], I32)
@@ -100,14 +103,13 @@ def tile_list_modp_gsigm_res_noneb_kernel(
                 in_=wg_scales[a].rearrange("b (r x) -> (b r) x", r=2).bitcast(I32),
             )
         nc.scalar.activation(out=warm[:, 1:2], in_=warm[:, 0:1], func=ACT.Sigmoid)
-        nc.sync.dma_start(out=tab_s[TABLE_ROWS:, :], in_=tab_scales.rearrange("a b x -> b a x").bitcast(I32))
+        nc.sync.dma_start(out=tab_s[DENSE_ROWS:, :], in_=tab_scales.rearrange("a b x -> b a x").bitcast(I32))
         wg_raw = [load_wg(0)]
         tab_w = sbuf("tab_w", [P, T], I32)
         nc.sync.dma_start(out=tab_w[:], in_=tab_words[0].rearrange("p t x -> p (t x)").bitcast(I32))
         wg_s_ordered = sbuf("wg_s_ordered", [P, PLACES, P], U8)
         by_place = wg_s_rows[:].bitcast(U8).rearrange("p (m t) -> p t m", t=PLACES)
         nc.vector.tensor_copy(out=wg_s_ordered[:], in_=by_place)
-
         for q in range(P // QUADRANT):
             nc.sync.dma_start(
                 out=wg_s[QUADRANT * q : QUADRANT * q + 4].rearrange("p r a t m -> p (r a t m)").bitcast(I32),
@@ -120,12 +122,12 @@ def tile_list_modp_gsigm_res_noneb_kernel(
         for q in range(P // QUADRANT):
             nc.sync.dma_start(
                 out=tok_s[QUADRANT * q : QUADRANT * q + 4].bitcast(I32),
-                in_=tok_s_rows[TABLE_ROWS + 8 * q : TABLE_ROWS + 8 * q + 8, :].bitcast(I32),
+                in_=tok_s_rows[DENSE_ROWS + 8 * q : DENSE_ROWS + 8 * q + 8, :].bitcast(I32),
             )
         wu_raw[0, 1] = load_wu(0, 1)
         wg_raw.append(load_wg(1))
         wu_raw[1, 0] = load_wu(1, 0)
-        wu_raw[1, 1] = load_wu(1, 1, RAW_11)
+        wu_raw[1, 1] = load_wu(1, 1, LAST_WU)
         wd8_w = sbuf("wd8_w", [P, 2, N], I32)
         nc.sync.dma_start(out=wd8_w[:], in_=wd8_words.rearrange("a p n x -> p a (n x)").bitcast(I32))
         load_scales(wd_s[:, 1], wd8_scales)
@@ -183,8 +185,9 @@ def tile_list_modp_gsigm_res_noneb_kernel(
             return wu_w[key][:, columns].bitcast(FP8X4), wu_s[key][:, columns]
 
         def multiply(acc, stationary, moving, start, stop):
+            (lhs, lhs_scale), (rhs, rhs_scale) = stationary, moving
             nc.tensor.matmul_mx(
-                out=acc, lhsT=stationary[0], lhsT_scale=stationary[1], rhs=moving[0], rhs_scale=moving[1], start=start, stop=stop
+                out=acc, lhsT=lhs, lhsT_scale=lhs_scale, rhs=rhs, rhs_scale=rhs_scale, start=start, stop=stop
             )
 
         def gates(rb, first, count, banks, offset=None):
@@ -216,12 +219,13 @@ def tile_list_modp_gsigm_res_noneb_kernel(
                 MULT,
             )
 
-        def codes_of(keys, offset=None, scales_offset=None):
+        def codes_of(keys, offset=None):
             name = "_".join(f"{rb}{g}" for rb, g in keys)
             words = sbuf(f"h_w{name}", [P, GROUP * len(keys)], U32, offset)
-            scales = sbuf(f"h_s{name}", [P, GROUP * len(keys)], U8, scales_offset)
+            scales = sbuf(f"h_s{name}", [P, GROUP * len(keys)], U8)
             for c, key in enumerate(keys):
-                codes[key] = words[:, GROUP * c : GROUP * (c + 1)].bitcast(FP8X4), scales[:, GROUP * c : GROUP * (c + 1)]
+                tokens = slice(GROUP * c, GROUP * (c + 1))
+                codes[key] = words[:, tokens].bitcast(FP8X4), scales[:, tokens]
             return words, scales
 
         def quantize_h(target, first, h):
@@ -233,8 +237,9 @@ def tile_list_modp_gsigm_res_noneb_kernel(
 
         def down(n, groups, number):
             y = bank(f"y{n}{groups[0]}", [P, len(groups), GROUP], number)
-            wd4 = [(wd4_w[:].bitcast(U8)[:, rb, 2 * P * n : 2 * P * (n + 1)].bitcast(FP4X4), wd4_s[:, rb, P * n : P * (n + 1)]) for rb in range(2)]
-            wd8 = [(wd8_w[:, rb, P * n : P * (n + 1)].bitcast(FP8X4), wd8_s[:, rb, P * n : P * (n + 1)]) for rb in range(2)]
+            columns, packed = slice(P * n, P * (n + 1)), slice(2 * P * n, 2 * P * (n + 1))
+            wd4 = [(wd4_w[:].bitcast(U8)[:, rb, packed].bitcast(FP4X4), wd4_s[:, rb, columns]) for rb in range(2)]
+            wd8 = [(wd8_w[:, rb, columns].bitcast(FP8X4), wd8_s[:, rb, columns]) for rb in range(2)]
             for c, g in enumerate(groups):
                 for rb in range(2):
                     multiply(y[:, c, :], wd4[rb], codes[rb, g], rb == 0, False)
@@ -286,9 +291,10 @@ def tile_list_modp_gsigm_res_noneb_kernel(
 
         order_wg_words(0, on_scalar)
         idle = bank("idle", [P, HALF], 0)
-        all_columns = wg_w[0][:, 0].rearrange("p t x -> p (t x)").bitcast(FP4X4), wg_s[:, 0, 0].rearrange("p t m -> p (t m)")
+        all_words = wg_w[0][:, 0].rearrange("p t x -> p (t x)").bitcast(FP4X4)
+        all_scales = wg_s[:, 0, 0].rearrange("p t m -> p (t m)")
         for t in range(WARM_UPS):
-            multiply(idle[:], wg_columns(0, 0, t % PLACES), all_columns, True, True)
+            multiply(idle[:], wg_columns(0, 0, t), (all_words, all_scales), True, True)
         for half in range(2):
             part_words(half, gather_words(half))
         round_wu(0, 0, 0, on_scalar)
@@ -315,13 +321,14 @@ def tile_list_modp_gsigm_res_noneb_kernel(
         quantize_wu(1, 0, 2)
         round_wu(1, 1, 2, on_scalar, EARLY_H)
         round_wu(1, 1, 0, on_vector, ROWS[1])
-        gates(1, 0, GROUP, (1, 2), RAW_11 - 2 * KIB)
+        gates(1, 0, GROUP, (1, 2), LAST_WU - 2 * KIB)
         (filler,) = four_places("ub", wu_columns, 0, [HALF], [7])
         quantize_wu(1, 1, 2)
         quantize_wu(1, 1, 0)
         zeroed_rows(1)
-        gates(1, GROUP, GROUP, (3, 4), RAW_11 + 2 * KIB)
-        gated = factor("late_gate", wg_columns, 1, HALF, ACT.Sigmoid, [0], RAW_11 + 6 * KIB)
+
+        gates(1, GROUP, GROUP, (3, 4), LAST_WU + 2 * KIB)
+        gated = factor("late_gate", wg_columns, 1, HALF, ACT.Sigmoid, [0], LAST_WU + 6 * KIB)
         h02 = sbuf("h02", [P, GROUP, PLACES], BF16, EARLY_H)
         product(0, HALF, filler, h02[:, :P])
         h10 = sbuf("h10", [P, GROUP, PLACES], BF16)
@@ -338,48 +345,48 @@ def tile_list_modp_gsigm_res_noneb_kernel(
         zeroed_rows(2)
 
         weigh_and_scatter(3, [0], add_bias(3, [0], [5], FIRST_Y))
-        weighted = {n: sbuf(f"y_weighted{n}", [P, HALF], F32) for n in range(2)}
+        weighted = {n: sbuf(f"y_weighted{n}", [P, HALF], F32, offset) for n, offset in enumerate((LATE_H, None))}
         weigh_in_bank(0, [0, 1], down(0, [0, 1], 3), weighted[0][:])
         weigh_in_bank(1, [0], down(1, [0], 4), weighted[1][:, :GROUP])
         quantize_h(codes_of([(0, 2)], FIRST_Y), 0, h02)
 
         scatter(0, [0, 1], weighted[0][:])
         up = factor("late_up", wu_columns, 1, HALF, ACT.Copy, [5])
-        h = sbuf("h12a", [P, P, PLACES], BF16, EARLY_H + 512)
-        product_on_gpsimd(gated[:], up[:], h[:])
-        weigh_on_gpsimd([1], add_bias(1, [1], [0], EARLY_H + 1536), weighted[1][:, GROUP:])
-        weighted[2] = sbuf("y_weighted2", [P, HALF], F32, EARLY_H + 2432)
-        weigh_in_bank(2, [0], down(2, [0], 1), weighted[2][:, :GROUP])
-        target = codes_of([(1, 2)], scales_offset=EARLY_H + 2048)
-        quantize_h(target, 0, h)
+        first_half = sbuf("h12a", [P, P, PLACES], BF16, EARLY_H)
+        product_on_gpsimd(gated[:], up[:], first_half[:])
+        weigh_on_gpsimd([1], add_bias(1, [1], [0], EARLY_H + KIB), weighted[1][:, GROUP:])
 
         scatter(1, [0, 1], weighted[1][:])
-        gated = factor("late_gate", wg_columns, 1, HALF + P, ACT.Sigmoid, [5])
-        up = factor("late_up", wu_columns, 1, HALF + P, ACT.Copy, [4])
-        h = sbuf("h12b", [P, P, PLACES], BF16, EARLY_H)
+        gated = factor("late_gate", wg_columns, 1, HALF + P, ACT.Sigmoid, [5], HALF_GATE)
+        up = factor("late_up", wu_columns, 1, HALF + P, ACT.Copy, [4], HALF_UP)
+        h = sbuf("h12b", [P, P, PLACES], BF16, LATE_H)
         product_on_gpsimd(gated[:], up[:], h[:])
-        weigh_on_gpsimd([1], add_bias(2, [1], [2], EARLY_H + 1024), weighted[2][:, GROUP:])
+        weighted[2] = sbuf("y_weighted2", [P, HALF], F32, HALF_UP)
+        weigh_on_gpsimd([1], add_bias(2, [1], [2]), weighted[2][:, GROUP:])
+        weigh_in_bank(2, [0], down(2, [0], 1), weighted[2][:, :GROUP])
         y = down(3, [1], 7)
+        target = codes_of([(1, 2)], HALF_GATE)
+        quantize_h(target, 0, first_half)
         quantize_h(target, P, h)
 
         scatter(2, [0, 1], weighted[2][:])
         gated = factor("late_gate", wg_columns, 0, 3 * GROUP, ACT.Sigmoid, (3, 0))
-        up = factor("late_up", wu_columns, 0, 3 * GROUP, ACT.Copy, (5, 4), UP[0])
-        h = sbuf("h03", [P, GROUP, PLACES], BF16, EARLY_H)
+        up = factor("late_up", wu_columns, 0, 3 * GROUP, ACT.Copy, (5, 4), LATE_UP[0])
+        h = sbuf("h03", [P, GROUP, PLACES], BF16, LATE_H)
         product_on_gpsimd(gated[:], up[:], h[:])
-        weighted[3] = sbuf("y_weighted3", [P, HALF], F32, UP[0])
-        gated = factor("late_gate", wg_columns, 1, 3 * GROUP, ACT.Sigmoid, (1, 2))
-        up = factor("late_up", wu_columns, 1, 3 * GROUP, ACT.Copy, (3, 0), UP[1])
+        weighted[3] = sbuf("y_weighted3", [P, HALF], F32, LATE_UP[0])
+        gated = factor("late_gate", wg_columns, 1, 3 * GROUP, ACT.Sigmoid, (2, 3))
+        up = factor("late_up", wu_columns, 1, 3 * GROUP, ACT.Copy, (0, 5), LATE_UP[1])
         for c, y in enumerate((y, down(3, [2], 6))):
             weigh_in_bank(3, [1 + c], y, weighted[3][:, GROUP * c : GROUP * (c + 1)])
         quantize_h(codes_of([(0, 3)]), 0, h)
 
         scatter(3, [1, 2], weighted[3][:])
-        h = sbuf("h13", [P, GROUP, PLACES], BF16, EARLY_H)
+        h = sbuf("h13", [P, GROUP, PLACES], BF16, LATE_H)
         product_on_gpsimd(gated[:], up[:], h[:])
         quantize_h(codes_of([(1, 3)]), 0, h)
 
-        weigh_and_scatter(0, [2], add_bias(0, [2], [5], UP[1]))
-        for n, groups, number in ((3, [3], 4), (0, [3], 1), (1, [2, 3], 2), (2, [2, 3], 7)):
+        weigh_and_scatter(0, [2], add_bias(0, [2], [4], LATE_UP[1]))
+        for n, groups, number in ((3, [3], 2), (0, [3], 1), (1, [2, 3], 3), (2, [2, 3], 7)):
             weigh_and_scatter(n, groups, add_bias(n, groups, [number]))
             store(n)

@@ -30,14 +30,12 @@ BLOCK = 8 * KIB
 DENSE_ROWS = 96
 WARM_UPS = 4
 
-ROWS = {3: 0, 0: BLOCK, 1: 2 * BLOCK, 2: 3 * BLOCK}
-LAST_WU = 34 * KIB
-TOKEN_WORDS = 42 * KIB
-FIRST_Y = 44 * KIB
-LATE_UP = [46 * KIB, 50 * KIB]
-EARLY_H = 54 * KIB
-HALF_GATE, HALF_UP = 56 * KIB, 58 * KIB
-LATE_H = 60 * KIB
+ROWS = {0: None, 1: 0, 2: BLOCK, 3: 2 * BLOCK}
+LAST_WU = 26 * KIB
+TOKEN_WORDS = 36 * KIB
+EARLY_H = 38 * KIB
+LATE_H = 40 * KIB
+LAST_UP = 42 * KIB
 
 
 def tile_list_modp_gsigm_res_noneb_kernel(
@@ -65,9 +63,9 @@ def tile_list_modp_gsigm_res_noneb_kernel(
                 rows_r = src[:, r:16:4, :].rearrange("a q x -> q a x")
                 nc.sync.dma_start(out=tile[r:P:QUADRANT], in_=rows_r.bitcast(I32))
 
-        def zeroed_rows(n):
+        def zeroed_rows(n, engine):
             rows[n] = sbuf(f"rows{n}", [P, T], F32, ROWS[n])
-            nc.gpsimd.memset(rows[n][:].bitcast(I32), 0)
+            engine.memset(rows[n][:].bitcast(I32), 0)
 
         def load_wg(rb):
             raw = sbuf(f"wg_raw{rb}", [P, 2, PASS // 2], I32)
@@ -84,7 +82,7 @@ def tile_list_modp_gsigm_res_noneb_kernel(
         rows = {}
         warm = sbuf("warm", [P, 2], F32)
         nc.vector.memset(warm[:, 0:1], 0.0)
-        wg_s_rows = sbuf("wg_s_rows", [P, PASS // 4], I32, ROWS[3])
+        wg_s_rows = sbuf("wg_s_rows", [P, PASS // 4], I32, ROWS[1])
         nc.vector.memset(wg_s_rows[2 * QUADRANT :], 0)
         wg_s = sbuf("wg_s", [P, 2, 2, PLACES, P], U8)
         nc.vector.memset(wg_s[:].bitcast(I32), 0)
@@ -94,6 +92,7 @@ def tile_list_modp_gsigm_res_noneb_kernel(
         nc.vector.memset(tok_s[:].bitcast(I32), 0)
         wd_s = sbuf("wd_s", [P, 2, 2, N // 4], I32)
         nc.vector.memset(wd_s[:], 0)
+        zeroed_rows(0, nc.vector)
 
         offsets = keep.tile([P, J // LIST_COLUMN], U16, name="offsets")
         nc.sync.dma_start(offsets[:], offs)
@@ -115,7 +114,7 @@ def tile_list_modp_gsigm_res_noneb_kernel(
                 out=wg_s[QUADRANT * q : QUADRANT * q + 4].rearrange("p r a t m -> p (r a t m)").bitcast(I32),
                 in_=wg_s_ordered[16 * q : 16 * q + 16].rearrange("p t m -> p (t m)").bitcast(I32),
             )
-        zeroed_rows(3)
+        zeroed_rows(1, nc.gpsimd)
         wu_raw = {(0, 0): load_wu(0, 0)}
         tok_s_rows = sbuf("tok_s_rows", [P, J], U8)
         nc.vector.tensor_copy(tok_s_rows[:], tab_s[:].bitcast(U8).indirect(offsets[:]))
@@ -235,24 +234,21 @@ def tile_list_modp_gsigm_res_noneb_kernel(
                 out=words[:, tokens].bitcast(FP8X4), scales=scales[:, tokens], in_=h[:].rearrange("p j t -> p (j t)")
             )
 
-        def down(n, groups, number):
+        def down(n, groups, number, halves=(1, 0)):
             y = bank(f"y{n}{groups[0]}", [P, len(groups), GROUP], number)
             columns, packed = slice(P * n, P * (n + 1)), slice(2 * P * n, 2 * P * (n + 1))
             wd4 = [(wd4_w[:].bitcast(U8)[:, rb, packed].bitcast(FP4X4), wd4_s[:, rb, columns]) for rb in range(2)]
             wd8 = [(wd8_w[:, rb, columns].bitcast(FP8X4), wd8_s[:, rb, columns]) for rb in range(2)]
             for c, g in enumerate(groups):
-                for rb in range(2):
-                    multiply(y[:, c, :], wd4[rb], codes[rb, g], rb == 0, False)
-                    multiply(y[:, c, :], wd8[rb], codes[rb, g], False, rb == 1)
+                for rb in halves:
+                    multiply(y[:, c, :], wd4[rb], codes[rb, g], rb == halves[0], False)
+                    multiply(y[:, c, :], wd8[rb], codes[rb, g], False, rb == halves[1])
             return y[:].rearrange("p c j -> p (c j)")
 
-        def add_bias(n, groups, banks, offset=None):
+        def add_bias(n, groups, number, offset=None, halves=(1, 0)):
             biased = sbuf(f"y_biased{n}{groups[0]}", [P, GROUP * len(groups)], F32, offset)
-            share = len(groups) // len(banks)
-            for c, number in zip(range(0, len(groups), share), banks):
-                y = down(n, groups[c : c + share], number)
-                target = biased[:, GROUP * c : GROUP * (c + share)]
-                nc.scalar.activation(out=target, in_=y, func=ACT.Identity, bias=bias[:, n : n + 1])
+            y = down(n, groups, number, halves)
+            nc.scalar.activation(out=biased[:], in_=y, func=ACT.Identity, bias=bias[:, n : n + 1])
             return biased
 
         def weights(groups):
@@ -264,14 +260,16 @@ def tile_list_modp_gsigm_res_noneb_kernel(
         def weigh_and_scatter(n, groups, biased):
             nc.vector.tensor_tensor(window(n, groups), biased[:], weights(groups), MULT)
 
-        def weigh_in_bank(n, groups, y, target):
-            nc.vector.scalar_tensor_tensor(target, y, bias[:, n : n + 1], weights(groups), ADD, MULT)
+        def weigh_in_bank(n, g, y):
+            weighted = sbuf(f"y_weighted{n}{g}", [P, GROUP], F32)
+            nc.vector.scalar_tensor_tensor(weighted[:], y, bias[:, n : n + 1], weights([g]), ADD, MULT)
+            return weighted
 
-        def weigh_on_gpsimd(groups, biased, target):
-            nc.gpsimd.tensor_tensor(target, biased[:], weights(groups), MULT)
-
-        def scatter(n, groups, weighted):
-            nc.vector.tensor_copy(window(n, groups), weighted)
+        def weigh_on_gpsimd_and_scatter(n, g, number):
+            biased = add_bias(n, [g], number)
+            weighted = sbuf(f"y_weighted{n}{g}", [P, GROUP], F32)
+            nc.gpsimd.tensor_tensor(weighted[:], biased[:], weights([g]), MULT)
+            nc.vector.tensor_copy(window(n, [g]), weighted[:])
 
         def factor(name, columns, rb, first, func, banks, offset=None):
             values = sbuf(f"{name}{rb}{first}", [P, P * len(banks), PLACES], F32, offset)
@@ -280,9 +278,11 @@ def tile_list_modp_gsigm_res_noneb_kernel(
                 nc.scalar.activation(out=values[:, j0 : j0 + P, :], in_=acc[:].rearrange("p t j -> p j t"), func=func)
             return values
 
-        def product_on_gpsimd(gated, up, h):
+        def group_on_gpsimd(rb, g, gated, up):
             flat = "p j t -> p (j t)"
-            nc.gpsimd.tensor_tensor(h.rearrange(flat), gated.rearrange(flat), up.rearrange(flat), MULT)
+            h = sbuf(f"h{rb}{g}", [P, GROUP, PLACES], BF16, LATE_H)
+            nc.gpsimd.tensor_tensor(h[:].rearrange(flat), gated[:].rearrange(flat), up[:].rearrange(flat), MULT)
+            quantize_h(codes_of([(rb, g)]), 0, h)
 
         def store(n):
             nc.sync.dma_start(out=out[P * n : P * (n + 1), :], in_=rows[n][:])
@@ -304,11 +304,11 @@ def tile_list_modp_gsigm_res_noneb_kernel(
         quantize_wu(0, 0, 0)
         quantize_wu(0, 0, 2)
         round_wu(0, 1, 0, on_vector)
-        round_wu(0, 1, 2, on_vector, ROWS[0])
+        round_wu(0, 1, 2, on_vector, ROWS[2])
         quantize_wu(0, 1, 0)
         quantize_wu(0, 1, 2)
         order_wg_words(1, on_vector)
-        zeroed_rows(0)
+        zeroed_rows(2, nc.gpsimd)
 
         h = sbuf("h00", [P, HALF, PLACES], BF16)
         for firsts, banks in (((0, P), (7, 0)), ((2 * P, 3 * P), (5, 6))):
@@ -320,73 +320,45 @@ def tile_list_modp_gsigm_res_noneb_kernel(
         quantize_h(codes_of([(0, 0), (0, 1)]), 0, h)
         quantize_wu(1, 0, 2)
         round_wu(1, 1, 2, on_scalar, EARLY_H)
-        round_wu(1, 1, 0, on_vector, ROWS[1])
+        round_wu(1, 1, 0, on_vector, ROWS[3])
         gates(1, 0, GROUP, (1, 2), LAST_WU - 2 * KIB)
         (filler,) = four_places("ub", wu_columns, 0, [HALF], [7])
         quantize_wu(1, 1, 2)
         quantize_wu(1, 1, 0)
-        zeroed_rows(1)
+        zeroed_rows(3, nc.gpsimd)
 
         gates(1, GROUP, GROUP, (3, 4), LAST_WU + 2 * KIB)
-        gated = factor("late_gate", wg_columns, 1, HALF, ACT.Sigmoid, [0], LAST_WU + 6 * KIB)
         h02 = sbuf("h02", [P, GROUP, PLACES], BF16, EARLY_H)
         product(0, HALF, filler, h02[:, :P])
         h10 = sbuf("h10", [P, GROUP, PLACES], BF16)
         for first, ub in zip((0, P), four_places("ub", wu_columns, 1, (0, P), (5, 6), (2, 3, 0, 1))):
             product(1, first, ub, h10[:, first : first + P])
-        h11 = sbuf("h11", [P, GROUP, PLACES], BF16, ROWS[2])
+        h11 = sbuf("h11", [P, GROUP, PLACES], BF16)
         ubs = four_places("ub", wu_columns, 1, (GROUP, GROUP + P), (1, 2))
         (filler,) = four_places("ub", wu_columns, 0, [HALF + P], [6])
+        gated = factor("late_gate", wg_columns, 1, HALF, ACT.Sigmoid, (0, 7), LAST_WU + 6 * KIB)
         product(1, GROUP, ubs[0], h11[:, :P])
         quantize_h(codes_of([(1, 0)]), 0, h10)
         product(1, GROUP + P, ubs[1], h11[:, P:])
         product(0, HALF + P, filler, h02[:, P:])
         quantize_h(codes_of([(1, 1)]), 0, h11)
-        zeroed_rows(2)
+        weighted = weigh_in_bank(0, 0, down(0, [0], 3, (0, 1)))
+        quantize_h(codes_of([(0, 2)]), 0, h02)
 
-        weigh_and_scatter(3, [0], add_bias(3, [0], [5], FIRST_Y))
-        weighted = {n: sbuf(f"y_weighted{n}", [P, HALF], F32, offset) for n, offset in enumerate((LATE_H, None))}
-        weigh_in_bank(0, [0, 1], down(0, [0, 1], 3), weighted[0][:])
-        weigh_in_bank(1, [0], down(1, [0], 4), weighted[1][:, :GROUP])
-        quantize_h(codes_of([(0, 2)], FIRST_Y), 0, h02)
+        nc.vector.tensor_copy(window(0, [0]), weighted[:])
+        for n, number in ((1, 4), (2, 5), (3, 0)):
+            weigh_on_gpsimd_and_scatter(n, 0, number)
+        group_on_gpsimd(1, 2, gated, factor("late_up", wu_columns, 1, HALF, ACT.Copy, (3, 4)))
+        for n, number in ((0, 1), (1, 2), (2, 6)):
+            weigh_on_gpsimd_and_scatter(n, 1, number)
+        gated = factor("late_gate", wg_columns, 0, 3 * GROUP, ACT.Sigmoid, (5, 0))
+        group_on_gpsimd(0, 3, gated, factor("late_up", wu_columns, 0, 3 * GROUP, ACT.Copy, (3, 4)))
+        weigh_on_gpsimd_and_scatter(3, 1, 5)
+        weigh_on_gpsimd_and_scatter(0, 2, 1)
+        gated = factor("late_gate", wg_columns, 1, 3 * GROUP, ACT.Sigmoid, (2, 6))
+        group_on_gpsimd(1, 3, gated, factor("late_up", wu_columns, 1, 3 * GROUP, ACT.Copy, (0, 3), LAST_UP))
 
-        scatter(0, [0, 1], weighted[0][:])
-        up = factor("late_up", wu_columns, 1, HALF, ACT.Copy, [5])
-        first_half = sbuf("h12a", [P, P, PLACES], BF16, EARLY_H)
-        product_on_gpsimd(gated[:], up[:], first_half[:])
-        weigh_on_gpsimd([1], add_bias(1, [1], [0], EARLY_H + KIB), weighted[1][:, GROUP:])
-
-        scatter(1, [0, 1], weighted[1][:])
-        gated = factor("late_gate", wg_columns, 1, HALF + P, ACT.Sigmoid, [5], HALF_GATE)
-        up = factor("late_up", wu_columns, 1, HALF + P, ACT.Copy, [4], HALF_UP)
-        h = sbuf("h12b", [P, P, PLACES], BF16, LATE_H)
-        product_on_gpsimd(gated[:], up[:], h[:])
-        weighted[2] = sbuf("y_weighted2", [P, HALF], F32, HALF_UP)
-        weigh_on_gpsimd([1], add_bias(2, [1], [2]), weighted[2][:, GROUP:])
-        weigh_in_bank(2, [0], down(2, [0], 1), weighted[2][:, :GROUP])
-        y = down(3, [1], 7)
-        target = codes_of([(1, 2)], HALF_GATE)
-        quantize_h(target, 0, first_half)
-        quantize_h(target, P, h)
-
-        scatter(2, [0, 1], weighted[2][:])
-        gated = factor("late_gate", wg_columns, 0, 3 * GROUP, ACT.Sigmoid, (3, 0))
-        up = factor("late_up", wu_columns, 0, 3 * GROUP, ACT.Copy, (5, 4), LATE_UP[0])
-        h = sbuf("h03", [P, GROUP, PLACES], BF16, LATE_H)
-        product_on_gpsimd(gated[:], up[:], h[:])
-        weighted[3] = sbuf("y_weighted3", [P, HALF], F32, LATE_UP[0])
-        gated = factor("late_gate", wg_columns, 1, 3 * GROUP, ACT.Sigmoid, (2, 3))
-        up = factor("late_up", wu_columns, 1, 3 * GROUP, ACT.Copy, (0, 5), LATE_UP[1])
-        for c, y in enumerate((y, down(3, [2], 6))):
-            weigh_in_bank(3, [1 + c], y, weighted[3][:, GROUP * c : GROUP * (c + 1)])
-        quantize_h(codes_of([(0, 3)]), 0, h)
-
-        scatter(3, [1, 2], weighted[3][:])
-        h = sbuf("h13", [P, GROUP, PLACES], BF16, LATE_H)
-        product_on_gpsimd(gated[:], up[:], h[:])
-        quantize_h(codes_of([(1, 3)]), 0, h)
-
-        weigh_and_scatter(0, [2], add_bias(0, [2], [4], LATE_UP[1]))
-        for n, groups, number in ((3, [3], 2), (0, [3], 1), (1, [2, 3], 3), (2, [2, 3], 7)):
-            weigh_and_scatter(n, groups, add_bias(n, groups, [number]))
+        weigh_and_scatter(1, [2], add_bias(1, [2], 4, LAST_UP))
+        for n, groups, number in ((0, [3], 7), (1, [3], 5), (2, [2, 3], 1), (3, [2, 3], 2)):
+            weigh_and_scatter(n, groups, add_bias(n, groups, number, None, (0, 1)))
             store(n)

@@ -298,7 +298,7 @@ def tile_list_modp_gsigm_res_noneb_kernel(
         for half in range(2):
             part_words(half, gather_words(half))
         round_wu(0, 0, 0, on_scalar)
-        round_wu(0, 0, 2, on_scalar)
+        round_wu(0, 0, 2, on_vector)
         gates(0, 0, HALF, (1, 2, 3, 4))
         gates(0, HALF, GROUP, (5, 6))
         quantize_wu(0, 0, 0)
@@ -311,7 +311,7 @@ def tile_list_modp_gsigm_res_noneb_kernel(
         zeroed_rows(2, nc.gpsimd)
 
         h = sbuf("h00", [P, HALF, PLACES], BF16)
-        for firsts, banks in (((0, P), (7, 0)), ((2 * P, 3 * P), (5, 6))):
+        for firsts, banks in (((0, P), (7, 0)), ((2 * P, 3 * P), (1, 2))):
             for first, ub in zip(firsts, four_places("ub", wu_columns, 0, firsts, banks)):
                 product(0, first, ub, h[:, first : first + P])
         round_wu(1, 0, 0, on_scalar)
@@ -321,44 +321,44 @@ def tile_list_modp_gsigm_res_noneb_kernel(
         quantize_wu(1, 0, 2)
         round_wu(1, 1, 2, on_scalar, EARLY_H)
         round_wu(1, 1, 0, on_vector, ROWS[3])
-        gates(1, 0, GROUP, (1, 2), LAST_WU - 2 * KIB)
+        gates(1, 0, GROUP, (3, 4), LAST_WU - 2 * KIB)
         (filler,) = four_places("ub", wu_columns, 0, [HALF], [7])
         quantize_wu(1, 1, 2)
         quantize_wu(1, 1, 0)
         zeroed_rows(3, nc.gpsimd)
 
-        gates(1, GROUP, GROUP, (3, 4), LAST_WU + 2 * KIB)
+        gates(1, GROUP, GROUP, (5, 6), LAST_WU + 2 * KIB)
         h02 = sbuf("h02", [P, GROUP, PLACES], BF16, EARLY_H)
         product(0, HALF, filler, h02[:, :P])
         h10 = sbuf("h10", [P, GROUP, PLACES], BF16)
-        for first, ub in zip((0, P), four_places("ub", wu_columns, 1, (0, P), (5, 6), (2, 3, 0, 1))):
+        for first, ub in zip((0, P), four_places("ub", wu_columns, 1, (0, P), (0, 1), (2, 3, 0, 1))):
             product(1, first, ub, h10[:, first : first + P])
         h11 = sbuf("h11", [P, GROUP, PLACES], BF16)
-        ubs = four_places("ub", wu_columns, 1, (GROUP, GROUP + P), (1, 2))
-        (filler,) = four_places("ub", wu_columns, 0, [HALF + P], [6])
-        gated = factor("late_gate", wg_columns, 1, HALF, ACT.Sigmoid, (0, 7), LAST_WU + 6 * KIB)
+        ubs = four_places("ub", wu_columns, 1, (GROUP, GROUP + P), (2, 3))
+        (filler,) = four_places("ub", wu_columns, 0, [HALF + P], [7])
+        gated = factor("late_gate", wg_columns, 1, HALF, ACT.Sigmoid, (4, 5), LAST_WU + 6 * KIB)
         product(1, GROUP, ubs[0], h11[:, :P])
         quantize_h(codes_of([(1, 0)]), 0, h10)
         product(1, GROUP + P, ubs[1], h11[:, P:])
         product(0, HALF + P, filler, h02[:, P:])
         quantize_h(codes_of([(1, 1)]), 0, h11)
-        weighted = weigh_in_bank(0, 0, down(0, [0], 3, (0, 1)))
+        weighted = weigh_in_bank(0, 0, down(0, [0], 6, (0, 1)))
         quantize_h(codes_of([(0, 2)]), 0, h02)
 
         nc.vector.tensor_copy(window(0, [0]), weighted[:])
-        for n, number in ((1, 4), (2, 5), (3, 0)):
+        for n, number in ((1, 0), (2, 1), (3, 2)):
             weigh_on_gpsimd_and_scatter(n, 0, number)
-        group_on_gpsimd(1, 2, gated, factor("late_up", wu_columns, 1, HALF, ACT.Copy, (3, 4)))
-        for n, number in ((0, 1), (1, 2), (2, 6)):
+        group_on_gpsimd(1, 2, gated, factor("late_up", wu_columns, 1, HALF, ACT.Copy, (6, 0)))
+        for n, number in ((0, 3), (1, 7), (2, 4)):
             weigh_on_gpsimd_and_scatter(n, 1, number)
-        gated = factor("late_gate", wg_columns, 0, 3 * GROUP, ACT.Sigmoid, (5, 0))
-        group_on_gpsimd(0, 3, gated, factor("late_up", wu_columns, 0, 3 * GROUP, ACT.Copy, (3, 4)))
-        weigh_on_gpsimd_and_scatter(3, 1, 5)
-        weigh_on_gpsimd_and_scatter(0, 2, 1)
-        gated = factor("late_gate", wg_columns, 1, 3 * GROUP, ACT.Sigmoid, (2, 6))
-        group_on_gpsimd(1, 3, gated, factor("late_up", wu_columns, 1, 3 * GROUP, ACT.Copy, (0, 3), LAST_UP))
+        gated = factor("late_gate", wg_columns, 0, 3 * GROUP, ACT.Sigmoid, (1, 2))
+        group_on_gpsimd(0, 3, gated, factor("late_up", wu_columns, 0, 3 * GROUP, ACT.Copy, (6, 0)))
+        weigh_on_gpsimd_and_scatter(3, 1, 1)
+        weigh_on_gpsimd_and_scatter(0, 2, 3)
+        gated = factor("late_gate", wg_columns, 1, 3 * GROUP, ACT.Sigmoid, (7, 4))
+        group_on_gpsimd(1, 3, gated, factor("late_up", wu_columns, 1, 3 * GROUP, ACT.Copy, (2, 6), LAST_UP))
 
-        weigh_and_scatter(1, [2], add_bias(1, [2], 4, LAST_UP))
-        for n, groups, number in ((0, [3], 7), (1, [3], 5), (2, [2, 3], 1), (3, [2, 3], 2)):
+        weigh_and_scatter(1, [2], add_bias(1, [2], 0, LAST_UP))
+        for n, groups, number in ((0, [3], 5), (1, [3], 1), (2, [2, 3], 3), (3, [2, 3], 7)):
             weigh_and_scatter(n, groups, add_bias(n, groups, number, None, (0, 1)))
             store(n)

@@ -30,12 +30,12 @@ BLOCK = 8 * KIB
 DENSE_ROWS = 96
 WARM_UPS = 4
 
-ROWS = {0: None, 1: 0, 2: BLOCK, 3: 2 * BLOCK}
-LAST_WU = 26 * KIB
-TOKEN_WORDS = 36 * KIB
-EARLY_H = 38 * KIB
-LATE_H = 40 * KIB
-LAST_UP = 42 * KIB
+ROWS = [0, BLOCK, 2 * BLOCK, 3 * BLOCK]
+EARLY_H = 4 * BLOCK
+SECOND_WU = 34 * KIB
+LAST_WU = 44 * KIB
+LATE_H = {(1, 2): 51 * KIB, (0, 3): 50 * KIB, (1, 3): 49 * KIB}
+LAST_UP = 54 * KIB
 
 
 def tile_list_modp_gsigm_res_noneb_kernel(
@@ -67,15 +67,15 @@ def tile_list_modp_gsigm_res_noneb_kernel(
             rows[n] = sbuf(f"rows{n}", [P, T], F32, ROWS[n])
             engine.memset(rows[n][:].bitcast(I32), 0)
 
-        def load_wg(rb):
-            raw = sbuf(f"wg_raw{rb}", [P, 2, PASS // 2], I32)
+        def load_wg(rb, offset=None):
+            raw = sbuf(f"wg_raw{rb}", [P, 2, PASS // 2], I32, offset)
             columns = wg_words[:, :, 2 * PASS * rb : 2 * PASS * (rb + 1)]
             nc.sync.dma_start(out=raw[:], in_=columns.rearrange("a p x -> p a x").bitcast(I32))
             return raw
 
-        def load_wu(rb, a, offset=None):
-            raw = sbuf(f"wu_raw{rb}{a}", [P, PLACES, PASS], F32, offset)
-            block = wu[PASS * a : PASS * (a + 1), PASS * rb : PASS * (rb + 1)]
+        def load_wu(rb, a, offset=None, first=0, count=PASS):
+            raw = sbuf(f"wu_raw{rb}{a}{first}", [P, PLACES, count], F32, offset)
+            block = wu[PASS * a : PASS * (a + 1), PASS * rb + first : PASS * rb + first + count]
             nc.sync.dma_start(out=raw[:], in_=block.rearrange("(p i) c -> p i c", i=PLACES))
             return raw
 
@@ -86,13 +86,12 @@ def tile_list_modp_gsigm_res_noneb_kernel(
         nc.vector.memset(wg_s_rows[2 * QUADRANT :], 0)
         wg_s = sbuf("wg_s", [P, 2, 2, PLACES, P], U8)
         nc.vector.memset(wg_s[:].bitcast(I32), 0)
-        tab_s = sbuf("tab_s", [P, T // 4], I32)
+        tab_s = sbuf("tab_s", [P, T // 4], I32, ROWS[0])
         nc.vector.memset(tab_s[:DENSE_ROWS], 0)
         tok_s = sbuf("tok_s", [P, 2, J], U8)
         nc.vector.memset(tok_s[:].bitcast(I32), 0)
         wd_s = sbuf("wd_s", [P, 2, 2, N // 4], I32)
         nc.vector.memset(wd_s[:], 0)
-        zeroed_rows(0, nc.vector)
 
         offsets = keep.tile([P, J // LIST_COLUMN], U16, name="offsets")
         nc.sync.dma_start(offsets[:], offs)
@@ -118,15 +117,16 @@ def tile_list_modp_gsigm_res_noneb_kernel(
         wu_raw = {(0, 0): load_wu(0, 0)}
         tok_s_rows = sbuf("tok_s_rows", [P, J], U8)
         nc.vector.tensor_copy(tok_s_rows[:], tab_s[:].bitcast(U8).indirect(offsets[:]))
+        zeroed_rows(0, nc.gpsimd)
         for q in range(P // QUADRANT):
             nc.sync.dma_start(
                 out=tok_s[QUADRANT * q : QUADRANT * q + 4].bitcast(I32),
                 in_=tok_s_rows[DENSE_ROWS + 8 * q : DENSE_ROWS + 8 * q + 8, :].bitcast(I32),
             )
-        wu_raw[0, 1] = load_wu(0, 1)
+        wu_raw[0, 1] = load_wu(0, 1, SECOND_WU)
         wg_raw.append(load_wg(1))
         wu_raw[1, 0] = load_wu(1, 0)
-        wu_raw[1, 1] = load_wu(1, 1, LAST_WU)
+        last_wu = [load_wu(1, 1, LAST_WU, 0, PASS // 2), load_wu(1, 1, None, PASS // 2, PASS // 2)]
         wd8_w = sbuf("wd8_w", [P, 2, N], I32)
         nc.sync.dma_start(out=wd8_w[:], in_=wd8_words.rearrange("a p n x -> p a (n x)").bitcast(I32))
         load_scales(wd_s[:, 1], wd8_scales)
@@ -143,13 +143,13 @@ def tile_list_modp_gsigm_res_noneb_kernel(
 
         tok_w, wg_w, rounded, wu_w, wu_s, gate, codes = {}, {}, {}, {}, {}, {}, {}
 
-        def order_wg_words(rb, copy):
-            wg_w[rb] = sbuf(f"wg_w{rb}", [P, 2, PLACES, 2 * P], U8)
+        def order_wg_words(rb, copy, offset=None):
+            wg_w[rb] = sbuf(f"wg_w{rb}", [P, 2, PLACES, 2 * P], U8, offset)
             columns = wg_raw[rb][:].bitcast(U16).rearrange("p a (m t) -> p a t m", t=PLACES)
             copy(out=wg_w[rb][:].bitcast(U16), in_=columns)
 
         def gather_words(half):
-            both = sbuf(f"tok_both{half}", [P, HALF], U32, TOKEN_WORDS)
+            both = sbuf(f"tok_both{half}", [P, HALF], U32)
             nc.vector.tensor_copy(both[:], tab_w[:].bitcast(U32).indirect(listed(half * HALF, HALF)))
             return both
 
@@ -166,6 +166,14 @@ def tile_list_modp_gsigm_res_noneb_kernel(
             rounded[rb, a, t0] = sbuf(f"wu_rounded{rb}{a}{t0}", [P, 2, P, PLACES], BF16, offset)
             source = wu_raw[rb, a][:].rearrange("p i (m t) -> p m i t", t=PLACES)
             copy(out=rounded[rb, a, t0][:].rearrange("p t m i -> p m i t"), in_=source[:, :, :, t0 : t0 + 2])
+
+        def round_last_block(copies, offsets):
+            for t0, offset in zip((0, 2), offsets):
+                rounded[1, 1, t0] = sbuf(f"wu_rounded11{t0}", [P, 2, P, PLACES], BF16, offset)
+                for half, copy in enumerate(copies):
+                    target = rounded[1, 1, t0][:, :, P // 2 * half : P // 2 * (half + 1), :]
+                    source = last_wu[half][:].rearrange("p i (m t) -> p m i t", t=PLACES)
+                    copy(out=target.rearrange("p t m i -> p m i t"), in_=source[:, :, :, t0 : t0 + 2])
 
         def quantize_wu(rb, a, t0):
             wu_w[rb, a, t0] = sbuf(f"wu_w{rb}{a}{t0}", [P, 2 * P], U32)
@@ -265,22 +273,23 @@ def tile_list_modp_gsigm_res_noneb_kernel(
             nc.vector.scalar_tensor_tensor(weighted[:], y, bias[:, n : n + 1], weights([g]), ADD, MULT)
             return weighted
 
-        def weigh_on_gpsimd_and_scatter(n, g, number):
+        def weigh_on_gpsimd_and_scatter(n, g, number, offset=None):
             biased = add_bias(n, [g], number)
-            weighted = sbuf(f"y_weighted{n}{g}", [P, GROUP], F32)
+            weighted = sbuf(f"y_weighted{n}{g}", [P, GROUP], F32, offset)
             nc.gpsimd.tensor_tensor(weighted[:], biased[:], weights([g]), MULT)
             nc.vector.tensor_copy(window(n, [g]), weighted[:])
 
-        def factor(name, columns, rb, first, func, banks, offset=None):
-            values = sbuf(f"{name}{rb}{first}", [P, P * len(banks), PLACES], F32, offset)
-            for j0, number in zip(range(0, P * len(banks), P), banks):
+        def factor(name, columns, rb, first, func, banks, offset=None, values=None, j1=0):
+            if values is None:
+                values = sbuf(f"{name}{rb}{first}", [P, GROUP, PLACES], F32, offset)
+            for j0, number in zip(range(j1, GROUP, P), banks):
                 (acc,) = four_places(name, columns, rb, [first + j0], [number])
                 nc.scalar.activation(out=values[:, j0 : j0 + P, :], in_=acc[:].rearrange("p t j -> p j t"), func=func)
             return values
 
         def group_on_gpsimd(rb, g, gated, up):
             flat = "p j t -> p (j t)"
-            h = sbuf(f"h{rb}{g}", [P, GROUP, PLACES], BF16, LATE_H)
+            h = sbuf(f"h{rb}{g}", [P, GROUP, PLACES], BF16, LATE_H[rb, g])
             nc.gpsimd.tensor_tensor(h[:].rearrange(flat), gated[:].rearrange(flat), up[:].rearrange(flat), MULT)
             quantize_h(codes_of([(rb, g)]), 0, h)
 
@@ -295,19 +304,20 @@ def tile_list_modp_gsigm_res_noneb_kernel(
         all_scales = wg_s[:, 0, 0].rearrange("p t m -> p (t m)")
         for t in range(WARM_UPS):
             multiply(idle[:], wg_columns(0, 0, t), (all_words, all_scales), True, True)
-        for half in range(2):
-            part_words(half, gather_words(half))
+        for half, both in enumerate([gather_words(half) for half in range(2)]):
+            part_words(half, both)
         round_wu(0, 0, 0, on_scalar)
         round_wu(0, 0, 2, on_vector)
-        gates(0, 0, HALF, (1, 2, 3, 4))
-        gates(0, HALF, GROUP, (5, 6))
+        gates(0, 0, GROUP, (1, 2))
         quantize_wu(0, 0, 0)
         quantize_wu(0, 0, 2)
         round_wu(0, 1, 0, on_vector)
-        round_wu(0, 1, 2, on_vector, ROWS[2])
+        order_wg_words(1, on_vector)
+        round_wu(0, 1, 2, on_scalar, ROWS[2])
+        gates(0, GROUP, GROUP, (3, 4), SECOND_WU)
+        gates(0, HALF, GROUP, (5, 6), SECOND_WU + 4 * KIB)
         quantize_wu(0, 1, 0)
         quantize_wu(0, 1, 2)
-        order_wg_words(1, on_vector)
         zeroed_rows(2, nc.gpsimd)
 
         h = sbuf("h00", [P, HALF, PLACES], BF16)
@@ -318,25 +328,24 @@ def tile_list_modp_gsigm_res_noneb_kernel(
         round_wu(1, 0, 2, on_scalar)
         quantize_wu(1, 0, 0)
         quantize_h(codes_of([(0, 0), (0, 1)]), 0, h)
+        round_last_block((on_scalar, on_vector), (None, EARLY_H - KIB))
         quantize_wu(1, 0, 2)
-        round_wu(1, 1, 2, on_scalar, EARLY_H)
-        round_wu(1, 1, 0, on_vector, ROWS[3])
         gates(1, 0, GROUP, (3, 4), LAST_WU - 2 * KIB)
         (filler,) = four_places("ub", wu_columns, 0, [HALF], [7])
-        quantize_wu(1, 1, 2)
         quantize_wu(1, 1, 0)
+        quantize_wu(1, 1, 2)
         zeroed_rows(3, nc.gpsimd)
 
         gates(1, GROUP, GROUP, (5, 6), LAST_WU + 2 * KIB)
         h02 = sbuf("h02", [P, GROUP, PLACES], BF16, EARLY_H)
         product(0, HALF, filler, h02[:, :P])
         h10 = sbuf("h10", [P, GROUP, PLACES], BF16)
-        for first, ub in zip((0, P), four_places("ub", wu_columns, 1, (0, P), (0, 1), (2, 3, 0, 1))):
+        for first, ub in zip((0, P), four_places("ub", wu_columns, 1, (0, P), (0, 1))):
             product(1, first, ub, h10[:, first : first + P])
         h11 = sbuf("h11", [P, GROUP, PLACES], BF16)
         ubs = four_places("ub", wu_columns, 1, (GROUP, GROUP + P), (2, 3))
         (filler,) = four_places("ub", wu_columns, 0, [HALF + P], [7])
-        gated = factor("late_gate", wg_columns, 1, HALF, ACT.Sigmoid, (4, 5), LAST_WU + 6 * KIB)
+        gated = factor("late_gate", wg_columns, 1, HALF, ACT.Sigmoid, (4,))
         product(1, GROUP, ubs[0], h11[:, :P])
         quantize_h(codes_of([(1, 0)]), 0, h10)
         product(1, GROUP + P, ubs[1], h11[:, P:])
@@ -348,17 +357,19 @@ def tile_list_modp_gsigm_res_noneb_kernel(
         nc.vector.tensor_copy(window(0, [0]), weighted[:])
         for n, number in ((1, 0), (2, 1), (3, 2)):
             weigh_on_gpsimd_and_scatter(n, 0, number)
-        group_on_gpsimd(1, 2, gated, factor("late_up", wu_columns, 1, HALF, ACT.Copy, (6, 0)))
-        for n, number in ((0, 3), (1, 7), (2, 4)):
-            weigh_on_gpsimd_and_scatter(n, 1, number)
-        gated = factor("late_gate", wg_columns, 0, 3 * GROUP, ACT.Sigmoid, (1, 2))
-        group_on_gpsimd(0, 3, gated, factor("late_up", wu_columns, 0, 3 * GROUP, ACT.Copy, (6, 0)))
-        weigh_on_gpsimd_and_scatter(3, 1, 1)
+        factor("late_gate", wg_columns, 1, HALF, ACT.Sigmoid, (6,), None, gated, P)
+        group_on_gpsimd(1, 2, gated, factor("late_up", wu_columns, 1, HALF, ACT.Copy, (0, 1)))
+        weigh_on_gpsimd_and_scatter(0, 1, 3)
+        weigh_on_gpsimd_and_scatter(1, 1, 7)
+        weigh_on_gpsimd_and_scatter(2, 1, 4, LATE_H[1, 2] + KIB)
+        gated = factor("late_gate", wg_columns, 0, 3 * GROUP, ACT.Sigmoid, (6, 2))
+        group_on_gpsimd(0, 3, gated, factor("late_up", wu_columns, 0, 3 * GROUP, ACT.Copy, (0, 1)))
+        weigh_on_gpsimd_and_scatter(3, 1, 6)
         weigh_on_gpsimd_and_scatter(0, 2, 3)
         gated = factor("late_gate", wg_columns, 1, 3 * GROUP, ACT.Sigmoid, (7, 4))
-        group_on_gpsimd(1, 3, gated, factor("late_up", wu_columns, 1, 3 * GROUP, ACT.Copy, (2, 6), LAST_UP))
+        group_on_gpsimd(1, 3, gated, factor("late_up", wu_columns, 1, 3 * GROUP, ACT.Copy, (2, 0), LAST_UP))
 
-        weigh_and_scatter(1, [2], add_bias(1, [2], 0, LAST_UP))
-        for n, groups, number in ((0, [3], 5), (1, [3], 1), (2, [2, 3], 3), (3, [2, 3], 7)):
+        weigh_and_scatter(1, [2], add_bias(1, [2], 1, LAST_UP))
+        for n, groups, number in ((0, [3], 5), (1, [3], 6), (2, [2, 3], 3), (3, [2, 3], 7)):
             weigh_and_scatter(n, groups, add_bias(n, groups, number, None, (0, 1)))
             store(n)

@@ -21,21 +21,30 @@ P = 128
 PASS = 512
 PLACES = 4
 QUADRANT = 32
+QUADRANTS = P // QUADRANT
 LIST_COLUMN = 16
 HALF = J // 2
 GROUP = 256
 BANK = 2048
 KIB = 1024
 BLOCK = 8 * KIB
+ALIGN = 256
 DENSE_ROWS = 96
 WARM_UPS = 4
+VECTOR_SHARE = 80
 
-ROWS = [0, BLOCK, 2 * BLOCK, 3 * BLOCK]
-EARLY_H = 4 * BLOCK
-SECOND_WU = 34 * KIB
-LAST_WU = 44 * KIB
+BY_PASS = ((0, (0, 1, 2, 3)), (1, (0, 1, 2, 3)))
+BY_PAIR = ((0, (0, 1)), (1, (0, 1)), (0, (2, 3)), (1, (2, 3)))
+
+ROWS = [None, 0, BLOCK, 2 * BLOCK]
+SECOND_WU = 3 * BLOCK
+LAST_WU = 33 * KIB
+SECOND_WG = 41 * KIB
+FIRST_CODES = SECOND_WG + 2 * KIB
+THIRD_CODES = FIRST_CODES + 2 * KIB
 LATE_H = {(1, 2): 51 * KIB, (0, 3): 50 * KIB, (1, 3): 49 * KIB}
-LAST_UP = 54 * KIB
+LAST_UP = 53 * KIB
+WD_SCALES = 57 * KIB
 
 
 def tile_list_modp_gsigm_res_noneb_kernel(
@@ -46,102 +55,51 @@ def tile_list_modp_gsigm_res_noneb_kernel(
         keep = ctx.enter_context(tc.tile_pool(name="keep", bufs=1))
         shared = ctx.enter_context(tc.tile_pool(name="shared", bufs=1))
         psum = ctx.enter_context(tc.psum_pool(name="psum", bufs=1))
+        rows, wg_raw, wu_raw, tok_w, wg_w, rounded, wu_w, wu_s, gate, codes = ({} for kind in range(10))
+        on_scalar, on_vector = nc.scalar.copy, nc.vector.tensor_copy
 
         def sbuf(name, shape, dtype, offset=None):
             if offset is None:
-                return keep.tile(shape, dtype, name=name, align_bytes=64)
-            return shared.tile(shape, dtype, name=name, align_bytes=64, offset=offset)
+                return keep.tile(shape, dtype, name=name, align_bytes=ALIGN)
+            return shared.tile(shape, dtype, name=name, align_bytes=ALIGN, offset=offset)
 
         def bank(name, shape, number):
             return psum.tile(shape, F32, name=name, offset=number * BANK)
 
+        def load(tile, source):
+            nc.sync.dma_start(out=tile, in_=source)
+
         def listed(first, count):
             return offsets[:, first // LIST_COLUMN : (first + count) // LIST_COLUMN]
 
-        def load_scales(tile, src):
-            for r in range(4):
-                rows_r = src[:, r:16:4, :].rearrange("a q x -> q a x")
-                nc.sync.dma_start(out=tile[r:P:QUADRANT], in_=rows_r.bitcast(I32))
-
-        def zeroed_rows(n, engine):
+        def zero_rows(n, engine):
             rows[n] = sbuf(f"rows{n}", [P, T], F32, ROWS[n])
             engine.memset(rows[n][:].bitcast(I32), 0)
 
-        def load_wg(rb, offset=None):
-            raw = sbuf(f"wg_raw{rb}", [P, 2, PASS // 2], I32, offset)
+        def load_wg(rb):
+            wg_raw[rb] = sbuf(f"wg_raw{rb}", [P, 2, PASS // 2], I32)
             columns = wg_words[:, :, 2 * PASS * rb : 2 * PASS * (rb + 1)]
-            nc.sync.dma_start(out=raw[:], in_=columns.rearrange("a p x -> p a x").bitcast(I32))
-            return raw
+            load(wg_raw[rb][:], columns.rearrange("a p x -> p a x").bitcast(I32))
 
-        def load_wu(rb, a, offset=None, first=0, count=PASS):
-            raw = sbuf(f"wu_raw{rb}{a}{first}", [P, PLACES, count], F32, offset)
-            block = wu[PASS * a : PASS * (a + 1), PASS * rb + first : PASS * rb + first + count]
-            nc.sync.dma_start(out=raw[:], in_=block.rearrange("(p i) c -> p i c", i=PLACES))
-            return raw
+        def load_wu(rb, a, offset=None):
+            wu_raw[rb, a] = sbuf(f"wu_raw{rb}{a}", [P, PLACES, PASS], F32, offset)
+            block = wu[PASS * a : PASS * (a + 1), PASS * rb : PASS * (rb + 1)]
+            load(wu_raw[rb, a][:], block.rearrange("(p i) c -> p i c", i=PLACES))
 
-        rows = {}
-        warm = sbuf("warm", [P, 2], F32)
-        nc.vector.memset(warm[:, 0:1], 0.0)
-        wg_s_rows = sbuf("wg_s_rows", [P, PASS // 4], I32, ROWS[1])
-        nc.vector.memset(wg_s_rows[2 * QUADRANT :], 0)
-        wg_s = sbuf("wg_s", [P, 2, 2, PLACES, P], U8)
-        nc.vector.memset(wg_s[:].bitcast(I32), 0)
-        tab_s = sbuf("tab_s", [P, T // 4], I32, ROWS[0])
-        nc.vector.memset(tab_s[:DENSE_ROWS], 0)
-        tok_s = sbuf("tok_s", [P, 2, J], U8)
-        nc.vector.memset(tok_s[:].bitcast(I32), 0)
-        wd_s = sbuf("wd_s", [P, 2, 2, N // 4], I32)
-        nc.vector.memset(wd_s[:], 0)
+        def load_wd_scales(tile, source):
+            for r in range(4):
+                load(tile[r:P:QUADRANT], source[:, r:16:4, :].rearrange("a q x -> q a x").bitcast(I32))
 
-        offsets = keep.tile([P, J // LIST_COLUMN], U16, name="offsets")
-        nc.sync.dma_start(offsets[:], offs)
-        for a in range(2):
-            nc.sync.dma_start(
-                out=wg_s_rows[a : 2 * QUADRANT : 2, :],
-                in_=wg_scales[a].rearrange("b (r x) -> (b r) x", r=2).bitcast(I32),
-            )
-        nc.scalar.activation(out=warm[:, 1:2], in_=warm[:, 0:1], func=ACT.Sigmoid)
-        nc.sync.dma_start(out=tab_s[DENSE_ROWS:, :], in_=tab_scales.rearrange("a b x -> b a x").bitcast(I32))
-        wg_raw = [load_wg(0)]
-        tab_w = sbuf("tab_w", [P, T], I32)
-        nc.sync.dma_start(out=tab_w[:], in_=tab_words[0].rearrange("p t x -> p (t x)").bitcast(I32))
-        wg_s_ordered = sbuf("wg_s_ordered", [P, PLACES, P], U8)
-        by_place = wg_s_rows[:].bitcast(U8).rearrange("p (m t) -> p t m", t=PLACES)
-        nc.vector.tensor_copy(out=wg_s_ordered[:], in_=by_place)
-        for q in range(P // QUADRANT):
-            nc.sync.dma_start(
-                out=wg_s[QUADRANT * q : QUADRANT * q + 4].rearrange("p r a t m -> p (r a t m)").bitcast(I32),
-                in_=wg_s_ordered[16 * q : 16 * q + 16].rearrange("p t m -> p (t m)").bitcast(I32),
-            )
-        zeroed_rows(1, nc.gpsimd)
-        wu_raw = {(0, 0): load_wu(0, 0)}
-        tok_s_rows = sbuf("tok_s_rows", [P, J], U8)
-        nc.vector.tensor_copy(tok_s_rows[:], tab_s[:].bitcast(U8).indirect(offsets[:]))
-        zeroed_rows(0, nc.gpsimd)
-        for q in range(P // QUADRANT):
-            nc.sync.dma_start(
-                out=tok_s[QUADRANT * q : QUADRANT * q + 4].bitcast(I32),
-                in_=tok_s_rows[DENSE_ROWS + 8 * q : DENSE_ROWS + 8 * q + 8, :].bitcast(I32),
-            )
-        wu_raw[0, 1] = load_wu(0, 1, SECOND_WU)
-        wg_raw.append(load_wg(1))
-        wu_raw[1, 0] = load_wu(1, 0)
-        last_wu = [load_wu(1, 1, LAST_WU, 0, PASS // 2), load_wu(1, 1, None, PASS // 2, PASS // 2)]
-        wd8_w = sbuf("wd8_w", [P, 2, N], I32)
-        nc.sync.dma_start(out=wd8_w[:], in_=wd8_words.rearrange("a p n x -> p a (n x)").bitcast(I32))
-        load_scales(wd_s[:, 1], wd8_scales)
-        wd4_w = sbuf("wd4_w", [P, 2, N // 2], I32)
-        nc.sync.dma_start(out=wd4_w[:], in_=wd4_words.rearrange("a p x -> p a x").bitcast(I32))
-        load_scales(wd_s[:, 0], wd4_scales)
-        wd4_s, wd8_s = wd_s[:, 0].bitcast(U8), wd_s[:, 1].bitcast(U8)
-        bias = sbuf("bias", [P, N // P], F32)
-        with nc.allow_non_contiguous_dma(reason="one bias value for each partition and output tile"):
-            nc.sync.dma_start(out=bias[:], in_=b.rearrange("(c p) -> p c", p=P))
-        weight = sbuf("weight", [P, J], F32)
-        nc.sync.dma_start(out=weight[:, HALF:], in_=wgo[:, HALF:])
-        nc.sync.dma_start(out=weight[:, :HALF], in_=wgo[:, :HALF])
+        def move_wg_scales(rb):
+            for q in range(QUADRANTS):
+                target = wg_s[QUADRANT * q : QUADRANT * q + 4, rb].rearrange("p a t m -> p (a t m)")
+                source = wg_s_ordered[16 * q + rb : 16 * q + 16 : 2].rearrange("p t m -> p (t m)")
+                load(target.bitcast(I32), source.bitcast(I32))
 
-        tok_w, wg_w, rounded, wu_w, wu_s, gate, codes = {}, {}, {}, {}, {}, {}, {}
+        def move_token_scales():
+            for q in range(QUADRANTS):
+                source = tok_s_rows[DENSE_ROWS + 8 * q : DENSE_ROWS + 8 * q + 8, :]
+                load(tok_s[QUADRANT * q : QUADRANT * q + 4].bitcast(I32), source.bitcast(I32))
 
         def order_wg_words(rb, copy, offset=None):
             wg_w[rb] = sbuf(f"wg_w{rb}", [P, 2, PLACES, 2 * P], U8, offset)
@@ -160,23 +118,21 @@ def tile_list_modp_gsigm_res_noneb_kernel(
 
         def token_operand(a, first, count):
             half, j0 = divmod(first, HALF)
-            return tok_w[half][:, a, 2 * j0 : 2 * (j0 + count)].bitcast(FP4X4), tok_s[:, a, first : first + count]
+            words = tok_w[half][:, a, 2 * j0 : 2 * (j0 + count)].bitcast(FP4X4)
+            return words, tok_s[:, a, first : first + count]
 
-        def round_wu(rb, a, t0, copy, offset=None):
+        def round_wu(rb, a, t0, shares, offset=None):
             rounded[rb, a, t0] = sbuf(f"wu_rounded{rb}{a}{t0}", [P, 2, P, PLACES], BF16, offset)
             source = wu_raw[rb, a][:].rearrange("p i (m t) -> p m i t", t=PLACES)
-            copy(out=rounded[rb, a, t0][:].rearrange("p t m i -> p m i t"), in_=source[:, :, :, t0 : t0 + 2])
+            target = rounded[rb, a, t0][:].rearrange("p t m i -> p m i t")
+            for copy, columns in shares:
+                copy(out=target[:, columns], in_=source[:, columns, :, t0 : t0 + 2])
 
-        def round_last_block(copies, offsets):
-            for t0, offset in zip((0, 2), offsets):
-                rounded[1, 1, t0] = sbuf(f"wu_rounded11{t0}", [P, 2, P, PLACES], BF16, offset)
-                for half, copy in enumerate(copies):
-                    target = rounded[1, 1, t0][:, :, P // 2 * half : P // 2 * (half + 1), :]
-                    source = last_wu[half][:].rearrange("p i (m t) -> p m i t", t=PLACES)
-                    copy(out=target.rearrange("p t m i -> p m i t"), in_=source[:, :, :, t0 : t0 + 2])
+        all_on_scalar, all_on_vector = [(on_scalar, slice(0, P))], [(on_vector, slice(0, P))]
+        on_both = [(on_vector, slice(0, VECTOR_SHARE)), (on_scalar, slice(VECTOR_SHARE, P))]
 
-        def quantize_wu(rb, a, t0):
-            wu_w[rb, a, t0] = sbuf(f"wu_w{rb}{a}{t0}", [P, 2 * P], U32)
+        def quantize_wu(rb, a, t0, offset=None):
+            wu_w[rb, a, t0] = sbuf(f"wu_w{rb}{a}{t0}", [P, 2 * P], U32, offset)
             wu_s[rb, a, t0] = sbuf(f"wu_s{rb}{a}{t0}", [P, 2 * P], U8)
             nc.vector.quantize_mx(
                 out=wu_w[rb, a, t0][:].bitcast(FP8X4),
@@ -197,52 +153,49 @@ def tile_list_modp_gsigm_res_noneb_kernel(
                 out=acc, lhsT=lhs, lhsT_scale=lhs_scale, rhs=rhs, rhs_scale=rhs_scale, start=start, stop=stop
             )
 
-        def gates(rb, first, count, banks, offset=None):
-            places = HALF // count
-            tile = sbuf(f"gate{rb}{first}", [P, PLACES, count], F32, offset)
-            for j0 in range(0, count, P):
-                gate[rb, first + j0] = tile[:, :, j0 : j0 + P]
-            for t0, number in zip(range(0, PLACES, places), banks):
-                ga = bank(f"ga{rb}{first}{t0}", [P, places, count], number)
-                for t in range(t0, t0 + places):
+        def gates(rb, g, banks, offset=None):
+            tile = sbuf(f"gate{rb}{g}", [P, PLACES, GROUP], F32, offset)
+            gate[rb, g] = tile
+            for t0, number in zip((0, 2), banks):
+                ga = bank(f"ga{rb}{g}{t0}", [P, 2, GROUP], number)
+                for t in (t0, t0 + 1):
                     for a in range(2):
-                        multiply(ga[:, t - t0, :], wg_columns(rb, a, t), token_operand(a, first, count), a == 0, a == 1)
-                nc.scalar.activation(out=tile[:, t0 : t0 + places, :], in_=ga[:], func=ACT.Sigmoid)
+                        tokens = token_operand(a, GROUP * g, GROUP)
+                        multiply(ga[:, t - t0, :], wg_columns(rb, a, t), tokens, a == 0, a == 1)
+                nc.scalar.activation(out=tile[:, t0 : t0 + 2, :], in_=ga[:], func=ACT.Sigmoid)
 
-        def four_places(name, columns, rb, firsts, banks, places=(0, 1, 2, 3)):
+        def four_places(name, columns, rb, firsts, banks, steps=BY_PASS):
             accs = [bank(f"{name}{rb}{first}", [P, PLACES, P], number) for first, number in zip(firsts, banks)]
-            for a in range(2):
+            for a, places in steps:
                 for acc, first in zip(accs, firsts):
                     for t in places:
-                        start, stop = (a, t) == (0, places[0]), (a, t) == (1, places[-1])
+                        start, stop = (a, t) == (0, 0), (a, t) == (1, PLACES - 1)
                         multiply(acc[:, t, :], columns(rb, a, t), token_operand(a, first, P), start, stop)
             return accs
 
-        def product(rb, first, ub, h):
+        def up_sums(rb, g, banks):
+            steps = (BY_PASS, BY_PAIR)[rb]
+            return four_places("ub", wu_columns, rb, (GROUP * g, GROUP * g + P), banks, steps)
+
+        def product(rb, g, c, ub, h):
+            tokens = slice(P * c, P * (c + 1))
             nc.vector.tensor_tensor(
-                h.rearrange("p (c e) t -> p c t e", e=2),
+                h[:, tokens].rearrange("p (c e) t -> p c t e", e=2),
                 ub[:].rearrange("p t (c e) -> p c t e", e=2),
-                gate[rb, first].rearrange("p t (c e) -> p c t e", e=2),
+                gate[rb, g][:, :, tokens].rearrange("p t (c e) -> p c t e", e=2),
                 MULT,
             )
 
-        def codes_of(keys, offset=None):
+        def quantize_h(keys, h, offset=None):
             name = "_".join(f"{rb}{g}" for rb, g in keys)
             words = sbuf(f"h_w{name}", [P, GROUP * len(keys)], U32, offset)
             scales = sbuf(f"h_s{name}", [P, GROUP * len(keys)], U8)
             for c, key in enumerate(keys):
                 tokens = slice(GROUP * c, GROUP * (c + 1))
                 codes[key] = words[:, tokens].bitcast(FP8X4), scales[:, tokens]
-            return words, scales
+            nc.vector.quantize_mx(out=words[:].bitcast(FP8X4), scales=scales[:], in_=h.rearrange("p j t -> p (j t)"))
 
-        def quantize_h(target, first, h):
-            words, scales = target
-            tokens = slice(first, first + h[:].shape[1])
-            nc.vector.quantize_mx(
-                out=words[:, tokens].bitcast(FP8X4), scales=scales[:, tokens], in_=h[:].rearrange("p j t -> p (j t)")
-            )
-
-        def down(n, groups, number, halves=(1, 0)):
+        def down(n, groups, number, halves):
             y = bank(f"y{n}{groups[0]}", [P, len(groups), GROUP], number)
             columns, packed = slice(P * n, P * (n + 1)), slice(2 * P * n, 2 * P * (n + 1))
             wd4 = [(wd4_w[:].bitcast(U8)[:, rb, packed].bitcast(FP4X4), wd4_s[:, rb, columns]) for rb in range(2)]
@@ -253,7 +206,7 @@ def tile_list_modp_gsigm_res_noneb_kernel(
                     multiply(y[:, c, :], wd8[rb], codes[rb, g], False, rb == halves[1])
             return y[:].rearrange("p c j -> p (c j)")
 
-        def add_bias(n, groups, number, offset=None, halves=(1, 0)):
+        def add_bias(n, groups, number, halves, offset=None):
             biased = sbuf(f"y_biased{n}{groups[0]}", [P, GROUP * len(groups)], F32, offset)
             y = down(n, groups, number, halves)
             nc.scalar.activation(out=biased[:], in_=y, func=ACT.Identity, bias=bias[:, n : n + 1])
@@ -268,22 +221,16 @@ def tile_list_modp_gsigm_res_noneb_kernel(
         def weigh_and_scatter(n, groups, biased):
             nc.vector.tensor_tensor(window(n, groups), biased[:], weights(groups), MULT)
 
-        def weigh_in_bank(n, g, y):
-            weighted = sbuf(f"y_weighted{n}{g}", [P, GROUP], F32)
-            nc.vector.scalar_tensor_tensor(weighted[:], y, bias[:, n : n + 1], weights([g]), ADD, MULT)
-            return weighted
-
         def weigh_on_gpsimd_and_scatter(n, g, number, offset=None):
-            biased = add_bias(n, [g], number)
+            biased = add_bias(n, [g], number, (1, 0))
             weighted = sbuf(f"y_weighted{n}{g}", [P, GROUP], F32, offset)
             nc.gpsimd.tensor_tensor(weighted[:], biased[:], weights([g]), MULT)
             nc.vector.tensor_copy(window(n, [g]), weighted[:])
 
-        def factor(name, columns, rb, first, func, banks, offset=None, values=None, j1=0):
-            if values is None:
-                values = sbuf(f"{name}{rb}{first}", [P, GROUP, PLACES], F32, offset)
-            for j0, number in zip(range(j1, GROUP, P), banks):
-                (acc,) = four_places(name, columns, rb, [first + j0], [number])
+        def factor(name, columns, rb, g, func, banks, offset=None):
+            values = sbuf(f"{name}{rb}{g}", [P, GROUP, PLACES], F32, offset)
+            for j0, number in zip((0, P), banks):
+                (acc,) = four_places(name, columns, rb, [GROUP * g + j0], [number])
                 nc.scalar.activation(out=values[:, j0 : j0 + P, :], in_=acc[:].rearrange("p t j -> p j t"), func=func)
             return values
 
@@ -291,12 +238,45 @@ def tile_list_modp_gsigm_res_noneb_kernel(
             flat = "p j t -> p (j t)"
             h = sbuf(f"h{rb}{g}", [P, GROUP, PLACES], BF16, LATE_H[rb, g])
             nc.gpsimd.tensor_tensor(h[:].rearrange(flat), gated[:].rearrange(flat), up[:].rearrange(flat), MULT)
-            quantize_h(codes_of([(rb, g)]), 0, h)
+            quantize_h([(rb, g)], h[:])
 
-        def store(n):
-            nc.sync.dma_start(out=out[P * n : P * (n + 1), :], in_=rows[n][:])
+        warm = sbuf("warm", [P, 2], F32)
+        nc.vector.memset(warm[:, 0:1], 0.0)
+        wg_s_rows = sbuf("wg_s_rows", [P, PASS // 4], I32, ROWS[1])
+        nc.vector.memset(wg_s_rows[2 * QUADRANT :], 0)
+        wg_s = sbuf("wg_s", [P, 2, 2, PLACES, P], U8)
+        nc.vector.memset(wg_s[:].bitcast(I32), 0)
+        tab_s = sbuf("tab_s", [P, T // 4], I32, ROWS[2])
+        nc.vector.memset(tab_s[:DENSE_ROWS], 0)
+        tok_s = sbuf("tok_s", [P, 2, J], U8)
+        nc.vector.memset(tok_s[:].bitcast(I32), 0)
+        zero_rows(0, nc.vector)
 
-        on_scalar, on_vector = nc.scalar.copy, nc.vector.tensor_copy
+        offsets = keep.tile([P, J // LIST_COLUMN], U16, name="offsets")
+        nc.sync.dma_start(offsets[:], offs)
+        for rb in range(2):
+            columns = wg_scales[:, :, PASS * rb : PASS * (rb + 1)]
+            load(wg_s_rows[rb : 2 * QUADRANT : 2, :], columns.rearrange("a b x -> b a x").bitcast(I32))
+        nc.scalar.activation(out=warm[:, 1:2], in_=warm[:, 0:1], func=ACT.Sigmoid)
+        load(tab_s[DENSE_ROWS:, :], tab_scales.rearrange("a b x -> b a x").bitcast(I32))
+        load_wg(0)
+        tab_w = sbuf("tab_w", [P, T], I32)
+        load(tab_w[:], tab_words[0].rearrange("p t x -> p (t x)").bitcast(I32))
+        wg_s_ordered = sbuf("wg_s_ordered", [P, PLACES, P], U8)
+        by_place = wg_s_rows[:].bitcast(U8).rearrange("p (m t) -> p t m", t=PLACES)
+        nc.vector.tensor_copy(out=wg_s_ordered[:], in_=by_place)
+        move_wg_scales(0)
+        zero_rows(1, nc.gpsimd)
+        load_wu(0, 0)
+        tok_s_rows = sbuf("tok_s_rows", [P, J], U8)
+        nc.vector.tensor_copy(tok_s_rows[:], tab_s[:].bitcast(U8).indirect(offsets[:]))
+        zero_rows(2, nc.gpsimd)
+        move_token_scales()
+        load_wu(0, 1, SECOND_WU)
+        load_wg(1)
+        move_wg_scales(1)
+        load_wu(1, 0)
+        load_wu(1, 1, LAST_WU)
 
         order_wg_words(0, on_scalar)
         idle = bank("idle", [P, HALF], 0)
@@ -306,70 +286,82 @@ def tile_list_modp_gsigm_res_noneb_kernel(
             multiply(idle[:], wg_columns(0, 0, t), (all_words, all_scales), True, True)
         for half, both in enumerate([gather_words(half) for half in range(2)]):
             part_words(half, both)
-        round_wu(0, 0, 0, on_scalar)
-        round_wu(0, 0, 2, on_vector)
-        gates(0, 0, GROUP, (1, 2))
+        round_wu(0, 0, 0, all_on_scalar, WD_SCALES)
+        round_wu(0, 0, 2, all_on_vector)
+        gates(0, 0, (1, 2))
         quantize_wu(0, 0, 0)
         quantize_wu(0, 0, 2)
-        round_wu(0, 1, 0, on_vector)
-        order_wg_words(1, on_vector)
-        round_wu(0, 1, 2, on_scalar, ROWS[2])
-        gates(0, GROUP, GROUP, (3, 4), SECOND_WU)
-        gates(0, HALF, GROUP, (5, 6), SECOND_WU + 4 * KIB)
+        wd_s = sbuf("wd_s", [P, 2, 2, N // 4], I32, WD_SCALES)
+        nc.vector.memset(wd_s[:], 0)
+        wd8_w = sbuf("wd8_w", [P, 2, N], I32)
+        load(wd8_w[:], wd8_words.rearrange("a p n x -> p a (n x)").bitcast(I32))
+        load_wd_scales(wd_s[:, 1], wd8_scales)
+        wd4_w = sbuf("wd4_w", [P, 2, N // 2], I32)
+        load(wd4_w[:], wd4_words.rearrange("a p x -> p a x").bitcast(I32))
+        load_wd_scales(wd_s[:, 0], wd4_scales)
+        wd4_s, wd8_s = wd_s[:, 0].bitcast(U8), wd_s[:, 1].bitcast(U8)
+        bias = sbuf("bias", [P, N // P], F32)
+        with nc.allow_non_contiguous_dma(reason="one bias value for each partition and output tile"):
+            load(bias[:], b.rearrange("(c p) -> p c", p=P))
+        weight = sbuf("weight", [P, J], F32)
+        load(weight[:, :HALF], wgo[:, :HALF])
+        load(weight[:, HALF:], wgo[:, HALF:])
+
+        round_wu(0, 1, 0, on_both, SECOND_WG)
+        round_wu(0, 1, 2, on_both, ROWS[3])
+        gates(0, 1, (3, 4), SECOND_WU)
+        gates(0, 2, (5, 6), SECOND_WU + 4 * KIB)
         quantize_wu(0, 1, 0)
         quantize_wu(0, 1, 2)
-        zeroed_rows(2, nc.gpsimd)
+        order_wg_words(1, on_vector, SECOND_WG)
+        zero_rows(3, nc.gpsimd)
 
-        h = sbuf("h00", [P, HALF, PLACES], BF16)
-        for firsts, banks in (((0, P), (7, 0)), ((2 * P, 3 * P), (1, 2))):
-            for first, ub in zip(firsts, four_places("ub", wu_columns, 0, firsts, banks)):
-                product(0, first, ub, h[:, first : first + P])
-        round_wu(1, 0, 0, on_scalar)
-        round_wu(1, 0, 2, on_scalar)
+        first_h = sbuf("h0", [P, 3 * GROUP, PLACES], BF16)
+        for g, banks in enumerate(((7, 0), (1, 2), (3, 4))):
+            for c, ub in enumerate(up_sums(0, g, banks)):
+                product(0, g, c, ub, first_h[:, GROUP * g : GROUP * (g + 1)])
+        round_wu(1, 0, 0, all_on_scalar)
+        round_wu(1, 0, 2, all_on_scalar)
         quantize_wu(1, 0, 0)
-        quantize_h(codes_of([(0, 0), (0, 1)]), 0, h)
-        round_last_block((on_scalar, on_vector), (None, EARLY_H - KIB))
-        quantize_wu(1, 0, 2)
-        gates(1, 0, GROUP, (3, 4), LAST_WU - 2 * KIB)
-        (filler,) = four_places("ub", wu_columns, 0, [HALF], [7])
+        round_wu(1, 1, 0, on_both, FIRST_CODES)
+        round_wu(1, 1, 2, on_both)
+        gates(1, 0, (5, 6), LAST_WU - KIB)
+        gates(1, 1, (7, 0), LAST_WU + 3 * KIB)
         quantize_wu(1, 1, 0)
+        quantize_wu(1, 0, 2, LAST_WU + 7 * KIB)
         quantize_wu(1, 1, 2)
-        zeroed_rows(3, nc.gpsimd)
+        quantize_h([(0, 0), (0, 1)], first_h[:, :HALF], FIRST_CODES)
 
-        gates(1, GROUP, GROUP, (5, 6), LAST_WU + 2 * KIB)
-        h02 = sbuf("h02", [P, GROUP, PLACES], BF16, EARLY_H)
-        product(0, HALF, filler, h02[:, :P])
-        h10 = sbuf("h10", [P, GROUP, PLACES], BF16)
-        for first, ub in zip((0, P), four_places("ub", wu_columns, 1, (0, P), (0, 1))):
-            product(1, first, ub, h10[:, first : first + P])
+        h10 = sbuf("h10", [P, GROUP, PLACES], BF16, THIRD_CODES)
+        for c, ub in enumerate(up_sums(1, 0, (1, 2))):
+            product(1, 0, c, ub, h10)
         h11 = sbuf("h11", [P, GROUP, PLACES], BF16)
-        ubs = four_places("ub", wu_columns, 1, (GROUP, GROUP + P), (2, 3))
-        (filler,) = four_places("ub", wu_columns, 0, [HALF + P], [7])
-        gated = factor("late_gate", wg_columns, 1, HALF, ACT.Sigmoid, (4,))
-        product(1, GROUP, ubs[0], h11[:, :P])
-        quantize_h(codes_of([(1, 0)]), 0, h10)
-        product(1, GROUP + P, ubs[1], h11[:, P:])
-        product(0, HALF + P, filler, h02[:, P:])
-        quantize_h(codes_of([(1, 1)]), 0, h11)
-        weighted = weigh_in_bank(0, 0, down(0, [0], 6, (0, 1)))
-        quantize_h(codes_of([(0, 2)]), 0, h02)
+        ubs = up_sums(1, 1, (3, 4))
+        gated = factor("late_gate", wg_columns, 1, 2, ACT.Sigmoid, (7, 0))
+        product(1, 1, 0, ubs[0], h11)
+        quantize_h([(1, 0)], h10[:])
+        product(1, 1, 1, ubs[1], h11)
+        quantize_h([(0, 2)], first_h[:, HALF:], THIRD_CODES)
+        quantize_h([(1, 1)], h11[:])
+        weighted = sbuf("y_weighted00", [P, GROUP], F32)
+        y = down(0, [0], 5, (0, 1))
+        nc.vector.scalar_tensor_tensor(weighted[:], y, bias[:, 0:1], weights([0]), ADD, MULT)
 
         nc.vector.tensor_copy(window(0, [0]), weighted[:])
-        for n, number in ((1, 0), (2, 1), (3, 2)):
+        for n, number in ((1, 6), (2, 1), (3, 2)):
             weigh_on_gpsimd_and_scatter(n, 0, number)
-        factor("late_gate", wg_columns, 1, HALF, ACT.Sigmoid, (6,), None, gated, P)
-        group_on_gpsimd(1, 2, gated, factor("late_up", wu_columns, 1, HALF, ACT.Copy, (0, 1)))
+        group_on_gpsimd(1, 2, gated, factor("late_up", wu_columns, 1, 2, ACT.Copy, (5, 6)))
         weigh_on_gpsimd_and_scatter(0, 1, 3)
-        weigh_on_gpsimd_and_scatter(1, 1, 7)
-        weigh_on_gpsimd_and_scatter(2, 1, 4, LATE_H[1, 2] + KIB)
-        gated = factor("late_gate", wg_columns, 0, 3 * GROUP, ACT.Sigmoid, (6, 2))
-        group_on_gpsimd(0, 3, gated, factor("late_up", wu_columns, 0, 3 * GROUP, ACT.Copy, (0, 1)))
-        weigh_on_gpsimd_and_scatter(3, 1, 6)
+        weigh_on_gpsimd_and_scatter(1, 1, 4)
+        weigh_on_gpsimd_and_scatter(2, 1, 7, LATE_H[1, 2] + KIB)
+        gated = factor("late_gate", wg_columns, 0, 3, ACT.Sigmoid, (1, 2))
+        group_on_gpsimd(0, 3, gated, factor("late_up", wu_columns, 0, 3, ACT.Copy, (5, 6)))
+        weigh_on_gpsimd_and_scatter(3, 1, 1)
         weigh_on_gpsimd_and_scatter(0, 2, 3)
-        gated = factor("late_gate", wg_columns, 1, 3 * GROUP, ACT.Sigmoid, (7, 4))
-        group_on_gpsimd(1, 3, gated, factor("late_up", wu_columns, 1, 3 * GROUP, ACT.Copy, (2, 0), LAST_UP))
+        gated = factor("late_gate", wg_columns, 1, 3, ACT.Sigmoid, (4, 7))
+        group_on_gpsimd(1, 3, gated, factor("late_up", wu_columns, 1, 3, ACT.Copy, (2, 5), LAST_UP))
 
-        weigh_and_scatter(1, [2], add_bias(1, [2], 1, LAST_UP))
-        for n, groups, number in ((0, [3], 5), (1, [3], 6), (2, [2, 3], 3), (3, [2, 3], 7)):
-            weigh_and_scatter(n, groups, add_bias(n, groups, number, None, (0, 1)))
-            store(n)
+        weigh_and_scatter(1, [2], add_bias(1, [2], 6, (1, 0), LAST_UP))
+        for n, groups, number in ((0, [3], 0), (1, [3], 1), (2, [2, 3], 3), (3, [2, 3], 4)):
+            weigh_and_scatter(n, groups, add_bias(n, groups, number, (0, 1)))
+            load(out[P * n : P * (n + 1), :], rows[n][:])

@@ -128,7 +128,8 @@ def tile_list_modp_gsigm_res_noneb_kernel(
             for copy, columns in shares:
                 copy(out=target[:, columns], in_=source[:, columns, :, t0 : t0 + 2])
 
-        all_on_scalar, all_on_vector = [(on_scalar, slice(0, P))], [(on_vector, slice(0, P))]
+        all_on_scalar = [(on_scalar, slice(0, P))]
+        in_halves = [(on_vector, slice(0, P // 2)), (on_scalar, slice(P // 2, P))]
         on_both = [(on_vector, slice(0, VECTOR_SHARE)), (on_scalar, slice(VECTOR_SHARE, P))]
 
         def quantize_wu(rb, a, t0, offset=None):
@@ -287,7 +288,7 @@ def tile_list_modp_gsigm_res_noneb_kernel(
         for half, both in enumerate([gather_words(half) for half in range(2)]):
             part_words(half, both)
         round_wu(0, 0, 0, all_on_scalar, WD_SCALES)
-        round_wu(0, 0, 2, all_on_vector)
+        round_wu(0, 0, 2, in_halves)
         gates(0, 0, (1, 2))
         quantize_wu(0, 0, 0)
         quantize_wu(0, 0, 2)
@@ -304,8 +305,8 @@ def tile_list_modp_gsigm_res_noneb_kernel(
         with nc.allow_non_contiguous_dma(reason="one bias value for each partition and output tile"):
             load(bias[:], b.rearrange("(c p) -> p c", p=P))
         weight = sbuf("weight", [P, J], F32)
-        load(weight[:, :HALF], wgo[:, :HALF])
-        load(weight[:, HALF:], wgo[:, HALF:])
+        load(weight[:, :GROUP], wgo[:, :GROUP])
+        load(weight[:, GROUP:], wgo[:, GROUP:])
 
         round_wu(0, 1, 0, on_both, SECOND_WG)
         round_wu(0, 1, 2, on_both, ROWS[3])

from contextlib import ExitStack

import concourse.mybir as mybir

K, R, N, T, J = 1024, 1024, 512, 2048, 1024
FLOPS = 2 * J * (2 * K * R + 2 * R * N)

F32 = mybir.dt.float32
BF16 = mybir.dt.bfloat16
I32 = mybir.dt.int32
U32 = mybir.dt.uint32
U16 = mybir.dt.uint16
U8 = mybir.dt.uint8
FP8X4 = mybir.dt.float8_e4m3fn_x4
FP4X4 = mybir.dt.float4_e2m1fn_x4
ACT = mybir.ActivationFunctionType
MULT = mybir.AluOpType.mult
ADD = mybir.AluOpType.add

P = 128
PASS = 512
PLACES = 4
QUADRANT = 32
QUADRANTS = P // QUADRANT
LIST_COLUMN = 16
HALF = J // 2
GROUP = 256
BANK = 2048
KIB = 1024
BLOCK = 8 * KIB
ALIGN = 256
DENSE_ROWS = 96
WARM_UPS = 4
VECTOR_SHARE = 80

BY_PASS = ((0, (0, 1, 2, 3)), (1, (0, 1, 2, 3)))
BY_PAIR = ((0, (0, 1)), (1, (0, 1)), (0, (2, 3)), (1, (2, 3)))

ROWS = [None, 0, BLOCK, 2 * BLOCK]
SECOND_WU = 3 * BLOCK
LAST_WU = 33 * KIB
SECOND_WG = 41 * KIB
FIRST_CODES = SECOND_WG + 2 * KIB
THIRD_CODES = FIRST_CODES + 2 * KIB
LATE_H = {(1, 2): 51 * KIB, (0, 3): 50 * KIB, (1, 3): 49 * KIB}
LAST_UP = 53 * KIB
WD_SCALES = 57 * KIB


def tile_list_modp_gsigm_res_noneb_kernel(
    tc, tab_words, tab_scales, wg_words, wg_scales, wu, wd4_words, wd4_scales, wd8_words, wd8_scales, b, wgo, offs, out
):
    nc = tc.nc
    with ExitStack() as ctx:
        keep = ctx.enter_context(tc.tile_pool(name="keep", bufs=1))
        shared = ctx.enter_context(tc.tile_pool(name="shared", bufs=1))
        psum = ctx.enter_context(tc.psum_pool(name="psum", bufs=1))
        rows, wg_raw, wu_raw, tok_w, wg_w, rounded, wu_w, wu_s, gate, codes = ({} for kind in range(10))
        on_scalar, on_vector = nc.scalar.copy, nc.vector.tensor_copy

        def sbuf(name, shape, dtype, offset=None):
            if offset is None:
                return keep.tile(shape, dtype, name=name, align_bytes=ALIGN)
            return shared.tile(shape, dtype, name=name, align_bytes=ALIGN, offset=offset)

        def bank(name, shape, number):
            return psum.tile(shape, F32, name=name, offset=number * BANK)

        def load(tile, source):
            nc.sync.dma_start(out=tile, in_=source)

        def listed(first, count):
            return offsets[:, first // LIST_COLUMN : (first + count) // LIST_COLUMN]

        def zero_rows(n, engine):
            rows[n] = sbuf(f"rows{n}", [P, T], F32, ROWS[n])
            engine.memset(rows[n][:].bitcast(I32), 0)

        def load_wg(rb):
            wg_raw[rb] = sbuf(f"wg_raw{rb}", [P, 2, PASS // 2], I32)
            columns = wg_words[:, :, 2 * PASS * rb : 2 * PASS * (rb + 1)]
            load(wg_raw[rb][:], columns.rearrange("a p x -> p a x").bitcast(I32))

        def load_wu(rb, a, offset=None):
            wu_raw[rb, a] = sbuf(f"wu_raw{rb}{a}", [P, PLACES, PASS], F32, offset)
            block = wu[PASS * a : PASS * (a + 1), PASS * rb : PASS * (rb + 1)]
            load(wu_raw[rb, a][:], block.rearrange("(p i) c -> p i c", i=PLACES))

        def load_wd_scales(tile, source):
            for r in range(4):
                load(tile[r:P:QUADRANT], source[:, r:16:4, :].rearrange("a q x -> q a x").bitcast(I32))

        def move_wg_scales(rb):
            for q in range(QUADRANTS):
                target = wg_s[QUADRANT * q : QUADRANT * q + 4, rb].rearrange("p a t m -> p (a t m)")
                source = wg_s_ordered[16 * q + rb : 16 * q + 16 : 2].rearrange("p t m -> p (t m)")
                load(target.bitcast(I32), source.bitcast(I32))

        def move_token_scales():
            for q in range(QUADRANTS):
                source = tok_s_rows[DENSE_ROWS + 8 * q : DENSE_ROWS + 8 * q + 8, :]
                load(tok_s[QUADRANT * q : QUADRANT * q + 4].bitcast(I32), source.bitcast(I32))

        def order_wg_words(rb, copy, offset=None):
            wg_w[rb] = sbuf(f"wg_w{rb}", [P, 2, PLACES, 2 * P], U8, offset)
            columns = wg_raw[rb][:].bitcast(U16).rearrange("p a (m t) -> p a t m", t=PLACES)
            copy(out=wg_w[rb][:].bitcast(U16), in_=columns)

        def gather_words(half):
            both = sbuf(f"tok_both{half}", [P, HALF], U32)
            nc.vector.tensor_copy(both[:], tab_w[:].bitcast(U32).indirect(listed(half * HALF, HALF)))
            return both

        def part_words(half, both):
            tok_w[half] = sbuf(f"tok_w{half}", [P, 2, 2 * HALF], U8)
            by_pass = both[:].bitcast(U16).rearrange("p (j a) -> p a j", a=2)
            nc.vector.tensor_copy(out=tok_w[half][:].bitcast(U16), in_=by_pass)

        def token_operand(a, first, count):
            half, j0 = divmod(first, HALF)
            words = tok_w[half][:, a, 2 * j0 : 2 * (j0 + count)].bitcast(FP4X4)
            return words, tok_s[:, a, first : first + count]

        def round_wu(rb, a, t0, shares, offset=None):
            rounded[rb, a, t0] = sbuf(f"wu_rounded{rb}{a}{t0}", [P, 2, P, PLACES], BF16, offset)
            source = wu_raw[rb, a][:].rearrange("p i (m t) -> p m i t", t=PLACES)
            target = rounded[rb, a, t0][:].rearrange("p t m i -> p m i t")
            for copy, columns in shares:
                copy(out=target[:, columns], in_=source[:, columns, :, t0 : t0 + 2])

        all_on_scalar = [(on_scalar, slice(0, P))]
        in_halves = [(on_vector, slice(0, P // 2)), (on_scalar, slice(P // 2, P))]
        on_both = [(on_vector, slice(0, VECTOR_SHARE)), (on_scalar, slice(VECTOR_SHARE, P))]

        def quantize_wu(rb, a, t0, offset=None):
            wu_w[rb, a, t0] = sbuf(f"wu_w{rb}{a}{t0}", [P, 2 * P], U32, offset)
            wu_s[rb, a, t0] = sbuf(f"wu_s{rb}{a}{t0}", [P, 2 * P], U8)
            nc.vector.quantize_mx(
                out=wu_w[rb, a, t0][:].bitcast(FP8X4),
                scales=wu_s[rb, a, t0][:],
                in_=rounded[rb, a, t0][:].rearrange("p t m i -> p (t m i)"),
            )

        def wg_columns(rb, a, t):
            return wg_w[rb][:, a, t, :].bitcast(FP4X4), wg_s[:, rb, a, t, :]

        def wu_columns(rb, a, t):
            key, columns = (rb, a, t - t % 2), slice(P * (t % 2), P * (t % 2 + 1))
            return wu_w[key][:, columns].bitcast(FP8X4), wu_s[key][:, columns]

        def multiply(acc, stationary, moving, start, stop):
            (lhs, lhs_scale), (rhs, rhs_scale) = stationary, moving
            nc.tensor.matmul_mx(
                out=acc, lhsT=lhs, lhsT_scale=lhs_scale, rhs=rhs, rhs_scale=rhs_scale, start=start, stop=stop
            )

        def gates(rb, g, banks, offset=None):
            tile = sbuf(f"gate{rb}{g}", [P, PLACES, GROUP], F32, offset)
            gate[rb, g] = tile
            for t0, number in zip((0, 2), banks):
                ga = bank(f"ga{rb}{g}{t0}", [P, 2, GROUP], number)
                for t in (t0, t0 + 1):
                    for a in range(2):
                        tokens = token_operand(a, GROUP * g, GROUP)
                        multiply(ga[:, t - t0, :], wg_columns(rb, a, t), tokens, a == 0, a == 1)
                nc.scalar.activation(out=tile[:, t0 : t0 + 2, :], in_=ga[:], func=ACT.Sigmoid)

        def four_places(name, columns, rb, firsts, banks, steps=BY_PASS):
            accs = [bank(f"{name}{rb}{first}", [P, PLACES, P], number) for first, number in zip(firsts, banks)]
            for a, places in steps:
                for acc, first in zip(accs, firsts):
                    for t in places:
                        start, stop = (a, t) == (0, 0), (a, t) == (1, PLACES - 1)
                        multiply(acc[:, t, :], columns(rb, a, t), token_operand(a, first, P), start, stop)
            return accs

        def up_sums(rb, g, banks):
            steps = (BY_PASS, BY_PAIR)[rb]
            return four_places("ub", wu_columns, rb, (GROUP * g, GROUP * g + P), banks, steps)

        def product(rb, g, c, ub, h):
            tokens = slice(P * c, P * (c + 1))
            nc.vector.tensor_tensor(
                h[:, tokens].rearrange("p (c e) t -> p c t e", e=2),
                ub[:].rearrange("p t (c e) -> p c t e", e=2),
                gate[rb, g][:, :, tokens].rearrange("p t (c e) -> p c t e", e=2),
                MULT,
            )

        def quantize_h(keys, h, offset=None):
            name = "_".join(f"{rb}{g}" for rb, g in keys)
            words = sbuf(f"h_w{name}", [P, GROUP * len(keys)], U32, offset)
            scales = sbuf(f"h_s{name}", [P, GROUP * len(keys)], U8)
            for c, key in enumerate(keys):
                tokens = slice(GROUP * c, GROUP * (c + 1))
                codes[key] = words[:, tokens].bitcast(FP8X4), scales[:, tokens]
            nc.vector.quantize_mx(out=words[:].bitcast(FP8X4), scales=scales[:], in_=h.rearrange("p j t -> p (j t)"))

        def down(n, groups, number, halves):
            y = bank(f"y{n}{groups[0]}", [P, len(groups), GROUP], number)
            columns, packed = slice(P * n, P * (n + 1)), slice(2 * P * n, 2 * P * (n + 1))
            wd4 = [(wd4_w[:].bitcast(U8)[:, rb, packed].bitcast(FP4X4), wd4_s[:, rb, columns]) for rb in range(2)]
            wd8 = [(wd8_w[:, rb, columns].bitcast(FP8X4), wd8_s[:, rb, columns]) for rb in range(2)]
            for c, g in enumerate(groups):
                for rb in halves:
                    multiply(y[:, c, :], wd4[rb], codes[rb, g], rb == halves[0], False)
                    multiply(y[:, c, :], wd8[rb], codes[rb, g], False, rb == halves[1])
            return y[:].rearrange("p c j -> p (c j)")

        def add_bias(n, groups, number, halves, offset=None):
            biased = sbuf(f"y_biased{n}{groups[0]}", [P, GROUP * len(groups)], F32, offset)
            y = down(n, groups, number, halves)
            nc.scalar.activation(out=biased[:], in_=y, func=ACT.Identity, bias=bias[:, n : n + 1])
            return biased

        def weights(groups):
            return weight[:, GROUP * groups[0] : GROUP * (groups[-1] + 1)]

        def window(n, groups):
            return rows[n][:].indirect(listed(GROUP * groups[0], GROUP * len(groups)))

        def weigh_and_scatter(n, groups, biased):
            nc.vector.tensor_tensor(window(n, groups), biased[:], weights(groups), MULT)

        def weigh_on_gpsimd_and_scatter(n, g, number, offset=None):
            biased = add_bias(n, [g], number, (1, 0))
            weighted = sbuf(f"y_weighted{n}{g}", [P, GROUP], F32, offset)
            nc.gpsimd.tensor_tensor(weighted[:], biased[:], weights([g]), MULT)
            nc.vector.tensor_copy(window(n, [g]), weighted[:])

        def factor(name, columns, rb, g, func, banks, offset=None):
            values = sbuf(f"{name}{rb}{g}", [P, GROUP, PLACES], F32, offset)
            for j0, number in zip((0, P), banks):
                (acc,) = four_places(name, columns, rb, [GROUP * g + j0], [number])
                nc.scalar.activation(out=values[:, j0 : j0 + P, :], in_=acc[:].rearrange("p t j -> p j t"), func=func)
            return values

        def group_on_gpsimd(rb, g, gated, up):
            flat = "p j t -> p (j t)"
            h = sbuf(f"h{rb}{g}", [P, GROUP, PLACES], BF16, LATE_H[rb, g])
            nc.gpsimd.tensor_tensor(h[:].rearrange(flat), gated[:].rearrange(flat), up[:].rearrange(flat), MULT)
            quantize_h([(rb, g)], h[:])

        warm = sbuf("warm", [P, 2], F32)
        nc.vector.memset(warm[:, 0:1], 0.0)
        wg_s_rows = sbuf("wg_s_rows", [P, PASS // 4], I32, ROWS[1])
        nc.vector.memset(wg_s_rows[2 * QUADRANT :], 0)
        wg_s = sbuf("wg_s", [P, 2, 2, PLACES, P], U8)
        nc.vector.memset(wg_s[:].bitcast(I32), 0)
        tab_s = sbuf("tab_s", [P, T // 4], I32, ROWS[2])
        nc.vector.memset(tab_s[:DENSE_ROWS], 0)
        tok_s = sbuf("tok_s", [P, 2, J], U8)
        nc.vector.memset(tok_s[:].bitcast(I32), 0)
        zero_rows(0, nc.vector)

        offsets = keep.tile([P, J // LIST_COLUMN], U16, name="offsets")
        nc.sync.dma_start(offsets[:], offs)
        for rb in range(2):
            columns = wg_scales[:, :, PASS * rb : PASS * (rb + 1)]
            load(wg_s_rows[rb : 2 * QUADRANT : 2, :], columns.rearrange("a b x -> b a x").bitcast(I32))
        nc.scalar.activation(out=warm[:, 1:2], in_=warm[:, 0:1], func=ACT.Sigmoid)
        load(tab_s[DENSE_ROWS:, :], tab_scales.rearrange("a b x -> b a x").bitcast(I32))
        load_wg(0)
        tab_w = sbuf("tab_w", [P, T], I32)
        load(tab_w[:], tab_words[0].rearrange("p t x -> p (t x)").bitcast(I32))
        wg_s_ordered = sbuf("wg_s_ordered", [P, PLACES, P], U8)
        by_place = wg_s_rows[:].bitcast(U8).rearrange("p (m t) -> p t m", t=PLACES)
        nc.vector.tensor_copy(out=wg_s_ordered[:], in_=by_place)
        move_wg_scales(0)
        zero_rows(1, nc.gpsimd)
        load_wu(0, 0)
        tok_s_rows = sbuf("tok_s_rows", [P, J], U8)
        nc.vector.tensor_copy(tok_s_rows[:], tab_s[:].bitcast(U8).indirect(offsets[:]))
        zero_rows(2, nc.gpsimd)
        move_token_scales()
        load_wu(0, 1, SECOND_WU)
        load_wg(1)
        move_wg_scales(1)
        load_wu(1, 0)
        load_wu(1, 1, LAST_WU)

        order_wg_words(0, on_scalar)
        idle = bank("idle", [P, HALF], 0)
        all_words = wg_w[0][:, 0].rearrange("p t x -> p (t x)").bitcast(FP4X4)
        all_scales = wg_s[:, 0, 0].rearrange("p t m -> p (t m)")
        for t in range(WARM_UPS):
            multiply(idle[:], wg_columns(0, 0, t), (all_words, all_scales), True, True)
        for half, both in enumerate([gather_words(half) for half in range(2)]):
            part_words(half, both)
        round_wu(0, 0, 0, all_on_scalar, WD_SCALES)
        round_wu(0, 0, 2, in_halves)
        gates(0, 0, (1, 2))
        quantize_wu(0, 0, 0)
        quantize_wu(0, 0, 2)
        wd_s = sbuf("wd_s", [P, 2, 2, N // 4], I32, WD_SCALES)
        nc.vector.memset(wd_s[:], 0)
        wd8_w = sbuf("wd8_w", [P, 2, N], I32)
        load(wd8_w[:], wd8_words.rearrange("a p n x -> p a (n x)").bitcast(I32))
        load_wd_scales(wd_s[:, 1], wd8_scales)
        wd4_w = sbuf("wd4_w", [P, 2, N // 2], I32)
        load(wd4_w[:], wd4_words.rearrange("a p x -> p a x").bitcast(I32))
        load_wd_scales(wd_s[:, 0], wd4_scales)
        wd4_s, wd8_s = wd_s[:, 0].bitcast(U8), wd_s[:, 1].bitcast(U8)
        bias = sbuf("bias", [P, N // P], F32)
        with nc.allow_non_contiguous_dma(reason="one bias value for each partition and output tile"):
            load(bias[:], b.rearrange("(c p) -> p c", p=P))
        weight = sbuf("weight", [P, J], F32)
        load(weight[:, :GROUP], wgo[:, :GROUP])
        load(weight[:, GROUP:], wgo[:, GROUP:])

        round_wu(0, 1, 0, on_both, SECOND_WG)
        round_wu(0, 1, 2, on_both, ROWS[3])
        gates(0, 1, (3, 4), SECOND_WU)
        gates(0, 2, (5, 6), SECOND_WU + 4 * KIB)
        quantize_wu(0, 1, 0)
        quantize_wu(0, 1, 2)
        order_wg_words(1, on_vector, SECOND_WG)
        zero_rows(3, nc.gpsimd)

        first_h = sbuf("h0", [P, 3 * GROUP, PLACES], BF16)
        for g, banks in enumerate(((7, 0), (1, 2), (3, 4))):
            for c, ub in enumerate(up_sums(0, g, banks)):
                product(0, g, c, ub, first_h[:, GROUP * g : GROUP * (g + 1)])
        round_wu(1, 0, 0, all_on_scalar)
        round_wu(1, 0, 2, all_on_scalar)
        quantize_wu(1, 0, 0)
        round_wu(1, 1, 0, on_both, FIRST_CODES)
        round_wu(1, 1, 2, on_both)
        gates(1, 0, (5, 6), LAST_WU - KIB)
        gates(1, 1, (7, 0), LAST_WU + 3 * KIB)
        quantize_wu(1, 1, 0)
        quantize_wu(1, 0, 2, LAST_WU + 7 * KIB)
        quantize_wu(1, 1, 2)
        quantize_h([(0, 0), (0, 1)], first_h[:, :HALF], FIRST_CODES)

        h10 = sbuf("h10", [P, GROUP, PLACES], BF16, THIRD_CODES)
        for c, ub in enumerate(up_sums(1, 0, (1, 2))):
            product(1, 0, c, ub, h10)
        h11 = sbuf("h11", [P, GROUP, PLACES], BF16)
        ubs = up_sums(1, 1, (3, 4))
        gated = factor("late_gate", wg_columns, 1, 2, ACT.Sigmoid, (7, 0))
        product(1, 1, 0, ubs[0], h11)
        quantize_h([(1, 0)], h10[:])
        product(1, 1, 1, ubs[1], h11)
        quantize_h([(0, 2)], first_h[:, HALF:], THIRD_CODES)
        quantize_h([(1, 1)], h11[:])
        weighted = sbuf("y_weighted00", [P, GROUP], F32)
        y = down(0, [0], 5, (0, 1))
        nc.vector.scalar_tensor_tensor(weighted[:], y, bias[:, 0:1], weights([0]), ADD, MULT)

        nc.vector.tensor_copy(window(0, [0]), weighted[:])
        for n, number in ((1, 6), (2, 1), (3, 2)):
            weigh_on_gpsimd_and_scatter(n, 0, number)
        group_on_gpsimd(1, 2, gated, factor("late_up", wu_columns, 1, 2, ACT.Copy, (5, 6)))
        weigh_on_gpsimd_and_scatter(0, 1, 3)
        weigh_on_gpsimd_and_scatter(1, 1, 4)
        weigh_on_gpsimd_and_scatter(2, 1, 7, LATE_H[1, 2] + KIB)
        gated = factor("late_gate", wg_columns, 0, 3, ACT.Sigmoid, (1, 2))
        group_on_gpsimd(0, 3, gated, factor("late_up", wu_columns, 0, 3, ACT.Copy, (5, 6)))
        weigh_on_gpsimd_and_scatter(3, 1, 1)
        weigh_on_gpsimd_and_scatter(0, 2, 3)
        gated = factor("late_gate", wg_columns, 1, 3, ACT.Sigmoid, (4, 7))
        group_on_gpsimd(1, 3, gated, factor("late_up", wu_columns, 1, 3, ACT.Copy, (2, 5), LAST_UP))

        weigh_and_scatter(1, [2], add_bias(1, [2], 6, (1, 0), LAST_UP))
        for n, groups, number in ((0, [3], 0), (1, [3], 1), (2, [2, 3], 3), (3, [2, 3], 4)):
            weigh_and_scatter(n, groups, add_bias(n, groups, number, (0, 1)))
            load(out[P * n : P * (n + 1), :], rows[n][:])
